import numpy as np, ml_dtypes
CORES = [10,34,74,98]
N = 4
BF = ml_dtypes.bfloat16
def gentries(a):
    return np.ascontiguousarray(a.reshape(8, 16, -1).transpose(0, 2, 1)).reshape(8, -1)
def gtable(e):
    e = np.asarray(e); return np.ascontiguousarray(e.reshape(8, -1, 16).transpose(0, 2, 1)).reshape(128, -1).astype(np.int32)
W, L, RO, PE, ES, LAST = 4096, 256, 4, 2, 1, 1
def names(rng): return rng.integers(0, W, (N, 8, L, 16))
def pack(x, s, z):
    return {"cont": np.ascontiguousarray(np.reshape(x, (N, 128, W))).astype(np.float32).astype(BF),
            "enz": np.stack([gtable(a.reshape(8, -1)) for a in s]), "subs": np.stack([gtable(a.reshape(8, -1)) for a in z])}
def setup_inputs(rng):
    x = np.where(rng.random((N, 8, 1, W)) < 0.3, 51 * rng.integers(0, 6, (N, 8, 16, W)), rng.integers(0, 256, (N, 8, 16, W)))
    s, z = names(rng), names(rng); u = rng.random((N, 8, L, 1))
    z = np.where((u < 0.15) & (rng.random(z.shape) < 0.3), s[..., 15:], z)
    z = np.where((u > 0.9) & (rng.random(z.shape) < 0.5), z[..., 7:8], z)
    return pack(x, s, z)
def setup_inputs_spread(rng):
    x = np.minimum((np.exp2(3 + 5.5 * rng.random((N, 8, 1, W))) * rng.random((N, 8, 16, W))).astype(np.int64), 255)
    e = rng.choice(np.array([1.0, 1.5, 2.0, 3.0, 4.0]), (N, 8, 1, 1))
    s = np.minimum((W * rng.random((N, 8, L, 16)) ** e).astype(np.int64), W - 1)
    z = W - 1 - np.minimum((W * rng.random((N, 8, L, 16)) ** e).astype(np.int64), W - 1)
    return pack(x, s, z)
def setup_inputs_ends(rng):
    x = 255 * (rng.random((N, 8, 16, W)) < rng.choice(np.array([0.0, 0.1, 0.3, 0.5, 0.7, 0.9, 1.0]), (N, 8, 1, W)))
    near = (np.arange(16)[:, None] == rng.integers(0, 16, (N, 8, 1, W))) & (rng.random((N, 8, 1, W)) < 0.3)
    x = np.where(near, np.where(x == 0, 1, 254), x)
    m = np.stack([np.concatenate([rng.permutation(np.array([0, 10, 6, 8, 7, 9, 12])), np.array([16])]) for q in range(N)])
    top = np.argsort(rng.random((N, 8, 16)), axis=-1) < m[..., None]
    x[..., W - 1] = np.where(top, 255, 0); x[..., 0] = np.where(top, 0, 255)
    x[:, 7, :, W - 2] = 255; x[:, 7, 15, W - 2] = 254; x[:, 7, :, 1] = 0; x[:, 7, 0, 1] = 1
    x[:, 7, :, W - 3] = 255; x[:, 7, 14:, W - 3] = 254
    sz = []
    for i in range(2):
        fr = rng.choice(np.array([1.0, 0.6]), (N, 8, L, 1))
        sz.append(np.where(rng.random((N, 8, L, 16)) < fr, (W - 1) * rng.integers(0, 2, (N, 8, L, 16)), names(rng)))
    s, z = sz; alt = np.where(np.arange(16) & 1 == 1, W - 1, 0)
    for a, b, c in ((L - 1, L - 2, L - 3), (0, 1, 2)):
        s[:, 7, a] = W - 1 - alt; z[:, 7, a] = W - 1; z[:, 7, a, 9] = W - 2; z[:, 7, a, 15] = W - 2
        s[:, 7, b] = alt; z[:, 7, b] = 0
        s[:, 7, c] = alt; z[:, 7, c] = W - 1
        z[:, 7, c, 5] = W - 31
    for i, (p1, p2) in enumerate(((6, 11), (1, 14), (0, 15))):
        for a in (L - 4 - i, 3 + i):
            s[:, 7, a] = W - 1 - alt; z[:, 7, a] = W - 1; z[:, 7, a, p1] = W - 2; z[:, 7, a, p2] = W - 3
    return pack(x, s, z)
def setup_inputs_corners(rng):
    B = W // 16; kind = rng.integers(0, 7, (N, 8, B))
    for q in range(N):
        g = rng.permutation(8); kind[q, g[0]] = 0; kind[q, g[1]] = 3
    opts = ([0, 2, 4], [0, 2, 4], [5, 7, 9, 11], [6, 7, 8, 9], [10, 11, 12, 13], [5, 6, 7, 9, 10], list(range(17)))
    cs = np.zeros((N, 8, B, 16), np.int64)
    for i, o in enumerate(opts): cs = np.where(kind[..., None] == i, rng.choice(np.array(o), cs.shape), cs)
    cs[..., 0] = np.where(kind == 1, rng.choice(np.array([1, 3, 5]), kind.shape), cs[..., 0])
    down = (np.argsort(rng.random((N, 8, B, 16, 16)), axis=-1) < cs[..., None]).transpose(0, 1, 2, 4, 3).copy()
    down[..., 0] &= ~np.all(down, axis=-1)
    st = rng.integers(1, 17, down.shape); v = np.zeros(down.shape, np.int64); cur = np.full(down.shape[:-1], 255)
    for k in range(32):
        v[..., k & 15] = cur; cur = np.where(down[..., k & 15], cur - st[..., k & 15], 255)
    x = np.ascontiguousarray(v.transpose(0, 1, 3, 2, 4)).reshape(N, 8, 16, W)
    blk = np.concatenate([np.argsort(rng.random((N, 8, B)), axis=-1) for i in range(2)], axis=-1)[..., :L]
    rot = np.where(np.arange(L) < B, 0, rng.integers(0, 16, (N, 8, L)))
    s = 16 * blk[..., None] + ((np.arange(16) + rot[..., None]) & 15)
    inv = np.argsort(rng.random((N, 8, W)), axis=-1); new = np.argsort(inv, axis=-1)
    x = np.take_along_axis(x, inv[:, :, None], 3); s = np.take_along_axis(new, s.reshape(N, 8, -1), 2).reshape(N, 8, L, 16)
    one = rng.choice(np.array([0, W - 1, W // 2, 5]), (N, 8, L, 1)); s = np.where(rng.random((N, 8, L, 1)) < 0.1, one, s)
    z = names(rng); zk = rng.integers(0, 7, (N, 8, L, 1)); p = np.arange(16); own = s[..., 15:]
    z = np.where((zk == 1) & (p == 15), own, z); z = np.where((zk == 2) & ((p == 0) | (p == 15)), own, z)
    z = np.where(zk == 3, own, z); z = np.where(zk == 4, s, z)
    z = np.where(zk == 5, (W - 1) * rng.integers(0, 2, z.shape), z); z = np.where((zk == 6) & (p == rng.integers(0, 16, zk.shape)), own, z)
    return pack(x, s, z)
def setup_inputs_ties(rng):
    lev = np.array([[0, 1, 254, 255], [3, 4, 5, 250]])[np.arange(8) & 1]
    x = np.take_along_axis(np.broadcast_to(lev[None], (N, 8, 4)), rng.integers(0, 4, (N, 8, 16 * W)), 2).reshape(N, 8, 16, W)
    pool = rng.integers(0, W, (N, 8, 24)); pool[..., 0] = 0; pool[..., 1] = W - 1
    s = np.take_along_axis(pool, rng.integers(0, 24, (N, 8, L * 16)), 2).reshape(N, 8, L, 16)
    z = np.take_along_axis(pool, rng.integers(0, 24, (N, 8, L * 16)), 2).reshape(N, 8, L, 16)
    u = rng.random((N, 8, L, 1)); z = np.where(u < 0.2, s, z); z = np.where(u > 0.85, z[..., 3:4], z)
    return pack(x, s, z)
def setup_inputs_full(rng):
    B = W // 16; kind = np.stack([rng.permutation(np.array([0, 0, 0, 1, 1, 2, 2, 2])) for q in range(N)]); kind[0, 7] = 1; kind[N - 1, 7] = 0
    k4 = kind[:, :, None, None]
    cs = np.where(k4 == 0, rng.choice(np.array([10, 12, 14]), (N, 8, B, 16)), rng.integers(6, 16, (N, 8, B, 16)))
    cs[..., 0] += ((kind[:, :, None] == 0) & (rng.random((N, 8, B)) < 0.5)).astype(np.int64)
    t1 = np.argsort(rng.random((N, 8, B, 16)), axis=-1); t2 = np.argsort(rng.random((N, 8, B, 16)), axis=-1)
    down = ((t1[..., :, None] + t2[..., None, :]) & 15) < cs[..., None, :]
    st = rng.integers(1, 17, down.shape); v = np.zeros(down.shape, np.int64); cur = np.full(down.shape[:-1], 255)
    for k in range(32):
        v[..., k & 15] = cur; cur = np.where(down[..., k & 15], cur - st[..., k & 15], 255)
    x = np.ascontiguousarray(v.transpose(0, 1, 3, 2, 4)).reshape(N, 8, 16, W)
    blk = np.concatenate([np.argsort(rng.random((N, 8, B)), axis=-1) for i in range(2)], axis=-1)[..., :L]
    s = 16 * blk[..., None] + np.arange(16)
    inv = np.argsort(rng.random((N, 8, W)), axis=-1); new = np.argsort(inv, axis=-1)
    x = np.take_along_axis(x, inv[:, :, None], 3); s = np.take_along_axis(new, s.reshape(N, 8, -1), 2).reshape(N, 8, L, 16)
    hi = np.arange(W - 96, W); ok = ((hi[:, None] * np.arange(W) >> 5) & (W - 1)) + hi[:, None] + 77 == 2 * W
    made = np.where(np.any(ok, axis=1), np.argmax(ok, axis=1), -1); y = W - 32 + ((-((hi & 31) ** 7)) & 31)
    mate = np.full(W, -1); mate[W - 96:] = np.where(((hi & 1) == 1) & (hi * (y + 32) > 2 ** 24), y, made)
    zu = np.where(mate[s] >= 0, mate[s], names(rng)); zu[..., 0] = s[..., 15]
    way = 1 - 2 * (np.take_along_axis(cs[..., 0], blk, 2) & 1)
    p = (rng.integers(0, 16, (N, 8, L, 1)) + way[..., None] * np.arange(16)) & 15
    z = np.take_along_axis(zu, np.argsort(p, axis=-1), 3)
    z = np.where(rng.random((N, 8, L, 1)) < 0.75, z, names(rng))
    pm = np.argsort(rng.random((N, 8, W)), axis=-1); cl = (np.argsort(pm, axis=-1) >> 9)[:, :, None]
    few = rng.integers(0, 4, (N, 8, 16, W)); x2 = rng.integers(0, 256, (N, 8, 16, W)); x2 = np.where(cl == 0, few, x2)
    for i, b in ((1, 134), (2, 198), (3, 255)): x2 = np.where(cl == i, b - few, x2)
    s2 = names(rng); s2[..., 15] = np.take_along_axis(pm, rng.integers(0, 512, (N, 8, L)), 2)
    zi = 512 * rng.integers(1, 4, (N, 8, L, 1)) + rng.integers(0, 512, (N, 8, L, 16))
    z2 = np.take_along_axis(pm, zi.reshape(N, 8, -1), 2).reshape(N, 8, L, 16)
    return pack(np.where(k4 == 2, x2, x), np.where(k4 == 2, s2, s), np.where(k4 == 2, z2, z))
def check_inputs(d):
    bad = []
    c = np.asarray(d["cont"]).astype(np.float32)
    if not np.all((c >= 0) & (c <= 255)): bad.append("range of cont")
    elif not np.all(c == np.floor(c)): bad.append("whole numbers in cont")
    for k in ("enz", "subs"):
        if np.min(d[k]) < 0 or np.max(d[k]) > W - 1: bad.append("range of " + k)
    return bad
def edit(x, s, z, a, t):
    v = np.take_along_axis(x, s.reshape(8, 1, -1), 2).reshape(8, 16, L, 16)
    y = np.take_along_axis(x, z.reshape(8, 1, -1), 2).reshape(8, 16, L, 16)
    c = np.sum((v > np.roll(v, -1, axis=3)).astype(np.int64), axis=1)
    dist = np.sum(np.abs(y - v[..., 15:16]).astype(np.int64), axis=1)
    step = 1 - 2 * (np.add.accumulate(c, axis=2) & 1); step[..., 0] = np.argmin(dist, axis=2)
    pos = np.add.accumulate(step, axis=2) & 15
    hit = pos[:, :, None, :] == np.arange(16)[:, None]
    e = 15 - np.argmax(hit[..., ::-1], axis=3) if LAST else np.argmax(hit, axis=3)
    has = np.any(hit, axis=3); ce = np.take_along_axis(c, e, 2); se = np.take_along_axis(s, e, 2)
    gone = has & (ce <= 5 + (a & 1)[..., None])
    new = np.where(has, np.where(ce <= 9, se, ((se * z >> 5) + se + 77 * t) & (W - 1)), z)
    n = np.sum(gone.astype(np.int64), axis=2); i = np.arange(16) - (16 - n)[..., None]
    kept = np.take_along_axis(new, np.argsort(gone, axis=2, kind="stable"), 2)
    return np.where(i < 0, kept, np.take_along_axis(s, np.maximum(i, 0), 2)), n
def reference(cont, enz, subs):
    x = cont.astype(np.float32).astype(np.int16).reshape(N, 8, 16, W)
    s = np.stack([gentries(a) for a in enz]).astype(np.int64).reshape(N, 8, L, 16)
    z = np.stack([gentries(a) for a in subs]).astype(np.int64).reshape(N, 8, L, 16)
    dels = np.zeros((N, 8, L), np.int64)
    for t in range(1, RO + 1):
        both = [edit(x[r], s[r], z[r], dels[r], t) for r in range(N)]
        dels = np.stack([b[1] for b in both])
        z = np.roll(s, ES, axis=0)
        s = np.roll(np.stack([b[0] for b in both]), PE, axis=0)
    return {"yenz": np.stack([gtable(a.reshape(8, -1)) for a in s]).astype(np.float32), "ysub": np.stack([gtable(a.reshape(8, -1)) for a in z]).astype(np.float32)}

@@ -1,0 +1,616 @@
+import math
+from concourse.mybir import AluOpType as A, ActivationFunctionType as AF
+
+RO, LH = 4, 128
+NH = 2
+FV, FS = 20.0, 30.0
+SC = 0.83
+PC = 0.5
+GC = 1.35
+NET = 4500.0
+LAG = 150.0
+RW, BONUS = 10500.0, {"XB": 1500.0, "AB": -5000.0, "po": -8000.0, "h": 1500.0, "km": 5000.0, "fi": -8000.0, "E2": 5000.0, "d": 5000.0, "X": 12000.0,
+                      "q1": 5000.0, "F": 3000.0, "ps": -1500.0, "S": 1500.0, "PP": 3000.0, "pr": 3000.0, "Y": -1500.0, "hS": -1500.0}
+NV = 12
+VCUT = [("S", 32), ("V", 32), ("S", 32), ("S", 32)]
+YCUT = [("S", 32)] * 4
+SCRATCH, SEMAPHORES = {}, []
+
+
+def _sb(name, cols, dtype="bfloat16"):
+    SCRATCH[name] = ("sbuf", [128, cols], dtype)
+
+
+F32, BF, I32, U16, F16 = "float32", "bfloat16", "int32", "uint16", "float16"
+_sb("ct", 4096)
+_sb("ei", 256, I32); _sb("zi", 256, I32)
+_sb("eo", 1280, U16); _sb("es", 1280, F16); _sb("zo", 1280, U16); _sb("zs", 1280, F16)
+_sb("po", 1024, U16); _sb("ps", 768, F16)
+_sb("pz", 256, F32); _sb("ef", 256, F32); _sb("yz", 256, F32)
+CB = {}
+for _n, _w in [("I", 128), ("nI", 128), ("I128", 128), ("p127", 128), ("p128", 128), ("m127", 128), ("m128", 128), ("m4096", 128), ("m64", 128),
+               ("p32", 128), ("P2", 128), ("Sp", 128), ("ones", 128), ("c16", 128), ("cD", 128), ("cC", 256), ("neg", 128), ("pos", 128),
+               ("keep", 128), ("b16", 16), ("b16x", 16)]:
+    CB[_n] = (sum(w for _, w in CB.values()), _w)
+_sb("cb", sum(w for _, w in CB.values()))
+CF = {}
+for _n in ("DA", "DB", "TC", "TS", "IV", "IF"):
+    CF[_n] = (128 * len(CF), 128)
+_sb("cf", 128 * len(CF), F32)
+CH = {}
+for _n, _w in [("b128", 16), ("b1", 16), ("I", 128), ("tri", 128), ("odd", 128)] + [(_x + _y, 128) for _y in "hl" for _x in ("DA", "DB", "TC", "TS")]:
+    CH[_n] = (sum(w for _, w in CH.values()), _w)
+_sb("ch", sum(w for _, w in CH.values()), F16)
+_sb("b8", 8, F32)
+_sb("col", 16, F32)
+for _n, _w, _d in (("KI", 128, F32), ("KD", 128, F32), ("KT", 128, F32), ("UM", 128, F32), ("GG", 128, F32), ("t1", 128, F32),
+                   ("t2", 128, F32), ("ki", 128, I32), ("pi", 2, I32), ("K8", 8, F32), ("u16f", 16, F32), ("f16", 16, F32), ("im16", 16, F32),
+                   ("n80", 80, F32), ("n80i", 80, I32), ("w80", 80, F32), ("x80", 80, F32), ("a80", 80, F32)):
+    _sb("k_" + _n, _w, _d)
+for _h in range(NH):
+    for _n, _w, _d in (("V", 2048, BF), ("Y", 2048, BF), ("cmp", 2048, BF), ("mx", 2048, BF), ("PA", 2048, F16), ("PB", 2048, F16), ("km", 128, F32),
+                       ("r8", 8, F32), ("d", 128, BF), ("q1", 128, BF), ("q2", 128, BF), ("r", 128, F32), ("X", 128, BF), ("Mx", 128, BF),
+                       ("Mn", 128, BF), ("LT", 128, BF), ("r16", 128, BF), ("hS", 128, BF), ("XA", 256, F16), ("XB", 256, F16), ("v", 128, I32),
+                       ("S", 128, I32), ("cd", 128, I32), ("q", 128, F32), ("Zq", 128, F32), ("pr", 128, I32), ("F", 128, I32), ("m2", 128, F32),
+                       ("val", 128, F32), ("del", 128, BF), ("E2", 128, BF), ("h2", 128, BF), ("EL", 128, BF), ("h", 128, F16),
+                       ("AB", 256, F32), ("PP", 256, F32), ("fi", 128, F32), ("fm", 128, F32), ("w", 128, I32), ("pi", 128, I32), ("pf", 128, F16)):
+        _sb("%s%d" % (_n, _h), _w, _d)
+    for _n in "abcd":
+        SCRATCH["ps%s%d" % (_n, _h)] = ("psum", [128, 512], F32)
+SEMAPHORES += ["qP", "qV", "qS", "qG", "ld0", "ld1", "ld2", "snt", "out"]
+for _t in range(1, RO + 1):
+    for _h in range(NH):
+        SEMAPHORES += ["%s%d%d" % (_k, _t, _h) for _k in ("eo", "es", "zo", "zs")]
+
+
+def R(buf, c0, c1, step=1):
+    return (buf, c0, c1, step)
+
+
+def cb(n, lo=0, hi=None):
+    c, w = CB[n]
+    return R("cb", c + lo, c + (w if hi is None else hi))
+
+
+def cf(n):
+    c, w = CF[n]
+    return R("cf", c, c + w)
+
+
+def ch(n, w=None):
+    return R("ch", CH[n][0], CH[n][0] + (w or CH[n][1]))
+
+
+def ap(T, r):
+    if r[3] == -1:
+        return T[r[0]][:, r[2] - 1:r[1] - 1:-1] if r[1] else T[r[0]][:, r[2] - 1::-1]
+    return T[r[0]][:, r[1]:r[2]:r[3]] if r[3] != 1 else T[r[0]][:, r[1]:r[2]]
+
+
+def ncol(r):
+    s = abs(r[3])
+    return (r[2] - r[1] + s - 1) // s
+
+
+def dts(r):
+    return SCRATCH[r[0]][2]
+
+
+def isp(r):
+    return SCRATCH[r[0]][0] == "psum"
+
+
+OPS, MARK = [], []
+
+
+def op(eng, dur, fns, reads, writes, sem=None, inc=1, dep=None):
+    OPS.append({"e": eng, "d": dur, "f": fns, "r": reads, "w": writes, "sem": sem, "inc": inc, "dep": dep})
+    return len(OPS) - 1
+
+
+def two(rs):
+    return all(dts(r) in (BF, F16, U16) and not isp(r) for r in rs)
+
+
+def cyc(n, x):
+    return n * x * SC + FV
+
+
+def ts(out, a, s1, op0, s2=None, op1=None):
+    cols = [s for s in (s1, s2) if isinstance(s, tuple)]
+
+    def f(g, T):
+        x = ap(T, s1) if isinstance(s1, tuple) else s1
+        y = ap(T, s2) if isinstance(s2, tuple) else s2
+        if op1 is None:
+            return g.vector.tensor_scalar(ap(T, out), ap(T, a), x, None, op0)
+        return g.vector.tensor_scalar(ap(T, out), ap(T, a), x, y, op0, op1)
+    return op("V", cyc(ncol(out), 0.5 if two([out, a]) else 1), [f], [a] + cols, [out])
+
+
+def tt(out, a, b, o):
+    return op("V", cyc(ncol(out), 1 if isp(a) or isp(b) else 2), [lambda g, T: g.vector.tensor_tensor(ap(T, out), ap(T, a), ap(T, b), o)], [a, b], [out])
+
+
+def cp(out, a):
+    return op("V", cyc(ncol(out), 0.5 if two([out, a]) else 1), [lambda g, T: g.vector.tensor_copy(ap(T, out), ap(T, a))], [a], [out])
+
+
+def fill(out, c):
+    return op("V", cyc(ncol(out), 0.5), [lambda g, T: g.vector.memset(ap(T, out), c)], [], [out])
+
+
+def scan(out, d0, d1, o0, o1):
+    return op("V", cyc(ncol(out), 0.5 if two([out, d0, d1]) else 1),
+              [lambda g, T: g.vector.tensor_tensor_scan(ap(T, out), ap(T, d0), ap(T, d1), 0.0, o0, o1)], [d0, d1], [out])
+
+
+def act(out, a, func, bias=None, scale=None):
+    def f(g, T):
+        kw = {}
+        if bias is not None:
+            kw["bias"] = bias
+        if scale is not None:
+            kw["scale"] = ap(T, scale) if isinstance(scale, tuple) else scale
+        return g.scalar.activation(ap(T, out), ap(T, a), func, **kw)
+    return op("S", ncol(out) * SC + FS, [f], [a] + ([scale] if isinstance(scale, tuple) else []), [out])
+
+
+def gather(eng, out, offs):
+    n = ncol(out)
+    if eng == "S":
+        f = lambda g, T: g.scalar.activation(ap(T, out), T["ct"][:, 0:4096].indirect(ap(T, offs)), AF.Copy)
+    else:
+        f = lambda g, T: g.vector.tensor_copy(ap(T, out), T["ct"][:, 0:4096].indirect(ap(T, offs)))
+    return op(eng, n * GC * SC + 60, [f], [R("ct", 0, 4096), offs], [out])
+
+
+def mm(lst):
+    fns, rd, wr, d = [], [], [], 0.0
+    for out, l, r, st, sp in lst:
+        fns.append(lambda g, T, out=out, l=l, r=r, st=st, sp=sp: g.tensor.matmul(ap(T, out), ap(T, l), ap(T, r), st, sp))
+        rd += [l, r]; wr.append(out)
+        d += max(64, ncol(r)) * PC * (4 if dts(l) == F32 else 1)
+    return op("P", d, fns, rd, wr)
+
+
+def group(out, terms):
+    return [(out, l, r, i == 0, i == len(terms) - 1) for i, (l, r) in enumerate(terms)]
+
+
+def iota(out, pattern, base, cm):
+    kw = {} if dts(out) == I32 else {"allow_small_or_imprecise_dtypes": True}
+    return op("G", 130 + 2 * ncol(out) * SC, [lambda g, T: g.iota(ap(T, out), pattern, base, cm, **kw)], [], [out])
+
+
+def constants():
+    K = lambda n, w: R("k_" + n, 0, w)
+    KI, KD, KT, UM, GG, t1, t2 = [K(n, 128) for n in ("KI", "KD", "KT", "UM", "GG", "t1", "t2")]
+    ki, pi, K8 = K("ki", 128), K("pi", 2), K("K8", 8)
+    col = lambda j: R("col", j, j + 1)
+    iota(KI, [[-16, 8], [0, 16]], 0, 1)
+    iota(KD, [[1, 128]], 0, -1)
+    iota(K8, [[-16, 8]], 0, 1)
+    iota(UM, [[0, 8], [1, 16]], 0, 0)
+    iota(pi, [[0, 2]], 0, 1)
+    iota(KT, [[16, 8], [1, 16]], 0, -1)
+    for n, c in (("I", 1.0), ("nI", -1.0), ("I128", 1.0 / 128), ("p127", 127.0), ("p128", 128.0), ("m127", -127.0), ("m128", -128.0), ("m4096", -4096.0), ("m64", -32.0), ("p32", 16.0)):
+        if n == "I":
+            ts(cb(n), KD, 0.0, A.is_equal)
+        else:
+            act(cb(n), cb("I"), AF.Copy, scale=c)
+    fill(cb("ones"), 1.0); fill(cb("c16"), 16.0); fill(cb("cC"), 0.0)
+    ts(R("cb", CB["cC"][0], CB["cC"][0] + 128), UM, 0.0, A.is_equal, -1.0 / 128, A.mult)
+    b8, t8 = R("b8", 0, 8), R("k_t1", 0, 8)
+    ts(t8, K8, 0.0, A.is_ge)
+    ts(b8, K8, 15.0, A.is_le)
+    tt(b8, b8, t8, A.mult)
+    for half in (0, 8):
+        act(cb("b16", half, half + 8), b8, AF.Copy)
+    act(cb("b16x", 0, 8), b8, AF.Copy, scale=16.0)
+    ts(ch("b128", 8), b8, 128.0, A.mult)
+    ts(ch("b1", 8), b8, 1.0, A.mult)
+    cp(ch("I"), cb("I"))
+    ts(GG, KI, 0.0, A.is_ge)
+    ts(t1, KI, 15.0, A.is_le)
+    tt(GG, GG, t1, A.mult)
+    ts(t1, UM, 7.5, A.subtract, 1.0 / 128, A.mult)
+    cp(cb("cD"), t1)
+    ts(cb("neg"), UM, 0.0, A.is_equal, -1000.0, A.mult)
+    ts(cb("pos"), UM, 0.0, A.is_equal, 1048576.0, A.mult)
+    ts(cb("keep"), UM, 1.0, A.is_ge)
+    cp(ki, KI)
+    ts(ki, ki, 1, A.bitwise_and)
+    tt(t1, ki, GG, A.mult)
+    ts(ch("odd"), t1, -2.0, A.mult)
+    ts(cb("P2"), KI, 15.0, A.is_equal)
+    ts(t1, KD, 0.0, A.is_equal, 4096.0, A.mult)
+    ts(t2, KD, -1.0, A.is_equal, 4096.0, A.mult)
+    tt(t1, t1, t2, A.subtract)
+    ts(t2, UM, 14.0, A.is_le)
+    tt(cb("Sp"), t1, t2, A.mult)
+    act(cf("IF"), cb("I"), AF.Copy)
+    ts(t1, KT, 0.0, A.is_ge)
+    tt(ch("tri"), t1, GG, A.mult)
+    ts(pi, pi, 15, A.bitwise_and)
+    ri = col(0)
+    cp(ri, R("k_pi", 0, 1))
+    ts(col(1), ri, 14.0, A.is_le, -4096.0, A.mult)
+    ts(col(2), col(1), 960.0 + 16512.0 + 2048.0, A.add)
+    ts(col(1), col(1), 127 * 7.5 + 96 - 129 - 16, A.add)
+    ts(col(3), ri, 127.0, A.mult, -129.0, A.add)
+    ts(col(4), ri, 128.0, A.mult, 16512.0, A.add)
+    ts(col(5), ri, -1.0, A.mult, 16.0, A.add)
+    u, f16, im = K("u16f", 16), K("f16", 16), K("im16", 16)
+    cp(u, R("k_UM", 0, 16))
+    ts(im, u, 9.0, A.is_ge)
+    ts(f16, im, -8.0, A.mult)
+    tt(f16, f16, u, A.add)
+    ts(im, im, 4.0, A.mult)
+    ts(col(6), ri, 9.0, A.is_ge)
+    ts(col(7), col(6), -8.0, A.mult)
+    tt(col(7), col(7), ri, A.add)
+    ts(col(6), col(6), 4.0, A.mult)
+    ts(col(8), col(7), 0.0, A.is_equal)
+    ts(col(9), col(7), 8.0, A.is_equal)
+    tt(col(8), col(8), col(9), A.add)
+    ts(col(8), col(8), -1.0 / 16, A.mult, 2.0 / 16, A.add)
+    n = lambda j: R("k_n80", 16 * j, 16 * j + 16)
+    ts(n(2), f16, ri, A.mult)
+    tt(n(0), n(2), im, A.add)
+    ts(n(1), n(0), 4.0, A.add)
+    ts(n(3), n(2), 12.0, A.add)
+    ts(n(4), u, col(7), A.mult, col(6), A.add)
+    N, NI, W, X2, AC = K("n80", 80), K("n80i", 80), K("w80", 80), K("x80", 80), K("a80", 80)
+    cp(NI, N)
+    ts(NI, NI, 15, A.bitwise_and)
+    cp(N, NI)
+    ts(W, N, -1.0, A.mult, 16.0, A.add)
+    tt(W, W, N, A.min)
+    ts(W, W, -1.0, A.mult, 4.0, A.add)
+    tt(X2, W, W, A.mult)
+    cc = [(-1) ** k * (math.pi / 8) ** (2 * k + 1) / math.factorial(2 * k + 1) for k in range(7)]
+    ts(AC, X2, cc[6], A.mult, cc[5], A.add)
+    for k in (4, 3, 2, 1, 0):
+        tt(AC, AC, X2, A.mult)
+        ts(AC, AC, cc[k], A.add)
+    tt(AC, AC, W, A.mult)
+    iv = R("k_a80", 64, 80)
+    ts(iv, iv, col(8), A.mult)
+    for j, name in enumerate(("DA", "DB", "TC", "TS", "IV")):
+        c = CF[name][0]
+        for q in range(8):
+            act(R("cf", c + 16 * q, c + 16 * q + 16), R("k_a80", 16 * j, 16 * j + 16), AF.Copy, scale=R("b8", q, q + 1))
+    hi, lo = R("ch", CH["DAh"][0], CH["DAh"][0] + 512), R("ch", CH["DAl"][0], CH["DAl"][0] + 512)
+    cp(hi, R("cf", 0, 512))
+    tt(lo, R("cf", 0, 512), hi, A.subtract)
+
+
+M4, M16 = 1.5 * 2 ** 25, 1.5 * 2 ** 27
+
+
+def half_round(t, h, hop):
+    MARK.append((len(OPS), 2 * t + h))
+    b = lambda n, lo=0, hi=128: R("%s%d" % (n, h), lo, hi)
+    pa, pb, pc, pd = ["ps%s%d" % (x, h) for x in "abcd"]
+    q = lambda p, j, k=1: R(p, 128 * j, 128 * (j + k))
+    o = 256 * (t - 1) + 128 * h
+    eo, es, zo, zs = R("eo", o, o + 128), R("es", o, o + 128), R("zo", o, o + 128), R("zs", o, o + 128)
+    col = lambda j: R("col", j, j + 1)
+    hop(t, h, "z")
+    for buf, ls, cuts in (("V", (eo[0], eo[1]), VCUT), ("Y", (zo[0], zo[1]), YCUT)):
+        c = 0
+        for eng, w in cuts:
+            gather(eng, b(buf, 16 * c, 16 * (c + w)), R(ls[0], ls[1] + c, ls[1] + c + w))
+            c += w
+    ts(b("hS"), es, 2048 + 16448.5, A.add)
+    v15 = R("V%d" % h, 15, 2048, 16)
+    for c in range(0, 16 - NV, 4):
+        for j in range(4):
+            mm(group(q(pd, j), [(cb("I"), R("Y%d" % h, c + j, 2048, 16)), (cb("nI"), v15)]))
+        act(b("mx", 128 * c, 128 * c + 512), q(pd, 0, 4), AF.Abs)
+    if NV:
+        mm([(q(pc, 0), cb("I"), v15, True, True)])
+        for p in range(16 - NV, 16):
+            tt(b("mx", 128 * p, 128 * p + 128), R("Y%d" % h, p, 2048, 16), q(pc, 0), A.subtract)
+        for p in range(16 - NV, 16, 4):
+            x = b("mx", 128 * p, 128 * min(16, p + 4))
+            act(x, x, AF.Abs)
+    mm([(q(pd, 1), cb("ones"), cb("cD"), True, False)])
+    for p in range(16):
+        mm([(R(pd, 128 + p, 256, 16), b("mx", 128 * p, 128 * p + 128), cb("b16x", 0, 8), False, p == 15)])
+    scan(b("km"), cb("pos"), q(pd, 1), A.add, A.min)
+    km = R("km%d" % h, 15, 128, 16)
+    ts(b("r8", 0, 8), km, M16, A.add, M16, A.subtract)
+    for c in range(4):
+        bank = pa if c % 2 == 0 else pb
+        for j in range(4):
+            k = 4 * c + j
+            mm(group(q(bank, j), [(cb("I"), R("V%d" % h, k, 2048, 16)), (cb("nI"), R("V%d" % h, (k + 1) % 16, 2048, 16))]))
+        act(b("cmp", 512 * c, 512 * c + 512), q(bank, 0, 4), AF.Sign, -0.5)
+    mm([(q(pa, 0, 2), cb("ones"), cb("cC"), True, False)] + ([(q(pa, 1), b("h"), ch("odd"), False, False)] if t > 1 else []))
+    for k in range(0, 16, 4):
+        mm([(R(pa, j, 256, 16), b("cmp", 128 * j, 128 * j + 128), cb("b16"), False, j == 15) for j in range(k, k + 4)])
+    act(b("q1"), q(pa, 1), AF.Sign, 5.0)
+    act(b("q2"), q(pa, 0), AF.Sign, -2.5)
+    scan(q(pc, 0), cb("keep"), q(pa, 0), A.mult, A.add)
+    ts(b("r"), q(pc, 0), M4, A.add, M4, A.subtract)
+    tt(b("d"), b("r"), q(pc, 0), A.subtract)
+    tt(R("d%d" % h, 0, 128, 16), km, b("r8", 0, 8), A.subtract)
+    scan(b("X"), cb("keep"), b("d"), A.mult, A.add)
+    rev = lambda n: R("%s%d" % (n, h), 0, 128, -1)
+    scan(rev("Mx"), cb("neg"), rev("X"), A.add, A.max)
+    scan(rev("Mn"), cb("pos"), rev("X"), A.add, A.min)
+    ts(b("r16"), b("X"), M16, A.add, M16, A.subtract)
+    mm(group(q(pb, 0), [(b("Mx"), cb("I")), (b("Mn"), cb("nI"))]))
+    act(b("LT"), q(pb, 0), AF.Copy)
+    XA, XB = q(pc, 1), q(pd, 2)
+    mm([(XA, b("q1"), cb("m64"), True, False), (XA, b("q2"), cb("p32"), False, False), (XA, cb("I128"), b("hS"), False, False)])
+    mm([(XB, ch("I"), es, True, False), (XB, cb("nI"), b("hS"), False, False)])
+    mm([(XA, b("X"), cb("p127"), False, False), (XA, b("r16"), cb("m127"), False, False)])
+    mm([(XB, b("X"), cb("p128"), False, False), (XB, b("r16"), cb("m128"), False, False)])
+    mm([(XA, cb("Sp"), b("LT"), False, True)])
+    mm([(XB, cb("Sp"), b("LT"), False, True)])
+
+    def keys(ka, kb, ca, cc):
+        ts(b("XA"), ka, ca, A.add)
+        ts(b("XA", 128, 256), ka, ca, A.add, -8 * 127.0, A.add)
+        ts(b("XB"), kb, cc, A.add)
+        ts(b("XB", 128, 256), kb, cc, A.add, -8 * 128.0, A.add)
+
+    def route(bank):
+        for p in range(8):
+            ts(b("PA", 256 * p, 256 * p + 256), b("XA", 0, 256), 127.0 * p, A.max, 127.0 * (p + 1), A.min)
+            ts(b("PB", 256 * p, 256 * p + 256), b("XB", 0, 256), 128.0 * p, A.max, 128.0 * (p + 1), A.min)
+            for k in (0, 1):
+                c = 256 * p + 128 * k
+                mm(group(R(bank, p + 8 * k, 128, 16), [(b("PA", c, c + 128), ch("b128", 8)), (b("PB", c, c + 128), ch("b1", 8))]))
+
+    keys(XA, XB, col(1), col(2))
+    mm(group(q(pc, 2), [(ch("DAh"), es), (ch("DAl"), es)]) + group(q(pc, 3), [(ch("DBh"), es), (ch("DBl"), es)]))
+    act(b("AB", 0, 256), q(pc, 2, 2), AF.Copy)
+    mm(group(q(pa, 0), [(zs, ch("I")), (cb("ones"), cb("c16"))]))
+    route(pd)
+    cp(b("v"), q(pd, 0))
+    ts(b("S"), b("v"), 4095, A.bitwise_and)
+    ts(b("cd"), b("v"), 12, A.arith_shift_right, 3, A.bitwise_and)
+    tt(b("pr"), b("S"), q(pa, 0), A.mult)
+    ts(b("del"), b("cd"), 3.0, A.is_ge)
+    ts(b("F"), b("pr"), 5, A.arith_shift_right, 4095, A.bitwise_and)
+    ts(q(pa, 1), b("cd"), 2.0, A.is_ge)
+    scan(b("E2"), cb("keep"), b("del"), A.mult, A.add)
+    ts(q(pa, 2), b("cd"), 2.0, A.is_ge, 77.0 * t, A.mult)
+    ts(b("q"), b("cd"), 0.0, A.is_equal)
+    tt(b("m2"), b("S"), q(pa, 2), A.add)
+    tt(q(pa, 3), b("q"), q(pa, 0), A.mult)
+    tt(q(pa, 2), b("m2"), q(pa, 3), A.add)
+    tt(b("Zq"), b("F"), q(pa, 1), A.mult)
+    tt(b("val"), b("Zq"), q(pa, 2), A.add)
+    act(b("h2"), b("val"), AF.Identity, 16448.5)
+    XA, XB = q(pb, 0), q(pc, 2)
+    mm([(XA, b("E2"), cb("m127"), True, False), (XA, b("del"), cb("m4096"), False, False)])
+    mm([(XB, b("E2"), cb("m128"), True, False), (XB, b("del"), cb("m4096"), False, False)])
+    mm(group(q(pd, 3), [(b("E2"), cb("I"))]))
+    act(b("EL"), q(pd, 3), AF.Copy)
+    mm(group(q(pd, 2), [(cb("P2"), b("EL"))]))
+    ts(b("h"), q(pd, 2), col(5), A.is_equal)
+    mm([(XB, b("val"), cf("IF"), False, False)])
+    mm([(XA, b("h2"), cb("I128"), False, True)])
+    mm([(XB, b("h2"), cb("nI"), False, True)])
+    keys(XA, XB, col(3), col(4))
+    mm(group(q(pd, 0), [(ch("TCh"), b("h")), (ch("TCl"), b("h"))]) + group(q(pd, 1), [(ch("TSh"), b("h")), (ch("TSl"), b("h"))]) +
+       group(q(pd, 2), [(b("h"), ch("tri"))]))
+    tt(b("PP", 0, 256), b("AB", 0, 256), q(pd, 0, 2), A.mult)
+    mm(group(q(pc, 0), [(b("PP", 0, 128), cf("IV")), (b("PP", 128, 256), cf("IV"))]))
+    act(b("fi"), q(pc, 0), AF.Copy, 2048.0)
+    tt(b("fm"), b("fi"), q(pd, 2), A.mult)
+    route(pb)
+    tt(b("w"), b("fm"), q(pb, 0), A.add)
+    ts(b("pi"), b("w"), 4095, A.bitwise_and)
+    ts(b("pf"), b("pi"), -2048.0, A.add)
+    mm(group(q(pa, 0), [(b("pf"), ch("I"))]))
+    if t < RO:
+        ts(R("po", o, o + 128), q(pa, 0), 2048.0, A.add)
+        cp(R("ps", o, o + 128), q(pa, 0))
+    else:
+        act(R("pz", 128 * h, 128 * h + 128), q(pa, 0), AF.Copy, 2048.0)
+    hop(t, h, "e")
+
+
+def build():
+    def load(q, sem, dst, src):
+        op(q, 60, [lambda g, T: g.sync.dma_start(ap(T, dst), T[src][:])], [], [("dma_" + sem, 0, 1, 1)])
+        op("X", 2500, [], [("dma_" + sem, 0, 1, 1)], [dst], sem=sem, inc=16)
+
+    load("Y", "ld0", R("ei", 0, 256), "enz")
+    load("Y", "ld1", R("ct", 0, 4096), "cont")
+    load("Y", "ld2", R("zi", 0, 256), "subs")
+
+    def send(dst_of, src, dst, sem):
+        def f(g, T, core, topo):
+            to = T.cores[(T.rank_of(core) + dst_of) % len(T.cores)]
+            rid, pid, _ = topo.addr(to)
+            m = sum(1 << e for e in topo.engines(core, to))
+            g.remote_dma(ap(T, dst), ap(T, src), T.sem[sem], T.sem.snt, pid, rid, m)
+            return bin(m).count("1")
+        op("R", 1000, [f], [src], [("net_" + sem, 0, 1, 1)])
+        op("X", NET, [], [("net_" + sem, 0, 1, 1)], [dst], sem=sem, inc=8)
+
+    def hop(t, h, kind):
+        o = 256 * (t - 1) + 128 * h
+        n = o + 256
+        for x in ("o", "s"):
+            if x == "o" and t == RO:
+                continue
+            s = (kind + x if kind == "z" else kind + x) + "%d%d" % (t, h)
+            src = ("e" + x) if kind == "z" else ("p" + x)
+            if kind == "e" and t == RO:
+                send(2, R("pz", 128 * h, 128 * h + 128), R("ef", 128 * h, 128 * h + 128), s)
+            else:
+                send(1 if kind == "z" else 2, R(src, o, o + 128), R(kind + x, n, n + 128), s)
+
+    for k in "ez":
+        for h in range(NH):
+            c = R(k + "i", 128 * h, 128 * h + 128)
+            cp(R(k + "o", 128 * h, 128 * h + 128), c)
+            ts(R(k + "s", 128 * h, 128 * h + 128), c, -2048.0, A.add)
+    constants()
+    for t in range(1, RO + 1):
+        for h in range(NH):
+            half_round(t, h, hop)
+    o = 256 * RO
+    for h in range(NH):
+        ts(R("yz", 128 * h, 128 * h + 128), R("zs", o + 128 * h, o + 128 * h + 128), 2048.0, A.add)
+    for src, dst in (("yz", "ysub"), ("ef", "yenz")):
+        for h in range(NH):
+            op("Y", 60, [lambda g, T, src=src, dst=dst, h=h: g.sync.dma_start(T[dst][:, 128 * h:128 * h + 128], T[src][:, 128 * h:128 * h + 128])],
+               [R(src, 128 * h, 128 * h + 128)], [], sem="out", inc=16)
+
+
+def analyse():
+    hist = {}
+    for i, x in enumerate(OPS):
+        deps = {}
+        if x["dep"] is not None:
+            deps[x["dep"]] = True
+        acc = [(r, False) for r in x["r"]] + [(w, True) for w in x["w"]]
+        for (buf, lo, hi, stp), wr in acc:
+            psum = buf in SCRATCH and SCRATCH[buf][0] == "psum"
+            for (l2, h2, s2, w2, j) in hist.get(buf, []):
+                over = lo < h2 and l2 < hi
+                y = OPS[j]
+                if over and stp == s2 and stp > 1 and (lo - l2) % stp != 0:
+                    over = False
+                if psum and y["e"] != x["e"]:
+                    deps[j] = True
+                elif psum and x["e"] == "P":
+                    deps[j] = deps.get(j, False)
+                elif over and w2 and not wr:
+                    deps[j] = True
+                elif over and (wr or w2):
+                    deps[j] = deps.get(j, False) or y["e"] != x["e"] or x["e"] != "P"
+        x["deps"] = deps
+        for (buf, lo, hi, stp), wr in acc:
+            lst = hist.setdefault(buf, [])
+            psum = buf in SCRATCH and SCRATCH[buf][0] == "psum"
+            if wr and stp == 1:
+                lst[:] = [e for e in lst if not (lo <= e[0] and e[1] <= hi and not (psum and OPS[e[4]]["e"] != x["e"] and False)) or e[4] == i]
+            if psum and wr and x["e"] == "P" and lo == 0 and False:
+                lst.clear()
+            lst.append((lo, hi, stp, wr, i))
+            if psum:
+                while len(lst) > 400:
+                    lst.pop(0)
+
+
+def schedule(rw=RW, bonus=BONUS):
+    n = len(OPS)
+    rk = [0] * n
+    for (a, k), (z, _) in zip(MARK, MARK[1:] + [(n, 0)]):
+        for i in range(a, z):
+            rk[i] = k
+    succ, nd = [[] for _ in range(n)], [0] * n
+    for i, x in enumerate(OPS):
+        nd[i] = len(x["deps"])
+        for j in x["deps"]:
+            succ[j].append(i)
+    path = [0.0] * n
+    for i in range(n - 1, -1, -1):
+        path[i] = OPS[i]["d"] + max([path[s] + LAG for s in succ[i]], default=0.0)
+        if rk[i] == 0:
+            rk[i] = min([rk[s] for s in succ[i]], default=99)
+    pri = [path[i] - rw * rk[i] + bonus.get(OPS[i]["w"][0][0][:-1] if OPS[i]["w"] else "", 0.0) for i in range(n)]
+    ready, t0, free, order, end = {}, [0.0] * n, {}, [], [0.0] * n
+    for i in range(n):
+        if nd[i] == 0:
+            ready.setdefault(OPS[i]["e"], set()).add(i)
+    while len(order) < n:
+        best = None
+        for e, s in ready.items():
+            f = 0.0 if e == "X" else free.get(e, 0.0)
+            for i in s:
+                k = (max(f, t0[i]), -pri[i], i)
+                if best is None or k < best[0]:
+                    best = (k, i, e)
+        (st, _, _), i, e = best
+        ready[e].discard(i)
+        end[i] = st + OPS[i]["d"]
+        if e != "X":
+            free[e] = end[i]
+        order.append(i)
+        for s in succ[i]:
+            t0[s] = max(t0[s], end[i] + (LAG if OPS[s]["deps"][i] else 0.0))
+            nd[s] -= 1
+            if nd[s] == 0:
+                ready.setdefault(OPS[s]["e"], set()).add(s)
+    return order, max(end)
+
+
+PLAN = []
+
+
+def plan():
+    if not PLAN:
+        build()
+        analyse()
+        order, tot = schedule()
+        PLAN.append(order)
+        PLAN.append(tot)
+    return PLAN[0]
+
+
+QS = {"P": "qP", "V": "qV", "S": "qS", "G": "qG"}
+
+
+def rank_program(g, core, T, topo):
+    if T.rank_of(core) is None:
+        return
+    order = plan()
+    queue = {"P": g.tensor, "V": g.vector, "S": g.scalar, "G": g, "R": g, "Y": g.sync}
+    qname = {"G": "g", "R": "g"}
+    cnt, done, know, clock, sent = {}, {}, {}, {}, 0
+    for i in order:
+        x = OPS[i]
+        e = x["e"]
+        if e == "X":
+            done[i] = (x["sem"], x["inc"])
+            clock[i] = {}
+            continue
+        qn = qname.get(e, e)
+        kn = know.setdefault(qn, {})
+        need = {}
+        for j, w in x["deps"].items():
+            if w and done.get(j) is not None:
+                s, v = done[j]
+                if need.get(s, (0, 0))[0] < v:
+                    need[s] = (v, j)
+        for s, (v, j) in sorted(need.items(), key=lambda z: -z[1][1]):
+            if kn.get(s, 0) >= v:
+                continue
+            queue[e].wait_ge(T.sem[s], v)
+            for s2, v2 in clock[j].items():
+                kn[s2] = max(kn.get(s2, 0), v2)
+            kn[s] = max(kn.get(s, 0), v)
+        clock[i] = dict(kn)
+        if e in QS:
+            s = QS[e]
+            for f in x["f"]:
+                f(g, T).then_inc(T.sem[s], 1)
+                cnt[s] = cnt.get(s, 0) + 1
+            done[i] = (s, cnt[s])
+        elif e == "R":
+            for f in x["f"]:
+                sent += f(g, T, core, topo)
+            done[i] = None
+        else:
+            sem = x["sem"]
+            if sem is None:
+                sem = OPS[i]["w"][0][0][4:]
+            for f in x["f"]:
+                f(g, T).then_inc(T.sem[sem], 16)
+                cnt[sem] = cnt.get(sem, 0) + 16
+            done[i] = None
+    for s in list(QS.values()) + ["out", "ld0", "ld1", "ld2"]:
+        if cnt.get(s, 0):
+            g.sync.wait_ge(T.sem[s], cnt[s])
+    g.wait_ge(T.sem.snt, sent)

@@ -9,11 +9,10 @@ PC = 0.5
 GC = 1.35
 NET = 4500.0
 LAG = 150.0
-RW, BONUS = 10500.0, {"XB": 1500.0, "AB": -5000.0, "po": -8000.0, "h": 1500.0, "km": 5000.0, "fi": -8000.0, "E2": 5000.0, "d": 5000.0, "X": 12000.0,
-                      "q1": 5000.0, "F": 3000.0, "ps": -1500.0, "S": 1500.0, "PP": 3000.0, "pr": 3000.0, "Y": -1500.0, "hS": -1500.0}
-NV = 12
-VCUT = [("S", 32), ("V", 32), ("S", 32), ("S", 32)]
-YCUT = [("S", 32)] * 4
+RW, BONUS = 6000.0, {}
+NV = 16
+VCUT = "SVSS"
+YCUT = "SSSS"
 SCRATCH, SEMAPHORES = {}, []
 
 
@@ -25,20 +24,25 @@ F32, BF, I32, U16, F16 = "float32", "bfloat16", "int32", "uint16", "float16"
 _sb("ct", 4096)
 _sb("ei", 256, I32); _sb("zi", 256, I32)
 _sb("eo", 1280, U16); _sb("es", 1280, F16); _sb("zo", 1280, U16); _sb("zs", 1280, F16)
-_sb("po", 1024, U16); _sb("ps", 768, F16)
+_sb("po", 768, U16)
 _sb("pz", 256, F32); _sb("ef", 256, F32); _sb("yz", 256, F32)
+IDENT = {"nI": -1.0, "I128": 1.0 / 128, "n127": -127.0 / 128, "p256": 256.0, "m256": -256.0, "wq1": -113.0, "wq2": 16.5,
+         "pB": 2.0 ** 21, "mB": -2.0 ** 21, "mh": -0.5, "m2048": -2048.0}
+for _t in range(1, RO + 1):
+    IDENT["wt%d" % _t] = (77 * _t - 95) / 2
 CB = {}
-for _n, _w in [("I", 128), ("nI", 128), ("I128", 128), ("p127", 128), ("p128", 128), ("m127", 128), ("m128", 128), ("m4096", 128), ("m64", 128),
-               ("p32", 128), ("P2", 128), ("Sp", 128), ("ones", 128), ("c16", 128), ("cD", 128), ("cC", 256), ("neg", 128), ("pos", 128),
-               ("keep", 128), ("b16", 16), ("b16x", 16)]:
+for _n, _w in [("I", 128)] + [(_x, 128) for _x in IDENT] + [
+        ("Sp", 128), ("ones", 128), ("c16", 128), ("cD", 128), ("cC", 256), ("neg", 128), ("pos", 128),
+        ("keep", 128), ("U0", 128), ("b16", 16), ("b16x", 16), ("b32", 16), ("bm16", 16)]:
     CB[_n] = (sum(w for _, w in CB.values()), _w)
 _sb("cb", sum(w for _, w in CB.values()))
 CF = {}
-for _n in ("DA", "DB", "TC", "TS", "IV", "IF"):
+for _n in ("DA", "DB", "TC", "TS", "IV"):
     CF[_n] = (128 * len(CF), 128)
 _sb("cf", 128 * len(CF), F32)
 CH = {}
-for _n, _w in [("b128", 16), ("b1", 16), ("I", 128), ("tri", 128), ("odd", 128)] + [(_x + _y, 128) for _y in "hl" for _x in ("DA", "DB", "TC", "TS")]:
+for _n, _w in ([("wa", 16), ("wb", 16), ("I", 128), ("triP", 128), ("triM", 128), ("odd", 128)] + [("Sh%d" % _x, 128) for _x in range(4)]
+               + [(_x + _y, 128) for _y in "hl" for _x in ("DA", "DB", "TC", "TS")]):
     CH[_n] = (sum(w for _, w in CH.values()), _w)
 _sb("ch", sum(w for _, w in CH.values()), F16)
 _sb("b8", 8, F32)
@@ -48,19 +52,19 @@ for _n, _w, _d in (("KI", 128, F32), ("KD", 128, F32), ("KT", 128, F32), ("UM", 
                    ("n80", 80, F32), ("n80i", 80, I32), ("w80", 80, F32), ("x80", 80, F32), ("a80", 80, F32)):
     _sb("k_" + _n, _w, _d)
 for _h in range(NH):
-    for _n, _w, _d in (("V", 2048, BF), ("Y", 2048, BF), ("cmp", 2048, BF), ("mx", 2048, BF), ("PA", 2048, F16), ("PB", 2048, F16), ("km", 128, F32),
+    for _n, _w, _d in (("V", 2048, BF), ("Y", 2048, BF), ("cmp", 2048, BF), ("mx", 2048, BF), ("PK", 2048, F16), ("km", 128, F32),
                        ("r8", 8, F32), ("d", 128, BF), ("q1", 128, BF), ("q2", 128, BF), ("r", 128, F32), ("X", 128, BF), ("Mx", 128, BF),
-                       ("Mn", 128, BF), ("LT", 128, BF), ("r16", 128, BF), ("hS", 128, BF), ("XA", 256, F16), ("XB", 256, F16), ("v", 128, I32),
-                       ("S", 128, I32), ("cd", 128, I32), ("q", 128, F32), ("Zq", 128, F32), ("pr", 128, I32), ("F", 128, I32), ("m2", 128, F32),
-                       ("val", 128, F32), ("del", 128, BF), ("E2", 128, BF), ("h2", 128, BF), ("EL", 128, BF), ("h", 128, F16),
-                       ("AB", 256, F32), ("PP", 256, F32), ("fi", 128, F32), ("fm", 128, F32), ("w", 128, I32), ("pi", 128, I32), ("pf", 128, F16)):
+                       ("Mn", 128, BF), ("LT", 128, BF), ("r16", 128, BF), ("r2", 128, BF), ("hS", 128, BF), ("XK", 256, F16), ("Bs", 64, F32),
+                       ("v", 128, I32), ("w", 128, I32), ("S2", 128, F32), ("pr", 128, I32), ("F", 128, I32), ("v0", 128, I32), ("v1", 128, I32),
+                       ("val", 128, F16), ("del", 128, BF), ("E2", 128, BF), ("rb", 384, BF), ("N", 128, BF), ("mk", 512, BF), ("tk", 512, F16),
+                       ("h", 128, F16), ("AB", 256, F32), ("PP", 256, F32), ("fm", 128, F16)):
         _sb("%s%d" % (_n, _h), _w, _d)
     for _n in "abcd":
         SCRATCH["ps%s%d" % (_n, _h)] = ("psum", [128, 512], F32)
 SEMAPHORES += ["qP", "qV", "qS", "qG", "ld0", "ld1", "ld2", "snt", "out"]
 for _t in range(1, RO + 1):
     for _h in range(NH):
-        SEMAPHORES += ["%s%d%d" % (_k, _t, _h) for _k in ("eo", "es", "zo", "zs")]
+        SEMAPHORES += ["%s%d%d" % (_k, _t, _h) for _k in "ez"]
 
 
 def R(buf, c0, c1, step=1):
@@ -77,8 +81,9 @@ def cf(n):
     return R("cf", c, c + w)
 
 
-def ch(n, w=None):
-    return R("ch", CH[n][0], CH[n][0] + (w or CH[n][1]))
+def ch(n, lo=0, hi=None):
+    c, w = CH[n]
+    return R("ch", c + lo, c + (w if hi is None else hi))
 
 
 def ap(T, r):
@@ -194,11 +199,9 @@ def constants():
     iota(UM, [[0, 8], [1, 16]], 0, 0)
     iota(pi, [[0, 2]], 0, 1)
     iota(KT, [[16, 8], [1, 16]], 0, -1)
-    for n, c in (("I", 1.0), ("nI", -1.0), ("I128", 1.0 / 128), ("p127", 127.0), ("p128", 128.0), ("m127", -127.0), ("m128", -128.0), ("m4096", -4096.0), ("m64", -32.0), ("p32", 16.0)):
-        if n == "I":
-            ts(cb(n), KD, 0.0, A.is_equal)
-        else:
-            act(cb(n), cb("I"), AF.Copy, scale=c)
+    ts(cb("I"), KD, 0.0, A.is_equal)
+    for n, c in IDENT.items():
+        act(cb(n), cb("I"), AF.Copy, scale=c)
     fill(cb("ones"), 1.0); fill(cb("c16"), 16.0); fill(cb("cC"), 0.0)
     ts(R("cb", CB["cC"][0], CB["cC"][0] + 128), UM, 0.0, A.is_equal, -1.0 / 128, A.mult)
     b8, t8 = R("b8", 0, 8), R("k_t1", 0, 8)
@@ -207,9 +210,8 @@ def constants():
     tt(b8, b8, t8, A.mult)
     for half in (0, 8):
         act(cb("b16", half, half + 8), b8, AF.Copy)
-    act(cb("b16x", 0, 8), b8, AF.Copy, scale=16.0)
-    ts(ch("b128", 8), b8, 128.0, A.mult)
-    ts(ch("b1", 8), b8, 1.0, A.mult)
+    for n, c in (("b16x", 16.0), ("b32", 32.0), ("bm16", -16.0)):
+        act(cb(n, 0, 8), b8, AF.Copy, scale=c)
     cp(ch("I"), cb("I"))
     ts(GG, KI, 0.0, A.is_ge)
     ts(t1, KI, 15.0, A.is_le)
@@ -223,24 +225,32 @@ def constants():
     ts(ki, ki, 1, A.bitwise_and)
     tt(t1, ki, GG, A.mult)
     ts(ch("odd"), t1, -2.0, A.mult)
-    ts(cb("P2"), KI, 15.0, A.is_equal)
     ts(t1, KD, 0.0, A.is_equal, 4096.0, A.mult)
     ts(t2, KD, -1.0, A.is_equal, 4096.0, A.mult)
     tt(t1, t1, t2, A.subtract)
     ts(t2, UM, 14.0, A.is_le)
     tt(cb("Sp"), t1, t2, A.mult)
-    act(cf("IF"), cb("I"), AF.Copy)
-    ts(t1, KT, 0.0, A.is_ge)
-    tt(ch("tri"), t1, GG, A.mult)
+    ts(t1, KT, 0.0, A.is_ge, 8192.0, A.mult)
+    tt(ch("triP"), t1, GG, A.mult)
+    ts(ch("triM"), ch("triP"), -0.25, A.mult)
+    for s, c in enumerate((1.0, 0.5, 0.25, -0.25)):
+        ts(t1, KD, -float(2 ** s), A.is_equal)
+        tt(t2, t1, cb("I"), A.subtract)
+        ts(ch("Sh%d" % s), t2, c, A.mult)
     ts(pi, pi, 15, A.bitwise_and)
     ri = col(0)
     cp(ri, R("k_pi", 0, 1))
     ts(col(1), ri, 14.0, A.is_le, -4096.0, A.mult)
-    ts(col(2), col(1), 960.0 + 16512.0 + 2048.0, A.add)
-    ts(col(1), col(1), 127 * 7.5 + 96 - 129 - 16, A.add)
-    ts(col(3), ri, 127.0, A.mult, -129.0, A.add)
-    ts(col(4), ri, 128.0, A.mult, 16512.0, A.add)
     ts(col(5), ri, -1.0, A.mult, 16.0, A.add)
+    ts(R("k_pi", 1, 2), R("k_pi", 1, 2), 1, A.bitwise_and)
+    cp(col(2), R("k_pi", 1, 2))
+    ts(col(3), col(2), -1.0, A.mult, 1.0, A.add)
+    for c in (0, 1):
+        ts(ch("wa", 8 * c, 8 * c + 8), b8, col(3 - c), A.mult, 127.0, A.mult)
+        ts(ch("wb", 8 * c, 8 * c + 8), b8, col(3 - c), A.mult)
+    ts(col(4), col(2), -2.0 ** 15, A.mult, -390.0 * 2 ** 14, A.add)
+    ts(cb("U0", 0, 64), cb("ones", 0, 64), col(4), A.mult)
+    fill(cb("U0", 64, 128), 0.0)
     u, f16, im = K("u16f", 16), K("f16", 16), K("im16", 16)
     cp(u, R("k_UM", 0, 16))
     ts(im, u, 9.0, A.is_ge)
@@ -286,7 +296,7 @@ def constants():
     tt(lo, R("cf", 0, 512), hi, A.subtract)
 
 
-M4, M16 = 1.5 * 2 ** 25, 1.5 * 2 ** 27
+M1, M4, M16 = 1.5 * 2 ** 23, 1.5 * 2 ** 25, 1.5 * 2 ** 27
 
 
 def half_round(t, h, hop):
@@ -299,121 +309,110 @@ def half_round(t, h, hop):
     col = lambda j: R("col", j, j + 1)
     hop(t, h, "z")
     for buf, ls, cuts in (("V", (eo[0], eo[1]), VCUT), ("Y", (zo[0], zo[1]), YCUT)):
-        c = 0
-        for eng, w in cuts:
-            gather(eng, b(buf, 16 * c, 16 * (c + w)), R(ls[0], ls[1] + c, ls[1] + c + w))
-            c += w
+        for c, eng in enumerate(cuts):
+            gather(eng, b(buf, 512 * c, 512 * c + 512), R(ls[0], ls[1] + 32 * c, ls[1] + 32 * c + 32))
+    if t > 1:
+        ts(es, eo, -2048.0, A.add)
+        ts(zs, zo, -2048.0, A.add)
     ts(b("hS"), es, 2048 + 16448.5, A.add)
-    v15 = R("V%d" % h, 15, 2048, 16)
-    for c in range(0, 16 - NV, 4):
-        for j in range(4):
-            mm(group(q(pd, j), [(cb("I"), R("Y%d" % h, c + j, 2048, 16)), (cb("nI"), v15)]))
-        act(b("mx", 128 * c, 128 * c + 512), q(pd, 0, 4), AF.Abs)
-    if NV:
-        mm([(q(pc, 0), cb("I"), v15, True, True)])
-        for p in range(16 - NV, 16):
-            tt(b("mx", 128 * p, 128 * p + 128), R("Y%d" % h, p, 2048, 16), q(pc, 0), A.subtract)
-        for p in range(16 - NV, 16, 4):
-            x = b("mx", 128 * p, 128 * min(16, p + 4))
-            act(x, x, AF.Abs)
+    V, Y = "V%d" % h, "Y%d" % h
+    v15 = R(V, 15, 2048, 16)
+    NA = 16 - NV
+    if NA:
+        for j in range(NA):
+            mm(group(q(pc, j), [(cb("I"), R(Y, j, 2048, 16)), (cb("nI"), v15)]))
+        act(b("mx", 0, 128 * NA), q(pc, 0, NA), AF.Abs)
     mm([(q(pd, 1), cb("ones"), cb("cD"), True, False)])
-    for p in range(16):
-        mm([(R(pd, 128 + p, 256, 16), b("mx", 128 * p, 128 * p + 128), cb("b16x", 0, 8), False, p == 15)])
+    for k in range(NA, 16, 4):
+        mm([(R(pd, 128 + p, 256, 16), R(Y, p, 2048, 16), cb("bm16", 0, 8), False, False) for p in range(k, min(16, k + 4))])
+    mm([(q(pc, 0), cb("I"), v15, True, True)])
+    if NA:
+        mm([(R(pd, 128 + p, 256, 16), v15, cb("b16x", 0, 8), False, False) for p in range(NA)])
+    for p in range(NA, 16):
+        tt(b("mx", 128 * p, 128 * p + 128), R(Y, p, 2048, 16), q(pc, 0), A.max)
+    for p in range(0, 16, 2):
+        mm([(R(pd, 128 + j, 256, 16), b("mx", 128 * j, 128 * j + 128), cb("b16x" if j < NA else "b32", 0, 8), False, j == 15) for j in (p, p + 1)])
     scan(b("km"), cb("pos"), q(pd, 1), A.add, A.min)
     km = R("km%d" % h, 15, 128, 16)
     ts(b("r8", 0, 8), km, M16, A.add, M16, A.subtract)
     for c in range(4):
-        bank = pa if c % 2 == 0 else pb
-        for j in range(4):
-            k = 4 * c + j
-            mm(group(q(bank, j), [(cb("I"), R("V%d" % h, k, 2048, 16)), (cb("nI"), R("V%d" % h, (k + 1) % 16, 2048, 16))]))
-        act(b("cmp", 512 * c, 512 * c + 512), q(bank, 0, 4), AF.Sign, -0.5)
+        bank, c0 = (pa if c % 2 == 0 else pb), 512 * c
+        mm([(q(bank, 0, 4), cb("I"), R(V, c0, c0 + 512), True, False), (R(bank, 0, 511), cb("nI"), R(V, c0 + 1, c0 + 512), False, False),
+            (R(bank, 15, 496, 16), cb("I"), R(V, c0 + 16, c0 + 512, 16), False, False), (R(bank, 15, 512, 16), cb("nI"), R(V, c0, c0 + 512, 16), False, True)])
+        act(b("cmp", c0, c0 + 512), q(bank, 0, 4), AF.Sign, -0.5)
     mm([(q(pa, 0, 2), cb("ones"), cb("cC"), True, False)] + ([(q(pa, 1), b("h"), ch("odd"), False, False)] if t > 1 else []))
     for k in range(0, 16, 4):
-        mm([(R(pa, j, 256, 16), b("cmp", 128 * j, 128 * j + 128), cb("b16"), False, j == 15) for j in range(k, k + 4)])
+        mm([(R(pa, j, 256, 16), R("cmp%d" % h, j, 2048, 16), cb("b16"), False, j == 15) for j in range(k, k + 4)])
+    scan(q(pb, 1), cb("keep"), q(pa, 0), A.mult, A.add)
     act(b("q1"), q(pa, 1), AF.Sign, 5.0)
     act(b("q2"), q(pa, 0), AF.Sign, -2.5)
-    scan(q(pc, 0), cb("keep"), q(pa, 0), A.mult, A.add)
-    ts(b("r"), q(pc, 0), M4, A.add, M4, A.subtract)
-    tt(b("d"), b("r"), q(pc, 0), A.subtract)
+    ts(b("r"), q(pb, 1), M4, A.add, M4, A.subtract)
+    tt(b("d"), b("r"), q(pb, 1), A.subtract)
     tt(R("d%d" % h, 0, 128, 16), km, b("r8", 0, 8), A.subtract)
     scan(b("X"), cb("keep"), b("d"), A.mult, A.add)
     rev = lambda n: R("%s%d" % (n, h), 0, 128, -1)
     scan(rev("Mx"), cb("neg"), rev("X"), A.add, A.max)
     scan(rev("Mn"), cb("pos"), rev("X"), A.add, A.min)
     ts(b("r16"), b("X"), M16, A.add, M16, A.subtract)
+    ts(b("r2"), b("X"), 391.0, A.add)
     mm(group(q(pb, 0), [(b("Mx"), cb("I")), (b("Mn"), cb("nI"))]))
     act(b("LT"), q(pb, 0), AF.Copy)
     XA, XB = q(pc, 1), q(pd, 2)
-    mm([(XA, b("q1"), cb("m64"), True, False), (XA, b("q2"), cb("p32"), False, False), (XA, cb("I128"), b("hS"), False, False)])
-    mm([(XB, ch("I"), es, True, False), (XB, cb("nI"), b("hS"), False, False)])
-    mm([(XA, b("X"), cb("p127"), False, False), (XA, b("r16"), cb("m127"), False, False)])
-    mm([(XB, b("X"), cb("p128"), False, False), (XB, b("r16"), cb("m128"), False, False)])
+    mm([(XA, cb("I128"), b("hS"), True, False)])
+    mm([(XB, ch("I"), es, True, False), (XB, cb("n127"), b("hS"), False, False)])
+    mm([(XA, b("q1"), cb("wq1"), False, False), (XA, b("q2"), cb("wq2"), False, False), (XB, b("q2"), cb("wt%d" % t), False, False)])
+    mm([(XA, b("r2"), cb("p256"), False, False), (XA, b("r16"), cb("m256"), False, False)])
+    mm([(XB, b("r2"), cb("p256"), False, False), (XB, b("r16"), cb("m256"), False, False)])
     mm([(XA, cb("Sp"), b("LT"), False, True)])
     mm([(XB, cb("Sp"), b("LT"), False, True)])
-
-    def keys(ka, kb, ca, cc):
-        ts(b("XA"), ka, ca, A.add)
-        ts(b("XA", 128, 256), ka, ca, A.add, -8 * 127.0, A.add)
-        ts(b("XB"), kb, cc, A.add)
-        ts(b("XB", 128, 256), kb, cc, A.add, -8 * 128.0, A.add)
-
-    def route(bank):
-        for p in range(8):
-            ts(b("PA", 256 * p, 256 * p + 256), b("XA", 0, 256), 127.0 * p, A.max, 127.0 * (p + 1), A.min)
-            ts(b("PB", 256 * p, 256 * p + 256), b("XB", 0, 256), 128.0 * p, A.max, 128.0 * (p + 1), A.min)
-            for k in (0, 1):
-                c = 256 * p + 128 * k
-                mm(group(R(bank, p + 8 * k, 128, 16), [(b("PA", c, c + 128), ch("b128", 8)), (b("PB", c, c + 128), ch("b1", 8))]))
-
-    keys(XA, XB, col(1), col(2))
-    mm(group(q(pc, 2), [(ch("DAh"), es), (ch("DAl"), es)]) + group(q(pc, 3), [(ch("DBh"), es), (ch("DBl"), es)]))
-    act(b("AB", 0, 256), q(pc, 2, 2), AF.Copy)
+    ts(b("XK", 0, 128), XA, col(1), A.add, 161.5 - 129 - 256 * 384 - 2048, A.add)
+    ts(b("XK", 128, 256), XB, col(1), A.add, 16383 + (77 * t - 31) / 2 - 256 * 384, A.add)
+    mm(group(q(pa, 2), [(ch("DAh"), es), (ch("DAl"), es)]) + group(q(pa, 3), [(ch("DBh"), es), (ch("DBl"), es)]))
+    act(b("AB", 0, 256), q(pa, 2, 2), AF.Copy)
     mm(group(q(pa, 0), [(zs, ch("I")), (cb("ones"), cb("c16"))]))
-    route(pd)
-    cp(b("v"), q(pd, 0))
-    ts(b("S"), b("v"), 4095, A.bitwise_and)
-    ts(b("cd"), b("v"), 12, A.arith_shift_right, 3, A.bitwise_and)
-    tt(b("pr"), b("S"), q(pa, 0), A.mult)
-    ts(b("del"), b("cd"), 3.0, A.is_ge)
-    ts(b("F"), b("pr"), 5, A.arith_shift_right, 4095, A.bitwise_and)
-    ts(q(pa, 1), b("cd"), 2.0, A.is_ge)
+    U, UA = q(pb, 2), R(pb, 256, 320)
+    mm([(U, cb("ones"), cb("U0"), True, False), (UA, cb("mB"), R("X%d" % h, 0, 128, 2), False, False), (UA, cb("pB"), R("r2%d" % h, 0, 128, 2), False, False)])
+    for p in range(8):
+        ts(b("PK", 256 * p, 256 * p + 256), b("XK", 0, 256), 512.0 * (p - 4), A.max, 512.0 * (p - 3), A.min)
+        mm([(R(pb, 256 + p, 384, 8), b("PK", 256 * p + 128 * k, 256 * p + 128 * k + 128), ch("wa" if k == 0 else "wb"), False, p == 7 and k == 1) for k in (0, 1)])
+    act(b("Bs", 0, 64), R(pb, 320, 384), AF.Copy)
+    tt(R("v%d" % h, 0, 128, 2), b("Bs", 0, 64), UA, A.max)
+    tt(R("v%d" % h, 1, 128, 2), b("Bs", 0, 64), UA, A.min)
+    ts(b("w"), b("v"), 65535, A.bitwise_and)
+    ts(b("S2"), b("w"), -(8192.0 + 77 * t), A.add, 0.0, A.max)
+    ts(b("del"), b("w"), 32768.0, A.is_ge)
+    tt(b("pr"), b("S2"), q(pa, 0), A.mult)
     scan(b("E2"), cb("keep"), b("del"), A.mult, A.add)
-    ts(q(pa, 2), b("cd"), 2.0, A.is_ge, 77.0 * t, A.mult)
-    ts(b("q"), b("cd"), 0.0, A.is_equal)
-    tt(b("m2"), b("S"), q(pa, 2), A.add)
-    tt(q(pa, 3), b("q"), q(pa, 0), A.mult)
-    tt(q(pa, 2), b("m2"), q(pa, 3), A.add)
-    tt(b("Zq"), b("F"), q(pa, 1), A.mult)
-    tt(b("val"), b("Zq"), q(pa, 2), A.add)
-    act(b("h2"), b("val"), AF.Identity, 16448.5)
-    XA, XB = q(pb, 0), q(pc, 2)
-    mm([(XA, b("E2"), cb("m127"), True, False), (XA, b("del"), cb("m4096"), False, False)])
-    mm([(XB, b("E2"), cb("m128"), True, False), (XB, b("del"), cb("m4096"), False, False)])
-    mm(group(q(pd, 3), [(b("E2"), cb("I"))]))
-    act(b("EL"), q(pd, 3), AF.Copy)
-    mm(group(q(pd, 2), [(cb("P2"), b("EL"))]))
-    ts(b("h"), q(pd, 2), col(5), A.is_equal)
-    mm([(XB, b("val"), cf("IF"), False, False)])
-    mm([(XA, b("h2"), cb("I128"), False, True)])
-    mm([(XB, b("h2"), cb("nI"), False, True)])
-    keys(XA, XB, col(3), col(4))
-    mm(group(q(pd, 0), [(ch("TCh"), b("h")), (ch("TCl"), b("h"))]) + group(q(pd, 1), [(ch("TSh"), b("h")), (ch("TSl"), b("h"))]) +
-       group(q(pd, 2), [(b("h"), ch("tri"))]))
+    tt(q(pa, 1), b("w"), q(pa, 0), A.max)
+    ts(b("F"), b("pr"), 5, A.arith_shift_right, 4095, A.bitwise_and)
+    tt(b("v0"), b("F"), q(pa, 1), A.add)
+    ts(b("v1"), b("v0"), 32768 + 4095, A.bitwise_and)
+    ts(b("val"), b("v1"), -2048.0, A.add, 2048.0, A.min)
+    rb = lambda s: b("rb", 128 * (s - 1), 128 * s)
+    for s in (1, 2, 3):
+        ts(rb(s), b("E2"), 192.0 * 2 ** s - (2 ** s - 1) / 2, A.add)
+    scan(rev("N"), cb("neg"), rev("E2"), A.add, A.max)
+    mm(group(q(pc, 0), [(b("E2"), cb("I")), (rb(1), cb("nI"))]) + group(q(pc, 1), [(rb(1), cb("I")), (rb(2), cb("nI"))]))
+    act(b("mk", 0, 256), q(pc, 0, 2), AF.Copy, 384.0)
+    mm(group(q(pc, 2), [(rb(2), cb("I")), (rb(3), cb("nI"))]) + group(q(pc, 3), [(rb(3), cb("mh"))]))
+    act(b("mk", 256, 512), q(pc, 2, 2), AF.Copy, 768.0)
+    mm(group(q(pd, 0), [(b("N"), cb("I"))]))
+    ts(b("h"), q(pd, 0), col(5), A.is_equal)
+    mm(group(q(pd, 0), [(ch("TCh"), b("h")), (ch("TCl"), b("h"))]) + group(q(pd, 1), [(ch("TSh"), b("h")), (ch("TSl"), b("h"))]))
     tt(b("PP", 0, 256), b("AB", 0, 256), q(pd, 0, 2), A.mult)
-    mm(group(q(pc, 0), [(b("PP", 0, 128), cf("IV")), (b("PP", 128, 256), cf("IV"))]))
-    act(b("fi"), q(pc, 0), AF.Copy, 2048.0)
-    tt(b("fm"), b("fi"), q(pd, 2), A.mult)
-    route(pb)
-    tt(b("w"), b("fm"), q(pb, 0), A.add)
-    ts(b("pi"), b("w"), 4095, A.bitwise_and)
-    ts(b("pf"), b("pi"), -2048.0, A.add)
-    mm(group(q(pa, 0), [(b("pf"), ch("I"))]))
-    if t < RO:
-        ts(R("po", o, o + 128), q(pa, 0), 2048.0, A.add)
-        cp(R("ps", o, o + 128), q(pa, 0))
-    else:
-        act(R("pz", 128 * h, 128 * h + 128), q(pa, 0), AF.Copy, 2048.0)
+    mm(group(q(pd, 2), [(ch("triP"), b("h")), (cf("IV"), b("PP", 0, 128)), (cf("IV"), b("PP", 128, 256))]))
+    ts(b("fm"), q(pd, 2), -8192.0, A.add, -2048.0, A.max)
+    tk = lambda s: b("tk", 128 * s, 128 * s + 128)
+    for s, bank in enumerate((pb, pa, pc, pb, pa)):
+        K = q(bank, 0)
+        terms = [(b("del"), cb("m2048")), (b("val"), ch("I"))] + [(ch("Sh%d" % j), tk(j)) for j in range(s)]
+        if s == 4:
+            terms[2:2] = [(ch("triM"), b("h")), (ch("I"), b("fm"))]
+        for x in group(K, terms):
+            mm([x])
+        if s < 4:
+            tt(tk(s), b("mk", 128 * s, 128 * s + 128), K, A.mult)
+    ts(R("po", o, o + 128) if t < RO else R("pz", 128 * h, 128 * h + 128), K, 4096.0 + M1, A.add, M1, A.subtract)
     hop(t, h, "e")
 
 
@@ -439,15 +438,13 @@ def build():
     def hop(t, h, kind):
         o = 256 * (t - 1) + 128 * h
         n = o + 256
-        for x in ("o", "s"):
-            if x == "o" and t == RO:
-                continue
-            s = (kind + x if kind == "z" else kind + x) + "%d%d" % (t, h)
-            src = ("e" + x) if kind == "z" else ("p" + x)
-            if kind == "e" and t == RO:
-                send(2, R("pz", 128 * h, 128 * h + 128), R("ef", 128 * h, 128 * h + 128), s)
-            else:
-                send(1 if kind == "z" else 2, R(src, o, o + 128), R(kind + x, n, n + 128), s)
+        s = "%s%d%d" % (kind, t, h)
+        if kind == "z":
+            send(1, R("eo", o, o + 128), R("zo", n, n + 128), s)
+        elif t < RO:
+            send(2, R("po", o, o + 128), R("eo", n, n + 128), s)
+        else:
+            send(2, R("pz", 128 * h, 128 * h + 128), R("ef", 128 * h, 128 * h + 128), s)
 
     for k in "ez":
         for h in range(NH):
@@ -460,7 +457,7 @@ def build():
             half_round(t, h, hop)
     o = 256 * RO
     for h in range(NH):
-        ts(R("yz", 128 * h, 128 * h + 128), R("zs", o + 128 * h, o + 128 * h + 128), 2048.0, A.add)
+        cp(R("yz", 128 * h, 128 * h + 128), R("zo", o + 128 * h, o + 128 * h + 128))
     for src, dst in (("yz", "ysub"), ("ef", "yenz")):
         for h in range(NH):
             op("Y", 60, [lambda g, T, src=src, dst=dst, h=h: g.sync.dma_start(T[dst][:, 128 * h:128 * h + 128], T[src][:, 128 * h:128 * h + 128])],

@@ -1,4 +1,5 @@
 import math
+import numpy as np
 from concourse.mybir import AluOpType as A, ActivationFunctionType as AF
 
 RO, LH = 4, 128
@@ -9,9 +10,8 @@ PC = 0.5
 GC = 1.35
 NET = 4500.0
 LAG = 150.0
-RW, BONUS = 6000.0, {}
-NV = 16
-VCUT = "SVSS"
+LEAD, PASSES, BONUS = 3200.0, 12, {"Xr": 1000.0, "N": 4000.0}
+VCUT = "SVSV"
 YCUT = "SSSS"
 SCRATCH, SEMAPHORES = {}, []
 
@@ -27,13 +27,13 @@ _sb("eo", 1280, U16); _sb("es", 1280, F16); _sb("zo", 1280, U16); _sb("zs", 1280
 _sb("po", 768, U16)
 _sb("pz", 256, F32); _sb("ef", 256, F32); _sb("yz", 256, F32)
 IDENT = {"nI": -1.0, "I128": 1.0 / 128, "n127": -127.0 / 128, "p256": 256.0, "m256": -256.0, "wq1": -113.0, "wq2": 16.5,
-         "pB": 2.0 ** 21, "mB": -2.0 ** 21, "mh": -0.5, "m2048": -2048.0}
+         "pB": 2.0 ** 21, "mB": -2.0 ** 21, "mh": -0.5, "mq": -0.25, "pq": 0.25, "m2048": -2048.0, "p4096": 4096.0}
 for _t in range(1, RO + 1):
     IDENT["wt%d" % _t] = (77 * _t - 95) / 2
 CB = {}
-for _n, _w in [("I", 128)] + [(_x, 128) for _x in IDENT] + [
-        ("Sp", 128), ("ones", 128), ("c16", 128), ("cD", 128), ("cC", 256), ("neg", 128), ("pos", 128),
-        ("keep", 128), ("U0", 128), ("b16", 16), ("b16x", 16), ("b32", 16), ("bm16", 16)]:
+for _n, _w in [("I", 128)] + [(_x, 128) for _x in IDENT] + [(_x, 128) for _x in (
+        "Sp", "ones", "zero", "c16", "c256", "cD", "neg", "pos", "keep", "U0", "GG", "triP", "triM", "odd", "Sh0", "Sh1", "Sh2", "Sh3", "t1", "t2")] + [
+        ("cC", 256), ("b16", 16), ("b32", 16), ("bm16", 16), ("wa", 16), ("wb", 16)]:
     CB[_n] = (sum(w for _, w in CB.values()), _w)
 _sb("cb", sum(w for _, w in CB.values()))
 CF = {}
@@ -41,19 +41,16 @@ for _n in ("DA", "DB", "TC", "TS", "IV"):
     CF[_n] = (128 * len(CF), 128)
 _sb("cf", 128 * len(CF), F32)
 CH = {}
-for _n, _w in ([("wa", 16), ("wb", 16), ("I", 128), ("triP", 128), ("triM", 128), ("odd", 128)] + [("Sh%d" % _x, 128) for _x in range(4)]
-               + [(_x + _y, 128) for _y in "hl" for _x in ("DA", "DB", "TC", "TS")]):
+for _n, _w in [(_x + _y, 128) for _y in "hl" for _x in ("DA", "DB", "TC", "TS")]:
     CH[_n] = (sum(w for _, w in CH.values()), _w)
 _sb("ch", sum(w for _, w in CH.values()), F16)
-_sb("b8", 8, F32)
+_sb("b8", 24, F32)
 _sb("col", 16, F32)
-for _n, _w, _d in (("KI", 128, F32), ("KD", 128, F32), ("KT", 128, F32), ("UM", 128, F32), ("GG", 128, F32), ("t1", 128, F32),
-                   ("t2", 128, F32), ("ki", 128, I32), ("pi", 2, I32), ("K8", 8, F32), ("u16f", 16, F32), ("f16", 16, F32), ("im16", 16, F32),
-                   ("n80", 80, F32), ("n80i", 80, I32), ("w80", 80, F32), ("x80", 80, F32), ("a80", 80, F32)):
+for _n, _w, _d in (("pi", 2, I32), ("u64", 64, F32), ("o64", 64, F32), ("n64", 64, I32), ("w64", 64, F32), ("x64", 64, F32), ("a64", 64, F32)):
     _sb("k_" + _n, _w, _d)
 for _h in range(NH):
-    for _n, _w, _d in (("V", 2048, BF), ("Y", 2048, BF), ("cmp", 2048, BF), ("mx", 2048, BF), ("PK", 2048, F16), ("km", 128, F32),
-                       ("r8", 8, F32), ("d", 128, BF), ("q1", 128, BF), ("q2", 128, BF), ("r", 128, F32), ("X", 128, BF), ("Mx", 128, BF),
+    for _n, _w, _d in (("V", 2048, BF), ("Ya", 2048, BF), ("Yb", 2048, BF), ("cmp", 2048, BF), ("mx", 2048, BF), ("PK", 2048, F16), ("km", 128, F32),
+                       ("r8", 8, F32), ("d", 128, BF), ("q1", 128, BF), ("q2", 128, BF), ("r", 128, F32), ("Xr", 128, BF), ("X", 128, BF), ("Mx", 128, BF),
                        ("Mn", 128, BF), ("LT", 128, BF), ("r16", 128, BF), ("r2", 128, BF), ("hS", 128, BF), ("XK", 256, F16), ("Bs", 64, F32),
                        ("v", 128, I32), ("w", 128, I32), ("S2", 128, F32), ("pr", 128, I32), ("F", 128, I32), ("v0", 128, I32), ("v1", 128, I32),
                        ("val", 128, F16), ("del", 128, BF), ("E2", 128, BF), ("rb", 384, BF), ("N", 128, BF), ("mk", 512, BF), ("tk", 512, F16),
@@ -108,8 +105,8 @@ def isp(r):
 OPS, MARK = [], []
 
 
-def op(eng, dur, fns, reads, writes, sem=None, inc=1, dep=None):
-    OPS.append({"e": eng, "d": dur, "f": fns, "r": reads, "w": writes, "sem": sem, "inc": inc, "dep": dep})
+def op(eng, dur, fns, reads, writes, sem=None, inc=1):
+    OPS.append({"e": eng, "d": dur, "f": fns, "r": reads, "w": writes, "sem": sem, "inc": inc})
     return len(OPS) - 1
 
 
@@ -118,7 +115,7 @@ def two(rs):
 
 
 def cyc(n, x):
-    return n * x * SC + FV
+    return max(64, n * x) * SC + FV
 
 
 def ts(out, a, s1, op0, s2=None, op1=None):
@@ -188,112 +185,83 @@ def iota(out, pattern, base, cm):
     return op("G", 130 + 2 * ncol(out) * SC, [lambda g, T: g.iota(ap(T, out), pattern, base, cm, **kw)], [], [out])
 
 
+def select(out, a, pattern, base, cm, cmp, other):
+    return op("G", 170 + 2 * ncol(out) * SC, [lambda g, T: g.affine_select(ap(T, out), ap(T, a), pattern, cmp, other, base, cm)], [a], [out])
+
+
 def constants():
-    K = lambda n, w: R("k_" + n, 0, w)
-    KI, KD, KT, UM, GG, t1, t2 = [K(n, 128) for n in ("KI", "KD", "KT", "UM", "GG", "t1", "t2")]
-    ki, pi, K8 = K("ki", 128), K("pi", 2), K("K8", 8)
+    K = lambda n, lo=0, hi=64: R("k_" + n, lo, hi)
     col = lambda j: R("col", j, j + 1)
-    iota(KI, [[-16, 8], [0, 16]], 0, 1)
-    iota(KD, [[1, 128]], 0, -1)
-    iota(K8, [[-16, 8]], 0, 1)
-    iota(UM, [[0, 8], [1, 16]], 0, 0)
-    iota(pi, [[0, 2]], 0, 1)
-    iota(KT, [[16, 8], [1, 16]], 0, -1)
-    ts(cb("I"), KD, 0.0, A.is_equal)
-    for n, c in IDENT.items():
-        act(cb(n), cb("I"), AF.Copy, scale=c)
-    fill(cb("ones"), 1.0); fill(cb("c16"), 16.0); fill(cb("cC"), 0.0)
-    ts(R("cb", CB["cC"][0], CB["cC"][0] + 128), UM, 0.0, A.is_equal, -1.0 / 128, A.mult)
-    b8, t8 = R("b8", 0, 8), R("k_t1", 0, 8)
-    ts(t8, K8, 0.0, A.is_ge)
-    ts(b8, K8, 15.0, A.is_le)
-    tt(b8, b8, t8, A.mult)
+    diag, row, blk, flat = [[-1, 128]], [[0, 8], [1, 16]], [[-16, 8], [0, 16]], [[1, 128]]
+    fill(cb("zero"), 0.0); fill(cb("ones"), 1.0); fill(cb("c16"), 16.0); fill(cb("c256"), 1.0 / 256); fill(cb("cC", 128, 256), 0.0)
+    select(cb("I"), cb("zero"), diag, 0, 1, A.not_equal, 1.0)
+    for j, (n, c) in enumerate(IDENT.items()):
+        if j % 2:
+            act(cb(n), cb("I"), AF.Copy, scale=c)
+        else:
+            ts(cb(n), cb("I"), c, A.mult)
+    b8, t8, e8 = R("b8", 0, 8), R("b8", 8, 16), R("b8", 16, 24)
+    select(t8, cb("ones", 0, 8), [[-16, 8]], 0, 1, A.is_ge, 0.0)
+    select(b8, t8, [[16, 8]], 15, -1, A.is_ge, 0.0)
     for half in (0, 8):
         act(cb("b16", half, half + 8), b8, AF.Copy)
-    for n, c in (("b16x", 16.0), ("b32", 32.0), ("bm16", -16.0)):
+    for n, c in (("b32", 32.0), ("bm16", -16.0)):
         act(cb(n, 0, 8), b8, AF.Copy, scale=c)
-    cp(ch("I"), cb("I"))
-    ts(GG, KI, 0.0, A.is_ge)
-    ts(t1, KI, 15.0, A.is_le)
-    tt(GG, GG, t1, A.mult)
-    ts(t1, UM, 7.5, A.subtract, 1.0 / 128, A.mult)
-    cp(cb("cD"), t1)
-    ts(cb("neg"), UM, 0.0, A.is_equal, -1000.0, A.mult)
-    ts(cb("pos"), UM, 0.0, A.is_equal, 1048576.0, A.mult)
-    ts(cb("keep"), UM, 1.0, A.is_ge)
-    cp(ki, KI)
-    ts(ki, ki, 1, A.bitwise_and)
-    tt(t1, ki, GG, A.mult)
-    ts(ch("odd"), t1, -2.0, A.mult)
-    ts(t1, KD, 0.0, A.is_equal, 4096.0, A.mult)
-    ts(t2, KD, -1.0, A.is_equal, 4096.0, A.mult)
-    tt(t1, t1, t2, A.subtract)
-    ts(t2, UM, 14.0, A.is_le)
-    tt(cb("Sp"), t1, t2, A.mult)
-    ts(t1, KT, 0.0, A.is_ge, 8192.0, A.mult)
-    tt(ch("triP"), t1, GG, A.mult)
-    ts(ch("triM"), ch("triP"), -0.25, A.mult)
-    for s, c in enumerate((1.0, 0.5, 0.25, -0.25)):
-        ts(t1, KD, -float(2 ** s), A.is_equal)
-        tt(t2, t1, cb("I"), A.subtract)
-        ts(ch("Sh%d" % s), t2, c, A.mult)
-    ts(pi, pi, 15, A.bitwise_and)
+    act(e8, b8, AF.Copy, scale=0.125)
+    iota(cb("cD"), [[0, 8], [2, 16]], -15, 0)
+    select(cb("keep"), cb("ones"), row, 0, 0, A.not_equal, 0.0)
+    ts(cb("neg"), cb("keep"), 1000.0, A.mult, -1000.0, A.add)
+    ts(cb("pos"), cb("keep"), -1048576.0, A.mult, 1048576.0, A.add)
+    ts(cb("cC", 0, 128), cb("keep"), 1.0 / 128, A.mult, -1.0 / 128, A.add)
+    pi = K("pi", 0, 2)
+    iota(pi, [[0, 2]], 0, 1)
+    ts(K("pi", 0, 1), K("pi", 0, 1), 15, A.bitwise_and)
+    ts(K("pi", 1, 2), K("pi", 1, 2), 1, A.bitwise_and)
     ri = col(0)
-    cp(ri, R("k_pi", 0, 1))
-    ts(col(1), ri, 14.0, A.is_le, -4096.0, A.mult)
+    cp(R("col", 0, 2), pi)
+    ts(col(2), col(1), -1.0, A.mult, 1.0, A.add)
+    ts(col(3), ri, 14.0, A.is_le, -4096.0, A.mult)
+    ts(col(4), col(1), -2.0 ** 15, A.mult, -390.0 * 2 ** 14, A.add)
     ts(col(5), ri, -1.0, A.mult, 16.0, A.add)
-    ts(R("k_pi", 1, 2), R("k_pi", 1, 2), 1, A.bitwise_and)
-    cp(col(2), R("k_pi", 1, 2))
-    ts(col(3), col(2), -1.0, A.mult, 1.0, A.add)
+    ts(col(6), col(1), -2.0 / 8192, A.mult)
     for c in (0, 1):
-        ts(ch("wa", 8 * c, 8 * c + 8), b8, col(3 - c), A.mult, 127.0, A.mult)
-        ts(ch("wb", 8 * c, 8 * c + 8), b8, col(3 - c), A.mult)
-    ts(col(4), col(2), -2.0 ** 15, A.mult, -390.0 * 2 ** 14, A.add)
-    ts(cb("U0", 0, 64), cb("ones", 0, 64), col(4), A.mult)
+        act(cb("wb", 8 * c, 8 * c + 8), b8, AF.Copy, scale=col(2 - c))
+    act(cb("wa"), cb("wb"), AF.Copy, scale=127.0)
+    act(cb("U0", 0, 64), cb("ones", 0, 64), AF.Copy, scale=col(4))
     fill(cb("U0", 64, 128), 0.0)
-    u, f16, im = K("u16f", 16), K("f16", 16), K("im16", 16)
-    cp(u, R("k_UM", 0, 16))
-    ts(im, u, 9.0, A.is_ge)
-    ts(f16, im, -8.0, A.mult)
-    tt(f16, f16, u, A.add)
-    ts(im, im, 4.0, A.mult)
-    ts(col(6), ri, 9.0, A.is_ge)
-    ts(col(7), col(6), -8.0, A.mult)
-    tt(col(7), col(7), ri, A.add)
-    ts(col(6), col(6), 4.0, A.mult)
-    ts(col(8), col(7), 0.0, A.is_equal)
-    ts(col(9), col(7), 8.0, A.is_equal)
-    tt(col(8), col(8), col(9), A.add)
-    ts(col(8), col(8), -1.0 / 16, A.mult, 2.0 / 16, A.add)
-    n = lambda j: R("k_n80", 16 * j, 16 * j + 16)
-    ts(n(2), f16, ri, A.mult)
-    tt(n(0), n(2), im, A.add)
-    ts(n(1), n(0), 4.0, A.add)
-    ts(n(3), n(2), 12.0, A.add)
-    ts(n(4), u, col(7), A.mult, col(6), A.add)
-    N, NI, W, X2, AC = K("n80", 80), K("n80i", 80), K("w80", 80), K("x80", 80), K("a80", 80)
-    cp(NI, N)
-    ts(NI, NI, 15, A.bitwise_and)
-    cp(N, NI)
-    ts(W, N, -1.0, A.mult, 16.0, A.add)
-    tt(W, W, N, A.min)
-    ts(W, W, -1.0, A.mult, 4.0, A.add)
-    tt(X2, W, W, A.mult)
-    cc = [(-1) ** k * (math.pi / 8) ** (2 * k + 1) / math.factorial(2 * k + 1) for k in range(7)]
-    ts(AC, X2, cc[6], A.mult, cc[5], A.add)
-    for k in (4, 3, 2, 1, 0):
+    select(cb("t1"), cb("p4096"), diag, -1, 1, A.not_equal, -4096.0)
+    select(cb("Sp"), cb("t1"), row, -15, 0, A.not_equal, 0.0)
+    for s, (n, c) in enumerate((("nI", 1.0), ("mh", 0.5), ("mq", 0.25), ("pq", -0.25))):
+        select(cb("Sh%d" % s), cb(n), diag, -2 ** s, 1, A.not_equal, c)
+    fill(cb("t2"), 8192.0)
+    select(cb("t2"), cb("t2"), blk, 0, 1, A.is_ge, 0.0)
+    select(cb("GG"), cb("t2"), [[16, 8], [0, 16]], 15, -1, A.is_ge, 0.0)
+    select(cb("triP"), cb("GG"), flat, 0, -1, A.is_ge, 0.0)
+    act(cb("triM"), cb("triP"), AF.Copy, scale=-0.25)
+    act(cb("odd"), cb("GG"), AF.Copy, scale=col(6))
+    u, off, n, W, X2, AC = K("u64"), K("o64"), K("n64"), K("w64"), K("x64"), K("a64")
+    iota(u, [[0, 4], [1, 16]], 0, 0)
+    for j, c in enumerate((14.0, 2.0, 0.0, 12.0)):
+        ts(K("n64", 16 * j, 16 * j + 16), K("u64", 0, 16), ri, A.mult, c, A.add)
+    ts(n, n, 15, A.bitwise_and)
+    ts(off, n, -8.0, A.add)
+    act(off, off, AF.Abs)
+    act(W, off, AF.Copy, -4.0)
+    act(X2, W, AF.Square)
+    w4 = np.arange(1.0, 5.0)
+    cc = [float(c) for c in np.linalg.solve(np.stack([w4 ** (2 * k + 1) for k in range(4)], 1), np.sin(w4 * math.pi / 8))]
+    ts(AC, X2, cc[3], A.mult, cc[2], A.add)
+    for k in (1, 0):
         tt(AC, AC, X2, A.mult)
         ts(AC, AC, cc[k], A.add)
     tt(AC, AC, W, A.mult)
-    iv = R("k_a80", 64, 80)
-    ts(iv, iv, col(8), A.mult)
     for j, name in enumerate(("DA", "DB", "TC", "TS", "IV")):
         c = CF[name][0]
         for q in range(8):
-            act(R("cf", c + 16 * q, c + 16 * q + 16), R("k_a80", 16 * j, 16 * j + 16), AF.Copy, scale=R("b8", q, q + 1))
-    hi, lo = R("ch", CH["DAh"][0], CH["DAh"][0] + 512), R("ch", CH["DAl"][0], CH["DAl"][0] + 512)
-    cp(hi, R("cf", 0, 512))
-    tt(lo, R("cf", 0, 512), hi, A.subtract)
+            act(R("cf", c + 16 * q, c + 16 * q + 16), K("a64", 16 * (j % 4), 16 * (j % 4) + 16), AF.Copy, scale=R("b8", q + 16 * (j // 4), q + 16 * (j // 4) + 1))
+    for j in (0, 256):
+        cp(R("ch", j, j + 256), R("cf", j, j + 256))
+        tt(R("ch", 512 + j, 768 + j), R("cf", j, j + 256), R("ch", j, j + 256), A.subtract)
 
 
 M1, M4, M16 = 1.5 * 2 ** 23, 1.5 * 2 ** 25, 1.5 * 2 ** 27
@@ -307,40 +275,36 @@ def half_round(t, h, hop):
     o = 256 * (t - 1) + 128 * h
     eo, es, zo, zs = R("eo", o, o + 128), R("es", o, o + 128), R("zo", o, o + 128), R("zs", o, o + 128)
     col = lambda j: R("col", j, j + 1)
+    rev = lambda n: R("%s%d" % (n, h), 0, 128, -1)
     hop(t, h, "z")
-    for buf, ls, cuts in (("V", (eo[0], eo[1]), VCUT), ("Y", (zo[0], zo[1]), YCUT)):
+    V, Y = "V%d" % h, "Y%s%d" % ("ab"[t % 2], h)
+    for buf, ls, cuts in ((V, eo, VCUT), (Y, zo, YCUT)):
+        w = 128 // len(cuts)
         for c, eng in enumerate(cuts):
-            gather(eng, b(buf, 512 * c, 512 * c + 512), R(ls[0], ls[1] + 32 * c, ls[1] + 32 * c + 32))
+            gather(eng, R(buf, 16 * w * c, 16 * w * (c + 1)), R(ls[0], ls[1] + w * c, ls[1] + w * (c + 1)))
     if t > 1:
         ts(es, eo, -2048.0, A.add)
         ts(zs, zo, -2048.0, A.add)
     ts(b("hS"), es, 2048 + 16448.5, A.add)
-    V, Y = "V%d" % h, "Y%d" % h
     v15 = R(V, 15, 2048, 16)
-    NA = 16 - NV
-    if NA:
-        for j in range(NA):
-            mm(group(q(pc, j), [(cb("I"), R(Y, j, 2048, 16)), (cb("nI"), v15)]))
-        act(b("mx", 0, 128 * NA), q(pc, 0, NA), AF.Abs)
-    mm([(q(pd, 1), cb("ones"), cb("cD"), True, False)])
-    for k in range(NA, 16, 4):
-        mm([(R(pd, 128 + p, 256, 16), R(Y, p, 2048, 16), cb("bm16", 0, 8), False, False) for p in range(k, min(16, k + 4))])
+    mm([(q(pd, 1), cb("c256"), cb("cD"), True, False)])
+    for k in range(0, 16, 4):
+        mm([(R(pd, 128 + p, 256, 16), R(Y, p, 2048, 16), cb("bm16", 0, 8), False, False) for p in range(k, k + 4)])
     mm([(q(pc, 0), cb("I"), v15, True, True)])
-    if NA:
-        mm([(R(pd, 128 + p, 256, 16), v15, cb("b16x", 0, 8), False, False) for p in range(NA)])
-    for p in range(NA, 16):
+    for p in range(16):
         tt(b("mx", 128 * p, 128 * p + 128), R(Y, p, 2048, 16), q(pc, 0), A.max)
     for p in range(0, 16, 2):
-        mm([(R(pd, 128 + j, 256, 16), b("mx", 128 * j, 128 * j + 128), cb("b16x" if j < NA else "b32", 0, 8), False, j == 15) for j in (p, p + 1)])
+        mm([(R(pd, 128 + j, 256, 16), b("mx", 128 * j, 128 * j + 128), cb("b32", 0, 8), False, j == 15) for j in (p, p + 1)])
     scan(b("km"), cb("pos"), q(pd, 1), A.add, A.min)
     km = R("km%d" % h, 15, 128, 16)
     ts(b("r8", 0, 8), km, M16, A.add, M16, A.subtract)
     for c in range(4):
         bank, c0 = (pa if c % 2 == 0 else pb), 512 * c
-        mm([(q(bank, 0, 4), cb("I"), R(V, c0, c0 + 512), True, False), (R(bank, 0, 511), cb("nI"), R(V, c0 + 1, c0 + 512), False, False),
+        mm([(q(bank, 0, 4), cb("I"), R(V, c0, c0 + 512), True, False)])
+        mm([(R(bank, 0, 511), cb("nI"), R(V, c0 + 1, c0 + 512), False, False),
             (R(bank, 15, 496, 16), cb("I"), R(V, c0 + 16, c0 + 512, 16), False, False), (R(bank, 15, 512, 16), cb("nI"), R(V, c0, c0 + 512, 16), False, True)])
         act(b("cmp", c0, c0 + 512), q(bank, 0, 4), AF.Sign, -0.5)
-    mm([(q(pa, 0, 2), cb("ones"), cb("cC"), True, False)] + ([(q(pa, 1), b("h"), ch("odd"), False, False)] if t > 1 else []))
+    mm([(q(pa, 0, 2), cb("ones"), cb("cC"), True, False)] + ([(q(pa, 1), b("h"), cb("odd"), False, False)] if t > 1 else []))
     for k in range(0, 16, 4):
         mm([(R(pa, j, 256, 16), R("cmp%d" % h, j, 2048, 16), cb("b16"), False, j == 15) for j in range(k, k + 4)])
     scan(q(pb, 1), cb("keep"), q(pa, 0), A.mult, A.add)
@@ -348,33 +312,33 @@ def half_round(t, h, hop):
     act(b("q2"), q(pa, 0), AF.Sign, -2.5)
     ts(b("r"), q(pb, 1), M4, A.add, M4, A.subtract)
     tt(b("d"), b("r"), q(pb, 1), A.subtract)
-    tt(R("d%d" % h, 0, 128, 16), km, b("r8", 0, 8), A.subtract)
-    scan(b("X"), cb("keep"), b("d"), A.mult, A.add)
-    rev = lambda n: R("%s%d" % (n, h), 0, 128, -1)
-    scan(rev("Mx"), cb("neg"), rev("X"), A.add, A.max)
-    scan(rev("Mn"), cb("pos"), rev("X"), A.add, A.min)
-    ts(b("r16"), b("X"), M16, A.add, M16, A.subtract)
-    ts(b("r2"), b("X"), 391.0, A.add)
+    scan(b("Xr"), cb("keep"), b("d"), A.mult, A.add)
+    scan(rev("Mx"), cb("neg"), rev("Xr"), A.add, A.max)
+    scan(rev("Mn"), cb("pos"), rev("Xr"), A.add, A.min)
     mm(group(q(pb, 0), [(b("Mx"), cb("I")), (b("Mn"), cb("nI"))]))
     act(b("LT"), q(pb, 0), AF.Copy)
+    tt(R("d%d" % h, 0, 128, 16), km, b("r8", 0, 8), A.subtract)
+    scan(b("X"), cb("keep"), b("d"), A.mult, A.add)
+    ts(b("r16"), b("X"), M16, A.add, M16, A.subtract)
+    ts(b("r2"), b("X"), 391.0, A.add)
     XA, XB = q(pc, 1), q(pd, 2)
     mm([(XA, cb("I128"), b("hS"), True, False)])
-    mm([(XB, ch("I"), es, True, False), (XB, cb("n127"), b("hS"), False, False)])
+    mm([(XB, cb("I"), es, True, False), (XB, cb("n127"), b("hS"), False, False)])
     mm([(XA, b("q1"), cb("wq1"), False, False), (XA, b("q2"), cb("wq2"), False, False), (XB, b("q2"), cb("wt%d" % t), False, False)])
-    mm([(XA, b("r2"), cb("p256"), False, False), (XA, b("r16"), cb("m256"), False, False)])
-    mm([(XB, b("r2"), cb("p256"), False, False), (XB, b("r16"), cb("m256"), False, False)])
-    mm([(XA, cb("Sp"), b("LT"), False, True)])
-    mm([(XB, cb("Sp"), b("LT"), False, True)])
-    ts(b("XK", 0, 128), XA, col(1), A.add, 161.5 - 129 - 256 * 384 - 2048, A.add)
-    ts(b("XK", 128, 256), XB, col(1), A.add, 16383 + (77 * t - 31) / 2 - 256 * 384, A.add)
+    mm([(XA, cb("Sp"), b("LT"), False, False)])
+    mm([(XB, cb("Sp"), b("LT"), False, False)])
+    mm([(XA, b("r2"), cb("p256"), False, False), (XA, b("r16"), cb("m256"), False, True)])
+    mm([(XB, b("r2"), cb("p256"), False, False), (XB, b("r16"), cb("m256"), False, True)])
+    ts(b("XK", 0, 128), XA, col(3), A.add, 161.5 - 129 - 256 * 384 - 2048, A.add)
+    ts(b("XK", 128, 256), XB, col(3), A.add, 16383 + (77 * t - 31) / 2 - 256 * 384, A.add)
     mm(group(q(pa, 2), [(ch("DAh"), es), (ch("DAl"), es)]) + group(q(pa, 3), [(ch("DBh"), es), (ch("DBl"), es)]))
     act(b("AB", 0, 256), q(pa, 2, 2), AF.Copy)
-    mm(group(q(pa, 0), [(zs, ch("I")), (cb("ones"), cb("c16"))]))
+    mm(group(q(pa, 0), [(zs, cb("I")), (cb("ones"), cb("c16"))]))
     U, UA = q(pb, 2), R(pb, 256, 320)
     mm([(U, cb("ones"), cb("U0"), True, False), (UA, cb("mB"), R("X%d" % h, 0, 128, 2), False, False), (UA, cb("pB"), R("r2%d" % h, 0, 128, 2), False, False)])
     for p in range(8):
         ts(b("PK", 256 * p, 256 * p + 256), b("XK", 0, 256), 512.0 * (p - 4), A.max, 512.0 * (p - 3), A.min)
-        mm([(R(pb, 256 + p, 384, 8), b("PK", 256 * p + 128 * k, 256 * p + 128 * k + 128), ch("wa" if k == 0 else "wb"), False, p == 7 and k == 1) for k in (0, 1)])
+        mm([(R(pb, 256 + p, 384, 8), b("PK", 256 * p + 128 * k, 256 * p + 128 * k + 128), cb("wa" if k == 0 else "wb"), False, p == 7 and k == 1) for k in (0, 1)])
     act(b("Bs", 0, 64), R(pb, 320, 384), AF.Copy)
     tt(R("v%d" % h, 0, 128, 2), b("Bs", 0, 64), UA, A.max)
     tt(R("v%d" % h, 1, 128, 2), b("Bs", 0, 64), UA, A.min)
@@ -400,14 +364,15 @@ def half_round(t, h, hop):
     ts(b("h"), q(pd, 0), col(5), A.is_equal)
     mm(group(q(pd, 0), [(ch("TCh"), b("h")), (ch("TCl"), b("h"))]) + group(q(pd, 1), [(ch("TSh"), b("h")), (ch("TSl"), b("h"))]))
     tt(b("PP", 0, 256), b("AB", 0, 256), q(pd, 0, 2), A.mult)
-    mm(group(q(pd, 2), [(ch("triP"), b("h")), (cf("IV"), b("PP", 0, 128)), (cf("IV"), b("PP", 128, 256))]))
+    for x in group(q(pd, 2), [(cb("triP"), b("h")), (cf("IV"), b("PP", 0, 128)), (cf("IV"), b("PP", 128, 256))]):
+        mm([x])
     ts(b("fm"), q(pd, 2), -8192.0, A.add, -2048.0, A.max)
     tk = lambda s: b("tk", 128 * s, 128 * s + 128)
     for s, bank in enumerate((pb, pa, pc, pb, pa)):
         K = q(bank, 0)
-        terms = [(b("del"), cb("m2048")), (b("val"), ch("I"))] + [(ch("Sh%d" % j), tk(j)) for j in range(s)]
+        terms = [(b("del"), cb("m2048")), (b("val"), cb("I"))] + [(cb("Sh%d" % j), tk(j)) for j in range(s)]
         if s == 4:
-            terms[2:2] = [(ch("triM"), b("h")), (ch("I"), b("fm"))]
+            terms[4:4] = [(cb("triM"), b("h")), (cb("I"), b("fm"))]
         for x in group(K, terms):
             mm([x])
         if s < 4:
@@ -417,13 +382,13 @@ def half_round(t, h, hop):
 
 
 def build():
-    def load(q, sem, dst, src):
+    def load(q, sem, dst, src, dur):
         op(q, 60, [lambda g, T: g.sync.dma_start(ap(T, dst), T[src][:])], [], [("dma_" + sem, 0, 1, 1)])
-        op("X", 2500, [], [("dma_" + sem, 0, 1, 1)], [dst], sem=sem, inc=16)
+        op("X", dur, [], [("dma_" + sem, 0, 1, 1)], [dst], sem=sem, inc=16)
 
-    load("Y", "ld0", R("ei", 0, 256), "enz")
-    load("Y", "ld1", R("ct", 0, 4096), "cont")
-    load("Y", "ld2", R("zi", 0, 256), "subs")
+    load("Y", "ld0", R("ei", 0, 256), "enz", 2500)
+    load("Y", "ld2", R("zi", 0, 256), "subs", 2500)
+    load("Y", "ld1", R("ct", 0, 4096), "cont", 4000)
 
     def send(dst_of, src, dst, sem):
         def f(g, T, core, topo):
@@ -440,9 +405,11 @@ def build():
         n = o + 256
         s = "%s%d%d" % (kind, t, h)
         if kind == "z":
-            send(1, R("eo", o, o + 128), R("zo", n, n + 128), s)
+            if t == 1:
+                send(1, R("eo", o, o + 128), R("zo", n, n + 128), s)
         elif t < RO:
             send(2, R("po", o, o + 128), R("eo", n, n + 128), s)
+            send(3, R("po", o, o + 128), R("zo", n + 256, n + 384), "z%d%d" % (t + 1, h))
         else:
             send(2, R("pz", 128 * h, 128 * h + 128), R("ef", 128 * h, 128 * h + 128), s)
 
@@ -450,26 +417,24 @@ def build():
         for h in range(NH):
             c = R(k + "i", 128 * h, 128 * h + 128)
             cp(R(k + "o", 128 * h, 128 * h + 128), c)
-            ts(R(k + "s", 128 * h, 128 * h + 128), c, -2048.0, A.add)
+            ts(R(k + "s", 128 * h, 128 * h + 128), R(k + "o", 128 * h, 128 * h + 128), -2048.0, A.add)
     constants()
     for t in range(1, RO + 1):
         for h in range(NH):
             half_round(t, h, hop)
     o = 256 * RO
-    for h in range(NH):
-        cp(R("yz", 128 * h, 128 * h + 128), R("zo", o + 128 * h, o + 128 * h + 128))
-    for src, dst in (("yz", "ysub"), ("ef", "yenz")):
-        for h in range(NH):
-            op("Y", 60, [lambda g, T, src=src, dst=dst, h=h: g.sync.dma_start(T[dst][:, 128 * h:128 * h + 128], T[src][:, 128 * h:128 * h + 128])],
-               [R(src, 128 * h, 128 * h + 128)], [], sem="out", inc=16)
+    cp(R("yz", 0, 256), R("zo", o, o + 256))
+    for src, dst, parts in (("yz", "ysub", 1), ("ef", "yenz", NH)):
+        w = 256 // parts
+        for h in range(parts):
+            op("Y", 60, [lambda g, T, src=src, dst=dst, c=w * h, w=w: g.sync.dma_start(T[dst][:, c:c + w], T[src][:, c:c + w])],
+               [R(src, w * h, w * h + w)], [], sem="out", inc=16)
 
 
 def analyse():
     hist = {}
     for i, x in enumerate(OPS):
         deps = {}
-        if x["dep"] is not None:
-            deps[x["dep"]] = True
         acc = [(r, False) for r in x["r"]] + [(w, True) for w in x["w"]]
         for (buf, lo, hi, stp), wr in acc:
             psum = buf in SCRATCH and SCRATCH[buf][0] == "psum"
@@ -489,58 +454,63 @@ def analyse():
         x["deps"] = deps
         for (buf, lo, hi, stp), wr in acc:
             lst = hist.setdefault(buf, [])
-            psum = buf in SCRATCH and SCRATCH[buf][0] == "psum"
             if wr and stp == 1:
-                lst[:] = [e for e in lst if not (lo <= e[0] and e[1] <= hi and not (psum and OPS[e[4]]["e"] != x["e"] and False)) or e[4] == i]
-            if psum and wr and x["e"] == "P" and lo == 0 and False:
-                lst.clear()
+                lst[:] = [e for e in lst if not (lo <= e[0] and e[1] <= hi) or e[4] == i]
             lst.append((lo, hi, stp, wr, i))
-            if psum:
-                while len(lst) > 400:
-                    lst.pop(0)
 
 
-def schedule(rw=RW, bonus=BONUS):
+QN = {"G": "g", "R": "g"}
+
+
+def place(pred, succ, pri):
     n = len(OPS)
-    rk = [0] * n
-    for (a, k), (z, _) in zip(MARK, MARK[1:] + [(n, 0)]):
-        for i in range(a, z):
-            rk[i] = k
-    succ, nd = [[] for _ in range(n)], [0] * n
-    for i, x in enumerate(OPS):
-        nd[i] = len(x["deps"])
-        for j in x["deps"]:
-            succ[j].append(i)
-    path = [0.0] * n
-    for i in range(n - 1, -1, -1):
-        path[i] = OPS[i]["d"] + max([path[s] + LAG for s in succ[i]], default=0.0)
-        if rk[i] == 0:
-            rk[i] = min([rk[s] for s in succ[i]], default=99)
-    pri = [path[i] - rw * rk[i] + bonus.get(OPS[i]["w"][0][0][:-1] if OPS[i]["w"] else "", 0.0) for i in range(n)]
-    ready, t0, free, order, end = {}, [0.0] * n, {}, [], [0.0] * n
-    for i in range(n):
-        if nd[i] == 0:
-            ready.setdefault(OPS[i]["e"], set()).add(i)
-    while len(order) < n:
-        best = None
-        for e, s in ready.items():
-            f = 0.0 if e == "X" else free.get(e, 0.0)
-            for i in s:
-                k = (max(f, t0[i]), -pri[i], i)
-                if best is None or k < best[0]:
-                    best = (k, i, e)
-        (st, _, _), i, e = best
-        ready[e].discard(i)
-        end[i] = st + OPS[i]["d"]
+    left = [len(p) for p in pred]
+    ready = {(pri[i], i) for i in range(n) if left[i] == 0}
+    t0, st, busy = [0.0] * n, [0.0] * n, {}
+    while ready:
+        x = min(ready)
+        ready.discard(x)
+        i = x[1]
+        e, d, t = OPS[i]["e"], OPS[i]["d"], t0[i]
         if e != "X":
-            free[e] = end[i]
-        order.append(i)
-        for s in succ[i]:
-            t0[s] = max(t0[s], end[i] + (LAG if OPS[s]["deps"][i] else 0.0))
-            nd[s] -= 1
-            if nd[s] == 0:
-                ready.setdefault(OPS[s]["e"], set()).add(s)
-    return order, max(end)
+            a, z = busy.setdefault(QN.get(e, e), ([], []))
+            j = len(z)
+            while j and z[j - 1] > t:
+                j -= 1
+            while j < len(a) and a[j] < t + d:
+                t = max(t, z[j])
+                j += 1
+            a.insert(j, t)
+            z.insert(j, t + d)
+        st[i] = t
+        for s, w in succ[i]:
+            t0[s] = max(t0[s], t + d + (LAG if w else 0.0))
+            left[s] -= 1
+            if left[s] == 0:
+                ready.add((pri[s], s))
+    return st
+
+
+def schedule(lead=LEAD, passes=PASSES, bonus=BONUS):
+    n = len(OPS)
+    pred, succ, half, tail = [list(x["deps"].items()) for x in OPS], [[] for _ in range(n)], [0] * n, [0.0] * n
+    for i, p in enumerate(pred):
+        for j, w in p:
+            succ[j].append((i, w))
+    for (a, k), (z, _) in zip(MARK, MARK[1:] + [(n, 0)]):
+        half[a:z] = [k % 2] * (z - a)
+    for i in range(n - 1, -1, -1):
+        tail[i] = OPS[i]["d"] + max([tail[s] + (LAG if w else 0.0) for s, w in succ[i]], default=0.0)
+    pri = [lead * half[i] - tail[i] - bonus.get(OPS[i]["w"][0][0][:-1] if OPS[i]["w"] else "", 0.0) for i in range(n)]
+    best = None
+    for _ in range(passes):
+        st = place(pred, succ, pri)
+        tot = max(st[i] + OPS[i]["d"] for i in range(n))
+        if best is None or tot < best[0]:
+            best = (tot, st)
+        back = place(succ, pred, [-(st[i] + OPS[i]["d"]) for i in range(n)])
+        pri = [-(back[i] + OPS[i]["d"]) for i in range(n)]
+    return sorted(range(n), key=lambda i: (best[1][i], i)), best[0]
 
 
 PLAN = []
@@ -550,9 +520,7 @@ def plan():
     if not PLAN:
         build()
         analyse()
-        order, tot = schedule()
-        PLAN.append(order)
-        PLAN.append(tot)
+        PLAN.extend(schedule())
     return PLAN[0]
 
 
@@ -564,7 +532,6 @@ def rank_program(g, core, T, topo):
         return
     order = plan()
     queue = {"P": g.tensor, "V": g.vector, "S": g.scalar, "G": g, "R": g, "Y": g.sync}
-    qname = {"G": "g", "R": "g"}
     cnt, done, know, clock, sent = {}, {}, {}, {}, 0
     for i in order:
         x = OPS[i]
@@ -573,8 +540,7 @@ def rank_program(g, core, T, topo):
             done[i] = (x["sem"], x["inc"])
             clock[i] = {}
             continue
-        qn = qname.get(e, e)
-        kn = know.setdefault(qn, {})
+        kn = know.setdefault(QN.get(e, e), {})
         need = {}
         for j, w in x["deps"].items():
             if w and done.get(j) is not None:

@@ -7,12 +7,18 @@ NH = 2
 FV, FS = 20.0, 30.0
 SC = 0.83
 PC = 0.5
-GC = 1.35
-NET = 4500.0
+GC = 1.56
+OTHER = [(0.7, 0.8, 120.0), (1.15, 1.2, 200.0)]
+NET = 4000.0
 LAG = 150.0
-LEAD, PASSES, BONUS = 3200.0, 12, {"Xr": 1000.0, "N": 4000.0}
+LEAD, TRIES = 6000.0, 4000
 VCUT = "SVSV"
-YCUT = "SSSS"
+YCUT = ["VVVS"] + ["SSSS"] * 7
+ONS = ("r16", "r4", "zs", "hS", "del")
+XR = True
+SUB = 1
+BANKS = "caba"
+MXW = 4
 SCRATCH, SEMAPHORES = {}, []
 
 
@@ -27,24 +33,17 @@ _sb("eo", 1280, U16); _sb("es", 1280, F16); _sb("zo", 1280, U16); _sb("zs", 1280
 _sb("po", 768, U16)
 _sb("pz", 256, F32); _sb("ef", 256, F32); _sb("yz", 256, F32)
 IDENT = {"nI": -1.0, "I128": 1.0 / 128, "n127": -127.0 / 128, "p256": 256.0, "m256": -256.0, "wq1": -113.0, "wq2": 16.5,
-         "pB": 2.0 ** 21, "mB": -2.0 ** 21, "mh": -0.5, "mq": -0.25, "pq": 0.25, "m2048": -2048.0, "p4096": 4096.0}
+         "pB": 2.0 ** 21, "mB": -2.0 ** 21, "m2048": -2048.0, "p4096": 4096.0}
 for _t in range(1, RO + 1):
     IDENT["wt%d" % _t] = (77 * _t - 95) / 2
 CB = {}
 for _n, _w in [("I", 128)] + [(_x, 128) for _x in IDENT] + [(_x, 128) for _x in (
-        "Sp", "ones", "zero", "c16", "c256", "cD", "neg", "pos", "keep", "U0", "GG", "triP", "triM", "odd", "Sh0", "Sh1", "Sh2", "Sh3", "t1", "t2")] + [
+        "Sp", "ones", "zero", "c16", "c256", "cD", "neg", "pos", "keep", "U0", "GG", "triP", "triM", "odd", "Sh0", "Sh1", "Sh2", "Sh3", "Sh4", "Sh5", "t1", "t2")] + [
         ("cC", 256), ("b16", 16), ("b32", 16), ("bm16", 16), ("wa", 16), ("wb", 16)]:
     CB[_n] = (sum(w for _, w in CB.values()), _w)
 _sb("cb", sum(w for _, w in CB.values()))
-CF = {}
-for _n in ("DA", "DB", "TC", "TS", "IV"):
-    CF[_n] = (128 * len(CF), 128)
-_sb("cf", 128 * len(CF), F32)
-CH = {}
-for _n, _w in [(_x + _y, 128) for _y in "hl" for _x in ("DA", "DB", "TC", "TS")]:
-    CH[_n] = (sum(w for _, w in CH.values()), _w)
-_sb("ch", sum(w for _, w in CH.values()), F16)
-_sb("b8", 24, F32)
+_sb("cf", 512, F32); _sb("ch", 1024, F16)
+_sb("b8", 16, F32)
 _sb("col", 16, F32)
 for _n, _w, _d in (("pi", 2, I32), ("u64", 64, F32), ("o64", 64, F32), ("n64", 64, I32), ("w64", 64, F32), ("x64", 64, F32), ("a64", 64, F32)):
     _sb("k_" + _n, _w, _d)
@@ -53,8 +52,8 @@ for _h in range(NH):
                        ("r8", 8, F32), ("d", 128, BF), ("q1", 128, BF), ("q2", 128, BF), ("r", 128, F32), ("Xr", 128, BF), ("X", 128, BF), ("Mx", 128, BF),
                        ("Mn", 128, BF), ("LT", 128, BF), ("r16", 128, BF), ("r2", 128, BF), ("hS", 128, BF), ("XK", 256, F16), ("Bs", 64, F32),
                        ("v", 128, I32), ("w", 128, I32), ("S2", 128, F32), ("pr", 128, I32), ("F", 128, I32), ("v0", 128, I32), ("v1", 128, I32),
-                       ("val", 128, F16), ("del", 128, BF), ("E2", 128, BF), ("rb", 384, BF), ("N", 128, BF), ("mk", 512, BF), ("tk", 512, F16),
-                       ("h", 128, F16), ("AB", 256, F32), ("PP", 256, F32), ("fm", 128, F16)):
+                       ("val", 128, F16), ("del", 128, BF), ("E2", 128, BF), ("r4", 128, BF), ("de", 128, BF), ("mk", 768, BF), ("tk", 768, F16),
+                       ("h", 128, BF), ("AB", 256, F32), ("PP", 256, F32), ("fm", 128, F16)):
         _sb("%s%d" % (_n, _h), _w, _d)
     for _n in "abcd":
         SCRATCH["ps%s%d" % (_n, _h)] = ("psum", [128, 512], F32)
@@ -73,14 +72,8 @@ def cb(n, lo=0, hi=None):
     return R("cb", c + lo, c + (w if hi is None else hi))
 
 
-def cf(n):
-    c, w = CF[n]
-    return R("cf", c, c + w)
-
-
-def ch(n, lo=0, hi=None):
-    c, w = CH[n]
-    return R("ch", c + lo, c + (w if hi is None else hi))
+def table(j, x):
+    return [(R("ch", c + j, c + 512, 4), x) for c in (0, 512)]
 
 
 def ap(T, r):
@@ -151,11 +144,11 @@ def act(out, a, func, bias=None, scale=None):
     def f(g, T):
         kw = {}
         if bias is not None:
-            kw["bias"] = bias
+            kw["bias"] = ap(T, bias) if isinstance(bias, tuple) else bias
         if scale is not None:
             kw["scale"] = ap(T, scale) if isinstance(scale, tuple) else scale
         return g.scalar.activation(ap(T, out), ap(T, a), func, **kw)
-    return op("S", ncol(out) * SC + FS, [f], [a] + ([scale] if isinstance(scale, tuple) else []), [out])
+    return op("S", max(64, ncol(out)) * SC + FS, [f], [a] + [s for s in (bias, scale) if isinstance(s, tuple)], [out])
 
 
 def gather(eng, out, offs):
@@ -200,16 +193,16 @@ def constants():
             act(cb(n), cb("I"), AF.Copy, scale=c)
         else:
             ts(cb(n), cb("I"), c, A.mult)
-    b8, t8, e8 = R("b8", 0, 8), R("b8", 8, 16), R("b8", 16, 24)
+    b8, t8 = R("b8", 0, 8), R("b8", 8, 16)
     select(t8, cb("ones", 0, 8), [[-16, 8]], 0, 1, A.is_ge, 0.0)
     select(b8, t8, [[16, 8]], 15, -1, A.is_ge, 0.0)
     for half in (0, 8):
         act(cb("b16", half, half + 8), b8, AF.Copy)
     for n, c in (("b32", 32.0), ("bm16", -16.0)):
         act(cb(n, 0, 8), b8, AF.Copy, scale=c)
-    act(e8, b8, AF.Copy, scale=0.125)
     iota(cb("cD"), [[0, 8], [2, 16]], -15, 0)
-    select(cb("keep"), cb("ones"), row, 0, 0, A.not_equal, 0.0)
+    act(cb("keep"), cb("cD"), AF.Sigmoid, 128.0 * 14, 128.0)
+    OPS[-1]["d"] += 1300.0
     ts(cb("neg"), cb("keep"), 1000.0, A.mult, -1000.0, A.add)
     ts(cb("pos"), cb("keep"), -1048576.0, A.mult, 1048576.0, A.add)
     ts(cb("cC", 0, 128), cb("keep"), 1.0 / 128, A.mult, -1.0 / 128, A.add)
@@ -222,7 +215,7 @@ def constants():
     ts(col(2), col(1), -1.0, A.mult, 1.0, A.add)
     ts(col(3), ri, 14.0, A.is_le, -4096.0, A.mult)
     ts(col(4), col(1), -2.0 ** 15, A.mult, -390.0 * 2 ** 14, A.add)
-    ts(col(5), ri, -1.0, A.mult, 16.0, A.add)
+    ts(col(5), ri, -16384.0, A.mult, 131072.0, A.add)
     ts(col(6), col(1), -2.0 / 8192, A.mult)
     for c in (0, 1):
         act(cb("wb", 8 * c, 8 * c + 8), b8, AF.Copy, scale=col(2 - c))
@@ -231,8 +224,10 @@ def constants():
     fill(cb("U0", 64, 128), 0.0)
     select(cb("t1"), cb("p4096"), diag, -1, 1, A.not_equal, -4096.0)
     select(cb("Sp"), cb("t1"), row, -15, 0, A.not_equal, 0.0)
-    for s, (n, c) in enumerate((("nI", 1.0), ("mh", 0.5), ("mq", 0.25), ("pq", -0.25))):
-        select(cb("Sh%d" % s), cb(n), diag, -2 ** s, 1, A.not_equal, c)
+    for s, (was, now) in enumerate(((0, 1), (1, 2), (2, 3), (0, 4), (4, 8), (8, 12))):
+        if was:
+            select(cb("t1"), cb("zero"), diag, -was, 1, A.not_equal, -1.0)
+        select(cb("Sh%d" % s), cb("t1" if was else "nI"), diag, -now, 1, A.not_equal, 1.0)
     fill(cb("t2"), 8192.0)
     select(cb("t2"), cb("t2"), blk, 0, 1, A.is_ge, 0.0)
     select(cb("GG"), cb("t2"), [[16, 8], [0, 16]], 15, -1, A.is_ge, 0.0)
@@ -240,9 +235,9 @@ def constants():
     act(cb("triM"), cb("triP"), AF.Copy, scale=-0.25)
     act(cb("odd"), cb("GG"), AF.Copy, scale=col(6))
     u, off, n, W, X2, AC = K("u64"), K("o64"), K("n64"), K("w64"), K("x64"), K("a64")
-    iota(u, [[0, 4], [1, 16]], 0, 0)
+    iota(K("u64", 0, 16), [[1, 16]], 0, 0)
     for j, c in enumerate((14.0, 2.0, 0.0, 12.0)):
-        ts(K("n64", 16 * j, 16 * j + 16), K("u64", 0, 16), ri, A.mult, c, A.add)
+        ts(R("k_n64", j, 64, 4), K("u64", 0, 16), ri, A.mult, c, A.add)
     ts(n, n, 15, A.bitwise_and)
     ts(off, n, -8.0, A.add)
     act(off, off, AF.Abs)
@@ -255,10 +250,8 @@ def constants():
         tt(AC, AC, X2, A.mult)
         ts(AC, AC, cc[k], A.add)
     tt(AC, AC, W, A.mult)
-    for j, name in enumerate(("DA", "DB", "TC", "TS", "IV")):
-        c = CF[name][0]
-        for q in range(8):
-            act(R("cf", c + 16 * q, c + 16 * q + 16), K("a64", 16 * (j % 4), 16 * (j % 4) + 16), AF.Copy, scale=R("b8", q + 16 * (j // 4), q + 16 * (j // 4) + 1))
+    for q in range(8):
+        act(R("cf", 64 * q, 64 * q + 64), AC, AF.Copy, scale=R("b8", q, q + 1))
     for j in (0, 256):
         cp(R("ch", j, j + 256), R("cf", j, j + 256))
         tt(R("ch", 512 + j, 768 + j), R("cf", j, j + 256), R("ch", j, j + 256), A.subtract)
@@ -276,34 +269,39 @@ def half_round(t, h, hop):
     eo, es, zo, zs = R("eo", o, o + 128), R("es", o, o + 128), R("zo", o, o + 128), R("zs", o, o + 128)
     col = lambda j: R("col", j, j + 1)
     rev = lambda n: R("%s%d" % (n, h), 0, 128, -1)
+    rnd = lambda n, out, x, c: act(out, x, AF.Identity, c) if n in ONS else ts(out, x, c, A.add)
     hop(t, h, "z")
     V, Y = "V%d" % h, "Y%s%d" % ("ab"[t % 2], h)
-    for buf, ls, cuts in ((V, eo, VCUT), (Y, zo, YCUT)):
+    for buf, ls, cuts in ((V, eo, VCUT), (Y, zo, YCUT[2 * t + h - 2])):
         w = 128 // len(cuts)
         for c, eng in enumerate(cuts):
             gather(eng, R(buf, 16 * w * c, 16 * w * (c + 1)), R(ls[0], ls[1] + w * c, ls[1] + w * (c + 1)))
     if t > 1:
-        ts(es, eo, -2048.0, A.add)
-        ts(zs, zo, -2048.0, A.add)
-    ts(b("hS"), es, 2048 + 16448.5, A.add)
+        rnd("es", es, eo, -2048.0)
+        rnd("zs", zs, zo, -2048.0)
+    rnd("hS", b("hS"), es, 2048 + 16448.5)
     v15 = R(V, 15, 2048, 16)
+
+    def compare(c):
+        bank, c0 = "ps%s%d" % (BANKS[c], h), 512 * c
+        mm([(q(bank, 0, 4), cb("I"), R(V, c0, c0 + 512), True, False), (R(bank, 0, 511), cb("nI"), R(V, c0 + 1, c0 + 512), False, False),
+            (R(bank, 15, 496, 16), cb("I"), R(V, c0 + 16, c0 + 512, 16), False, False), (R(bank, 15, 512, 16), cb("nI"), R(V, c0, c0 + 512, 16), False, True)])
+        act(b("cmp", c0, c0 + 512), q(bank, 0, 4), AF.Sign, -0.5)
+
+    for c in range(4):
+        compare(c)
     mm([(q(pd, 1), cb("c256"), cb("cD"), True, False)])
     for k in range(0, 16, 4):
         mm([(R(pd, 128 + p, 256, 16), R(Y, p, 2048, 16), cb("bm16", 0, 8), False, False) for p in range(k, k + 4)])
-    mm([(q(pc, 0), cb("I"), v15, True, True)])
-    for p in range(16):
-        tt(b("mx", 128 * p, 128 * p + 128), R(Y, p, 2048, 16), q(pc, 0), A.max)
-    for p in range(0, 16, 2):
-        mm([(R(pd, 128 + j, 256, 16), b("mx", 128 * j, 128 * j + 128), cb("b32", 0, 8), False, j == 15) for j in (p, p + 1)])
+    mm([(R(pc, j, 128 * MXW, MXW), cb("I"), v15, True, True) for j in range(MXW)])
+    step, wide = 16 // MXW, 128 * MXW
+    for c in range(step):
+        tt(b("mx", wide * c, wide * (c + 1)), R(Y, c, 2048, step), q(pc, 0, MXW), A.max)
+        mm([(R(pd, 128 + c + step * j, 256, 16), R("mx%d" % h, wide * c + j, wide * (c + 1), MXW), cb("b32", 0, 8), False, c + step * j == 15)
+            for j in range(MXW)])
     scan(b("km"), cb("pos"), q(pd, 1), A.add, A.min)
     km = R("km%d" % h, 15, 128, 16)
     ts(b("r8", 0, 8), km, M16, A.add, M16, A.subtract)
-    for c in range(4):
-        bank, c0 = (pa if c % 2 == 0 else pb), 512 * c
-        mm([(q(bank, 0, 4), cb("I"), R(V, c0, c0 + 512), True, False)])
-        mm([(R(bank, 0, 511), cb("nI"), R(V, c0 + 1, c0 + 512), False, False),
-            (R(bank, 15, 496, 16), cb("I"), R(V, c0 + 16, c0 + 512, 16), False, False), (R(bank, 15, 512, 16), cb("nI"), R(V, c0, c0 + 512, 16), False, True)])
-        act(b("cmp", c0, c0 + 512), q(bank, 0, 4), AF.Sign, -0.5)
     mm([(q(pa, 0, 2), cb("ones"), cb("cC"), True, False)] + ([(q(pa, 1), b("h"), cb("odd"), False, False)] if t > 1 else []))
     for k in range(0, 16, 4):
         mm([(R(pa, j, 256, 16), R("cmp%d" % h, j, 2048, 16), cb("b16"), False, j == 15) for j in range(k, k + 4)])
@@ -312,28 +310,39 @@ def half_round(t, h, hop):
     act(b("q2"), q(pa, 0), AF.Sign, -2.5)
     ts(b("r"), q(pb, 1), M4, A.add, M4, A.subtract)
     tt(b("d"), b("r"), q(pb, 1), A.subtract)
-    scan(b("Xr"), cb("keep"), b("d"), A.mult, A.add)
-    scan(rev("Mx"), cb("neg"), rev("Xr"), A.add, A.max)
-    scan(rev("Mn"), cb("pos"), rev("Xr"), A.add, A.min)
-    mm(group(q(pb, 0), [(b("Mx"), cb("I")), (b("Mn"), cb("nI"))]))
-    act(b("LT"), q(pb, 0), AF.Copy)
+    if XR:
+        scan(b("Xr"), b("r"), q(pb, 1), A.add, A.subtract)
     tt(R("d%d" % h, 0, 128, 16), km, b("r8", 0, 8), A.subtract)
     scan(b("X"), cb("keep"), b("d"), A.mult, A.add)
-    ts(b("r16"), b("X"), M16, A.add, M16, A.subtract)
-    ts(b("r2"), b("X"), 391.0, A.add)
+    scan(rev("Mx"), cb("neg"), rev("Xr" if XR else "X"), A.add, A.max)
+    scan(rev("Mn"), cb("pos"), rev("Xr" if XR else "X"), A.add, A.min)
+    mm(group(q(pb, 0), [(b("Mx"), cb("I")), (b("Mn"), cb("nI"))]))
+    act(b("LT"), q(pb, 0), AF.Copy)
+    editor = [(cb("Sp"), b("LT"))]
+    rnd("r16", b("r16"), b("X"), 3072.0)
+    rnd("r2", b("r2"), b("X"), 391.0)
     XA, XB = q(pc, 1), q(pd, 2)
     mm([(XA, cb("I128"), b("hS"), True, False)])
     mm([(XB, cb("I"), es, True, False), (XB, cb("n127"), b("hS"), False, False)])
     mm([(XA, b("q1"), cb("wq1"), False, False), (XA, b("q2"), cb("wq2"), False, False), (XB, b("q2"), cb("wt%d" % t), False, False)])
-    mm([(XA, cb("Sp"), b("LT"), False, False)])
-    mm([(XB, cb("Sp"), b("LT"), False, False)])
-    mm([(XA, b("r2"), cb("p256"), False, False), (XA, b("r16"), cb("m256"), False, True)])
-    mm([(XB, b("r2"), cb("p256"), False, False), (XB, b("r16"), cb("m256"), False, True)])
-    ts(b("XK", 0, 128), XA, col(3), A.add, 161.5 - 129 - 256 * 384 - 2048, A.add)
-    ts(b("XK", 128, 256), XB, col(3), A.add, 16383 + (77 * t - 31) / 2 - 256 * 384, A.add)
-    mm(group(q(pa, 2), [(ch("DAh"), es), (ch("DAl"), es)]) + group(q(pa, 3), [(ch("DBh"), es), (ch("DBl"), es)]))
-    act(b("AB", 0, 256), q(pa, 2, 2), AF.Copy)
+    for X in (XA, XB):
+        mm([(X, b("r2"), cb("p256"), False, False)])
+        mm([(X, b("r16"), cb("m256"), False, False)])
+        mm([(X, cb("Sp"), b("LT"), False, True)])
+    ts(b("XK", 0, 128), XA, col(3), A.add, 161.5 - 129 + 256 * (3072 - 384) - 2048, A.add)
+    ts(b("XK", 128, 256), XB, col(3), A.add, 16383 + (77 * t - 31) / 2 + 256 * (3072 - 384), A.add)
+    mm(group(q(pa, 2), table(0, es)) + group(q(pa, 3), table(1, es)))
+    act(b("AB", 0, 256), q(pa, 2, 2), AF.Copy, scale=0.125)
     mm(group(q(pa, 0), [(zs, cb("I")), (cb("ones"), cb("c16"))]))
+    mm(group(q(pa, 1), [(b("q1"), cb("m256"))] + editor))
+    act(b("de"), q(pa, 1), AF.Sign, col(3))
+    mm(group(q(pa, 1), [(cb("GG"), b("de"))]))
+    ts(b("h"), q(pa, 1), col(5), A.is_equal)
+    mm(group(q(pd, 0), table(2, b("h"))) + group(q(pd, 1), table(3, b("h"))))
+    tt(b("PP", 0, 256), b("AB", 0, 256), q(pd, 0, 2), A.mult)
+    for x in group(q(pd, 2), [(cb("triP"), b("h")), (R("cf", 0, 512, 4), b("PP", 0, 128)), (R("cf", 0, 512, 4), b("PP", 128, 256))]):
+        mm([x])
+    ts(b("fm"), q(pd, 2), -8192.0, A.add, -2048.0, A.max)
     U, UA = q(pb, 2), R(pb, 256, 320)
     mm([(U, cb("ones"), cb("U0"), True, False), (UA, cb("mB"), R("X%d" % h, 0, 128, 2), False, False), (UA, cb("pB"), R("r2%d" % h, 0, 128, 2), False, False)])
     for p in range(8):
@@ -342,41 +351,39 @@ def half_round(t, h, hop):
     act(b("Bs", 0, 64), R(pb, 320, 384), AF.Copy)
     tt(R("v%d" % h, 0, 128, 2), b("Bs", 0, 64), UA, A.max)
     tt(R("v%d" % h, 1, 128, 2), b("Bs", 0, 64), UA, A.min)
-    ts(b("w"), b("v"), 65535, A.bitwise_and)
-    ts(b("S2"), b("w"), -(8192.0 + 77 * t), A.add, 0.0, A.max)
-    ts(b("del"), b("w"), 32768.0, A.is_ge)
-    tt(b("pr"), b("S2"), q(pa, 0), A.mult)
-    scan(b("E2"), cb("keep"), b("del"), A.mult, A.add)
-    tt(q(pa, 1), b("w"), q(pa, 0), A.max)
-    ts(b("F"), b("pr"), 5, A.arith_shift_right, 4095, A.bitwise_and)
-    tt(b("v0"), b("F"), q(pa, 1), A.add)
-    ts(b("v1"), b("v0"), 32768 + 4095, A.bitwise_and)
-    ts(b("val"), b("v1"), -2048.0, A.add, 2048.0, A.min)
-    rb = lambda s: b("rb", 128 * (s - 1), 128 * s)
-    for s in (1, 2, 3):
-        ts(rb(s), b("E2"), 192.0 * 2 ** s - (2 ** s - 1) / 2, A.add)
-    scan(rev("N"), cb("neg"), rev("E2"), A.add, A.max)
-    mm(group(q(pc, 0), [(b("E2"), cb("I")), (rb(1), cb("nI"))]) + group(q(pc, 1), [(rb(1), cb("I")), (rb(2), cb("nI"))]))
-    act(b("mk", 0, 256), q(pc, 0, 2), AF.Copy, 384.0)
-    mm(group(q(pc, 2), [(rb(2), cb("I")), (rb(3), cb("nI"))]) + group(q(pc, 3), [(rb(3), cb("mh"))]))
-    act(b("mk", 256, 512), q(pc, 2, 2), AF.Copy, 768.0)
-    mm(group(q(pd, 0), [(b("N"), cb("I"))]))
-    ts(b("h"), q(pd, 0), col(5), A.is_equal)
-    mm(group(q(pd, 0), [(ch("TCh"), b("h")), (ch("TCl"), b("h"))]) + group(q(pd, 1), [(ch("TSh"), b("h")), (ch("TSl"), b("h"))]))
-    tt(b("PP", 0, 256), b("AB", 0, 256), q(pd, 0, 2), A.mult)
-    for x in group(q(pd, 2), [(cb("triP"), b("h")), (cf("IV"), b("PP", 0, 128)), (cf("IV"), b("PP", 128, 256))]):
-        mm([x])
-    ts(b("fm"), q(pd, 2), -8192.0, A.add, -2048.0, A.max)
+    for c in range(SUB):
+        s = lambda n: R("%s%d" % (n, h), c, 128, SUB)
+        Z, mx = R(pa, c, 128, SUB), R(pa, 128 + c, 256, SUB)
+        ts(s("w"), s("v"), 65535, A.bitwise_and)
+        ts(s("S2"), s("w"), -(8192.0 + 77 * t), A.add, 0.0, A.max)
+        tt(s("pr"), s("S2"), Z, A.mult)
+        ts(s("F"), s("pr"), 5, A.arith_shift_right, 4095, A.bitwise_and)
+        if c == SUB - 1:
+            if "del" in ONS:
+                act(b("del"), b("w"), AF.Sigmoid, -32767.5 * 256, 256.0)
+            else:
+                ts(b("del"), b("w"), 32768.0, A.is_ge)
+            scan(b("E2"), cb("keep"), b("del"), A.mult, A.add)
+            tt(q(pa, 1), b("w"), q(pa, 0), A.max)
+    for c in range(SUB):
+        s = lambda n: R("%s%d" % (n, h), c, 128, SUB)
+        tt(s("v0"), s("F"), R(pa, 128 + c, 256, SUB), A.add)
+        ts(s("v1"), s("v0"), 32768 + 4095, A.bitwise_and)
+        ts(s("val"), s("v1"), -2048.0, A.add, 2048.0, A.min)
+    rnd("r4", b("r4"), b("E2"), 768.0 - 1.5)
+    mm(group(q(pc, 0), [(b("E2"), cb("I")), (b("r4"), cb("nI"))]) + group(q(pc, 1), [(b("E2"), cb("I"))]))
+    for j in range(6):
+        act(b("mk", 128 * j, 128 * j + 128), q(pc, j // 3), AF.Sigmoid, 256.0 * (767.5 - j if j < 3 else 8.5 - 4 * j), 256.0)
     tk = lambda s: b("tk", 128 * s, 128 * s + 128)
-    for s, bank in enumerate((pb, pa, pc, pb, pa)):
+    for s, bank in enumerate((pb, pa, pd)):
         K = q(bank, 0)
-        terms = [(b("del"), cb("m2048")), (b("val"), cb("I"))] + [(cb("Sh%d" % j), tk(j)) for j in range(s)]
-        if s == 4:
-            terms[4:4] = [(cb("triM"), b("h")), (cb("I"), b("fm"))]
+        terms = [(b("del"), cb("m2048")), (b("val"), cb("I"))] + [(cb("Sh%d" % j), tk(j)) for j in range(3 * s)]
+        if s == 2:
+            terms[:0] = [(cb("triM"), b("h")), (cb("I"), b("fm"))]
         for x in group(K, terms):
             mm([x])
-        if s < 4:
-            tt(tk(s), b("mk", 128 * s, 128 * s + 128), K, A.mult)
+        for j in range(3 * s, 3 * s + 3 if s < 2 else 0):
+            tt(tk(j), b("mk", 128 * j, 128 * j + 128), K, A.mult)
     ts(R("po", o, o + 128) if t < RO else R("pz", 128 * h, 128 * h + 128), K, 4096.0 + M1, A.add, M1, A.subtract)
     hop(t, h, "e")
 
@@ -435,7 +442,7 @@ def analyse():
     hist = {}
     for i, x in enumerate(OPS):
         deps = {}
-        acc = [(r, False) for r in x["r"]] + [(w, True) for w in x["w"]]
+        acc = [(r[:4], False) for r in x["r"]] + [(w[:4], True) for w in x["w"]]
         for (buf, lo, hi, stp), wr in acc:
             psum = buf in SCRATCH and SCRATCH[buf][0] == "psum"
             for (l2, h2, s2, w2, j) in hist.get(buf, []):
@@ -462,15 +469,15 @@ def analyse():
 QN = {"G": "g", "R": "g"}
 
 
-def place(pred, succ, pri):
+def place(pred, succ, pri, forward):
     n = len(OPS)
-    left = [len(p) for p in pred]
-    ready = {(pri[i], i) for i in range(n) if left[i] == 0}
+    pri = list(pri)
+    for i in (range(n) if forward else range(n - 1, -1, -1)):
+        for j, _ in pred[i]:
+            if pri[j] >= pri[i]:
+                pri[i] = pri[j] + 1e-3
     t0, st, busy = [0.0] * n, [0.0] * n, {}
-    while ready:
-        x = min(ready)
-        ready.discard(x)
-        i = x[1]
+    for i in sorted(range(n), key=lambda i: pri[i]):
         e, d, t = OPS[i]["e"], OPS[i]["d"], t0[i]
         if e != "X":
             a, z = busy.setdefault(QN.get(e, e), ([], []))
@@ -485,15 +492,21 @@ def place(pred, succ, pri):
         st[i] = t
         for s, w in succ[i]:
             t0[s] = max(t0[s], t + d + (LAG if w else 0.0))
-            left[s] -= 1
-            if left[s] == 0:
-                ready.add((pri[s], s))
     return st
 
 
-def schedule(lead=LEAD, passes=PASSES, bonus=BONUS):
+def schedule(lead=LEAD, tries=TRIES, seed=1):
     n = len(OPS)
-    pred, succ, half, tail = [list(x["deps"].items()) for x in OPS], [[] for _ in range(n)], [0] * n, [0.0] * n
+    pred, succ, half, tail, above = [], [[] for _ in range(n)], [0] * n, [0.0] * n, []
+    for x in OPS:
+        p, seen, every = [], 0, 0
+        for j in sorted(x["deps"], reverse=True):
+            if not seen >> j & 1:
+                p.append((j, x["deps"][j]))
+                seen |= above[j] if x["deps"][j] else 0
+            every |= above[j] | 1 << j
+        pred.append(p)
+        above.append(every)
     for i, p in enumerate(pred):
         for j, w in p:
             succ[j].append((i, w))
@@ -501,15 +514,50 @@ def schedule(lead=LEAD, passes=PASSES, bonus=BONUS):
         half[a:z] = [k % 2] * (z - a)
     for i in range(n - 1, -1, -1):
         tail[i] = OPS[i]["d"] + max([tail[s] + (LAG if w else 0.0) for s, w in succ[i]], default=0.0)
-    pri = [lead * half[i] - tail[i] - bonus.get(OPS[i]["w"][0][0][:-1] if OPS[i]["w"] else "", 0.0) for i in range(n)]
-    best = None
-    for _ in range(passes):
-        st = place(pred, succ, pri)
-        tot = max(st[i] + OPS[i]["d"] for i in range(n))
-        if best is None or tot < best[0]:
-            best = (tot, st)
-        back = place(succ, pred, [-(st[i] + OPS[i]["d"]) for i in range(n)])
-        pri = [-(back[i] + OPS[i]["d"]) for i in range(n)]
+    def passes(pri, k):
+        best = None
+        for j in range(k):
+            st = place(pred, succ, pri, True)
+            tot = max(st[i] + OPS[i]["d"] for i in range(n))
+            if best is None or tot < best[0]:
+                best = (tot, st)
+            if j < k - 1:
+                back = place(succ, pred, [-(st[i] + OPS[i]["d"]) for i in range(n)], False)
+                pri = [-(back[i] + OPS[i]["d"]) for i in range(n)]
+        return best
+
+    costs = [[x["d"] * (far if x["e"] == "X" and x["d"] == NET else jump if x["r"][:1] == [R("ct", 0, 4096)] else 1.0) for x in OPS]
+             for far, jump, _ in OTHER]
+    names = [QN.get(x["e"], x["e"]) for x in OPS]
+
+    def rate(new):
+        order, tot = sorted(range(n), key=lambda i: (new[1][i], i)), new[0]
+        for d, (_, _, lag) in zip(costs, OTHER):
+            end, free = [0.0] * n, {}
+            for i in order:
+                t = free.get(names[i], 0.0)
+                for j, w in pred[i]:
+                    if end[j] + lag * w > t:
+                        t = end[j] + lag * w
+                end[i] = t + d[i]
+                if names[i] != "X":
+                    free[names[i]] = end[i]
+            tot += max(end)
+        return tot / (1 + len(OTHER)), new[1]
+
+    best = rate(passes([lead * half[i] - tail[i] for i in range(n)], 12))
+    x = [seed]
+
+    def draw():
+        x[0] = (x[0] * 1103515245 + 12345) % 2 ** 31
+        return x[0] / 2 ** 31
+
+    for _ in range(tries):
+        lo = draw() * (best[0] + 10000) - 10000
+        hi, size = lo + 3000 + 27000 * draw(), 3000 * draw() ** 2
+        new = rate(passes([s + size * (draw() - 0.5) if lo < s < hi else s for s in best[1]], 2))
+        if new[0] <= best[0]:
+            best = new
     return sorted(range(n), key=lambda i: (best[1][i], i)), best[0]
 
 

@@ -5,20 +5,27 @@ from concourse.mybir import AluOpType as A, ActivationFunctionType as AF
 RO, LH = 4, 128
 NH = 2
 FV, FS = 20.0, 30.0
-SC = 0.83
+SC = 0.92
 PC = 0.5
 GC = 1.56
-OTHER = [(0.7, 0.8, 120.0), (1.15, 1.2, 200.0)]
-NET = 4000.0
-LAG = 150.0
-LEAD, TRIES = 6000.0, 4000
+OTHER = [(1.2, 0.8, 0.85, 140.0), (1.0, 1.2, 1.2, 140.0)]
+NET = 2500.0
+LAG = 130.0
+LEAD, TRIES, SWAPS = 3000.0, 1500, 5000
+VLANES = (32, 32, 32, 32)
 VCUT = "SVSV"
 YCUT = ["VVVS"] + ["SSSS"] * 7
-ONS = ("r16", "r4", "zs", "hS", "del")
+ONSC = [("del", "Bs", "XB"), ("r16", "rb", "zs", "hS", "del", "Bs", "XB", "r", "S2")]
+TOPS = (0, 0)
 XR = True
 SUB = 1
 BANKS = "caba"
-MXW = 4
+MXW = 2
+RADIX = "44"
+ALLMOVES = {"44": ((0, 1, 1.0), (1, 2, 1.0), (2, 3, 1.0), (0, 4, 1.0), (4, 8, 1.0), (8, 12, 1.0)),
+            "224": ((0, 1, 1.0), (0, 2, 0.5), (0, 4, 1.0), (4, 8, 1.0), (8, 12, 1.0)),
+            "2222": ((0, 1, 1.0), (0, 2, 0.5), (0, 4, 0.25), (0, 8, -0.25))}
+MOVES = ALLMOVES[RADIX]
 SCRATCH, SEMAPHORES = {}, []
 
 
@@ -33,13 +40,13 @@ _sb("eo", 1280, U16); _sb("es", 1280, F16); _sb("zo", 1280, U16); _sb("zs", 1280
 _sb("po", 768, U16)
 _sb("pz", 256, F32); _sb("ef", 256, F32); _sb("yz", 256, F32)
 IDENT = {"nI": -1.0, "I128": 1.0 / 128, "n127": -127.0 / 128, "p256": 256.0, "m256": -256.0, "wq1": -113.0, "wq2": 16.5,
-         "pB": 2.0 ** 21, "mB": -2.0 ** 21, "m2048": -2048.0, "p4096": 4096.0}
+         "pB": 2.0 ** 21, "mB": -2.0 ** 21, "m2048": -2048.0, "mh": -0.5, "p4096": 4096.0}
 for _t in range(1, RO + 1):
     IDENT["wt%d" % _t] = (77 * _t - 95) / 2
 CB = {}
 for _n, _w in [("I", 128)] + [(_x, 128) for _x in IDENT] + [(_x, 128) for _x in (
         "Sp", "ones", "zero", "c16", "c256", "cD", "neg", "pos", "keep", "U0", "GG", "triP", "triM", "odd", "Sh0", "Sh1", "Sh2", "Sh3", "Sh4", "Sh5", "t1", "t2")] + [
-        ("cC", 256), ("b16", 16), ("b32", 16), ("bm16", 16), ("wa", 16), ("wb", 16)]:
+        ("cC", 384), ("b16", 32), ("b32", 16), ("bm16", 16), ("wa", 16), ("wb", 16), ("na", 16), ("nb", 16)]:
     CB[_n] = (sum(w for _, w in CB.values()), _w)
 _sb("cb", sum(w for _, w in CB.values()))
 _sb("cf", 512, F32); _sb("ch", 1024, F16)
@@ -49,10 +56,10 @@ for _n, _w, _d in (("pi", 2, I32), ("u64", 64, F32), ("o64", 64, F32), ("n64", 6
     _sb("k_" + _n, _w, _d)
 for _h in range(NH):
     for _n, _w, _d in (("V", 2048, BF), ("Ya", 2048, BF), ("Yb", 2048, BF), ("cmp", 2048, BF), ("mx", 2048, BF), ("PK", 2048, F16), ("km", 128, F32),
-                       ("r8", 8, F32), ("d", 128, BF), ("q1", 128, BF), ("q2", 128, BF), ("r", 128, F32), ("Xr", 128, BF), ("X", 128, BF), ("Mx", 128, BF),
+                       ("r8", 8, F32), ("d", 128, BF), ("qq", 256, BF), ("r", 128, BF), ("Xr", 128, BF), ("X", 128, BF), ("Mx", 128, BF),
                        ("Mn", 128, BF), ("LT", 128, BF), ("r16", 128, BF), ("r2", 128, BF), ("hS", 128, BF), ("XK", 256, F16), ("Bs", 64, F32),
                        ("v", 128, I32), ("w", 128, I32), ("S2", 128, F32), ("pr", 128, I32), ("F", 128, I32), ("v0", 128, I32), ("v1", 128, I32),
-                       ("val", 128, F16), ("del", 128, BF), ("E2", 128, BF), ("r4", 128, BF), ("de", 128, BF), ("mk", 768, BF), ("tk", 768, F16),
+                       ("val", 128, F16), ("del", 128, BF), ("E2", 128, BF), ("rb", 384, BF), ("de", 128, BF), ("mk", 768, BF), ("tk", 768, F16),
                        ("h", 128, BF), ("AB", 256, F32), ("PP", 256, F32), ("fm", 128, F16)):
         _sb("%s%d" % (_n, _h), _w, _d)
     for _n in "abcd":
@@ -186,7 +193,8 @@ def constants():
     K = lambda n, lo=0, hi=64: R("k_" + n, lo, hi)
     col = lambda j: R("col", j, j + 1)
     diag, row, blk, flat = [[-1, 128]], [[0, 8], [1, 16]], [[-16, 8], [0, 16]], [[1, 128]]
-    fill(cb("zero"), 0.0); fill(cb("ones"), 1.0); fill(cb("c16"), 16.0); fill(cb("c256"), 1.0 / 256); fill(cb("cC", 128, 256), 0.0)
+    fill(cb("zero"), 0.0); fill(cb("ones"), 1.0); fill(cb("c16"), 16.0); fill(cb("c256"), 1.0 / 256)
+    fill(cb("cC", 128, 256), -3.0 / 128); fill(cb("cC", 256, 384), 5.0 / 128)
     select(cb("I"), cb("zero"), diag, 0, 1, A.not_equal, 1.0)
     for j, (n, c) in enumerate(IDENT.items()):
         if j % 2:
@@ -196,8 +204,8 @@ def constants():
     b8, t8 = R("b8", 0, 8), R("b8", 8, 16)
     select(t8, cb("ones", 0, 8), [[-16, 8]], 0, 1, A.is_ge, 0.0)
     select(b8, t8, [[16, 8]], 15, -1, A.is_ge, 0.0)
-    for half in (0, 8):
-        act(cb("b16", half, half + 8), b8, AF.Copy)
+    for c in (0, 8, 16):
+        act(cb("b16", c, c + 8), b8, AF.Copy)
     for n, c in (("b32", 32.0), ("bm16", -16.0)):
         act(cb(n, 0, 8), b8, AF.Copy, scale=c)
     iota(cb("cD"), [[0, 8], [2, 16]], -15, 0)
@@ -205,7 +213,11 @@ def constants():
     OPS[-1]["d"] += 1300.0
     ts(cb("neg"), cb("keep"), 1000.0, A.mult, -1000.0, A.add)
     ts(cb("pos"), cb("keep"), -1048576.0, A.mult, 1048576.0, A.add)
-    ts(cb("cC", 0, 128), cb("keep"), 1.0 / 128, A.mult, -1.0 / 128, A.add)
+    ts(cb("t2"), cb("keep"), -6.0, A.mult, 6.0, A.add)
+    ts(cb("t1"), cb("keep"), -5.0, A.mult, 5.0, A.add)
+    select(cb("t2"), cb("t2"), [[0, 128]], 0, 1, A.not_equal, 0.0)
+    select(cb("t1"), cb("t1"), [[0, 128]], 0, 1, A.is_equal, 0.0)
+    tt(cb("cC", 0, 128), cb("t1"), cb("t2"), A.add)
     pi = K("pi", 0, 2)
     iota(pi, [[0, 2]], 0, 1)
     ts(K("pi", 0, 1), K("pi", 0, 1), 15, A.bitwise_and)
@@ -217,17 +229,21 @@ def constants():
     ts(col(4), col(1), -2.0 ** 15, A.mult, -390.0 * 2 ** 14, A.add)
     ts(col(5), ri, -16384.0, A.mult, 131072.0, A.add)
     ts(col(6), col(1), -2.0 / 8192, A.mult)
+    ts(col(7), col(3), 161.5 - 129 + 256 * (3072 - 384) - 2048, A.add)
+    for t in range(1, RO + 1):
+        ts(col(7 + t), col(3), 16383 + (77 * t - 31) / 2 + 256 * (3072 - 384), A.add)
     for c in (0, 1):
         act(cb("wb", 8 * c, 8 * c + 8), b8, AF.Copy, scale=col(2 - c))
-    act(cb("wa"), cb("wb"), AF.Copy, scale=127.0)
+    for n, c in (("wa", 127.0), ("na", -127.0), ("nb", -1.0))[:3 if max(TOPS) > 1 else 1]:
+        act(cb(n), cb("wb"), AF.Copy, scale=c)
     act(cb("U0", 0, 64), cb("ones", 0, 64), AF.Copy, scale=col(4))
     fill(cb("U0", 64, 128), 0.0)
     select(cb("t1"), cb("p4096"), diag, -1, 1, A.not_equal, -4096.0)
     select(cb("Sp"), cb("t1"), row, -15, 0, A.not_equal, 0.0)
-    for s, (was, now) in enumerate(((0, 1), (1, 2), (2, 3), (0, 4), (4, 8), (8, 12))):
-        if was:
-            select(cb("t1"), cb("zero"), diag, -was, 1, A.not_equal, -1.0)
-        select(cb("Sh%d" % s), cb("t1" if was else "nI"), diag, -now, 1, A.not_equal, 1.0)
+    for s, (was, now, c) in enumerate(MOVES):
+        if s:
+            select(cb("t1"), cb("zero"), diag, -was, 1, A.not_equal, -c)
+        select(cb("Sh%d" % s), cb("t1" if s else "nI"), diag, -now, 1, A.not_equal, c)
     fill(cb("t2"), 8192.0)
     select(cb("t2"), cb("t2"), blk, 0, 1, A.is_ge, 0.0)
     select(cb("GG"), cb("t2"), [[16, 8], [0, 16]], 15, -1, A.is_ge, 0.0)
@@ -262,6 +278,7 @@ M1, M4, M16 = 1.5 * 2 ** 23, 1.5 * 2 ** 25, 1.5 * 2 ** 27
 
 def half_round(t, h, hop):
     MARK.append((len(OPS), 2 * t + h))
+    ONS, TOP = ONSC[t == RO], TOPS[t == RO]
     b = lambda n, lo=0, hi=128: R("%s%d" % (n, h), lo, hi)
     pa, pb, pc, pd = ["ps%s%d" % (x, h) for x in "abcd"]
     q = lambda p, j, k=1: R(p, 128 * j, 128 * (j + k))
@@ -272,10 +289,11 @@ def half_round(t, h, hop):
     rnd = lambda n, out, x, c: act(out, x, AF.Identity, c) if n in ONS else ts(out, x, c, A.add)
     hop(t, h, "z")
     V, Y = "V%d" % h, "Y%s%d" % ("ab"[t % 2], h)
-    for buf, ls, cuts in ((V, eo, VCUT), (Y, zo, YCUT[2 * t + h - 2])):
-        w = 128 // len(cuts)
-        for c, eng in enumerate(cuts):
-            gather(eng, R(buf, 16 * w * c, 16 * w * (c + 1)), R(ls[0], ls[1] + w * c, ls[1] + w * (c + 1)))
+    for buf, ls, cuts in ((V, eo, zip(VCUT, VLANES)), (Y, zo, [(e, 32) for e in YCUT[2 * t + h - 2]])):
+        c = 0
+        for eng, w in cuts:
+            gather(eng, R(buf, 16 * c, 16 * (c + w)), R(ls[0], ls[1] + c, ls[1] + c + w))
+            c += w
     if t > 1:
         rnd("es", es, eo, -2048.0)
         rnd("zs", zs, zo, -2048.0)
@@ -283,12 +301,12 @@ def half_round(t, h, hop):
     v15 = R(V, 15, 2048, 16)
 
     def compare(c):
-        bank, c0 = "ps%s%d" % (BANKS[c], h), 512 * c
-        mm([(q(bank, 0, 4), cb("I"), R(V, c0, c0 + 512), True, False), (R(bank, 0, 511), cb("nI"), R(V, c0 + 1, c0 + 512), False, False),
-            (R(bank, 15, 496, 16), cb("I"), R(V, c0 + 16, c0 + 512, 16), False, False), (R(bank, 15, 512, 16), cb("nI"), R(V, c0, c0 + 512, 16), False, True)])
-        act(b("cmp", c0, c0 + 512), q(bank, 0, 4), AF.Sign, -0.5)
+        bank, c0, w = "ps%s%d" % (BANKS[c], h), 16 * sum(VLANES[:c]), 16 * VLANES[c]
+        mm([(R(bank, 0, w), cb("I"), R(V, c0, c0 + w), True, False), (R(bank, 0, w - 1), cb("nI"), R(V, c0 + 1, c0 + w), False, False),
+            (R(bank, 15, w - 16, 16), cb("I"), R(V, c0 + 16, c0 + w, 16), False, False), (R(bank, 15, w, 16), cb("nI"), R(V, c0, c0 + w, 16), False, True)])
+        act(b("cmp", c0, c0 + w), R(bank, 0, w), AF.Sign, -0.5)
 
-    for c in range(4):
+    for c in range(len(BANKS)):
         compare(c)
     mm([(q(pd, 1), cb("c256"), cb("cD"), True, False)])
     for k in range(0, 16, 4):
@@ -302,13 +320,17 @@ def half_round(t, h, hop):
     scan(b("km"), cb("pos"), q(pd, 1), A.add, A.min)
     km = R("km%d" % h, 15, 128, 16)
     ts(b("r8", 0, 8), km, M16, A.add, M16, A.subtract)
-    mm([(q(pa, 0, 2), cb("ones"), cb("cC"), True, False)] + ([(q(pa, 1), b("h"), cb("odd"), False, False)] if t > 1 else []))
+    if BANKS[-1] == "a":
+        pa, pb = pb, pa
+    mm([(q(pa, 0, 3), cb("ones"), cb("cC"), True, False)] + ([(q(pa, 2), b("h"), cb("odd"), False, False)] if t > 1 else []))
     for k in range(0, 16, 4):
-        mm([(R(pa, j, 256, 16), R("cmp%d" % h, j, 2048, 16), cb("b16"), False, j == 15) for j in range(k, k + 4)])
+        mm([(R(pa, j, 384, 16), R("cmp%d" % h, j, 2048, 16), cb("b16", 0, 24), False, j == 15) for j in range(k, k + 4)])
     scan(q(pb, 1), cb("keep"), q(pa, 0), A.mult, A.add)
-    act(b("q1"), q(pa, 1), AF.Sign, 5.0)
-    act(b("q2"), q(pa, 0), AF.Sign, -2.5)
-    ts(b("r"), q(pb, 1), M4, A.add, M4, A.subtract)
+    if "r" in ONS:
+        act(b("r"), q(pb, 1), AF.Copy)
+    else:
+        scan(b("r"), cb("keep"), q(pa, 0), A.mult, A.add)
+    act(b("qq", 0, 256), q(pa, 1, 2), AF.Sign)
     tt(b("d"), b("r"), q(pb, 1), A.subtract)
     if XR:
         scan(b("Xr"), b("r"), q(pb, 1), A.add, A.subtract)
@@ -324,17 +346,18 @@ def half_round(t, h, hop):
     XA, XB = q(pc, 1), q(pd, 2)
     mm([(XA, cb("I128"), b("hS"), True, False)])
     mm([(XB, cb("I"), es, True, False), (XB, cb("n127"), b("hS"), False, False)])
-    mm([(XA, b("q1"), cb("wq1"), False, False), (XA, b("q2"), cb("wq2"), False, False), (XB, b("q2"), cb("wt%d" % t), False, False)])
+    q2, q1 = b("qq", 0, 128), b("qq", 128, 256)
+    mm([(XA, q1, cb("wq1"), False, False), (XA, q2, cb("wq2"), False, False), (XB, q2, cb("wt%d" % t), False, False)])
     for X in (XA, XB):
         mm([(X, b("r2"), cb("p256"), False, False)])
         mm([(X, b("r16"), cb("m256"), False, False)])
         mm([(X, cb("Sp"), b("LT"), False, True)])
-    ts(b("XK", 0, 128), XA, col(3), A.add, 161.5 - 129 + 256 * (3072 - 384) - 2048, A.add)
-    ts(b("XK", 128, 256), XB, col(3), A.add, 16383 + (77 * t - 31) / 2 + 256 * (3072 - 384), A.add)
+    rnd("XA", b("XK", 0, 128), XA, col(7))
+    rnd("XB", b("XK", 128, 256), XB, col(7 + t))
     mm(group(q(pa, 2), table(0, es)) + group(q(pa, 3), table(1, es)))
     act(b("AB", 0, 256), q(pa, 2, 2), AF.Copy, scale=0.125)
     mm(group(q(pa, 0), [(zs, cb("I")), (cb("ones"), cb("c16"))]))
-    mm(group(q(pa, 1), [(b("q1"), cb("m256"))] + editor))
+    mm(group(q(pa, 1), [(q1, cb("m256"))] + editor))
     act(b("de"), q(pa, 1), AF.Sign, col(3))
     mm(group(q(pa, 1), [(cb("GG"), b("de"))]))
     ts(b("h"), q(pa, 1), col(5), A.is_equal)
@@ -345,17 +368,29 @@ def half_round(t, h, hop):
     ts(b("fm"), q(pd, 2), -8192.0, A.add, -2048.0, A.max)
     U, UA = q(pb, 2), R(pb, 256, 320)
     mm([(U, cb("ones"), cb("U0"), True, False), (UA, cb("mB"), R("X%d" % h, 0, 128, 2), False, False), (UA, cb("pB"), R("r2%d" % h, 0, 128, 2), False, False)])
-    for p in range(8):
-        ts(b("PK", 256 * p, 256 * p + 256), b("XK", 0, 256), 512.0 * (p - 4), A.max, 512.0 * (p - 3), A.min)
-        mm([(R(pb, 256 + p, 384, 8), b("PK", 256 * p + 128 * k, 256 * p + 128 * k + 128), cb("wa" if k == 0 else "wb"), False, p == 7 and k == 1) for k in (0, 1)])
-    act(b("Bs", 0, 64), R(pb, 320, 384), AF.Copy)
+    for p in list(range(7, 7 - TOP, -1)) + list(range(8 - TOP)):
+        pk = lambda p, k: b("PK", 256 * p + 128 * k, 256 * p + 128 * k + 128)
+        terms = [(pk(p, 0), cb("wa")), (pk(p, 1), cb("wb"))]
+        if p < 8 - TOP:
+            ts(b("PK", 256 * p, 256 * p + 256), b("XK", 0, 256), 512.0 * (p - 4), A.max, 512.0 * (p - 3), A.min)
+        else:
+            act(b("PK", 256 * p, 256 * p + 256), b("XK", 0, 256), AF.Relu, -512.0 * (p - 4))
+            terms += [(pk(p + 1, 0), cb("na")), (pk(p + 1, 1), cb("nb"))] if p < 7 else []
+        mm([(R(pb, 256 + p, 384, 8), l, r, False, p == 7 - TOP and j == 1) for j, (l, r) in enumerate(terms)])
+    if "Bs" in ONS:
+        act(b("Bs", 0, 64), R(pb, 320, 384), AF.Copy)
+    else:
+        cp(b("Bs", 0, 64), R(pb, 320, 384))
     tt(R("v%d" % h, 0, 128, 2), b("Bs", 0, 64), UA, A.max)
     tt(R("v%d" % h, 1, 128, 2), b("Bs", 0, 64), UA, A.min)
     for c in range(SUB):
         s = lambda n: R("%s%d" % (n, h), c, 128, SUB)
         Z, mx = R(pa, c, 128, SUB), R(pa, 128 + c, 256, SUB)
         ts(s("w"), s("v"), 65535, A.bitwise_and)
-        ts(s("S2"), s("w"), -(8192.0 + 77 * t), A.add, 0.0, A.max)
+        if "S2" in ONS:
+            act(s("S2"), s("w"), AF.Relu, -(8192.0 + 77 * t))
+        else:
+            ts(s("S2"), s("w"), -(8192.0 + 77 * t), A.add, 0.0, A.max)
         tt(s("pr"), s("S2"), Z, A.mult)
         ts(s("F"), s("pr"), 5, A.arith_shift_right, 4095, A.bitwise_and)
         if c == SUB - 1:
@@ -370,21 +405,41 @@ def half_round(t, h, hop):
         tt(s("v0"), s("F"), R(pa, 128 + c, 256, SUB), A.add)
         ts(s("v1"), s("v0"), 32768 + 4095, A.bitwise_and)
         ts(s("val"), s("v1"), -2048.0, A.add, 2048.0, A.min)
-    rnd("r4", b("r4"), b("E2"), 768.0 - 1.5)
-    mm(group(q(pc, 0), [(b("E2"), cb("I")), (b("r4"), cb("nI"))]) + group(q(pc, 1), [(b("E2"), cb("I"))]))
-    for j in range(6):
-        act(b("mk", 128 * j, 128 * j + 128), q(pc, j // 3), AF.Sigmoid, 256.0 * (767.5 - j if j < 3 else 8.5 - 4 * j), 256.0)
+    rb = lambda s: b("rb", 128 * s - 128, 128 * s) if s else b("E2")
+    for s in {"44": (2,), "224": (1, 2), "2222": (1, 2, 3)}[RADIX]:
+        rnd("rb", rb(s), b("E2"), 192.0 * 2 ** s - (2 ** s - 1) / 2)
+    mk = lambda j, k=1: b("mk", 128 * j, 128 * (j + k))
+    if RADIX == "44":
+        mm(group(q(pc, 0), [(rb(0), cb("I")), (rb(2), cb("nI"))]))
+        for j in range(3):
+            act(mk(j), q(pc, 0), AF.Sigmoid, 256.0 * (767.5 - j), 256.0)
+    else:
+        mm(group(q(pc, 0), [(rb(0), cb("I")), (rb(1), cb("nI"))]) + group(q(pc, 1), [(rb(1), cb("I")), (rb(2), cb("nI"))]))
+        act(mk(0, 2), q(pc, 0, 2), AF.Copy, 384.0)
+    if RADIX == "2222":
+        mm(group(q(pc, 2), [(rb(2), cb("I")), (rb(3), cb("nI"))]) + group(q(pc, 3), [(rb(3), cb("mh"))]))
+        act(mk(2, 2), q(pc, 2, 2), AF.Copy, 768.0)
+    else:
+        mm(group(q(pc, 2), [(rb(0), cb("I"))]))
+        for j in range(3):
+            act(mk(len(MOVES) - 3 + j), q(pc, 2), AF.Sigmoid, 256.0 * (-3.5 - 4 * j), 256.0)
     tk = lambda s: b("tk", 128 * s, 128 * s + 128)
-    for s, bank in enumerate((pb, pa, pd)):
+    done = 0
+    for s, bank in enumerate({"44": (pb, pa, pd), "224": (pb, pa, pb, pd), "2222": (pb, pa, pc, pb, pd)}[RADIX]):
         K = q(bank, 0)
-        terms = [(b("del"), cb("m2048")), (b("val"), cb("I"))] + [(cb("Sh%d" % j), tk(j)) for j in range(3 * s)]
-        if s == 2:
+        terms = [(b("del"), cb("m2048")), (b("val"), cb("I"))] + [(cb("Sh%d" % j), tk(j)) for j in range(done)]
+        if s == len(RADIX):
             terms[:0] = [(cb("triM"), b("h")), (cb("I"), b("fm"))]
         for x in group(K, terms):
             mm([x])
-        for j in range(3 * s, 3 * s + 3 if s < 2 else 0):
-            tt(tk(j), b("mk", 128 * j, 128 * j + 128), K, A.mult)
-    ts(R("po", o, o + 128) if t < RO else R("pz", 128 * h, 128 * h + 128), K, 4096.0 + M1, A.add, M1, A.subtract)
+        for j in range(int(RADIX[s]) - 1 if s < len(RADIX) else 0):
+            tt(tk(done), mk(done), K, A.mult)
+            done += 1
+    out = R("po", o, o + 128) if t < RO else R("pz", 128 * h, 128 * h + 128)
+    if "po" in ONS and t < RO:
+        act(out, K, AF.Identity, 4096.0)
+    else:
+        ts(out, K, 4096.0 + M1, A.add, M1, A.subtract)
     hop(t, h, "e")
 
 
@@ -495,7 +550,7 @@ def place(pred, succ, pri, forward):
     return st
 
 
-def schedule(lead=LEAD, tries=TRIES, seed=1):
+def schedule(lead=LEAD, tries=TRIES, seed=1, swaps=SWAPS):
     n = len(OPS)
     pred, succ, half, tail, above = [], [[] for _ in range(n)], [0] * n, [0.0] * n, []
     for x in OPS:
@@ -526,13 +581,13 @@ def schedule(lead=LEAD, tries=TRIES, seed=1):
                 pri = [-(back[i] + OPS[i]["d"]) for i in range(n)]
         return best
 
-    costs = [[x["d"] * (far if x["e"] == "X" and x["d"] == NET else jump if x["r"][:1] == [R("ct", 0, 4096)] else 1.0) for x in OPS]
-             for far, jump, _ in OTHER]
+    costs = [[x["d"] * (far if x["e"] == "X" and x["d"] == NET else jump if x["r"][:1] == [R("ct", 0, 4096)] else pace if x["e"] in "VSP" else 1.0)
+              for x in OPS] for far, jump, pace, _ in OTHER]
     names = [QN.get(x["e"], x["e"]) for x in OPS]
 
     def rate(new):
         order, tot = sorted(range(n), key=lambda i: (new[1][i], i)), new[0]
-        for d, (_, _, lag) in zip(costs, OTHER):
+        for d, (_, _, _, lag) in zip(costs, OTHER):
             end, free = [0.0] * n, {}
             for i in order:
                 t = free.get(names[i], 0.0)
@@ -558,6 +613,70 @@ def schedule(lead=LEAD, tries=TRIES, seed=1):
         new = rate(passes([s + size * (draw() - 0.5) if lo < s < hi else s for s in best[1]], 2))
         if new[0] <= best[0]:
             best = new
+
+    d, prv, nxt, last, banned = [x["d"] for x in OPS], [-1] * n, [-1] * n, {}, {}
+    for i in sorted(range(n), key=lambda i: (best[1][i], i)):
+        if names[i] != "X":
+            if names[i] in last:
+                prv[i], nxt[last[names[i]]] = last[names[i]], i
+            last[names[i]] = i
+
+    def times():
+        left, r, t = [len(pred[i]) + (prv[i] >= 0) for i in range(n)], [0.0] * n, [0.0] * n
+        top = [i for i in range(n) if not left[i]]
+        for i in top:
+            for s, w in succ[i] + ([(nxt[i], 0)] if nxt[i] >= 0 else []):
+                if r[i] + d[i] + LAG * w > r[s]:
+                    r[s] = r[i] + d[i] + LAG * w
+                left[s] -= 1
+                if not left[s]:
+                    top.append(s)
+        if len(top) < n:
+            return None
+        for i in reversed(top):
+            m = t[nxt[i]] if nxt[i] >= 0 else 0.0
+            for s, w in succ[i]:
+                if t[s] + LAG * w > m:
+                    m = t[s] + LAG * w
+            t[i] = m + d[i]
+        return r, t, max(t)
+
+    def swap(u, v):
+        a, z = prv[u], nxt[v]
+        if a >= 0:
+            nxt[a] = v
+        if z >= 0:
+            prv[z] = u
+        prv[v], nxt[v], prv[u], nxt[u] = a, u, v, z
+
+    r, t, now = times()
+    least = now
+    for step in range(swaps):
+        moves = []
+        for u in range(n):
+            v = nxt[u]
+            if r[u] + t[u] > now - 0.01 and v >= 0 and t[u] - d[u] - t[v] < 0.01 and not above[v] >> u & 1 and banned.get((v, u), -1) < step:
+                a, z = prv[u], nxt[v]
+                rv = max([r[j] + d[j] + LAG * w for j, w in pred[v]] + [r[a] + d[a] if a >= 0 else 0.0])
+                ru = max([r[j] + d[j] + LAG * w for j, w in pred[u]] + [rv + d[v]])
+                tu = max([t[s] + LAG * w for s, w in succ[u]] + [t[z] if z >= 0 else 0.0]) + d[u]
+                tv = max([t[s] + LAG * w for s, w in succ[v]] + [tu]) + d[v]
+                moves.append((max(rv + tv, ru + tu) + draw(), u, v))
+        if not moves:
+            banned.clear()
+        for _, u, v in sorted(moves):
+            swap(u, v)
+            new = times()
+            if new:
+                r, t, now = new
+                banned[(u, v)] = step + 8 + int(18 * draw())
+                break
+            swap(v, u)
+        if now < least + 300:
+            least = min(least, now)
+            new = rate((now, r))
+            if new[0] < best[0]:
+                best = new
     return sorted(range(n), key=lambda i: (best[1][i], i)), best[0]
 
 

@@ -8,24 +8,17 @@ FV, FS = 20.0, 30.0
 SC = 0.92
 PC = 0.5
 GC = 1.56
-OTHER = [(1.2, 0.8, 0.85, 140.0), (1.0, 1.2, 1.2, 140.0)]
-NET = 2500.0
+OTHER = [(1.5, 0.8, 0.85, 140.0), (1.0, 1.2, 1.2, 140.0)]
+ISSUE, NET = 600.0, 1600.0
 LAG = 130.0
 LEAD, TRIES, SWAPS = 3000.0, 1500, 5000
-VLANES = (32, 32, 32, 32)
-VCUT = "SVSV"
+VCUT = ["SVSV"] * 8
 YCUT = ["VVVS"] + ["SSSS"] * 7
-ONSC = [("del", "Bs", "XB"), ("r16", "rb", "zs", "hS", "del", "Bs", "XB", "r", "S2")]
-TOPS = (0, 0)
-XR = True
-SUB = 1
+CMODE = "PPPP"
+ONSC = [("S2",), ("r2", "zs", "S2")]
 BANKS = "caba"
 MXW = 2
-RADIX = "44"
-ALLMOVES = {"44": ((0, 1, 1.0), (1, 2, 1.0), (2, 3, 1.0), (0, 4, 1.0), (4, 8, 1.0), (8, 12, 1.0)),
-            "224": ((0, 1, 1.0), (0, 2, 0.5), (0, 4, 1.0), (4, 8, 1.0), (8, 12, 1.0)),
-            "2222": ((0, 1, 1.0), (0, 2, 0.5), (0, 4, 0.25), (0, 8, -0.25))}
-MOVES = ALLMOVES[RADIX]
+OFF = 256.0 if "V" in CMODE else 0.0
 SCRATCH, SEMAPHORES = {}, []
 
 
@@ -34,33 +27,36 @@ def _sb(name, cols, dtype="bfloat16"):
 
 
 F32, BF, I32, U16, F16 = "float32", "bfloat16", "int32", "uint16", "float16"
+CON = F16 if OFF else BF
 _sb("ct", 4096)
 _sb("ei", 256, I32); _sb("zi", 256, I32)
 _sb("eo", 1280, U16); _sb("es", 1280, F16); _sb("zo", 1280, U16); _sb("zs", 1280, F16)
 _sb("po", 768, U16)
 _sb("pz", 256, F32); _sb("ef", 256, F32); _sb("yz", 256, F32)
-IDENT = {"nI": -1.0, "I128": 1.0 / 128, "n127": -127.0 / 128, "p256": 256.0, "m256": -256.0, "wq1": -113.0, "wq2": 16.5,
-         "pB": 2.0 ** 21, "mB": -2.0 ** 21, "m2048": -2048.0, "mh": -0.5, "p4096": 4096.0}
+IDENT = {"nI": -1.0, "p4096": 4096.0, "m4096": -4096.0, "pX": 65536.0, "mX": -65536.0, "mD": -32768.0,
+         "pB": 2.0 ** 22, "mB": -2.0 ** 22}
 for _t in range(1, RO + 1):
-    IDENT["wt%d" % _t] = (77 * _t - 95) / 2
+    IDENT["wt%d" % _t] = 77.0 * _t
 CB = {}
 for _n, _w in [("I", 128)] + [(_x, 128) for _x in IDENT] + [(_x, 128) for _x in (
-        "Sp", "ones", "zero", "c16", "c256", "cD", "neg", "pos", "keep", "U0", "GG", "triP", "triM", "odd", "Sh0", "Sh1", "Sh2", "Sh3", "Sh4", "Sh5", "t1", "t2")] + [
-        ("cC", 384), ("b16", 32), ("b32", 16), ("bm16", 16), ("wa", 16), ("wb", 16), ("na", 16), ("nb", 16)]:
+        "Sp", "ones", "zero", "c16", "c256", "cD", "neg", "pos", "keep", "U0", "GG", "tri", "odd", "Sh0", "Sh1", "Sh2", "Sh3", "t1", "t2")] + [
+        ("b24", 32), ("b32", 16), ("bm16", 16)]:
     CB[_n] = (sum(w for _, w in CB.values()), _w)
 _sb("cb", sum(w for _, w in CB.values()))
 _sb("cf", 512, F32); _sb("ch", 1024, F16)
-_sb("b8", 16, F32)
+_sb("c511", 128, F16)
+_sb("b8", 16, F32); _sb("w16", 16, F32)
 _sb("col", 16, F32)
-for _n, _w, _d in (("pi", 2, I32), ("u64", 64, F32), ("o64", 64, F32), ("n64", 64, I32), ("w64", 64, F32), ("x64", 64, F32), ("a64", 64, F32)):
+for _n, _w, _d in (("pi", 2, I32), ("u64", 64, F32), ("o64", 64, F32), ("n64", 64, I32), ("w64", 64, F32), ("x64", 64, F32), ("a64", 64, F32),
+                   ("hl", 128, F16)):
     _sb("k_" + _n, _w, _d)
 for _h in range(NH):
-    for _n, _w, _d in (("V", 2048, BF), ("Ya", 2048, BF), ("Yb", 2048, BF), ("cmp", 2048, BF), ("mx", 2048, BF), ("PK", 2048, F16), ("km", 128, F32),
-                       ("r8", 8, F32), ("d", 128, BF), ("qq", 256, BF), ("r", 128, BF), ("Xr", 128, BF), ("X", 128, BF), ("Mx", 128, BF),
-                       ("Mn", 128, BF), ("LT", 128, BF), ("r16", 128, BF), ("r2", 128, BF), ("hS", 128, BF), ("XK", 256, F16), ("Bs", 64, F32),
+    for _n, _w, _d in (("V", 2048, CON), ("Ya", 2048, CON), ("Yb", 2048, CON), ("D", 2048, F16), ("cmp", 2048, BF), ("mx", 2048, CON), ("PK", 1024, F32),
+                       ("km", 128, F32), ("r8", 8, F32), ("P", 128, F16), ("d", 128, BF), ("qq", 256, BF), ("r", 128, BF), ("Xr", 128, BF), ("X", 128, BF),
+                       ("Mx", 128, BF), ("Mn", 128, BF), ("LT", 128, BF), ("r16", 128, BF), ("r2", 64, BF), ("Bs", 64, F32),
                        ("v", 128, I32), ("w", 128, I32), ("S2", 128, F32), ("pr", 128, I32), ("F", 128, I32), ("v0", 128, I32), ("v1", 128, I32),
-                       ("val", 128, F16), ("del", 128, BF), ("E2", 128, BF), ("rb", 384, BF), ("de", 128, BF), ("mk", 768, BF), ("tk", 768, F16),
-                       ("h", 128, BF), ("AB", 256, F32), ("PP", 256, F32), ("fm", 128, F16)):
+                       ("val", 128, F16), ("del", 144, BF), ("rb", 640, BF), ("tk", 512, F16),
+                       ("h", 128, BF), ("H", 128, F32), ("PP", 256, F32), ("fm", 128, F16)):
         _sb("%s%d" % (_n, _h), _w, _d)
     for _n in "abcd":
         SCRATCH["ps%s%d" % (_n, _h)] = ("psum", [128, 512], F32)
@@ -80,7 +76,7 @@ def cb(n, lo=0, hi=None):
 
 
 def table(j, x):
-    return [(R("ch", c + j, c + 512, 4), x) for c in (0, 512)]
+    return [(R("ch", 2 * j + c, 1024, 8), x) for c in (0, 1)]
 
 
 def ap(T, r):
@@ -142,9 +138,13 @@ def fill(out, c):
     return op("V", cyc(ncol(out), 0.5), [lambda g, T: g.vector.memset(ap(T, out), c)], [], [out])
 
 
-def scan(out, d0, d1, o0, o1):
+def scan(out, d0, d1, o0, o1, first=0.0):
     return op("V", cyc(ncol(out), 0.5 if two([out, d0, d1]) else 1),
-              [lambda g, T: g.vector.tensor_tensor_scan(ap(T, out), ap(T, d0), ap(T, d1), 0.0, o0, o1)], [d0, d1], [out])
+              [lambda g, T: g.vector.tensor_tensor_scan(ap(T, out), ap(T, d0), ap(T, d1), first, o0, o1)], [d0, d1], [out])
+
+
+def less(out, a, b):
+    return scan(out, a, b, A.max, A.subtract)
 
 
 def act(out, a, func, bias=None, scale=None):
@@ -160,10 +160,13 @@ def act(out, a, func, bias=None, scale=None):
 
 def gather(eng, out, offs):
     n = ncol(out)
+    win = lambda T: T["ct"][:, 0:4096].indirect(ap(T, offs))
     if eng == "S":
-        f = lambda g, T: g.scalar.activation(ap(T, out), T["ct"][:, 0:4096].indirect(ap(T, offs)), AF.Copy)
+        f = lambda g, T: g.scalar.activation(ap(T, out), win(T), AF.Copy, bias=OFF)
+    elif OFF:
+        f = lambda g, T: g.vector.tensor_scalar(ap(T, out), win(T), OFF, None, A.add)
     else:
-        f = lambda g, T: g.vector.tensor_copy(ap(T, out), T["ct"][:, 0:4096].indirect(ap(T, offs)))
+        f = lambda g, T: g.vector.tensor_copy(ap(T, out), win(T))
     return op(eng, n * GC * SC + 60, [f], [R("ct", 0, 4096), offs], [out])
 
 
@@ -180,6 +183,11 @@ def group(out, terms):
     return [(out, l, r, i == 0, i == len(terms) - 1) for i, (l, r) in enumerate(terms)]
 
 
+def apart(out, terms):
+    for x in group(out, terms):
+        mm([x])
+
+
 def iota(out, pattern, base, cm):
     kw = {} if dts(out) == I32 else {"allow_small_or_imprecise_dtypes": True}
     return op("G", 130 + 2 * ncol(out) * SC, [lambda g, T: g.iota(ap(T, out), pattern, base, cm, **kw)], [], [out])
@@ -189,12 +197,17 @@ def select(out, a, pattern, base, cm, cmp, other):
     return op("G", 170 + 2 * ncol(out) * SC, [lambda g, T: g.affine_select(ap(T, out), ap(T, a), pattern, cmp, other, base, cm)], [a], [out])
 
 
+ALPHA, BETA = 27.0 / 256, 47.0 / 256
+BASE = 2048.0 + 4096 + 32768
+
+
 def constants():
     K = lambda n, lo=0, hi=64: R("k_" + n, lo, hi)
     col = lambda j: R("col", j, j + 1)
     diag, row, blk, flat = [[-1, 128]], [[0, 8], [1, 16]], [[-16, 8], [0, 16]], [[1, 128]]
     fill(cb("zero"), 0.0); fill(cb("ones"), 1.0); fill(cb("c16"), 16.0); fill(cb("c256"), 1.0 / 256)
-    fill(cb("cC", 128, 256), -3.0 / 128); fill(cb("cC", 256, 384), 5.0 / 128)
+    for h in range(NH):
+        fill(R("del%d" % h, 0, 16), 0.0)
     select(cb("I"), cb("zero"), diag, 0, 1, A.not_equal, 1.0)
     for j, (n, c) in enumerate(IDENT.items()):
         if j % 2:
@@ -204,8 +217,8 @@ def constants():
     b8, t8 = R("b8", 0, 8), R("b8", 8, 16)
     select(t8, cb("ones", 0, 8), [[-16, 8]], 0, 1, A.is_ge, 0.0)
     select(b8, t8, [[16, 8]], 15, -1, A.is_ge, 0.0)
-    for c in (0, 8, 16):
-        act(cb("b16", c, c + 8), b8, AF.Copy)
+    for j, c in enumerate((2.0, ALPHA, BETA)):
+        act(cb("b24", 8 * j, 8 * j + 8), b8, AF.Copy, scale=c)
     for n, c in (("b32", 32.0), ("bm16", -16.0)):
         act(cb(n, 0, 8), b8, AF.Copy, scale=c)
     iota(cb("cD"), [[0, 8], [2, 16]], -15, 0)
@@ -213,50 +226,39 @@ def constants():
     OPS[-1]["d"] += 1300.0
     ts(cb("neg"), cb("keep"), 1000.0, A.mult, -1000.0, A.add)
     ts(cb("pos"), cb("keep"), -1048576.0, A.mult, 1048576.0, A.add)
-    ts(cb("t2"), cb("keep"), -6.0, A.mult, 6.0, A.add)
-    ts(cb("t1"), cb("keep"), -5.0, A.mult, 5.0, A.add)
-    select(cb("t2"), cb("t2"), [[0, 128]], 0, 1, A.not_equal, 0.0)
-    select(cb("t1"), cb("t1"), [[0, 128]], 0, 1, A.is_equal, 0.0)
-    tt(cb("cC", 0, 128), cb("t1"), cb("t2"), A.add)
+    ts(R("c511", 0, 128), cb("keep"), 1000.0, A.mult, 511.0, A.add)
     pi = K("pi", 0, 2)
     iota(pi, [[0, 2]], 0, 1)
     ts(K("pi", 0, 1), K("pi", 0, 1), 15, A.bitwise_and)
     ts(K("pi", 1, 2), K("pi", 1, 2), 1, A.bitwise_and)
     ri = col(0)
     cp(R("col", 0, 2), pi)
-    ts(col(2), col(1), -1.0, A.mult, 1.0, A.add)
-    ts(col(3), ri, 14.0, A.is_le, -4096.0, A.mult)
-    ts(col(4), col(1), -2.0 ** 15, A.mult, -390.0 * 2 ** 14, A.add)
-    ts(col(5), ri, -16384.0, A.mult, 131072.0, A.add)
-    ts(col(6), col(1), -2.0 / 8192, A.mult)
-    ts(col(7), col(3), 161.5 - 129 + 256 * (3072 - 384) - 2048, A.add)
-    for t in range(1, RO + 1):
-        ts(col(7 + t), col(3), 16383 + (77 * t - 31) / 2 + 256 * (3072 - 384), A.add)
+    act(col(2), col(1), AF.Copy, 1.0, -1.0)
+    act(col(3), ri, AF.Copy, scale=512.0)
+    over = 8 * BASE % 65536 / 128
+    act(col(4), col(1), AF.Copy, -384.0 * 65536, 383.0 * 65536 + 2 * over)
+    act(col(5), ri, AF.Copy, 16.0, -1.0)
+    act(col(6), col(1), AF.Copy, scale=BETA / 8192)
     for c in (0, 1):
-        act(cb("wb", 8 * c, 8 * c + 8), b8, AF.Copy, scale=col(2 - c))
-    for n, c in (("wa", 127.0), ("na", -127.0), ("nb", -1.0))[:3 if max(TOPS) > 1 else 1]:
-        act(cb(n), cb("wb"), AF.Copy, scale=c)
+        act(R("w16", 8 * c, 8 * c + 8), b8, AF.Copy, scale=col(2 - c))
     act(cb("U0", 0, 64), cb("ones", 0, 64), AF.Copy, scale=col(4))
-    fill(cb("U0", 64, 128), 0.0)
+    fill(cb("U0", 64, 128), over)
     select(cb("t1"), cb("p4096"), diag, -1, 1, A.not_equal, -4096.0)
     select(cb("Sp"), cb("t1"), row, -15, 0, A.not_equal, 0.0)
-    for s, (was, now, c) in enumerate(MOVES):
-        if s:
-            select(cb("t1"), cb("zero"), diag, -was, 1, A.not_equal, -c)
-        select(cb("Sh%d" % s), cb("t1" if s else "nI"), diag, -now, 1, A.not_equal, c)
-    fill(cb("t2"), 8192.0)
+    for s in range(4):
+        select(cb("Sh%d" % s), cb("nI"), diag, -2 ** s, 1, A.not_equal, 1.0)
+        select(cb("Sh%d" % s, 120, 128), cb("Sh%d" % s, 120, 128), [[-1, 8]], 8 - 2 ** s, 1, A.not_equal, 1.0)
+    fill(cb("t2"), -8192.0)
     select(cb("t2"), cb("t2"), blk, 0, 1, A.is_ge, 0.0)
     select(cb("GG"), cb("t2"), [[16, 8], [0, 16]], 15, -1, A.is_ge, 0.0)
-    select(cb("triP"), cb("GG"), flat, 0, -1, A.is_ge, 0.0)
-    act(cb("triM"), cb("triP"), AF.Copy, scale=-0.25)
+    select(cb("tri"), cb("GG"), flat, 0, -1, A.is_ge, 0.0)
     act(cb("odd"), cb("GG"), AF.Copy, scale=col(6))
-    u, off, n, W, X2, AC = K("u64"), K("o64"), K("n64"), K("w64"), K("x64"), K("a64")
+    off, n, W, X2, AC = K("o64"), K("n64"), K("w64"), K("x64"), K("a64")
     iota(K("u64", 0, 16), [[1, 16]], 0, 0)
-    for j, c in enumerate((14.0, 2.0, 0.0, 12.0)):
+    for j, c in enumerate((14.0, 2.0, 0.0, 4.0)):
         ts(R("k_n64", j, 64, 4), K("u64", 0, 16), ri, A.mult, c, A.add)
     ts(n, n, 15, A.bitwise_and)
-    ts(off, n, -8.0, A.add)
-    act(off, off, AF.Abs)
+    act(off, n, AF.Abs, -8.0)
     act(W, off, AF.Copy, -4.0)
     act(X2, W, AF.Square)
     w4 = np.arange(1.0, 5.0)
@@ -264,50 +266,50 @@ def constants():
     ts(AC, X2, cc[3], A.mult, cc[2], A.add)
     for k in (1, 0):
         tt(AC, AC, X2, A.mult)
-        ts(AC, AC, cc[k], A.add)
+        act(AC, AC, AF.Copy, cc[k])
     tt(AC, AC, W, A.mult)
+    hi, lo = R("k_hl", 0, 128, 2), R("k_hl", 1, 128, 2)
+    cp(hi, AC)
+    tt(lo, AC, hi, A.subtract)
     for q in range(8):
         act(R("cf", 64 * q, 64 * q + 64), AC, AF.Copy, scale=R("b8", q, q + 1))
-    for j in (0, 256):
-        cp(R("ch", j, j + 256), R("cf", j, j + 256))
-        tt(R("ch", 512 + j, 768 + j), R("cf", j, j + 256), R("ch", j, j + 256), A.subtract)
+        ts(R("ch", 128 * q, 128 * q + 128), K("hl", 0, 128), R("b8", q, q + 1), A.mult)
 
 
-M1, M4, M16 = 1.5 * 2 ** 23, 1.5 * 2 ** 25, 1.5 * 2 ** 27
+M1, M16 = 1.5 * 2 ** 23, 1.5 * 2 ** 27
 
 
 def half_round(t, h, hop):
     MARK.append((len(OPS), 2 * t + h))
-    ONS, TOP = ONSC[t == RO], TOPS[t == RO]
+    ONS = ONSC[t == RO]
     b = lambda n, lo=0, hi=128: R("%s%d" % (n, h), lo, hi)
     pa, pb, pc, pd = ["ps%s%d" % (x, h) for x in "abcd"]
     q = lambda p, j, k=1: R(p, 128 * j, 128 * (j + k))
     o = 256 * (t - 1) + 128 * h
     eo, es, zo, zs = R("eo", o, o + 128), R("es", o, o + 128), R("zo", o, o + 128), R("zs", o, o + 128)
     col = lambda j: R("col", j, j + 1)
-    rev = lambda n: R("%s%d" % (n, h), 0, 128, -1)
+    rev = lambda r: r[:3] + (-1,)
     rnd = lambda n, out, x, c: act(out, x, AF.Identity, c) if n in ONS else ts(out, x, c, A.add)
     hop(t, h, "z")
     V, Y = "V%d" % h, "Y%s%d" % ("ab"[t % 2], h)
-    for buf, ls, cuts in ((V, eo, zip(VCUT, VLANES)), (Y, zo, [(e, 32) for e in YCUT[2 * t + h - 2]])):
-        c = 0
-        for eng, w in cuts:
-            gather(eng, R(buf, 16 * c, 16 * (c + w)), R(ls[0], ls[1] + c, ls[1] + c + w))
-            c += w
+    for buf, ls, cuts in ((V, eo, VCUT[2 * t + h - 2]), (Y, zo, YCUT[2 * t + h - 2])):
+        w = 128 // len(cuts)
+        for c, eng in enumerate(cuts):
+            gather(eng, R(buf, 16 * w * c, 16 * w * (c + 1)), R(ls[0], ls[1] + w * c, ls[1] + w * (c + 1)))
     if t > 1:
         rnd("es", es, eo, -2048.0)
         rnd("zs", zs, zo, -2048.0)
-    rnd("hS", b("hS"), es, 2048 + 16448.5)
     v15 = R(V, 15, 2048, 16)
-
-    def compare(c):
-        bank, c0, w = "ps%s%d" % (BANKS[c], h), 16 * sum(VLANES[:c]), 16 * VLANES[c]
-        mm([(R(bank, 0, w), cb("I"), R(V, c0, c0 + w), True, False), (R(bank, 0, w - 1), cb("nI"), R(V, c0 + 1, c0 + w), False, False),
-            (R(bank, 15, w - 16, 16), cb("I"), R(V, c0 + 16, c0 + w, 16), False, False), (R(bank, 15, w, 16), cb("nI"), R(V, c0, c0 + w, 16), False, True)])
-        act(b("cmp", c0, c0 + w), R(bank, 0, w), AF.Sign, -0.5)
-
-    for c in range(len(BANKS)):
-        compare(c)
+    for c, mode in enumerate(CMODE):
+        bank, c0, w = "ps%s%d" % (BANKS[c], h), 512 * c, 512
+        if mode == "P":
+            mm([(R(bank, 0, w), cb("I"), R(V, c0, c0 + w), True, False), (R(bank, 0, w - 1), cb("nI"), R(V, c0 + 1, c0 + w), False, False),
+                (R(bank, 15, w - 16, 16), cb("I"), R(V, c0 + 16, c0 + w, 16), False, False), (R(bank, 15, w, 16), cb("nI"), R(V, c0, c0 + w, 16), False, True)])
+            act(b("cmp", c0, c0 + w), R(bank, 0, w), AF.Sigmoid, -128.0, 256.0)
+        else:
+            less(b("D", c0, c0 + w - 1), R(V, c0, c0 + w - 1), R(V, c0 + 1, c0 + w))
+            less(R("D%d" % h, c0 + 15, c0 + w, 16), R(V, c0 + 15, c0 + w, 16), R(V, c0, c0 + w, 16))
+            ts(b("cmp", c0, c0 + w), b("D", c0, c0 + w), 0.5, A.is_ge)
     mm([(q(pd, 1), cb("c256"), cb("cD"), True, False)])
     for k in range(0, 16, 4):
         mm([(R(pd, 128 + p, 256, 16), R(Y, p, 2048, 16), cb("bm16", 0, 8), False, False) for p in range(k, k + 4)])
@@ -322,124 +324,78 @@ def half_round(t, h, hop):
     ts(b("r8", 0, 8), km, M16, A.add, M16, A.subtract)
     if BANKS[-1] == "a":
         pa, pb = pb, pa
-    mm([(q(pa, 0, 3), cb("ones"), cb("cC"), True, False)] + ([(q(pa, 2), b("h"), cb("odd"), False, False)] if t > 1 else []))
     for k in range(0, 16, 4):
-        mm([(R(pa, j, 384, 16), R("cmp%d" % h, j, 2048, 16), cb("b16", 0, 24), False, j == 15) for j in range(k, k + 4)])
-    scan(q(pb, 1), cb("keep"), q(pa, 0), A.mult, A.add)
-    if "r" in ONS:
-        act(b("r"), q(pb, 1), AF.Copy)
-    else:
-        scan(b("r"), cb("keep"), q(pa, 0), A.mult, A.add)
-    act(b("qq", 0, 256), q(pa, 1, 2), AF.Sign)
-    tt(b("d"), b("r"), q(pb, 1), A.subtract)
-    if XR:
-        scan(b("Xr"), b("r"), q(pb, 1), A.add, A.subtract)
+        mm([(R(pa, j, 384, 16), R("cmp%d" % h, j, 2048, 16), cb("b24", 0, 24), j == 0, t == 1 and j == 15) for j in range(k, k + 4)])
+    if t > 1:
+        mm([(q(pa, 2), b("h"), cb("odd"), False, True)])
+    scan(b("P"), R("c511", 0, 128), q(pa, 0), A.min, A.add, 1000.0)
+    act(b("qq", 0, 256), q(pa, 1, 2), AF.Sigmoid, -4096.0, 4096.0)
+    cp(b("r"), b("P"))
+    scan(b("Xr"), b("r"), b("P"), A.add, A.subtract)
+    less(b("d"), b("r"), b("P"))
     tt(R("d%d" % h, 0, 128, 16), km, b("r8", 0, 8), A.subtract)
     scan(b("X"), cb("keep"), b("d"), A.mult, A.add)
-    scan(rev("Mx"), cb("neg"), rev("Xr" if XR else "X"), A.add, A.max)
-    scan(rev("Mn"), cb("pos"), rev("Xr" if XR else "X"), A.add, A.min)
+    scan(rev(b("Mx")), cb("neg"), rev(b("Xr")), A.add, A.max)
+    scan(rev(b("Mn")), cb("pos"), rev(b("Xr")), A.add, A.min)
     mm(group(q(pb, 0), [(b("Mx"), cb("I")), (b("Mn"), cb("nI"))]))
-    act(b("LT"), q(pb, 0), AF.Copy)
-    editor = [(cb("Sp"), b("LT"))]
-    rnd("r16", b("r16"), b("X"), 3072.0)
-    rnd("r2", b("r2"), b("X"), 391.0)
-    XA, XB = q(pc, 1), q(pd, 2)
-    mm([(XA, cb("I128"), b("hS"), True, False)])
-    mm([(XB, cb("I"), es, True, False), (XB, cb("n127"), b("hS"), False, False)])
+    act(b("LT"), q(pb, 0), AF.Identity, col(3), 512.0)
+    ts(b("r16"), b("X"), M16, A.add, M16, A.subtract)
+    even = R("X%d" % h, 0, 128, 2)
+    rnd("r2", b("r2", 0, 64), even, 385.0)
     q2, q1 = b("qq", 0, 128), b("qq", 128, 256)
-    mm([(XA, q1, cb("wq1"), False, False), (XA, q2, cb("wq2"), False, False), (XB, q2, cb("wt%d" % t), False, False)])
-    for X in (XA, XB):
-        mm([(X, b("r2"), cb("p256"), False, False)])
-        mm([(X, b("r16"), cb("m256"), False, False)])
-        mm([(X, cb("Sp"), b("LT"), False, True)])
-    rnd("XA", b("XK", 0, 128), XA, col(7))
-    rnd("XB", b("XK", 128, 256), XB, col(7 + t))
-    mm(group(q(pa, 2), table(0, es)) + group(q(pa, 3), table(1, es)))
-    act(b("AB", 0, 256), q(pa, 2, 2), AF.Copy, scale=0.125)
+    key = q(pc, 2)
+    apart(key, [(cb("I"), es), (q1, cb("mD")), (q2, cb("p4096")), (q2, cb("wt%d" % t)), (b("X"), cb("pX")), (cb("Sp"), b("LT")), (b("r16"), cb("mX"))])
+    mm(group(q(pa, 2), table(0, es)))
+    act(b("H"), q(pa, 2), AF.Copy, scale=0.125)
     mm(group(q(pa, 0), [(zs, cb("I")), (cb("ones"), cb("c16"))]))
-    mm(group(q(pa, 1), [(q1, cb("m256"))] + editor))
-    act(b("de"), q(pa, 1), AF.Sign, col(3))
-    mm(group(q(pa, 1), [(cb("GG"), b("de"))]))
-    ts(b("h"), q(pa, 1), col(5), A.is_equal)
-    mm(group(q(pd, 0), table(2, b("h"))) + group(q(pd, 1), table(3, b("h"))))
-    tt(b("PP", 0, 256), b("AB", 0, 256), q(pd, 0, 2), A.mult)
-    for x in group(q(pd, 2), [(cb("triP"), b("h")), (R("cf", 0, 512, 4), b("PP", 0, 128)), (R("cf", 0, 512, 4), b("PP", 128, 256))]):
-        mm([x])
-    ts(b("fm"), q(pd, 2), -8192.0, A.add, -2048.0, A.max)
     U, UA = q(pb, 2), R(pb, 256, 320)
-    mm([(U, cb("ones"), cb("U0"), True, False), (UA, cb("mB"), R("X%d" % h, 0, 128, 2), False, False), (UA, cb("pB"), R("r2%d" % h, 0, 128, 2), False, False)])
-    for p in list(range(7, 7 - TOP, -1)) + list(range(8 - TOP)):
-        pk = lambda p, k: b("PK", 256 * p + 128 * k, 256 * p + 128 * k + 128)
-        terms = [(pk(p, 0), cb("wa")), (pk(p, 1), cb("wb"))]
-        if p < 8 - TOP:
-            ts(b("PK", 256 * p, 256 * p + 256), b("XK", 0, 256), 512.0 * (p - 4), A.max, 512.0 * (p - 3), A.min)
-        else:
-            act(b("PK", 256 * p, 256 * p + 256), b("XK", 0, 256), AF.Relu, -512.0 * (p - 4))
-            terms += [(pk(p + 1, 0), cb("na")), (pk(p + 1, 1), cb("nb"))] if p < 7 else []
-        mm([(R(pb, 256 + p, 384, 8), l, r, False, p == 7 - TOP and j == 1) for j, (l, r) in enumerate(terms)])
-    if "Bs" in ONS:
-        act(b("Bs", 0, 64), R(pb, 320, 384), AF.Copy)
-    else:
-        cp(b("Bs", 0, 64), R(pb, 320, 384))
+    mm([(U, cb("ones"), cb("U0"), True, False), (UA, cb("mB"), even, False, False), (UA, cb("pB"), b("r2", 0, 64), False, False)])
+    for p in range(8):
+        lo = 65536 * (2 * p - 7.5) - BASE
+        ts(b("PK", 128 * p, 128 * p + 128), key, lo, A.max, lo + 131072, A.min)
+        mm([(R(pb, 256 + p, 384, 8), b("PK", 128 * p, 128 * p + 128), R("w16", 0, 16), False, p == 7)])
+    act(b("Bs", 0, 64), R(pb, 320, 384), AF.Copy)
     tt(R("v%d" % h, 0, 128, 2), b("Bs", 0, 64), UA, A.max)
     tt(R("v%d" % h, 1, 128, 2), b("Bs", 0, 64), UA, A.min)
-    for c in range(SUB):
-        s = lambda n: R("%s%d" % (n, h), c, 128, SUB)
-        Z, mx = R(pa, c, 128, SUB), R(pa, 128 + c, 256, SUB)
-        ts(s("w"), s("v"), 65535, A.bitwise_and)
-        if "S2" in ONS:
-            act(s("S2"), s("w"), AF.Relu, -(8192.0 + 77 * t))
-        else:
-            ts(s("S2"), s("w"), -(8192.0 + 77 * t), A.add, 0.0, A.max)
-        tt(s("pr"), s("S2"), Z, A.mult)
-        ts(s("F"), s("pr"), 5, A.arith_shift_right, 4095, A.bitwise_and)
-        if c == SUB - 1:
-            if "del" in ONS:
-                act(b("del"), b("w"), AF.Sigmoid, -32767.5 * 256, 256.0)
-            else:
-                ts(b("del"), b("w"), 32768.0, A.is_ge)
-            scan(b("E2"), cb("keep"), b("del"), A.mult, A.add)
-            tt(q(pa, 1), b("w"), q(pa, 0), A.max)
-    for c in range(SUB):
-        s = lambda n: R("%s%d" % (n, h), c, 128, SUB)
-        tt(s("v0"), s("F"), R(pa, 128 + c, 256, SUB), A.add)
-        ts(s("v1"), s("v0"), 32768 + 4095, A.bitwise_and)
-        ts(s("val"), s("v1"), -2048.0, A.add, 2048.0, A.min)
-    rb = lambda s: b("rb", 128 * s - 128, 128 * s) if s else b("E2")
-    for s in {"44": (2,), "224": (1, 2), "2222": (1, 2, 3)}[RADIX]:
-        rnd("rb", rb(s), b("E2"), 192.0 * 2 ** s - (2 ** s - 1) / 2)
-    mk = lambda j, k=1: b("mk", 128 * j, 128 * (j + k))
-    if RADIX == "44":
-        mm(group(q(pc, 0), [(rb(0), cb("I")), (rb(2), cb("nI"))]))
-        for j in range(3):
-            act(mk(j), q(pc, 0), AF.Sigmoid, 256.0 * (767.5 - j), 256.0)
+    ts(b("w"), b("v"), 65535, A.bitwise_and)
+    if "S2" in ONS:
+        act(b("S2"), b("w"), AF.Relu, -(8192.0 + 77 * t))
     else:
-        mm(group(q(pc, 0), [(rb(0), cb("I")), (rb(1), cb("nI"))]) + group(q(pc, 1), [(rb(1), cb("I")), (rb(2), cb("nI"))]))
-        act(mk(0, 2), q(pc, 0, 2), AF.Copy, 384.0)
-    if RADIX == "2222":
-        mm(group(q(pc, 2), [(rb(2), cb("I")), (rb(3), cb("nI"))]) + group(q(pc, 3), [(rb(3), cb("mh"))]))
-        act(mk(2, 2), q(pc, 2, 2), AF.Copy, 768.0)
-    else:
-        mm(group(q(pc, 2), [(rb(0), cb("I"))]))
-        for j in range(3):
-            act(mk(len(MOVES) - 3 + j), q(pc, 2), AF.Sigmoid, 256.0 * (-3.5 - 4 * j), 256.0)
+        ts(b("S2"), b("w"), -(8192.0 + 77 * t), A.add, 0.0, A.max)
+    gone = b("del", 16, 144)
+    act(gone, b("w"), AF.Sigmoid, -32767.5 * 256, 256.0)
+    tt(b("pr"), b("S2"), q(pa, 0), A.mult)
+    ts(b("F"), b("pr"), 5, A.arith_shift_right, 4095, A.bitwise_and)
+    tt(q(pa, 1), b("w"), q(pa, 0), A.max)
+    tt(b("v0"), b("F"), q(pa, 1), A.add)
+    ts(b("v1"), b("v0"), 32768 + 4095, A.bitwise_and)
+    ts(b("val"), b("v1"), -2048.0, A.add, 2048.0, A.min)
+    rb = lambda s: b("rb", 128 * s, 128 * s + 128)
+    scan(rb(0), b("del", 15, 143), cb("keep"), A.add, A.mult)
+    scan(rev(rb(4)), cb("keep"), rev(gone), A.mult, A.add)
+    under = (0.0, 384.0, 768.0, 0.0)
+    for s in (1, 2):
+        rnd("rb", rb(s), rb(0), under[s] - (2 ** s - 1) / 2)
+    ts(rb(3), rb(0), 8.0, A.is_ge, 8.0, A.mult)
+    mm(group(q(pd, 0), [(rb(0), cb("I")), (rb(4), cb("I"))]))
+    ts(b("h"), q(pd, 0), col(5), A.is_equal)
+    for j in (0, 1):
+        mm(group(q(pd, 1 + j), table(2 + j, b("h"))))
+    for j in (0, 1):
+        tt(b("PP", 128 * j, 128 * j + 128), b("H"), q(pd, 1 + j), A.mult)
+    apart(q(pd, 3), [(cb("tri"), b("h"))] + [(R("cf", j, 512, 4), b("PP", 128 * j, 128 * j + 128)) for j in (0, 1)])
+    ts(b("fm"), q(pd, 3), 8192.0, A.add, 2048.0, A.min)
     tk = lambda s: b("tk", 128 * s, 128 * s + 128)
-    done = 0
-    for s, bank in enumerate({"44": (pb, pa, pd), "224": (pb, pa, pb, pd), "2222": (pb, pa, pc, pb, pd)}[RADIX]):
+    for s, bank in enumerate((pc, pb, pa, pc, pb)):
         K = q(bank, 0)
-        terms = [(b("del"), cb("m2048")), (b("val"), cb("I"))] + [(cb("Sh%d" % j), tk(j)) for j in range(done)]
-        if s == len(RADIX):
-            terms[:0] = [(cb("triM"), b("h")), (cb("I"), b("fm"))]
-        for x in group(K, terms):
-            mm([x])
-        for j in range(int(RADIX[s]) - 1 if s < len(RADIX) else 0):
-            tt(tk(done), mk(done), K, A.mult)
-            done += 1
+        bit = [(rb(s), cb("m4096"))] + ([(rb(s + 1), cb("p4096"))] if s < 3 else []) if s < 4 else [(cb("I"), b("fm"))]
+        moved = [(cb("Sh%d" % j), tk(j)) for j in range(s)]
+        terms = bit + [(b("val"), cb("I"))] + moved if s < 4 else [(b("val"), cb("I"))] + moved[:3] + bit + moved[3:]
+        apart(K, terms)
+        if s < 4:
+            ts(tk(s), K, 4096.0 * (2 ** s + under[s] - (under[s + 1] if s < 3 else 0.0)), A.add, 2048.0, A.min)
     out = R("po", o, o + 128) if t < RO else R("pz", 128 * h, 128 * h + 128)
-    if "po" in ONS and t < RO:
-        act(out, K, AF.Identity, 4096.0)
-    else:
-        ts(out, K, 4096.0 + M1, A.add, M1, A.subtract)
+    ts(out, K, M1, A.add, M1, A.subtract)
     hop(t, h, "e")
 
 
@@ -449,8 +405,8 @@ def build():
         op("X", dur, [], [("dma_" + sem, 0, 1, 1)], [dst], sem=sem, inc=16)
 
     load("Y", "ld0", R("ei", 0, 256), "enz", 2500)
-    load("Y", "ld2", R("zi", 0, 256), "subs", 2500)
     load("Y", "ld1", R("ct", 0, 4096), "cont", 4000)
+    load("Y", "ld2", R("zi", 0, 256), "subs", 4200)
 
     def send(dst_of, src, dst, sem):
         def f(g, T, core, topo):
@@ -459,7 +415,7 @@ def build():
             m = sum(1 << e for e in topo.engines(core, to))
             g.remote_dma(ap(T, dst), ap(T, src), T.sem[sem], T.sem.snt, pid, rid, m)
             return bin(m).count("1")
-        op("R", 1000, [f], [src], [("net_" + sem, 0, 1, 1)])
+        op("R", ISSUE, [f], [src], [("net_" + sem, 0, 1, 1)])
         op("X", NET, [], [("net_" + sem, 0, 1, 1)], [dst], sem=sem, inc=8)
 
     def hop(t, h, kind):
@@ -479,7 +435,7 @@ def build():
         for h in range(NH):
             c = R(k + "i", 128 * h, 128 * h + 128)
             cp(R(k + "o", 128 * h, 128 * h + 128), c)
-            ts(R(k + "s", 128 * h, 128 * h + 128), R(k + "o", 128 * h, 128 * h + 128), -2048.0, A.add)
+        ts(R(k + "s", 0, 256), R(k + "o", 0, 256), -2048.0, A.add)
     constants()
     for t in range(1, RO + 1):
         for h in range(NH):

@@ -4,21 +4,31 @@ from concourse.mybir import AluOpType as A, ActivationFunctionType as AF
 
 RO, LH = 4, 128
 NH = 2
-FV, FS = 20.0, 30.0
+FV = 20.0
+FS = 50.0
 SC = 0.92
 PC = 0.5
-GC = 1.56
-OTHER = [(1.5, 0.8, 0.85, 140.0), (1.0, 1.2, 1.2, 140.0)]
+GC = 1.7
+OTHER = [(1.2, 0.7, 1.1, 130.0, 0.0), (1.0, 1.15, 1.1, 150.0, 15.0)]
 ISSUE, NET = 600.0, 1600.0
+DMA = 300.0
+FIRST = 3000.0
 LAG = 130.0
-LEAD, TRIES, SWAPS = 3000.0, 1500, 5000
-VCUT = ["SVSV"] * 8
-YCUT = ["VVVS"] + ["SSSS"] * 7
-CMODE = "PPPP"
-ONSC = [("S2",), ("r2", "zs", "S2")]
-BANKS = "caba"
-MXW = 2
-OFF = 256.0 if "V" in CMODE else 0.0
+LEAD = 3000.0
+TRIES = 100
+MOVES = 1300
+HEAT = 250.0
+WIDE = 40
+STEPS = 400
+SOFT = 0.03
+VCUT = ["EEEE"] * 8
+YCUT = ["EEEEEEEE"] * 8
+CUT = 1536
+PARTS = 2
+ABS = [()] * 8
+RAMPS = [1] * 8
+ONSC = [{}, {}]
+BOTH = any(c not in far for far in ABS for c in (0, 1, 4, 5))
 SCRATCH, SEMAPHORES = {}, []
 
 
@@ -27,40 +37,40 @@ def _sb(name, cols, dtype="bfloat16"):
 
 
 F32, BF, I32, U16, F16 = "float32", "bfloat16", "int32", "uint16", "float16"
-CON = F16 if OFF else BF
-_sb("ct", 4096)
+_sb("ct", 8192)
 _sb("ei", 256, I32); _sb("zi", 256, I32)
 _sb("eo", 1280, U16); _sb("es", 1280, F16); _sb("zo", 1280, U16); _sb("zs", 1280, F16)
 _sb("po", 768, U16)
 _sb("pz", 256, F32); _sb("ef", 256, F32); _sb("yz", 256, F32)
-IDENT = {"nI": -1.0, "p4096": 4096.0, "m4096": -4096.0, "pX": 65536.0, "mX": -65536.0, "mD": -32768.0,
-         "pB": 2.0 ** 22, "mB": -2.0 ** 22}
+IDENT = {"nI": -1.0, "p4096": 4096.0, "m4096": -4096.0, "pX": 131072.0, "mX": -131072.0, "pL": 12288.0,
+         "pB": 2.0 ** 23, "mB": -2.0 ** 23}
 for _t in range(1, RO + 1):
     IDENT["wt%d" % _t] = 77.0 * _t
 CB = {}
 for _n, _w in [("I", 128)] + [(_x, 128) for _x in IDENT] + [(_x, 128) for _x in (
-        "Sp", "ones", "zero", "c16", "c256", "cD", "neg", "pos", "keep", "U0", "GG", "tri", "odd", "Sh0", "Sh1", "Sh2", "Sh3", "t1", "t2")] + [
-        ("b24", 32), ("b32", 16), ("bm16", 16)]:
+        "Sp", "ones", "zero", "c16", "c256", "cD", "neg", "pos", "keep", "U0", "GG", "tri", "odd", "Sh0", "Sh1", "Sh2", "Sh3", "t1", "t2",
+        "two", "c32", "t3", "gam", "m129")] + [("NB", 256), ("b24", 16), ("b24s", 16), ("b16", 16), ("b32", 16), ("bm16", 16)]:
     CB[_n] = (sum(w for _, w in CB.values()), _w)
 _sb("cb", sum(w for _, w in CB.values()))
 _sb("cf", 512, F32); _sb("ch", 1024, F16)
-_sb("c511", 128, F16)
-_sb("b8", 16, F32); _sb("w16", 16, F32)
+_sb("c511", 128, F16); _sb("cL", 128, F16)
+_sb("b8", 16, F32); _sb("w16", 48, F32)
 _sb("col", 16, F32)
-for _n, _w, _d in (("pi", 2, I32), ("u64", 64, F32), ("o64", 64, F32), ("n64", 64, I32), ("w64", 64, F32), ("x64", 64, F32), ("a64", 64, F32),
+for _n, _w, _d in (("pi", 4, I32), ("u64", 64, F32), ("o64", 64, F32), ("n64", 64, I32), ("w64", 64, F32), ("x64", 64, F32), ("a64", 64, F32),
                    ("hl", 128, F16)):
     _sb("k_" + _n, _w, _d)
 for _h in range(NH):
-    for _n, _w, _d in (("V", 2048, CON), ("Ya", 2048, CON), ("Yb", 2048, CON), ("D", 2048, F16), ("cmp", 2048, BF), ("mx", 2048, CON), ("PK", 1024, F32),
-                       ("km", 128, F32), ("r8", 8, F32), ("P", 128, F16), ("d", 128, BF), ("qq", 256, BF), ("r", 128, BF), ("Xr", 128, BF), ("X", 128, BF),
+    for _n, _w, _d in (("V", 2080, BF), ("Ya", 2048, BF), ("Yb", 2048, BF), ("cmp", 2064, BF), ("c15", 128, BF), ("mx", 2048, BF), ("PK", 1024, F32),
+                       ("km", 128, F32), ("r8", 8, F32), ("P", 128, F16), ("d", 128, BF), ("L", 128, BF), ("r", 128, BF), ("Xr", 128, BF), ("X", 128, BF),
                        ("Mx", 128, BF), ("Mn", 128, BF), ("LT", 128, BF), ("r16", 128, BF), ("r2", 64, BF), ("Bs", 64, F32),
                        ("v", 128, I32), ("w", 128, I32), ("S2", 128, F32), ("pr", 128, I32), ("F", 128, I32), ("v0", 128, I32), ("v1", 128, I32),
                        ("val", 128, F16), ("del", 144, BF), ("rb", 640, BF), ("tk", 512, F16),
                        ("h", 128, BF), ("H", 128, F32), ("PP", 256, F32), ("fm", 128, F16)):
         _sb("%s%d" % (_n, _h), _w, _d)
     for _n in "abcd":
-        SCRATCH["ps%s%d" % (_n, _h)] = ("psum", [128, 512], F32)
-SEMAPHORES += ["qP", "qV", "qS", "qG", "ld0", "ld1", "ld2", "snt", "out"]
+        SCRATCH["ps%s%d" % (_n, _h)] = ("psum", [128, 64, 8] if _n == "b" else [128, 512], F32)
+LOADS = ["ld0", "ld2"] + ["lc%d" % _j for _j in range(PARTS)]
+SEMAPHORES += ["qP", "qV", "qS", "qG", "snt", "out"] + LOADS
 for _t in range(1, RO + 1):
     for _h in range(NH):
         SEMAPHORES += ["%s%d%d" % (_k, _t, _h) for _k in "ez"]
@@ -80,6 +90,11 @@ def table(j, x):
 
 
 def ap(T, r):
+    if r[0][:3] == "psb":
+        a, z, j = r[1] // 8, (r[2] + 7) // 8, r[1] % 8
+        return T[r[0]][:, a:z, j:j + r[4]] if len(r) > 4 else T[r[0]][:, a:z, j::r[3]] if r[3] < 8 else T[r[0]][:, a:z, j]
+    if len(r) > 4:
+        return T[r[0]][r[4]:r[5], r[1]:r[2]:r[3]]
     if r[3] == -1:
         return T[r[0]][:, r[2] - 1:r[1] - 1:-1] if r[1] else T[r[0]][:, r[2] - 1::-1]
     return T[r[0]][:, r[1]:r[2]:r[3]] if r[3] != 1 else T[r[0]][:, r[1]:r[2]]
@@ -104,6 +119,14 @@ OPS, MARK = [], []
 def op(eng, dur, fns, reads, writes, sem=None, inc=1):
     OPS.append({"e": eng, "d": dur, "f": fns, "r": reads, "w": writes, "sem": sem, "inc": inc})
     return len(OPS) - 1
+
+
+def either(*ways):
+    for f in ways:
+        f()
+    ys = [OPS.pop() for _ in ways][::-1]
+    op("VS", ys[0]["d"], ys[0]["f"], [r for y in ys for r in y["r"]], ys[0]["w"])
+    OPS[-1]["alt"] = {y["e"]: (y["d"], y["f"]) for y in ys}
 
 
 def two(rs):
@@ -158,16 +181,20 @@ def act(out, a, func, bias=None, scale=None):
     return op("S", max(64, ncol(out)) * SC + FS, [f], [a] + [s for s in (bias, scale) if isinstance(s, tuple)], [out])
 
 
+def times(out, a, c):
+    either(lambda: ts(out, a, c, A.mult), lambda: act(out, a, AF.Copy, scale=c))
+
+
 def gather(eng, out, offs):
+    if eng == "E":
+        return either(lambda: gather("V", out, offs), lambda: gather("S", out, offs))
     n = ncol(out)
-    win = lambda T: T["ct"][:, 0:4096].indirect(ap(T, offs))
+    win = lambda T: T["ct"][:, 0:8192].indirect(ap(T, offs))
     if eng == "S":
-        f = lambda g, T: g.scalar.activation(ap(T, out), win(T), AF.Copy, bias=OFF)
-    elif OFF:
-        f = lambda g, T: g.vector.tensor_scalar(ap(T, out), win(T), OFF, None, A.add)
+        f = lambda g, T: g.scalar.activation(ap(T, out), win(T), AF.Copy)
     else:
         f = lambda g, T: g.vector.tensor_copy(ap(T, out), win(T))
-    return op(eng, n * GC * SC + 60, [f], [R("ct", 0, 4096), offs], [out])
+    return op(eng, n * GC * SC + 60, [f], [R("ct", 0, 8192), offs], [out])
 
 
 def mm(lst):
@@ -197,62 +224,89 @@ def select(out, a, pattern, base, cm, cmp, other):
     return op("G", 170 + 2 * ncol(out) * SC, [lambda g, T: g.affine_select(ap(T, out), ap(T, a), pattern, cmp, other, base, cm)], [a], [out])
 
 
-ALPHA, BETA = 27.0 / 256, 47.0 / 256
-BASE = 2048.0 + 4096 + 32768
+ALPHA, BETA = 70.0 / 256, 48.0 / 256
+BASE = 8192.0 + 65536
+M1, M16 = 1.5 * 2 ** 23, 1.5 * 2 ** 27
+MID = 192 * 256 + 128.0
+
+
+def col(j):
+    return R("col", j, j + 1)
+
+
+def columns():
+    K = lambda n, lo=0, hi=64: R("k_" + n, lo, hi)
+    iota(K("pi", 0, 3), [[0, 3]], 0, 1)
+    for j, c in enumerate((15, 1, 2)):
+        ts(K("pi", j, j + 1), K("pi", j, j + 1), c, A.bitwise_and)
+    cp(R("col", 0, 2), K("pi", 0, 2))
+    ts(col(7), K("pi", 2, 3), 2048.0, A.mult)
+    act(col(8), col(7), AF.Copy, -2048.0, -1.0)
+    act(col(9), col(7), AF.Copy, M1, -1.0)
 
 
 def constants():
     K = lambda n, lo=0, hi=64: R("k_" + n, lo, hi)
-    col = lambda j: R("col", j, j + 1)
     diag, row, blk, flat = [[-1, 128]], [[0, 8], [1, 16]], [[-16, 8], [0, 16]], [[1, 128]]
-    fill(cb("zero"), 0.0); fill(cb("ones"), 1.0); fill(cb("c16"), 16.0); fill(cb("c256"), 1.0 / 256)
+    whole = lambda out, c: either(lambda: fill(out, float(c)), lambda: iota(out, [[0, ncol(out)]], c, 0))
+    fill(cb("zero"), 0.0); fill(cb("ones"), 1.0); whole(cb("c16"), 16); fill(cb("c256"), 1.0 / 256)
     for h in range(NH):
-        fill(R("del%d" % h, 0, 16), 0.0)
+        whole(R("del%d" % h, 0, 16), 0)
+        fill(R("V%d" % h, 14, 2080, 2051), 0.0)
+        fill(R("V%d" % h, 15, 2080, 2049), 0.0)
+    if BOTH:
+        whole(cb("two"), 2)
+        iota(cb("c32"), [[0, 32], [32, 2], [0, 2]], 0, 0)
+    whole(cb("m129"), -129)
+    whole(R("cL", 0, 128), (2048 - 129 * 12288) // 128)
+    fill(cb("gam"), 127.0 / 128)
     select(cb("I"), cb("zero"), diag, 0, 1, A.not_equal, 1.0)
-    for j, (n, c) in enumerate(IDENT.items()):
-        if j % 2:
-            act(cb(n), cb("I"), AF.Copy, scale=c)
-        else:
-            ts(cb(n), cb("I"), c, A.mult)
+    for n, c in IDENT.items():
+        either(lambda: ts(cb(n), cb("I"), c, A.mult), lambda: act(cb(n), cb("I"), AF.Copy, scale=c),
+               lambda: select(cb(n), cb("zero"), diag, 0, 1, A.not_equal, c))
     b8, t8 = R("b8", 0, 8), R("b8", 8, 16)
     select(t8, cb("ones", 0, 8), [[-16, 8]], 0, 1, A.is_ge, 0.0)
     select(b8, t8, [[16, 8]], 15, -1, A.is_ge, 0.0)
-    for j, c in enumerate((2.0, ALPHA, BETA)):
-        act(cb("b24", 8 * j, 8 * j + 8), b8, AF.Copy, scale=c)
-    for n, c in (("b32", 32.0), ("bm16", -16.0)):
-        act(cb(n, 0, 8), b8, AF.Copy, scale=c)
+    for j, c in enumerate((2.0, ALPHA)):
+        times(cb("b24", 8 * j, 8 * j + 8), b8, c)
+    times(cb("b24s"), cb("b24"), 1.0 / 256)
+    iota(cb("t3"), [[0, 64], [192, 2]], -96, 0)
+    fill(cb("t3") + (64, 128), 0.0)
+    fill(cb("t3", 3)[:3] + (4, 64, 128), 1.0)
+    select(cb("t3"), cb("t3"), row, -15, 0, A.not_equal, 0.0)
+    for j, c in enumerate((2.0, ALPHA)):
+        times(cb("NB", 128 * j, 128 * j + 128), cb("t3"), c / 2)
+    for n, c in (("b32", 32.0), ("bm16", -16.0), ("b16", 16.0)):
+        times(cb(n, 0, 8), b8, c)
     iota(cb("cD"), [[0, 8], [2, 16]], -15, 0)
     act(cb("keep"), cb("cD"), AF.Sigmoid, 128.0 * 14, 128.0)
     OPS[-1]["d"] += 1300.0
     ts(cb("neg"), cb("keep"), 1000.0, A.mult, -1000.0, A.add)
     ts(cb("pos"), cb("keep"), -1048576.0, A.mult, 1048576.0, A.add)
     ts(R("c511", 0, 128), cb("keep"), 1000.0, A.mult, 511.0, A.add)
-    pi = K("pi", 0, 2)
-    iota(pi, [[0, 2]], 0, 1)
-    ts(K("pi", 0, 1), K("pi", 0, 1), 15, A.bitwise_and)
-    ts(K("pi", 1, 2), K("pi", 1, 2), 1, A.bitwise_and)
     ri = col(0)
-    cp(R("col", 0, 2), pi)
     act(col(2), col(1), AF.Copy, 1.0, -1.0)
     act(col(3), ri, AF.Copy, scale=512.0)
-    over = 8 * BASE % 65536 / 128
-    act(col(4), col(1), AF.Copy, -384.0 * 65536, 383.0 * 65536 + 2 * over)
+    act(col(4), col(1), AF.Copy, -768.0 * 65536, 766.0 * 65536)
     act(col(5), ri, AF.Copy, 16.0, -1.0)
     act(col(6), col(1), AF.Copy, scale=BETA / 8192)
     for c in (0, 1):
-        act(R("w16", 8 * c, 8 * c + 8), b8, AF.Copy, scale=col(2 - c))
-    act(cb("U0", 0, 64), cb("ones", 0, 64), AF.Copy, scale=col(4))
-    fill(cb("U0", 64, 128), over)
+        times(R("w16", 8 * c, 8 * c + 8), b8, col(2 - c))
+    if any(RAMPS):
+        times(R("w16", 16, 48, 2), R("w16", 0, 16), -1.0)
+        times(R("w16", 17, 48, 2), R("w16", 0, 16), 1.0)
+    times(cb("U0", 0, 64), cb("ones", 0, 64), col(4))
+    whole(cb("U0", 64, 128), 0)
     select(cb("t1"), cb("p4096"), diag, -1, 1, A.not_equal, -4096.0)
     select(cb("Sp"), cb("t1"), row, -15, 0, A.not_equal, 0.0)
     for s in range(4):
         select(cb("Sh%d" % s), cb("nI"), diag, -2 ** s, 1, A.not_equal, 1.0)
         select(cb("Sh%d" % s, 120, 128), cb("Sh%d" % s, 120, 128), [[-1, 8]], 8 - 2 ** s, 1, A.not_equal, 1.0)
-    fill(cb("t2"), -8192.0)
+    whole(cb("t2"), -8192)
     select(cb("t2"), cb("t2"), blk, 0, 1, A.is_ge, 0.0)
     select(cb("GG"), cb("t2"), [[16, 8], [0, 16]], 15, -1, A.is_ge, 0.0)
     select(cb("tri"), cb("GG"), flat, 0, -1, A.is_ge, 0.0)
-    act(cb("odd"), cb("GG"), AF.Copy, scale=col(6))
+    times(cb("odd"), cb("GG"), col(6))
     off, n, W, X2, AC = K("o64"), K("n64"), K("w64"), K("x64"), K("a64")
     iota(K("u64", 0, 16), [[1, 16]], 0, 0)
     for j, c in enumerate((14.0, 2.0, 0.0, 4.0)):
@@ -271,12 +325,9 @@ def constants():
     hi, lo = R("k_hl", 0, 128, 2), R("k_hl", 1, 128, 2)
     cp(hi, AC)
     tt(lo, AC, hi, A.subtract)
-    for q in range(8):
-        act(R("cf", 64 * q, 64 * q + 64), AC, AF.Copy, scale=R("b8", q, q + 1))
-        ts(R("ch", 128 * q, 128 * q + 128), K("hl", 0, 128), R("b8", q, q + 1), A.mult)
-
-
-M1, M16 = 1.5 * 2 ** 23, 1.5 * 2 ** 27
+    for dst, src, w in (("cf", "k_a64", 64), ("ch", "k_hl", 128)):
+        for q in range(8):
+            times(R(dst, w * q, w * q + w), R(src, 0, w), R("b8", q, q + 1))
 
 
 def half_round(t, h, hop):
@@ -287,50 +338,69 @@ def half_round(t, h, hop):
     q = lambda p, j, k=1: R(p, 128 * j, 128 * (j + k))
     o = 256 * (t - 1) + 128 * h
     eo, es, zo, zs = R("eo", o, o + 128), R("es", o, o + 128), R("zo", o, o + 128), R("zs", o, o + 128)
-    col = lambda j: R("col", j, j + 1)
     rev = lambda r: r[:3] + (-1,)
-    rnd = lambda n, out, x, c: act(out, x, AF.Identity, c) if n in ONS else ts(out, x, c, A.add)
+
+    def who(n, v, s):
+        e = ONS.get(n, "E")
+        if e == "E":
+            either(v, s)
+        else:
+            (v if e == "V" else s)()
+
+    rnd = lambda n, out, x, c: who(n, lambda: ts(out, x, c, A.add), lambda: act(out, x, AF.Identity, c))
+    step = lambda n, out, x, c, k=256.0: who(n, lambda: ts(out, x, c, A.is_ge), lambda: act(out, x, AF.Sigmoid, -c * k, k))
     hop(t, h, "z")
     V, Y = "V%d" % h, "Y%s%d" % ("ab"[t % 2], h)
     for buf, ls, cuts in ((V, eo, VCUT[2 * t + h - 2]), (Y, zo, YCUT[2 * t + h - 2])):
         w = 128 // len(cuts)
         for c, eng in enumerate(cuts):
-            gather(eng, R(buf, 16 * w * c, 16 * w * (c + 1)), R(ls[0], ls[1] + w * c, ls[1] + w * (c + 1)))
+            c0 = 16 * (w * c + (buf == V))
+            gather(eng, R(buf, c0, c0 + 16 * w), R(ls[0], ls[1] + w * c, ls[1] + w * (c + 1)))
     if t > 1:
-        rnd("es", es, eo, -2048.0)
-        rnd("zs", zs, zo, -2048.0)
-    v15 = R(V, 15, 2048, 16)
-    for c, mode in enumerate(CMODE):
-        bank, c0, w = "ps%s%d" % (BANKS[c], h), 512 * c, 512
-        if mode == "P":
-            mm([(R(bank, 0, w), cb("I"), R(V, c0, c0 + w), True, False), (R(bank, 0, w - 1), cb("nI"), R(V, c0 + 1, c0 + w), False, False),
-                (R(bank, 15, w - 16, 16), cb("I"), R(V, c0 + 16, c0 + w, 16), False, False), (R(bank, 15, w, 16), cb("nI"), R(V, c0, c0 + w, 16), False, True)])
-            act(b("cmp", c0, c0 + w), R(bank, 0, w), AF.Sigmoid, -128.0, 256.0)
+        for n, out, x in (("es", es, eo), ("zs", zs, zo)):
+            rnd(n, out, x, col(8))
+    v0, v15 = R(V, 16, 2064, 16), R(V, 31, 2064, 16)
+    scan(b("cmp", 15, 15 + CUT), R(V, 14, 14 + CUT), R(V, 16, 16 + CUT), A.subtract, A.subtract, MID)
+    scan(rev(b("cmp", 16 + CUT, 2064)), rev(R(V, 16 + CUT, 2064)), rev(R(V, 18 + CUT, 2066)), A.subtract, A.subtract, MID)
+    far = ABS[2 * t + h - 2]
+    both = any(c not in far for c in (0, 1, 4, 5))
+    if both:
+        mm([(R(pc, j, 256, 2), cb("two"), cb("ones"), j == 0, False) for j in (0, 1)])
+    mm([(R(pc, 256 * (j // 2) + j % 2, 256 * (j // 2 + 1), 2), cb("I"), v15, j == 2 and not both, j == 3) for j in range(0 if both else 2, 4)])
+    mm(group(q(pb, 3), [(cb("I"), v15), (cb("nI"), v0)]))
+    step("c15", b("c15"), q(pb, 3), -255.5)
+    mm([(q(pd, 1), cb("c256"), cb("cD"), True, False), (q(pd, 1), cb("c16"), cb("c32"), False, False)][:1 + both])
+    rows = [p for p in range(16) if p % 8 not in far]
+    for k in range(0, len(rows), 4):
+        mm([(R(pd, 128 + p, 256, 16), R(Y, p, 2048, 16), cb("bm16", 0, 8), False, False) for p in rows[k:k + 4]])
+    for c in far:
+        if both and not c & 2:
+            mm([(R(pd, 128 + c, 256, 8), cb("c16"), R("cb", CB["c32"][0] + 2, CB["c32"][0] + 66, 4), False, False)])
+        mm([(R(pd, 128 + c + 8 * j, 256, 16), v15, cb("b16", 0, 8), False, False) for j in (0, 1)])
+    pairs = list(far) + [c for c in range(8) if c not in far]
+    for c in pairs:
+        mx = b("mx", 256 * c, 256 * (c + 1))
+        if c in far:
+            bank = (pb, pa)[far.index(c) % 2]
+            mm([(q(bank, 0, 2), cb("I"), R(Y, c, 2048, 8), True, False)])
+            mm([(R(bank, j, 256, 2), cb("nI"), v15, False, j == 1) for j in (0, 1)])
+            act(mx, q(bank, 0, 2), AF.Abs, 0.0 if c & 2 else -256.0)
         else:
-            less(b("D", c0, c0 + w - 1), R(V, c0, c0 + w - 1), R(V, c0 + 1, c0 + w))
-            less(R("D%d" % h, c0 + 15, c0 + w, 16), R(V, c0 + 15, c0 + w, 16), R(V, c0, c0 + w, 16))
-            ts(b("cmp", c0, c0 + w), b("D", c0, c0 + w), 0.5, A.is_ge)
-    mm([(q(pd, 1), cb("c256"), cb("cD"), True, False)])
-    for k in range(0, 16, 4):
-        mm([(R(pd, 128 + p, 256, 16), R(Y, p, 2048, 16), cb("bm16", 0, 8), False, False) for p in range(k, k + 4)])
-    mm([(R(pc, j, 128 * MXW, MXW), cb("I"), v15, True, True) for j in range(MXW)])
-    step, wide = 16 // MXW, 128 * MXW
-    for c in range(step):
-        tt(b("mx", wide * c, wide * (c + 1)), R(Y, c, 2048, step), q(pc, 0, MXW), A.max)
-        mm([(R(pd, 128 + c + step * j, 256, 16), R("mx%d" % h, wide * c + j, wide * (c + 1), MXW), cb("b32", 0, 8), False, c + step * j == 15)
-            for j in range(MXW)])
+            tt(mx, R(Y, c, 2048, 8), q(pc, c & 2, 2), A.max)
+        mm([(R(pd, 128 + c + 8 * j, 256, 16), R("mx%d" % h, 256 * c + j, 256 * (c + 1), 2), cb("b16" if c in far else "b32", 0, 8), False,
+             c == pairs[-1] and j == 1) for j in (0, 1)])
     scan(b("km"), cb("pos"), q(pd, 1), A.add, A.min)
     km = R("km%d" % h, 15, 128, 16)
     ts(b("r8", 0, 8), km, M16, A.add, M16, A.subtract)
-    if BANKS[-1] == "a":
-        pa, pb = pb, pa
-    for k in range(0, 16, 4):
-        mm([(R(pa, j, 384, 16), R("cmp%d" % h, j, 2048, 16), cb("b24", 0, 24), j == 0, t == 1 and j == 15) for j in range(k, k + 4)])
+    mm([(q(pa, 0, 2), cb("ones"), cb("NB"), True, False), (q(pa, 1), cb("ones"), cb("gam"), False, False)])
     if t > 1:
-        mm([(q(pa, 2), b("h"), cb("odd"), False, True)])
+        mm([(q(pa, 1), b("h"), cb("odd"), False, False)])
+    mm([(R(pa, 15, 256, 16), b("c15"), cb("b24"), False, False)])
+    for k in range(0, 15, 5):
+        mm([(R(pa, j, 256, 16), R("cmp%d" % h, 16 + j, 2064, 16), cb("b24s"), False, j == 14) for j in range(k, k + 5)])
     scan(b("P"), R("c511", 0, 128), q(pa, 0), A.min, A.add, 1000.0)
-    act(b("qq", 0, 256), q(pa, 1, 2), AF.Sigmoid, -4096.0, 4096.0)
-    cp(b("r"), b("P"))
+    ts(b("L"), q(pa, 1), 128.0, A.max, 130.0, A.min)
+    who("r", lambda: cp(b("r"), b("P")), lambda: act(b("r"), b("P"), AF.Copy))
     scan(b("Xr"), b("r"), b("P"), A.add, A.subtract)
     less(b("d"), b("r"), b("P"))
     tt(R("d%d" % h, 0, 128, 16), km, b("r8", 0, 8), A.subtract)
@@ -338,45 +408,49 @@ def half_round(t, h, hop):
     scan(rev(b("Mx")), cb("neg"), rev(b("Xr")), A.add, A.max)
     scan(rev(b("Mn")), cb("pos"), rev(b("Xr")), A.add, A.min)
     mm(group(q(pb, 0), [(b("Mx"), cb("I")), (b("Mn"), cb("nI"))]))
-    act(b("LT"), q(pb, 0), AF.Identity, col(3), 512.0)
+    who("LT", lambda: ts(b("LT"), q(pb, 0), 512.0, A.mult, col(3), A.add), lambda: act(b("LT"), q(pb, 0), AF.Identity, col(3), 512.0))
     ts(b("r16"), b("X"), M16, A.add, M16, A.subtract)
     even = R("X%d" % h, 0, 128, 2)
     rnd("r2", b("r2", 0, 64), even, 385.0)
-    q2, q1 = b("qq", 0, 128), b("qq", 128, 256)
-    key = q(pc, 2)
-    apart(key, [(cb("I"), es), (q1, cb("mD")), (q2, cb("p4096")), (q2, cb("wt%d" % t)), (b("X"), cb("pX")), (cb("Sp"), b("LT")), (b("r16"), cb("mX"))])
+    key, wt = q(pc, 2), cb("wt%d" % t)
+    terms = group(key, [(cb("ones"), R("cL", 0, 128)), (cb("m129"), wt), (cb("I"), es), (b("L"), cb("pL")), (b("L"), wt),
+                        (b("X"), cb("pX")), (cb("Sp"), b("LT")), (b("r16"), cb("mX"))])
+    for lo, hi in ((0, 3), (3, 5), (5, 6), (6, 7), (7, 8)):
+        mm(terms[lo:hi])
     mm(group(q(pa, 2), table(0, es)))
-    act(b("H"), q(pa, 2), AF.Copy, scale=0.125)
+    who("H", lambda: ts(b("H"), q(pa, 2), 0.125, A.mult), lambda: act(b("H"), q(pa, 2), AF.Copy, scale=0.125))
     mm(group(q(pa, 0), [(zs, cb("I")), (cb("ones"), cb("c16"))]))
-    U, UA = q(pb, 2), R(pb, 256, 320)
-    mm([(U, cb("ones"), cb("U0"), True, False), (UA, cb("mB"), even, False, False), (UA, cb("pB"), b("r2", 0, 64), False, False)])
+    UA = R(pb, 256, 320)
+    mm([(q(pb, 2), cb("ones"), cb("U0"), True, False), (UA, cb("mB"), even, False, False), (UA, cb("pB"), b("r2", 0, 64), False, False)])
     for p in range(8):
-        lo = 65536 * (2 * p - 7.5) - BASE
-        ts(b("PK", 128 * p, 128 * p + 128), key, lo, A.max, lo + 131072, A.min)
-        mm([(R(pb, 256 + p, 384, 8), b("PK", 128 * p, 128 * p + 128), R("w16", 0, 16), False, p == 7)])
-    act(b("Bs", 0, 64), R(pb, 320, 384), AF.Copy)
+        lo, pk = 131072 * (2 * p - 7.5) - BASE, b("PK", 128 * p, 128 * p + 128)
+        if RAMPS[2 * t + h - 2]:
+            act(pk, key, AF.Relu, -lo)
+        else:
+            ts(pk, key, lo, A.max, lo + 262144, A.min)
+        if RAMPS[2 * t + h - 2] and p:
+            mm([(R(pb, 255 + p, 384, 1) + (2,), pk, R("w16", 16, 48), False, p == 7)])
+        else:
+            mm([(R(pb, 256 + p, 384, 8), pk, R("w16", 0, 16), False, p == 7)])
+    who("Bs", lambda: cp(b("Bs", 0, 64), R(pb, 320, 384)), lambda: act(b("Bs", 0, 64), R(pb, 320, 384), AF.Copy))
     tt(R("v%d" % h, 0, 128, 2), b("Bs", 0, 64), UA, A.max)
     tt(R("v%d" % h, 1, 128, 2), b("Bs", 0, 64), UA, A.min)
     ts(b("w"), b("v"), 65535, A.bitwise_and)
-    if "S2" in ONS:
-        act(b("S2"), b("w"), AF.Relu, -(8192.0 + 77 * t))
-    else:
-        ts(b("S2"), b("w"), -(8192.0 + 77 * t), A.add, 0.0, A.max)
+    who("S2", lambda: ts(b("S2"), b("w"), -(20480.0 + 77 * t), A.add, 0.0, A.max), lambda: act(b("S2"), b("w"), AF.Relu, -(20480.0 + 77 * t)))
     gone = b("del", 16, 144)
-    act(gone, b("w"), AF.Sigmoid, -32767.5 * 256, 256.0)
+    step("del", gone, b("w"), 32767.5)
     tt(b("pr"), b("S2"), q(pa, 0), A.mult)
     ts(b("F"), b("pr"), 5, A.arith_shift_right, 4095, A.bitwise_and)
     tt(q(pa, 1), b("w"), q(pa, 0), A.max)
     tt(b("v0"), b("F"), q(pa, 1), A.add)
-    ts(b("v1"), b("v0"), 32768 + 4095, A.bitwise_and)
+    ts(b("v1"), b("v0"), 65536 + 32768 + 4095, A.bitwise_and)
     ts(b("val"), b("v1"), -2048.0, A.add, 2048.0, A.min)
     rb = lambda s: b("rb", 128 * s, 128 * s + 128)
     scan(rb(0), b("del", 15, 143), cb("keep"), A.add, A.mult)
     scan(rev(rb(4)), cb("keep"), rev(gone), A.mult, A.add)
-    under = (0.0, 384.0, 768.0, 0.0)
-    for s in (1, 2):
+    under = (0.0, 384.0, 768.0, 1536.0, 0.0)
+    for s in (1, 2, 3):
         rnd("rb", rb(s), rb(0), under[s] - (2 ** s - 1) / 2)
-    ts(rb(3), rb(0), 8.0, A.is_ge, 8.0, A.mult)
     mm(group(q(pd, 0), [(rb(0), cb("I")), (rb(4), cb("I"))]))
     ts(b("h"), q(pd, 0), col(5), A.is_equal)
     for j in (0, 1):
@@ -393,20 +467,23 @@ def half_round(t, h, hop):
         terms = bit + [(b("val"), cb("I"))] + moved if s < 4 else [(b("val"), cb("I"))] + moved[:3] + bit + moved[3:]
         apart(K, terms)
         if s < 4:
-            ts(tk(s), K, 4096.0 * (2 ** s + under[s] - (under[s + 1] if s < 3 else 0.0)), A.add, 2048.0, A.min)
+            ts(tk(s), K, 4096.0 * (2 ** s + under[s] - under[s + 1]), A.add, 2048.0, A.min)
     out = R("po", o, o + 128) if t < RO else R("pz", 128 * h, 128 * h + 128)
-    ts(out, K, M1, A.add, M1, A.subtract)
+    ts(out, K, M1, A.add, col(9) if t < RO else M1, A.subtract)
     hop(t, h, "e")
 
 
 def build():
     def load(q, sem, dst, src, dur):
-        op(q, 60, [lambda g, T: g.sync.dma_start(ap(T, dst), T[src][:])], [], [("dma_" + sem, 0, 1, 1)])
+        f = lambda g, T: (g.sync if q == "Y" else g.scalar).dma_start(ap(T, dst), T[src][:, dst[1]:dst[2]])
+        op(q, DMA, [f], [], [("dma_" + sem, 0, 1, 1)])
         op("X", dur, [], [("dma_" + sem, 0, 1, 1)], [dst], sem=sem, inc=16)
 
-    load("Y", "ld0", R("ei", 0, 256), "enz", 2500)
-    load("Y", "ld1", R("ct", 0, 4096), "cont", 4000)
-    load("Y", "ld2", R("zi", 0, 256), "subs", 4200)
+    load("Z", "ld0", R("ei", 0, 256), "enz", 2000)
+    w = 4096 // PARTS
+    for j in range(PARTS):
+        load("Y", "lc%d" % j, R("ct", w * j, w * j + w), "cont", 2000 + (1600 - DMA * PARTS) * (j + 1) / PARTS)
+    load("Z", "ld2", R("zi", 0, 256), "subs", 3000)
 
     def send(dst_of, src, dst, sem):
         def f(g, T, core, topo):
@@ -415,7 +492,8 @@ def build():
             m = sum(1 << e for e in topo.engines(core, to))
             g.remote_dma(ap(T, dst), ap(T, src), T.sem[sem], T.sem.snt, pid, rid, m)
             return bin(m).count("1")
-        op("R", ISSUE, [f], [src], [("net_" + sem, 0, 1, 1)])
+        first = [("first", 0, 1, 1)]
+        op("R", ISSUE + FIRST * (sem == "z10"), [f], [src] + first * (sem != "z10"), [("net_" + sem, 0, 1, 1)] + first * (sem == "z10"))
         op("X", NET, [], [("net_" + sem, 0, 1, 1)], [dst], sem=sem, inc=8)
 
     def hop(t, h, kind):
@@ -431,21 +509,24 @@ def build():
         else:
             send(2, R("pz", 128 * h, 128 * h + 128), R("ef", 128 * h, 128 * h + 128), s)
 
+    columns()
+    for j in range(PARTS):
+        low, x = R("ct", 4096 + w * j, 4096 + w * j + w), R("ct", w * j, w * j + w)
+        either(lambda: ts(low, x, -256.0, A.add), lambda: act(low, x, AF.Copy, -256.0))
     for k in "ez":
         for h in range(NH):
-            c = R(k + "i", 128 * h, 128 * h + 128)
-            cp(R(k + "o", 128 * h, 128 * h + 128), c)
-        ts(R(k + "s", 0, 256), R(k + "o", 0, 256), -2048.0, A.add)
+            ts(R(k + "o", 128 * h, 128 * h + 128), R(k + "i", 128 * h, 128 * h + 128), col(7), A.add)
+        ts(R(k + "s", 0, 256), R(k + "o", 0, 256), col(8), A.add)
     constants()
     for t in range(1, RO + 1):
         for h in range(NH):
             half_round(t, h, hop)
     o = 256 * RO
-    cp(R("yz", 0, 256), R("zo", o, o + 256))
+    ts(R("yz", 0, 256), R("zo", o, o + 256), col(7), A.subtract)
     for src, dst, parts in (("yz", "ysub", 1), ("ef", "yenz", NH)):
         w = 256 // parts
         for h in range(parts):
-            op("Y", 60, [lambda g, T, src=src, dst=dst, c=w * h, w=w: g.sync.dma_start(T[dst][:, c:c + w], T[src][:, c:c + w])],
+            op("Y", DMA, [lambda g, T, src=src, dst=dst, c=w * h, w=w: g.sync.dma_start(T[dst][:, c:c + w], T[src][:, c:c + w])],
                [R(src, w * h, w * h + w)], [], sem="out", inc=16)
 
 
@@ -461,7 +542,7 @@ def analyse():
                 y = OPS[j]
                 if over and stp == s2 and stp > 1 and (lo - l2) % stp != 0:
                     over = False
-                if psum and y["e"] != x["e"]:
+                if psum and (y["e"] != x["e"] or x["e"] == "VS"):
                     deps[j] = True
                 elif psum and x["e"] == "P":
                     deps[j] = deps.get(j, False)
@@ -472,48 +553,22 @@ def analyse():
         x["deps"] = deps
         for (buf, lo, hi, stp), wr in acc:
             lst = hist.setdefault(buf, [])
-            if wr and stp == 1:
+            if wr and stp == 1 and len(x["w"][0]) == 4 and buf[:2] != "ps":
                 lst[:] = [e for e in lst if not (lo <= e[0] and e[1] <= hi) or e[4] == i]
             lst.append((lo, hi, stp, wr, i))
 
 
-QN = {"G": "g", "R": "g"}
+QN = {"G": "g", "R": "g", "Z": "S"}
 
 
-def place(pred, succ, pri, forward):
-    n = len(OPS)
-    pri = list(pri)
-    for i in (range(n) if forward else range(n - 1, -1, -1)):
-        for j, _ in pred[i]:
-            if pri[j] >= pri[i]:
-                pri[i] = pri[j] + 1e-3
-    t0, st, busy = [0.0] * n, [0.0] * n, {}
-    for i in sorted(range(n), key=lambda i: pri[i]):
-        e, d, t = OPS[i]["e"], OPS[i]["d"], t0[i]
-        if e != "X":
-            a, z = busy.setdefault(QN.get(e, e), ([], []))
-            j = len(z)
-            while j and z[j - 1] > t:
-                j -= 1
-            while j < len(a) and a[j] < t + d:
-                t = max(t, z[j])
-                j += 1
-            a.insert(j, t)
-            z.insert(j, t + d)
-        st[i] = t
-        for s, w in succ[i]:
-            t0[s] = max(t0[s], t + d + (LAG if w else 0.0))
-    return st
-
-
-def schedule(lead=LEAD, tries=TRIES, seed=1, swaps=SWAPS):
+def schedule(lead=LEAD, tries=TRIES, seed=1, moves=MOVES):
     n = len(OPS)
     pred, succ, half, tail, above = [], [[] for _ in range(n)], [0] * n, [0.0] * n, []
     for x in OPS:
         p, seen, every = [], 0, 0
         for j in sorted(x["deps"], reverse=True):
             if not seen >> j & 1:
-                p.append((j, x["deps"][j]))
+                p.append((j, LAG if x["deps"][j] else 0.0))
                 seen |= above[j] if x["deps"][j] else 0
             every |= above[j] | 1 << j
         pred.append(p)
@@ -523,67 +578,214 @@ def schedule(lead=LEAD, tries=TRIES, seed=1, swaps=SWAPS):
             succ[j].append((i, w))
     for (a, k), (z, _) in zip(MARK, MARK[1:] + [(n, 0)]):
         half[a:z] = [k % 2] * (z - a)
+    can = [{QN.get(e, e): d for e, (d, _) in x["alt"].items()} if "alt" in x else {QN.get(x["e"], x["e"]): x["d"]} for x in OPS]
     for i in range(n - 1, -1, -1):
-        tail[i] = OPS[i]["d"] + max([tail[s] + (LAG if w else 0.0) for s, w in succ[i]], default=0.0)
-    def passes(pri, k):
-        best = None
-        for j in range(k):
-            st = place(pred, succ, pri, True)
-            tot = max(st[i] + OPS[i]["d"] for i in range(n))
-            if best is None or tot < best[0]:
-                best = (tot, st)
-            if j < k - 1:
-                back = place(succ, pred, [-(st[i] + OPS[i]["d"]) for i in range(n)], False)
-                pri = [-(back[i] + OPS[i]["d"]) for i in range(n)]
-        return best
-
-    costs = [[x["d"] * (far if x["e"] == "X" and x["d"] == NET else jump if x["r"][:1] == [R("ct", 0, 4096)] else pace if x["e"] in "VSP" else 1.0)
-              for x in OPS] for far, jump, pace, _ in OTHER]
-    names = [QN.get(x["e"], x["e"]) for x in OPS]
-
-    def rate(new):
-        order, tot = sorted(range(n), key=lambda i: (new[1][i], i)), new[0]
-        for d, (_, _, _, lag) in zip(costs, OTHER):
-            end, free = [0.0] * n, {}
-            for i in order:
-                t = free.get(names[i], 0.0)
-                for j, w in pred[i]:
-                    if end[j] + lag * w > t:
-                        t = end[j] + lag * w
-                end[i] = t + d[i]
-                if names[i] != "X":
-                    free[names[i]] = end[i]
-            tot += max(end)
-        return tot / (1 + len(OTHER)), new[1]
-
-    best = rate(passes([lead * half[i] - tail[i] for i in range(n)], 12))
+        tail[i] = min(can[i].values()) + max([tail[s] + w for s, w in succ[i]], default=0.0)
     x = [seed]
 
     def draw():
         x[0] = (x[0] * 1103515245 + 12345) % 2 ** 31
         return x[0] / 2 ** 31
 
+    def place(pri, forward, on, bias=0.0):
+        up, down = (pred, succ) if forward else (succ, pred)
+        pri = list(pri)
+        for i in (range(n) if forward else range(n - 1, -1, -1)):
+            for j, _ in up[i]:
+                if pri[j] >= pri[i]:
+                    pri[i] = pri[j] + 1e-3
+        t0, st, busy, got = [0.0] * n, [0.0] * n, {e: ([], []) for e in "VSPgY"}, [""] * n
+        for i in sorted(range(n), key=lambda i: pri[i]):
+            best = None
+            for e in (on[i] if on and on[i] else can[i]):
+                d, t, j = can[i][e], t0[i], 0
+                if e != "X":
+                    a, z = busy[e]
+                    j = len(z)
+                    while j and z[j - 1] > t:
+                        j -= 1
+                    while j < len(a) and a[j] < t + d:
+                        t = max(t, z[j])
+                        j += 1
+                c = t + d + (bias if e == "V" else 0.0)
+                if best is None or c < best[0]:
+                    best = (c, e, t, d, j)
+            _, e, t, d, j = best
+            if e != "X":
+                busy[e][0].insert(j, t)
+                busy[e][1].insert(j, t + d)
+            st[i], got[i] = t, e
+            t += d
+            for s, w in down[i]:
+                if t + w > t0[s]:
+                    t0[s] = t + w
+        return st, got
+
+    def passes(pri, k, on, bias):
+        best = None
+        for j in range(k):
+            st, got = place(pri, True, on, bias)
+            end = [st[i] + can[i][got[i]] for i in range(n)]
+            if best is None or max(end) < best[0]:
+                best = (max(end), st, got)
+            if j < k - 1:
+                back, _ = place([-e for e in end], False, got)
+                pri = [-(back[i] + can[i][got[i]]) for i in range(n)]
+        return best
+
+    def other(far, jump, pace, more):
+        return [{e: d * far if e == "X" and d == NET else d * jump * pace if y["r"][:1] == [R("ct", 0, 8192)] else
+                 (d + more * (e == "S")) * pace if e in "VSP" or y["e"] != "R" and e == "g" else d for e, d in c.items()} for y, c in zip(OPS, can)]
+
+    sets = [(other(far, jump, pace, more), lag / LAG, pace) for far, jump, pace, lag, more in OTHER]
+
+    def rate(new):
+        tot, st, on = new
+        order = sorted(range(n), key=lambda i: (st[i], i))
+        for c, k, pace in sets:
+            end, free = [0.0] * n, dict.fromkeys("VSPgYX", 0.0)
+            for i in order:
+                e = on[i]
+                t = free[e]
+                for j, w in pred[i]:
+                    if end[j] + k * w > t:
+                        t = end[j] + k * w
+                end[i] = t + c[i][e]
+                if e != "X":
+                    free[e] = end[i]
+            tot += max(end) / pace
+        return tot / (1 + len(sets)), st, on
+
+    best = min((rate(passes([lead * half[i] - tail[i] for i in range(n)], 8, None, bias)) for bias in (0.0, 150.0, 400.0)), key=lambda y: y[0])
     for _ in range(tries):
         lo = draw() * (best[0] + 10000) - 10000
         hi, size = lo + 3000 + 27000 * draw(), 3000 * draw() ** 2
-        new = rate(passes([s + size * (draw() - 0.5) if lo < s < hi else s for s in best[1]], 2))
+        on = ["" if lo < s < hi and draw() < 0.5 else e for s, e in zip(best[1], best[2])]
+        new = rate(passes([s + size * (draw() - 0.5) if lo < s < hi else s for s in best[1]], 2, on, 600 * draw() - 100))
         if new[0] <= best[0]:
             best = new
 
-    d, prv, nxt, last, banned = [x["d"] for x in OPS], [-1] * n, [-1] * n, {}, {}
-    for i in sorted(range(n), key=lambda i: (best[1][i], i)):
-        if names[i] != "X":
-            if names[i] in last:
-                prv[i], nxt[last[names[i]]] = last[names[i]], i
-            last[names[i]] = i
+    sets.insert(0, (can, 1.0, 1.0))
+    on = list(best[2])
+    order = sorted(range(n), key=lambda i: (best[1][i], i))
+    idle = dict.fromkeys("VSPgYX", 0.0)
 
-    def times():
-        left, r, t = [len(pred[i]) + (prv[i] >= 0) for i in range(n)], [0.0] * n, [0.0] * n
+    def reach(part, links, c, k):
+        end, free = {}, dict(idle)
+        for i in part:
+            e = on[i]
+            t = free[e]
+            for j, w in links[i]:
+                if end[j] + k * w > t:
+                    t = end[j] + k * w
+            end[i] = t + c[i][e]
+            if e != "X":
+                free[e] = end[i]
+        return end, free
+
+    for sweep in range(moves):
+        heat = HEAT * (1 - sweep / moves) ** 2 + 2.0
+        a = int(draw() * (n + WIDE)) - WIDE
+        a, z = max(a, 0), min(a + WIDE + int(4 * WIDE * draw() ** 2), n)
+        win = order[a:z]
+        if len(win) < 10:
+            continue
+        inside = set(win)
+        inn = {i: [(j, w) for j, w in pred[i] if j in inside] for i in win}
+        before = {i: [j for j, _ in inn[i]] for i in win}
+        after = {i: [j for j, _ in succ[i] if j in inside] for i in win}
+        edges = []
+        for c, k, pace in sets:
+            end, free = reach(order[:a], pred, c, k)
+            rest, late = reach(order[:z - 1:-1] if z < n else [], succ, c, k)
+            tail = lambda i: max([rest[j] + k * w for j, w in succ[i] if j in rest], default=0.0)
+            past = max([end[i] + tail(i) for i in order[max(0, a - 3 * WIDE):a]], default=0.0)
+            edges.append((c, pace, free, late, past, {i: (max([end[j] + k * w for j, w in pred[i] if j in end], default=0.0), tail(i),
+                                                          [(j, k * w) for j, w in inn[i]]) for i in win}))
+
+        def length():
+            tot = 0.0
+            for c, pace, free, late, most, near in edges:
+                free, end = dict(free), {}
+                for i in win:
+                    e = on[i]
+                    t, rest, ins = near[i]
+                    if free[e] > t:
+                        t = free[e]
+                    for j, w in ins:
+                        if end[j] + w > t:
+                            t = end[j] + w
+                    end[i] = t = t + c[i][e]
+                    if e != "X":
+                        free[e] = t
+                    if t + rest > most:
+                        most = t + rest
+                ends = [free[e] + late[e] for e in "VSPgY"]
+                tot += (max(most, max(ends)) + SOFT * (ends[0] + ends[1] + ends[2])) / pace
+            return tot
+
+        now = length()
+        least, kept, m = now, (list(win), [on[i] for i in win]), len(win)
+        for _ in range(STEPS):
+            p = int(draw() * m)
+            v = win[p]
+            was = on[v]
+            if was == "X":
+                continue
+            if len(can[v]) > 1 and draw() < 0.3:
+                es = [e for e in can[v] if e != was]
+                on[v] = es[int(draw() * len(es))]
+            e, j, skip = on[v], p, 1 + int(12 * draw() ** 4) - (on[v] != was)
+            if draw() < 0.5:
+                while skip and j and win[j - 1] not in before[v]:
+                    j -= 1
+                    skip -= on[win[j]] == e
+            else:
+                while skip and j < m - 1 and win[j + 1] not in after[v]:
+                    j += 1
+                    skip -= on[win[j]] == e
+            if j == p and e == was:
+                continue
+            win.insert(j, win.pop(p))
+            new = length()
+            if new <= now or draw() < math.exp((now - new) / heat):
+                now = new
+                if now < least:
+                    least, kept = now, (list(win), [on[i] for i in win])
+            else:
+                win.insert(p, win.pop(j))
+                on[v] = was
+        order[a:z] = kept[0]
+        for i, e in zip(*kept):
+            on[i] = e
+    tot = sum(max(reach(order, pred, c, k)[0].values()) / pace for c, k, pace in sets) / len(sets)
+    return order, tot, [e.upper() if "alt" in y else y["e"] for e, y in zip(on, OPS)]
+    d = [can[i][on[i]] for i in range(n)]
+    line = {e: [] for e in "VSPgYX"}
+    for i in sorted(range(n), key=lambda i: (best[1][i], i)):
+        line[on[i]].append(i)
+    line["X"] = []
+    waits = [len(p) for p in pred]
+
+    def lengths():
+        nxt, left, r, t = [-1] * n, list(waits), [0.0] * n, [0.0] * n
+        for q in line.values():
+            for u, v in zip(q, q[1:]):
+                nxt[u] = v
+                left[v] += 1
         top = [i for i in range(n) if not left[i]]
         for i in top:
-            for s, w in succ[i] + ([(nxt[i], 0)] if nxt[i] >= 0 else []):
-                if r[i] + d[i] + LAG * w > r[s]:
-                    r[s] = r[i] + d[i] + LAG * w
+            e = r[i] + d[i]
+            for s, w in succ[i]:
+                if e + w > r[s]:
+                    r[s] = e + w
+                left[s] -= 1
+                if not left[s]:
+                    top.append(s)
+            s = nxt[i]
+            if s >= 0:
+                if e > r[s]:
+                    r[s] = e
                 left[s] -= 1
                 if not left[s]:
                     top.append(s)
@@ -592,48 +794,66 @@ def schedule(lead=LEAD, tries=TRIES, seed=1, swaps=SWAPS):
         for i in reversed(top):
             m = t[nxt[i]] if nxt[i] >= 0 else 0.0
             for s, w in succ[i]:
-                if t[s] + LAG * w > m:
-                    m = t[s] + LAG * w
+                if t[s] + w > m:
+                    m = t[s] + w
             t[i] = m + d[i]
         return r, t, max(t)
 
-    def swap(u, v):
-        a, z = prv[u], nxt[v]
-        if a >= 0:
-            nxt[a] = v
-        if z >= 0:
-            prv[z] = u
-        prv[v], nxt[v], prv[u], nxt[u] = a, u, v, z
-
-    r, t, now = times()
-    least = now
-    for step in range(swaps):
-        moves = []
-        for u in range(n):
-            v = nxt[u]
-            if r[u] + t[u] > now - 0.01 and v >= 0 and t[u] - d[u] - t[v] < 0.01 and not above[v] >> u & 1 and banned.get((v, u), -1) < step:
-                a, z = prv[u], nxt[v]
-                rv = max([r[j] + d[j] + LAG * w for j, w in pred[v]] + [r[a] + d[a] if a >= 0 else 0.0])
-                ru = max([r[j] + d[j] + LAG * w for j, w in pred[u]] + [rv + d[v]])
-                tu = max([t[s] + LAG * w for s, w in succ[u]] + [t[z] if z >= 0 else 0.0]) + d[u]
-                tv = max([t[s] + LAG * w for s, w in succ[v]] + [tu]) + d[v]
-                moves.append((max(rv + tv, ru + tu) + draw(), u, v))
-        if not moves:
+    r, t, now = lengths()
+    least, banned = now, {}
+    for step in range(moves):
+        offers = []
+        at = {v: j for q in line.values() for j, v in enumerate(q)}
+        for v in range(n):
+            if r[v] + t[v] < now - 0.01 or on[v] == "X" or banned.get(v, -1) > step or draw() < 0.5:
+                continue
+            head = max([r[j] + d[j] + w for j, w in pred[v]], default=0.0)
+            rest = max([t[s] + w for s, w in succ[v]], default=0.0)
+            for e, dv in can[v].items():
+                q = line[e]
+                own = at[v] if e == on[v] else -1
+                lo, hi = 0, len(q)
+                while lo < hi:
+                    mid = (lo + hi) // 2
+                    if r[q[mid]] + d[q[mid]] > head:
+                        hi = mid
+                    else:
+                        lo = mid + 1
+                j = lo
+                while j <= len(q):
+                    u = j - 1 if j - 1 != own else j - 2
+                    w = j if j != own else j + 1
+                    if j != own and j != own + 1 or own < 0:
+                        a = max(head, r[q[u]] + d[q[u]] - (d[v] if own >= 0 and u > own else 0.0)) if u >= 0 else head
+                        z = max(rest, t[q[w]] - (d[v] if own >= 0 and w < own else 0.0)) if w < len(q) else rest
+                        offers.append((a + dv + z + (dv - d[v]) * 0.3 + 40 * draw(), v, e, j))
+                    if j == len(q) or t[q[j]] <= rest and j != own or above[q[j]] >> v & 1:
+                        break
+                    j += 1
+        if not offers:
             banned.clear()
-        for _, u, v in sorted(moves):
-            swap(u, v)
-            new = times()
+            continue
+        offers.sort()
+        for _, v, e, j in offers[:6]:
+            was, old = on[v], at[v]
+            line[was].pop(old)
+            line[e].insert(j - (e == was and j > old), v)
+            on[v], d[v] = e, can[v][e]
+            new = lengths()
             if new:
                 r, t, now = new
-                banned[(u, v)] = step + 8 + int(18 * draw())
+                banned[v] = step + 4 + int(14 * draw())
                 break
-            swap(v, u)
-        if now < least + 300:
+            line[e].remove(v)
+            line[was].insert(old, v)
+            on[v], d[v] = was, can[v][was]
+        if now < least + NEAR:
             least = min(least, now)
-            new = rate((now, r))
+            new = rate((now, r, on))
             if new[0] < best[0]:
-                best = new
-    return sorted(range(n), key=lambda i: (best[1][i], i)), best[0]
+                best = (new[0], r, list(on))
+    names = [e.upper() if "alt" in y else y["e"] for e, y in zip(best[2], OPS)]
+    return sorted(range(n), key=lambda i: (best[1][i], i)), best[0], names
 
 
 PLAN = []
@@ -654,11 +874,11 @@ def rank_program(g, core, T, topo):
     if T.rank_of(core) is None:
         return
     order = plan()
-    queue = {"P": g.tensor, "V": g.vector, "S": g.scalar, "G": g, "R": g, "Y": g.sync}
+    queue = {"P": g.tensor, "V": g.vector, "S": g.scalar, "G": g, "R": g, "Y": g.sync, "Z": g.scalar}
     cnt, done, know, clock, sent = {}, {}, {}, {}, 0
     for i in order:
         x = OPS[i]
-        e = x["e"]
+        e = PLAN[2][i]
         if e == "X":
             done[i] = (x["sem"], x["inc"])
             clock[i] = {}
@@ -680,7 +900,7 @@ def rank_program(g, core, T, topo):
         clock[i] = dict(kn)
         if e in QS:
             s = QS[e]
-            for f in x["f"]:
+            for f in x["alt"][e][1] if "alt" in x else x["f"]:
                 f(g, T).then_inc(T.sem[s], 1)
                 cnt[s] = cnt.get(s, 0) + 1
             done[i] = (s, cnt[s])
@@ -696,7 +916,7 @@ def rank_program(g, core, T, topo):
                 f(g, T).then_inc(T.sem[sem], 16)
                 cnt[sem] = cnt.get(sem, 0) + 16
             done[i] = None
-    for s in list(QS.values()) + ["out", "ld0", "ld1", "ld2"]:
+    for s in list(QS.values()) + ["out"] + LOADS:
         if cnt.get(s, 0):
             g.sync.wait_ge(T.sem[s], cnt[s])
     g.wait_ge(T.sem.snt, sent)

@@ -1,5 +1,6 @@
 import math
 import numpy as np
+from concourse.bass import DstId, RemoteDMATransfer
 from concourse.mybir import AluOpType as A, ActivationFunctionType as AF
 
 RO, LH = 4, 128
@@ -7,39 +8,66 @@ NH = 2
 FV = 20.0
 FS = 50.0
 SC = 0.92
-PC = 0.5
+PC = 0.46
 GC = 1.7
 OTHER = [(1.2, 0.7, 1.1, 130.0, 0.0), (1.0, 1.15, 1.1, 150.0, 15.0)]
 ISSUE, NET = 600.0, 1600.0
 DMA = 300.0
-FIRST = 3000.0
-LAG = 130.0
+FIRST = 4000.0
+LAG = 150.0
 LEAD = 3000.0
-TRIES = 100
-MOVES = 1300
+TRIES = 60
+MOVES = 2200
 HEAT = 250.0
 WIDE = 40
 STEPS = 400
-SOFT = 0.03
+SOFT = 0.1
+SETS = [(1.15, 2.0, 0.62, 26.0, 65.0, 160.0, 1600.0, 5000.0, 1.32), (0.9, 1.6, 0.48, 20.0, 50.0, 130.0, 1500.0, 3000.0, 0.96), (1.04, 1.15, 0.56, 24.0, 58.0, 135.0, 1900.0, 3000.0, 1.03)]
+PACE = [_x / 85.0 for _x in (81.5, 85.7, 86.2, 86.1, 93.4, 92.3, 96.2, 98.2, 102.3, 100.0, 105.0, 113.1)]
+EVEN = 1500.0
+RANGES = [(0.83, 1.245, 1), (1.04, 2.08, 5), (0.48, 0.54, 7), (12.0, 28.0, 7), (35.0, 60.0, 11), (140.0, 210.0, 7), (1300.0, 2100.0, 11), (2500.0, 5500.0, 5)]
+if RANGES:
+    SETS = []
+    for _k in range(12):
+        _v = [lo + (hi - lo) * ((_k * s + 3 * j) % 12 + 0.5) / 12 for j, (lo, hi, s) in enumerate(RANGES)]
+        _v[2] *= _v[0]
+        SETS.append(tuple(_v) + ((_v[0] * (37.0 + 17.0 * _v[1]) + 0.09 * _v[5] + 0.2 * _v[3] + 0.08 * _v[4] + 0.002 * _v[6]) / 80.0,))
+TRAIN = [(1.15, 1.95, 0.58, 24.0, 60.0, 165.0, 1500.0, 4500.0, 1.32), (0.86, 1.56, 0.44, 18.0, 48.0, 155.0, 1300.0, 3500.0, 0.95), (1.02, 1.25, 0.52, 20.0, 54.0, 155.0, 1600.0, 3500.0, 1.05)]
+SETS += TRAIN
+LEADS = [2100, 2300, 2400, 2500, 2600, 2700, 2900, 3100]
+LAPS = [(100, 400.0, 2, False), (300, 400.0, 1, False), (6000, 85.0, 1, True)]
+DRIFT = 0.0
+MEND = 40
+SPARE = 150.0
 VCUT = ["EEEE"] * 8
-YCUT = ["EEEEEEEE"] * 8
-CUT = 1536
-PARTS = 2
-ABS = [()] * 8
-RAMPS = [1] * 8
+YCUT = ["4444"] * 2 + ["6222211"] * 6
+CUT = 1024
+PARTS = [0, 2048, 3584, 4096]
+RUNS = False
+COPY = False
+LV = 4
+RW = 4
+EARLY = [0, 0, 1, 1, 1, 1]
+ABS = [0] * 8
+RAMPS = ["SSSSSSSS"] * 8
+SPLIT = 2
+FARB = ["psb0", "psb1"]
+MERGE = 1
+SIG = False
+LATE = False
+OWNX = True
 ONSC = [{}, {}]
-BOTH = any(c not in far for far in ABS for c in (0, 1, 4, 5))
 SCRATCH, SEMAPHORES = {}, []
 
 
 def _sb(name, cols, dtype="bfloat16"):
-    SCRATCH[name] = ("sbuf", [128, cols], dtype)
+    SCRATCH[name] = ("sbuf", [128] + (cols if isinstance(cols, list) else [cols]), dtype)
 
 
 F32, BF, I32, U16, F16 = "float32", "bfloat16", "int32", "uint16", "float16"
-_sb("ct", 8192)
+_sb("ct", 12288)
 _sb("ei", 256, I32); _sb("zi", 256, I32)
-_sb("eo", 1280, U16); _sb("es", 1280, F16); _sb("zo", 1280, U16); _sb("zs", 1280, F16)
+_sb("eo", 1024, U16); _sb("es", 1024, F16); _sb("zo", 1280, U16); _sb("zs", 1024, F16)
 _sb("po", 768, U16)
 _sb("pz", 256, F32); _sb("ef", 256, F32); _sb("yz", 256, F32)
 IDENT = {"nI": -1.0, "p4096": 4096.0, "m4096": -4096.0, "pX": 131072.0, "mX": -131072.0, "pL": 12288.0,
@@ -48,20 +76,22 @@ for _t in range(1, RO + 1):
     IDENT["wt%d" % _t] = 77.0 * _t
 CB = {}
 for _n, _w in [("I", 128)] + [(_x, 128) for _x in IDENT] + [(_x, 128) for _x in (
-        "Sp", "ones", "zero", "c16", "c256", "cD", "neg", "pos", "keep", "U0", "GG", "tri", "odd", "Sh0", "Sh1", "Sh2", "Sh3", "t1", "t2",
-        "two", "c32", "t3", "gam", "m129")] + [("NB", 256), ("b24", 16), ("b24s", 16), ("b16", 16), ("b32", 16), ("bm16", 16)]:
+        "ones", "zero", "c16", "c256", "cD", "neg", "pos", "keep", "U0", "GG", "tri", "odd", "Sh0", "Sh1", "Sh2", "Sh3", "t2",
+        "t3", "gam", "Sp")] + [("lev", 512), ("NB", 256), ("b24", 16), ("b24s", 16), ("b32", 16), ("bm16", 16), ("b16", 16)]:
     CB[_n] = (sum(w for _, w in CB.values()), _w)
 _sb("cb", sum(w for _, w in CB.values()))
 _sb("cf", 512, F32); _sb("ch", 1024, F16)
-_sb("c511", 128, F16); _sb("cL", 128, F16)
+_sb("c511", 128, F16); _sb("m256", 1024)
 _sb("b8", 16, F32); _sb("w16", 48, F32)
 _sb("col", 16, F32)
 for _n, _w, _d in (("pi", 4, I32), ("u64", 64, F32), ("o64", 64, F32), ("n64", 64, I32), ("w64", 64, F32), ("x64", 64, F32), ("a64", 64, F32),
                    ("hl", 128, F16)):
     _sb("k_" + _n, _w, _d)
 for _h in range(NH):
-    for _n, _w, _d in (("V", 2080, BF), ("Ya", 2048, BF), ("Yb", 2048, BF), ("cmp", 2064, BF), ("c15", 128, BF), ("mx", 2048, BF), ("PK", 1024, F32),
-                       ("km", 128, F32), ("r8", 8, F32), ("P", 128, F16), ("d", 128, BF), ("L", 128, BF), ("r", 128, BF), ("Xr", 128, BF), ("X", 128, BF),
+    _y = [128 // LV, 16 * (LV + 1)] if RUNS else 2048
+    for _n, _w, _d in (("V", 2080, BF), ("Ya", _y, F16), ("Yb", _y, F16), ("cmp", 2064, BF), ("c15", 128, BF), ("mx", _y, F16), ("PK", 1024, F32),
+                       ("Vr", [128 // LV, RW * (LV + 1)], F16),
+                       ("km", 720, F32), ("P", 128, F16), ("d", 688, BF), ("L", 128, BF), ("r", 128, BF), ("Xr", 128, BF), ("X", 128, BF),
                        ("Mx", 128, BF), ("Mn", 128, BF), ("LT", 128, BF), ("r16", 128, BF), ("r2", 64, BF), ("Bs", 64, F32),
                        ("v", 128, I32), ("w", 128, I32), ("S2", 128, F32), ("pr", 128, I32), ("F", 128, I32), ("v0", 128, I32), ("v1", 128, I32),
                        ("val", 128, F16), ("del", 144, BF), ("rb", 640, BF), ("tk", 512, F16),
@@ -69,15 +99,31 @@ for _h in range(NH):
         _sb("%s%d" % (_n, _h), _w, _d)
     for _n in "abcd":
         SCRATCH["ps%s%d" % (_n, _h)] = ("psum", [128, 64, 8] if _n == "b" else [128, 512], F32)
-LOADS = ["ld0", "ld2"] + ["lc%d" % _j for _j in range(PARTS)]
+LOADS = ["ld0", "ld2", "lcf", "lch", "lcc", "lcm", "lca"] + ["lc%d" % _j for _j in range(len(PARTS) - 1)]
 SEMAPHORES += ["qP", "qV", "qS", "qG", "snt", "out"] + LOADS
 for _t in range(1, RO + 1):
     for _h in range(NH):
-        SEMAPHORES += ["%s%d%d" % (_k, _t, _h) for _k in "ez"]
+        SEMAPHORES += ["%s%d%d" % (_k, _t, _h) for _k in "ey"]
 
 
 def R(buf, c0, c1, step=1):
     return (buf, c0, c1, step)
+
+
+def R3(buf, j0, j1, step=1, a0=0, a1=None):
+    return (buf, "3", (a0, SCRATCH[buf][1][1] if a1 is None else a1, -1 if step == -1 else 1), (j0, j1, step))
+
+
+def cut(a, z, s):
+    return slice(a, z, s) if s > 0 else slice(z - 1, a - 1 if a else None, -1)
+
+
+def cover(r):
+    if r[1] == "3":
+        w = SCRATCH[r[0]][1][2]
+        one = sum(1 << j for j in range(r[3][0], r[3][1], max(1, abs(r[3][2]))))
+        return sum(one << w * a for a in range(r[2][0], r[2][1]))
+    return (1 << r[2]) - (1 << r[1]) if abs(r[3]) == 1 else sum(1 << j for j in range(r[1], r[2], r[3]))
 
 
 def cb(n, lo=0, hi=None):
@@ -90,9 +136,12 @@ def table(j, x):
 
 
 def ap(T, r):
-    if r[0][:3] == "psb":
-        a, z, j = r[1] // 8, (r[2] + 7) // 8, r[1] % 8
-        return T[r[0]][:, a:z, j:j + r[4]] if len(r) > 4 else T[r[0]][:, a:z, j::r[3]] if r[3] < 8 else T[r[0]][:, a:z, j]
+    if r[1] == "3":
+        return T[r[0]][:, cut(*r[2]), cut(*r[3]) if r[3][2] else r[3][0]]
+    if r[0] in SCRATCH and len(SCRATCH[r[0]][1]) == 3:
+        w = SCRATCH[r[0]][1][2]
+        a, z, j = r[1] // w, (r[2] + w - 1) // w, r[1] % w
+        return T[r[0]][:, a:z, j::r[3]] if r[3] < w else T[r[0]][:, a:z, j]
     if len(r) > 4:
         return T[r[0]][r[4]:r[5], r[1]:r[2]:r[3]]
     if r[3] == -1:
@@ -101,7 +150,9 @@ def ap(T, r):
 
 
 def ncol(r):
-    s = abs(r[3])
+    if r[1] == "3":
+        return ncol((0,) + r[2]) * ncol((0,) + r[3])
+    s = max(1, abs(r[3]))
     return (r[2] - r[1] + s - 1) // s
 
 
@@ -113,20 +164,27 @@ def isp(r):
     return SCRATCH[r[0]][0] == "psum"
 
 
-OPS, MARK = [], []
+OPS, MARK, PART = [], [], [0, 0, "", 0]
 
 
 def op(eng, dur, fns, reads, writes, sem=None, inc=1):
-    OPS.append({"e": eng, "d": dur, "f": fns, "r": reads, "w": writes, "sem": sem, "inc": inc})
+    OPS.append({"e": eng, "d": dur, "f": fns, "r": reads, "w": writes, "sem": sem, "inc": inc, "tag": tuple(PART)})
+    PART[3] += 1
     return len(OPS) - 1
+
+
+def part(name, t=None, h=None):
+    PART[:] = [PART[0] if t is None else t, PART[1] if h is None else h, name, 0]
 
 
 def either(*ways):
     for f in ways:
         f()
     ys = [OPS.pop() for _ in ways][::-1]
+    PART[3] -= len(ways)
     op("VS", ys[0]["d"], ys[0]["f"], [r for y in ys for r in y["r"]], ys[0]["w"])
     OPS[-1]["alt"] = {y["e"]: (y["d"], y["f"]) for y in ys}
+    OPS[-1]["g"] = ys[0].get("g")
 
 
 def two(rs):
@@ -185,16 +243,20 @@ def times(out, a, c):
     either(lambda: ts(out, a, c, A.mult), lambda: act(out, a, AF.Copy, scale=c))
 
 
-def gather(eng, out, offs):
+def gather(eng, out, offs, width, more=0.0):
     if eng == "E":
-        return either(lambda: gather("V", out, offs), lambda: gather("S", out, offs))
+        return either(lambda: gather("V", out, offs, width, more), lambda: gather("S", out, offs, width, more))
     n = ncol(out)
-    win = lambda T: T["ct"][:, 0:8192].indirect(ap(T, offs))
+    win = lambda T: ap(T, width).indirect(ap(T, offs))
     if eng == "S":
-        f = lambda g, T: g.scalar.activation(ap(T, out), win(T), AF.Copy)
+        f = lambda g, T: g.scalar.activation(ap(T, out), win(T), AF.Copy, bias=more)
+    elif more:
+        f = lambda g, T: g.vector.tensor_scalar(ap(T, out), win(T), more, None, A.add)
     else:
         f = lambda g, T: g.vector.tensor_copy(ap(T, out), win(T))
-    return op(eng, n * GC * SC + 60, [f], [R("ct", 0, 8192), offs], [out])
+    i = op(eng, n * GC * SC + 60, [f], [width, offs], [out])
+    OPS[i]["g"] = True
+    return i
 
 
 def mm(lst):
@@ -202,7 +264,7 @@ def mm(lst):
     for out, l, r, st, sp in lst:
         fns.append(lambda g, T, out=out, l=l, r=r, st=st, sp=sp: g.tensor.matmul(ap(T, out), ap(T, l), ap(T, r), st, sp))
         rd += [l, r]; wr.append(out)
-        d += max(64, ncol(r)) * PC * (4 if dts(l) == F32 else 1)
+        d += max(min(64, ncol(l)), ncol(r)) * PC * (4 if dts(l) == F32 else 1)
     return op("P", d, fns, rd, wr)
 
 
@@ -243,6 +305,7 @@ def columns():
     ts(col(7), K("pi", 2, 3), 2048.0, A.mult)
     act(col(8), col(7), AF.Copy, -2048.0, -1.0)
     act(col(9), col(7), AF.Copy, M1, -1.0)
+    act(col(10), col(7), AF.Copy, scale=-1.0)
 
 
 def constants():
@@ -252,14 +315,17 @@ def constants():
     fill(cb("zero"), 0.0); fill(cb("ones"), 1.0); whole(cb("c16"), 16); fill(cb("c256"), 1.0 / 256)
     for h in range(NH):
         whole(R("del%d" % h, 0, 16), 0)
-        fill(R("V%d" % h, 14, 2080, 2051), 0.0)
-        fill(R("V%d" % h, 15, 2080, 2049), 0.0)
-    if BOTH:
-        whole(cb("two"), 2)
-        iota(cb("c32"), [[0, 32], [32, 2], [0, 2]], 0, 0)
-    whole(cb("m129"), -129)
-    whole(R("cL", 0, 128), (2048 - 129 * 12288) // 128)
-    fill(cb("gam"), 127.0 / 128)
+        whole(R("V%d" % h, 14, 16), 0)
+        whole(R("V%d" % h, 2064, 2066), 0)
+        fill(R("km%d" % h, 11, 720, 16), M16)
+        fill(R("km%d" % h, 27, 720, 80), -M16)
+        whole(R("km%d" % h, 43, 720, 80), 0)
+        for n in ("Ya", "Yb") * RUNS:
+            whole(R3("%s%d" % (n, h), LV, 16 * (LV + 1), LV + 1), 0)
+    if RUNS:
+        n = 128 // LV * (1 if COPY else RW)
+        iota(cb("lev", 0, n * (LV + 1)), [[0, n], [-2, LV + 1]], 2 * LV, 0)
+        fill(R("cb", CB["lev"][0] + LV, CB["lev"][0] + n * (LV + 1), LV + 1), 16.0)
     select(cb("I"), cb("zero"), diag, 0, 1, A.not_equal, 1.0)
     for n, c in IDENT.items():
         either(lambda: ts(cb(n), cb("I"), c, A.mult), lambda: act(cb(n), cb("I"), AF.Copy, scale=c),
@@ -272,33 +338,36 @@ def constants():
     times(cb("b24s"), cb("b24"), 1.0 / 256)
     iota(cb("t3"), [[0, 64], [192, 2]], -96, 0)
     fill(cb("t3") + (64, 128), 0.0)
-    fill(cb("t3", 3)[:3] + (4, 64, 128), 1.0)
-    select(cb("t3"), cb("t3"), row, -15, 0, A.not_equal, 0.0)
+    fill(cb("t3", 3)[:3] + (4, 64, 96), 2.0)
+    select(cb("t3") + (0, 64), cb("t3") + (0, 64), row, -15, 0, A.not_equal, -64.0)
+    fill(cb("t3", 15)[:3] + (16, 64, 96), 0.0)
     for j, c in enumerate((2.0, ALPHA)):
         times(cb("NB", 128 * j, 128 * j + 128), cb("t3"), c / 2)
-    for n, c in (("b32", 32.0), ("bm16", -16.0), ("b16", 16.0)):
+    fill(cb("NB", 128, 256) + (96, 128), 127.0 / 32)
+    for n, c in (("b32", 32.0), ("bm16", -16.0), ("b16", 16.0))[:2 + (any(ABS) and not SPLIT)]:
         times(cb(n, 0, 8), b8, c)
     iota(cb("cD"), [[0, 8], [2, 16]], -15, 0)
-    act(cb("keep"), cb("cD"), AF.Sigmoid, 128.0 * 14, 128.0)
-    OPS[-1]["d"] += 1300.0
-    ts(cb("neg"), cb("keep"), 1000.0, A.mult, -1000.0, A.add)
-    ts(cb("pos"), cb("keep"), -1048576.0, A.mult, 1048576.0, A.add)
-    ts(R("c511", 0, 128), cb("keep"), 1000.0, A.mult, 511.0, A.add)
+    if SIG:
+        act(cb("keep"), cb("cD"), AF.Sigmoid, 128.0 * 14, 128.0)
+        OPS[-1]["d"] += 1300.0
+    else:
+        either(lambda: ts(cb("keep"), cb("cD"), -14.0, A.is_ge), lambda: select(cb("keep"), cb("ones"), row, 0, 0, A.not_equal, 0.0))
+    for out, c, a in ((cb("neg"), 1024.0, -1024.0), (cb("pos"), -1048576.0, 1048576.0), (R("c511", 0, 128), 1000.0, 511.0)):
+        either(lambda: ts(out, cb("keep"), c, A.mult, a, A.add), lambda: act(out, cb("keep"), AF.Copy, a, c))
     ri = col(0)
     act(col(2), col(1), AF.Copy, 1.0, -1.0)
-    act(col(3), ri, AF.Copy, scale=512.0)
     act(col(4), col(1), AF.Copy, -768.0 * 65536, 766.0 * 65536)
     act(col(5), ri, AF.Copy, 16.0, -1.0)
     act(col(6), col(1), AF.Copy, scale=BETA / 8192)
     for c in (0, 1):
         times(R("w16", 8 * c, 8 * c + 8), b8, col(2 - c))
-    if any(RAMPS):
-        times(R("w16", 16, 48, 2), R("w16", 0, 16), -1.0)
-        times(R("w16", 17, 48, 2), R("w16", 0, 16), 1.0)
+    times(R("w16", 16, 48, 2), R("w16", 0, 16), -1.0)
+    times(R("w16", 17, 48, 2), R("w16", 0, 16), 1.0)
     times(cb("U0", 0, 64), cb("ones", 0, 64), col(4))
     whole(cb("U0", 64, 128), 0)
-    select(cb("t1"), cb("p4096"), diag, -1, 1, A.not_equal, -4096.0)
-    select(cb("Sp"), cb("t1"), row, -15, 0, A.not_equal, 0.0)
+    act(col(3), ri, AF.Copy, scale=512.0)
+    select(cb("Sp"), cb("p4096"), diag, -1, 1, A.not_equal, -4096.0)
+    select(cb("Sp"), cb("Sp"), row, -15, 0, A.not_equal, 0.0)
     for s in range(4):
         select(cb("Sh%d" % s), cb("nI"), diag, -2 ** s, 1, A.not_equal, 1.0)
         select(cb("Sh%d" % s, 120, 128), cb("Sh%d" % s, 120, 128), [[-1, 8]], 8 - 2 ** s, 1, A.not_equal, 1.0)
@@ -308,9 +377,10 @@ def constants():
     select(cb("tri"), cb("GG"), flat, 0, -1, A.is_ge, 0.0)
     times(cb("odd"), cb("GG"), col(6))
     off, n, W, X2, AC = K("o64"), K("n64"), K("w64"), K("x64"), K("a64")
-    iota(K("u64", 0, 16), [[1, 16]], 0, 0)
-    for j, c in enumerate((14.0, 2.0, 0.0, 4.0)):
-        ts(R("k_n64", j, 64, 4), K("u64", 0, 16), ri, A.mult, c, A.add)
+    iota(K("u64"), [[1, 16], [0, 4]], 0, 0)
+    iota(K("o64"), [[0, 16], [2, 4]], 14, 0)
+    ts(K("u64"), K("u64"), ri, A.mult)
+    tt(n, K("u64"), K("o64"), A.add)
     ts(n, n, 15, A.bitwise_and)
     act(off, n, AF.Abs, -8.0)
     act(W, off, AF.Copy, -4.0)
@@ -325,9 +395,12 @@ def constants():
     hi, lo = R("k_hl", 0, 128, 2), R("k_hl", 1, 128, 2)
     cp(hi, AC)
     tt(lo, AC, hi, A.subtract)
-    for dst, src, w in (("cf", "k_a64", 64), ("ch", "k_hl", 128)):
+    for dst, src, w in (("ch", "k_hl", 128), ("cf", "k_a64", 64)):
+        fill(R(dst, 0, 8 * w), 0.0)
         for q in range(8):
-            times(R(dst, w * q, w * q + w), R(src, 0, w), R("b8", q, q + 1))
+            f = lambda g, T, dst=dst, src=src, w=w, q=q: g.sync.dma_start(T[dst][16 * q:16 * q + 16, w * q:w * q + w], T[src][16 * q:16 * q + 16, 0:w])
+            op("Y", 2 * DMA, [f], [R(src, 0, w), R(dst, w * q, w * q + w)], [("dma_l" + dst, q, q + 1, 1)])
+        op("X", 3000.0, [], [("dma_l" + dst, 0, 8, 1)], [R(dst, 0, 8 * w)], sem="l" + dst, inc=128)
 
 
 def half_round(t, h, hop):
@@ -349,87 +422,172 @@ def half_round(t, h, hop):
 
     rnd = lambda n, out, x, c: who(n, lambda: ts(out, x, c, A.add), lambda: act(out, x, AF.Identity, c))
     step = lambda n, out, x, c, k=256.0: who(n, lambda: ts(out, x, c, A.is_ge), lambda: act(out, x, AF.Sigmoid, -c * k, k))
-    hop(t, h, "z")
     V, Y = "V%d" % h, "Y%s%d" % ("ab"[t % 2], h)
-    for buf, ls, cuts in ((V, eo, VCUT[2 * t + h - 2]), (Y, zo, YCUT[2 * t + h - 2])):
+    LI = 128 // LV
+
+    def substrates(t, bank):
+        o = 256 * (t - 1) + 128 * h
+        cuts, buf = YCUT[2 * t + h - 2], "Y%s%d" % ("ab"[t % 2], h)
         w = 128 // len(cuts)
-        for c, eng in enumerate(cuts):
-            c0 = 16 * (w * c + (buf == V))
-            gather(eng, R(buf, c0, c0 + 16 * w), R(ls[0], ls[1] + w * c, ls[1] + w * (c + 1)))
-    if t > 1:
-        for n, out, x in (("es", es, eo), ("zs", zs, zo)):
-            rnd(n, out, x, col(8))
+        if RUNS:
+            for c in range(LV):
+                for j in range(0, LI, w):
+                    gather(cuts[(LI * c + j) // w], R3(buf, c, 16 * (LV + 1), LV + 1, j, j + w),
+                           R("zo", o + LI * c + j, o + LI * c + j + w), 4096, 256.0 * (LV - 1 - c))
+        else:
+            a = 0
+            for c in cuts:
+                w = 8 * int(c)
+                gather("E", R(buf, 16 * a, 16 * (a + w)), R("zo", o + a, o + a + w), R("ct", 4096, 8192) if t == 1 else R("ct", 0, 8192), -256.0)
+                a += w
+
+    part("a", t, h)
+    hop(t, h, "z")
+    if t == 1:
+        substrates(t, pd)
+    else:
+        rnd("es", es, eo, col(8))
+        if h == 0:
+            rnd("zs", R("zs", o, o + 256), R("zo", o, o + 256), -2048.0 if t == 2 and LATE else col(8))
+    part("b")
+    cuts = VCUT[2 * t + h - 2]
+    for c, eng in enumerate(cuts):
+        w = 128 // len(cuts)
+        gather(eng, R(V, 16 + 16 * w * c, 16 + 16 * w * (c + 1)), R("eo", o + w * c, o + w * (c + 1)),
+               R("ct", 4096, 8192 if t == 1 and LATE else 12288))
+    part("b1")
+    if t == 1 and LATE:
+        for a in (16, 1040):
+            for j in (2, 3):
+                x = R(V, a + j, a + 1024, 4)
+                either(lambda: ts(x, x, -256.0, A.add), lambda: act(x, x, AF.Copy, -256.0))
+    part("b15")
+    early = False
     v0, v15 = R(V, 16, 2064, 16), R(V, 31, 2064, 16)
     scan(b("cmp", 15, 15 + CUT), R(V, 14, 14 + CUT), R(V, 16, 16 + CUT), A.subtract, A.subtract, MID)
     scan(rev(b("cmp", 16 + CUT, 2064)), rev(R(V, 16 + CUT, 2064)), rev(R(V, 18 + CUT, 2066)), A.subtract, A.subtract, MID)
-    far = ABS[2 * t + h - 2]
-    both = any(c not in far for c in (0, 1, 4, 5))
-    if both:
-        mm([(R(pc, j, 256, 2), cb("two"), cb("ones"), j == 0, False) for j in (0, 1)])
-    mm([(R(pc, 256 * (j // 2) + j % 2, 256 * (j // 2 + 1), 2), cb("I"), v15, j == 2 and not both, j == 3) for j in range(0 if both else 2, 4)])
-    mm(group(q(pb, 3), [(cb("I"), v15), (cb("nI"), v0)]))
-    step("c15", b("c15"), q(pb, 3), -255.5)
-    mm([(q(pd, 1), cb("c256"), cb("cD"), True, False), (q(pd, 1), cb("c16"), cb("c32"), False, False)][:1 + both])
-    rows = [p for p in range(16) if p % 8 not in far]
-    for k in range(0, len(rows), 4):
-        mm([(R(pd, 128 + p, 256, 16), R(Y, p, 2048, 16), cb("bm16", 0, 8), False, False) for p in rows[k:k + 4]])
-    for c in far:
-        if both and not c & 2:
-            mm([(R(pd, 128 + c, 256, 8), cb("c16"), R("cb", CB["c32"][0] + 2, CB["c32"][0] + 66, 4), False, False)])
-        mm([(R(pd, 128 + c + 8 * j, 256, 16), v15, cb("b16", 0, 8), False, False) for j in (0, 1)])
-    pairs = list(far) + [c for c in range(8) if c not in far]
-    for c in pairs:
-        mx = b("mx", 256 * c, 256 * (c + 1))
-        if c in far:
-            bank = (pb, pa)[far.index(c) % 2]
-            mm([(q(bank, 0, 2), cb("I"), R(Y, c, 2048, 8), True, False)])
-            mm([(R(bank, j, 256, 2), cb("nI"), v15, False, j == 1) for j in (0, 1)])
-            act(mx, q(bank, 0, 2), AF.Abs, 0.0 if c & 2 else -256.0)
-        else:
-            tt(mx, R(Y, c, 2048, 8), q(pc, c & 2, 2), A.max)
-        mm([(R(pd, 128 + c + 8 * j, 256, 16), R("mx%d" % h, 256 * c + j, 256 * (c + 1), 2), cb("b16" if c in far else "b32", 0, 8), False,
-             c == pairs[-1] and j == 1) for j in (0, 1)])
-    scan(b("km"), cb("pos"), q(pd, 1), A.add, A.min)
-    km = R("km%d" % h, 15, 128, 16)
-    ts(b("r8", 0, 8), km, M16, A.add, M16, A.subtract)
-    mm([(q(pa, 0, 2), cb("ones"), cb("NB"), True, False), (q(pa, 1), cb("ones"), cb("gam"), False, False)])
+    last = q(pa, 2) if SPLIT else q(pb, 3)
+    mm(group(last, [(cb("I"), v15), (cb("nI"), v0)]))
+    over = 128.5 + 255.5 / 1024
+    who("c15", lambda: ts(b("c15"), last, 1.0 / 1024, A.mult, over, A.add), lambda: act(b("c15"), last, AF.Copy, over, 1.0 / 1024))
+    mx = "mx%d" % h
+    mm([(q(pd, 1), cb("c256"), cb("cD"), True, False), (q(pd, 1), cb("ones"), cb("pX"), False, False)])
+    if RUNS:
+        run, wide = LV + 1, RW * (LV + 1)
+        line = lambda buf, p, k: R3(buf, run * p, run * p + k)
+        many = 1 if COPY else RW
+        vr = R(pc, 0, LI * run * many)
+        mm([(vr, cb("ones"), cb("lev", 0, LI * run * many), True, False)])
+        for c in range(LV):
+            mm([(R(pc, run * j + c, LI * run * many, run * many), cb("I"), R(V, 31 + 16 * LI * c, 31 + 16 * LI * (c + 1), 16), False,
+                 c == LV - 1 and j == many - 1) for j in range(many)])
+        first = line("Vr%d" % h, 0, run * many)
+        who("Vr", lambda: cp(first, vr), lambda: act(first, vr, AF.Copy))
+        for j in range(many, RW):
+            cp(line("Vr%d" % h, j, run), first)
+        sums = lambda buf, p, w, end: [(R(pd, 128 + p, 256, 16) + (LI * c, LI * c + LI), R3(buf, run * p + c, run * p + c + 1, 0),
+                                        cb(w, 0, 8), False, end and c == LV - 1) for c in range(LV)]
+        for p in range(0, 16, 2):
+            mm(sums(Y, p, "bm16", False) + sums(Y, p + 1, "bm16", False))
+        for k in range(0, 16, RW):
+            scan(line(mx, k, wide), line(Y, k, wide), line("Vr%d" % h, 0, wide), A.min, A.max, 4096.0)
+            mm([x for p in range(k, k + RW) for x in sums(mx, p, "b32", p == 15)])
+    elif SPLIT:
+        n, w, far = 16 // RW, 128 // SPLIT, ABS[2 * t + h - 2]
+        near = 128 - w * far
+        for k in range(0, 16, 4):
+            mm([(R(pd, 128 + p, 256, 16) + (0, near) * far, R(Y, p, 16 * near, 16), cb("bm16", 0, 8), False, False) for p in range(k, k + 4)])
+        for s in range(SPLIT):
+            part("b2%d" % s)
+            bank, last15 = (pc, pb)[s % 2], R(V, 31 + 16 * w * s, 31 + 16 * w * (s + 1), 16)
+            if s < SPLIT - far:
+                mm([(R(bank, j, w * RW, RW), cb("I"), last15, True, True) for j in range(RW)])
+            for c in range(n):
+                x, y = 128 * RW * c + w * RW * s, R(Y, c + 16 * w * s, 16 * w * (s + 1), n)
+                if s < SPLIT - far:
+                    tt(R(mx, x, x + w * RW), y, R(bank, 0, w * RW), A.max)
+                else:
+                    bank = (pb, FARB[h])[c % 2]
+                    mm([(R(bank, 0, w * RW), cb("I"), y, True, False)])
+                    mm([(R(bank, j, w * RW, RW), cb("nI"), last15, False, j == RW - 1) for j in range(RW)])
+                    act(R(mx, x, x + w * RW), R(bank, 0, w * RW), AF.Abs, scale=0.5)
+                if s == SPLIT - 1:
+                    mm([(R(pd, 128 + c + n * j, 256, 16), R(mx, 128 * RW * c + j, 128 * RW * (c + 1), RW), cb("b32", 0, 8), False,
+                         c == n - 1 and j == RW - 1) for j in range(RW)])
+    else:
+        n, far = 16 // RW, ABS[2 * t + h - 2]
+        rows = [p for p in range(16) if p % n >= far]
+        for k in range(0, len(rows), 4):
+            mm([(R(pd, 128 + p, 256, 16), R(Y, p, 2048, 16), cb("bm16", 0, 8), False, False) for p in rows[k:k + 4]])
+        mm([(R(pc, j, 128 * RW, RW), cb("I"), v15, True, True) for j in range(RW)])
+        part("b2")
+        for c in range(far):
+            x, bank = R(mx, 128 * RW * c, 128 * RW * (c + 1)), R((pb, pa)[c % 2], 0, 128 * RW)
+            mm([(R(pd, 128 + c + n * j, 256, 16), v15, cb("b16", 0, 8), False, False) for j in range(RW)])
+            mm([(bank, cb("I"), R(Y, c, 2048, n), True, False)])
+            mm([(R(bank[0], j, 128 * RW, RW), cb("nI"), v15, False, j == RW - 1) for j in range(RW)])
+            act(x, bank, AF.Abs)
+            mm([(R(pd, 128 + c + n * j, 256, 16), R(mx, x[1] + j, x[2], RW), cb("b16", 0, 8), False, False) for j in range(RW)])
+        for c in range(far, n):
+            part("b3%d" % c)
+            x = R(mx, 128 * RW * c, 128 * RW * (c + 1))
+            tt(x, R(Y, c, 2048, n), R(pc, 0, 128 * RW), A.max)
+            mm([(R(pd, 128 + c + n * j, 256, 16), R(mx, x[1] + j, x[2], RW), cb("b32", 0, 8), False, c == n - 1 and j == RW - 1) for j in range(RW)])
+        part("b4")
+    km = "km%d" % h
+    scan(R(km, 0, 640, 5), cb("pos"), q(pd, 1), A.add, A.min)
+    part("c")
+    if t < RO and not early:
+        substrates(t + 1, pd)
+    part("d")
+    mm([(q(pa, 0, 2), cb("ones"), cb("NB"), True, False)])
+    part("e")
     if t > 1:
         mm([(q(pa, 1), b("h"), cb("odd"), False, False)])
+    part("f")
     mm([(R(pa, 15, 256, 16), b("c15"), cb("b24"), False, False)])
     for k in range(0, 15, 5):
         mm([(R(pa, j, 256, 16), R("cmp%d" % h, 16 + j, 2064, 16), cb("b24s"), False, j == 14) for j in range(k, k + 5)])
     scan(b("P"), R("c511", 0, 128), q(pa, 0), A.min, A.add, 1000.0)
     ts(b("L"), q(pa, 1), 128.0, A.max, 130.0, A.min)
     who("r", lambda: cp(b("r"), b("P")), lambda: act(b("r"), b("P"), AF.Copy))
-    scan(b("Xr"), b("r"), b("P"), A.add, A.subtract)
-    less(b("d"), b("r"), b("P"))
-    tt(R("d%d" % h, 0, 128, 16), km, b("r8", 0, 8), A.subtract)
-    scan(b("X"), cb("keep"), b("d"), A.mult, A.add)
-    scan(rev(b("Mx")), cb("neg"), rev(b("Xr")), A.add, A.max)
-    scan(rev(b("Mn")), cb("pos"), rev(b("Xr")), A.add, A.min)
-    mm(group(q(pb, 0), [(b("Mx"), cb("I")), (b("Mn"), cb("nI"))]))
+    if OWNX:
+        scan(b("Xr"), b("r"), b("P"), A.add, A.subtract)
+    d = R("d%d" % h, 48, 688, 5)
+    less(d, b("P"), b("r"))
+    scan(R("d%d" % h, 0, 640, 16), R(km, 75, 715, 16), R(km, 27, 667, 16), A.max, A.subtract)
+    scan(b("X"), cb("keep"), d, A.mult, A.subtract)
+    walk = rev(b("Xr" if OWNX else "X"))
+    scan(rev(b("Mx")), cb("neg"), walk, A.add, A.max)
+    scan(rev(b("Mn")), cb("pos"), walk, A.add, A.min)
+    apart(q(pb, 0), [(b("Mx"), cb("I")), (b("Mn"), cb("nI"))])
     who("LT", lambda: ts(b("LT"), q(pb, 0), 512.0, A.mult, col(3), A.add), lambda: act(b("LT"), q(pb, 0), AF.Identity, col(3), 512.0))
     ts(b("r16"), b("X"), M16, A.add, M16, A.subtract)
     even = R("X%d" % h, 0, 128, 2)
     rnd("r2", b("r2", 0, 64), even, 385.0)
     key, wt = q(pc, 2), cb("wt%d" % t)
-    terms = group(key, [(cb("ones"), R("cL", 0, 128)), (cb("m129"), wt), (cb("I"), es), (b("L"), cb("pL")), (b("L"), wt),
-                        (b("X"), cb("pX")), (cb("Sp"), b("LT")), (b("r16"), cb("mX"))])
-    for lo, hi in ((0, 3), (3, 5), (5, 6), (6, 7), (7, 8)):
-        mm(terms[lo:hi])
+    ramps = RAMPS[2 * t + h - 2]
+    keys = {e: k for e, k in zip(sorted(set(ramps)), (key, q(pd, 2)))}
+    for k in keys.values():
+        part("k" + k[0])
+        terms = group(k, [(b("L"), cb("pL")), (b("L"), wt), (cb("I"), es), (b("X"), cb("pX")), (cb("Sp"), b("LT")), (b("r16"), cb("mX"))])
+        for lo, hi in ((0, 2), (2, 3), (3, 4), (4, 5), (5, 6)):
+            mm(terms[lo:hi])
+    part("g")
+    more = 129 * (12288 + 77 * t) - 2048
     mm(group(q(pa, 2), table(0, es)))
     who("H", lambda: ts(b("H"), q(pa, 2), 0.125, A.mult), lambda: act(b("H"), q(pa, 2), AF.Copy, scale=0.125))
     mm(group(q(pa, 0), [(zs, cb("I")), (cb("ones"), cb("c16"))]))
     UA = R(pb, 256, 320)
     mm([(q(pb, 2), cb("ones"), cb("U0"), True, False), (UA, cb("mB"), even, False, False), (UA, cb("pB"), b("r2", 0, 64), False, False)])
     for p in range(8):
-        lo, pk = 131072 * (2 * p - 7.5) - BASE, b("PK", 128 * p, 128 * p + 128)
-        if RAMPS[2 * t + h - 2]:
-            act(pk, key, AF.Relu, -lo)
+        lo, pk = 131072 * (2 * p - 7.5) - BASE + more, b("PK", 128 * p, 128 * p + 128)
+        if ramps[p] == "S":
+            act(pk, keys["S"], AF.Relu, -lo)
         else:
-            ts(pk, key, lo, A.max, lo + 262144, A.min)
-        if RAMPS[2 * t + h - 2] and p:
-            mm([(R(pb, 255 + p, 384, 1) + (2,), pk, R("w16", 16, 48), False, p == 7)])
+            ts(pk, keys["V"], -lo, A.add, 0.0, A.max)
+        if p:
+            mm([(R3(pb, p - 1, p + 1, 1, 32, 48), pk, R("w16", 16, 48), False, p == 7)])
         else:
             mm([(R(pb, 256 + p, 384, 8), pk, R("w16", 0, 16), False, p == 7)])
     who("Bs", lambda: cp(b("Bs", 0, 64), R(pb, 320, 384)), lambda: act(b("Bs", 0, 64), R(pb, 320, 384), AF.Copy))
@@ -438,7 +596,10 @@ def half_round(t, h, hop):
     ts(b("w"), b("v"), 65535, A.bitwise_and)
     who("S2", lambda: ts(b("S2"), b("w"), -(20480.0 + 77 * t), A.add, 0.0, A.max), lambda: act(b("S2"), b("w"), AF.Relu, -(20480.0 + 77 * t)))
     gone = b("del", 16, 144)
-    step("del", gone, b("w"), 32767.5)
+    if SIG:
+        step("del", gone, b("w"), 32767.5)
+    else:
+        ts(gone, b("w"), 32767.5, A.is_ge)
     tt(b("pr"), b("S2"), q(pa, 0), A.mult)
     ts(b("F"), b("pr"), 5, A.arith_shift_right, 4095, A.bitwise_and)
     tt(q(pa, 1), b("w"), q(pa, 0), A.max)
@@ -454,10 +615,10 @@ def half_round(t, h, hop):
     mm(group(q(pd, 0), [(rb(0), cb("I")), (rb(4), cb("I"))]))
     ts(b("h"), q(pd, 0), col(5), A.is_equal)
     for j in (0, 1):
-        mm(group(q(pd, 1 + j), table(2 + j, b("h"))))
+        mm(group(q(pd, 1 + j), table(1 + 2 * j, b("h"))))
     for j in (0, 1):
         tt(b("PP", 128 * j, 128 * j + 128), b("H"), q(pd, 1 + j), A.mult)
-    apart(q(pd, 3), [(cb("tri"), b("h"))] + [(R("cf", j, 512, 4), b("PP", 128 * j, 128 * j + 128)) for j in (0, 1)])
+    apart(q(pd, 3), [(cb("tri"), b("h"))] + [(R("cf", 2 * j, 512, 4), b("PP", 128 * j, 128 * j + 128)) for j in (0, 1)])
     ts(b("fm"), q(pd, 3), 8192.0, A.add, 2048.0, A.min)
     tk = lambda s: b("tk", 128 * s, 128 * s + 128)
     for s, bank in enumerate((pc, pb, pa, pc, pb)):
@@ -474,59 +635,94 @@ def half_round(t, h, hop):
 
 
 def build():
-    def load(q, sem, dst, src, dur):
-        f = lambda g, T: (g.sync if q == "Y" else g.scalar).dma_start(ap(T, dst), T[src][:, dst[1]:dst[2]])
-        op(q, DMA, [f], [], [("dma_" + sem, 0, 1, 1)])
+    def load(q, sem, dst, src, dur, behind=()):
+        f = lambda g, T: (g.sync if q == "Y" else g.scalar).dma_start(ap(T, dst), T[src][:, dst[1] % 4096:(dst[2] - 1) % 4096 + 1])
+        op(q, DMA, [f], list(behind), [("dma_" + sem, 0, 1, 1), ("turn" + q, 0, 1, 1)])
         op("X", dur, [], [("dma_" + sem, 0, 1, 1)], [dst], sem=sem, inc=16)
 
     load("Z", "ld0", R("ei", 0, 256), "enz", 2000)
-    w = 4096 // PARTS
-    for j in range(PARTS):
-        load("Y", "lc%d" % j, R("ct", w * j, w * j + w), "cont", 2000 + (1600 - DMA * PARTS) * (j + 1) / PARTS)
-    load("Z", "ld2", R("zi", 0, 256), "subs", 3000)
+    parts = list(zip(PARTS, PARTS[1:]))
+    for j, (a, z) in enumerate(parts):
+        load("YZ"[j % 2], "lc%d" % j, R("ct", 4096 + a, 4096 + z), "cont", 2400 + 1600 * z / 4096 - (DMA + LAG) * ((j + 1) // 2 + 1))
+    load("Z", "ld2", R("zi", 0, 256), "subs", 2900)
+    load("Y", "lcc", R("ct", 0, 4096), "cont", 5000, [R("ct", 4096, 8192)])
 
-    def send(dst_of, src, dst, sem):
+    def send(src, ways):
         def f(g, T, core, topo):
-            to = T.cores[(T.rank_of(core) + dst_of) % len(T.cores)]
-            rid, pid, _ = topo.addr(to)
-            m = sum(1 << e for e in topo.engines(core, to))
-            g.remote_dma(ap(T, dst), ap(T, src), T.sem[sem], T.sem.snt, pid, rid, m)
-            return bin(m).count("1")
-        first = [("first", 0, 1, 1)]
-        op("R", ISSUE + FIRST * (sem == "z10"), [f], [src] + first * (sem != "z10"), [("net_" + sem, 0, 1, 1)] + first * (sem == "z10"))
-        op("X", NET, [], [("net_" + sem, 0, 1, 1)], [dst], sem=sem, inc=8)
+            sent, tr = 0, []
+            for j, (ahead, dst, sem) in enumerate(ways):
+                to = T.cores[(T.rank_of(core) + ahead) % len(T.cores)]
+                rid, pid, _ = topo.addr(to)
+                es = topo.engines(core, to)
+                es = es[len(es) * j // len(ways):len(es) * (j + 1) // len(ways)]
+                m = sum(1 << e for e in es)
+                sent += len(es)
+                if len(ways) == 1:
+                    g.remote_dma(ap(T, dst), ap(T, src), T.sem[sem], T.sem.snt, pid, rid, m)
+                else:
+                    tr.append(RemoteDMATransfer(dst_ids=[DstId(rid=rid, pnc=pid)], dma_engine_mask=m, remote_sem=T.sem[sem],
+                                                src=ap(T, src), dst=ap(T, dst)))
+            if tr:
+                g.remote_dma_fused(tr, local_sem=T.sem.snt)
+            return sent
+        sem, first = ways[0][2], [("first", 0, 1, 1)]
+        op("R", ISSUE + FIRST * (sem == "y10"), [f], [src] + first * (sem != "y10"), [("net_" + sem, 0, 1, 1)] + first * (sem == "y10"))
+        for _, dst, s in ways:
+            op("X", NET + 1500.0 * (s[0] == "y"), [], [("net_" + sem, 0, 1, 1)], [dst], sem=s, inc=8 // len(ways))
 
     def hop(t, h, kind):
         o = 256 * (t - 1) + 128 * h
         n = o + 256
         s = "%s%d%d" % (kind, t, h)
         if kind == "z":
-            if t == 1:
-                send(1, R("eo", o, o + 128), R("zo", n, n + 128), s)
+            if t == 1 and (h == 0 or not MERGE):
+                w = 256 if MERGE else 128
+                send(R("eo", o, o + w), [(1, R("zo", n, n + w), "y%d%d" % (t, h))])
         elif t < RO:
-            send(2, R("po", o, o + 128), R("eo", n, n + 128), s)
-            send(3, R("po", o, o + 128), R("zo", n + 256, n + 384), "z%d%d" % (t + 1, h))
+            send(R("po", o, o + 128), [(2, R("eo", n, n + 128), s)])
+            if h == 1 or not MERGE:
+                a = o - 128 * MERGE
+                send(R("po", a, o + 128), [(3, R("zo", a + 512, o + 640), "y%d%d" % (t + 1, h))])
         else:
-            send(2, R("pz", 128 * h, 128 * h + 128), R("ef", 128 * h, 128 * h + 128), s)
+            send(R("pz", 128 * h, 128 * h + 128), [(2, R("ef", 128 * h, 128 * h + 128), s)])
 
     columns()
-    for j in range(PARTS):
-        low, x = R("ct", 4096 + w * j, 4096 + w * j + w), R("ct", w * j, w * j + w)
+    for a, z in parts * (not LATE):
+        low, x = R("ct", 8192 + a, 8192 + z), R("ct", 4096 + a, 4096 + z)
         either(lambda: ts(low, x, -256.0, A.add), lambda: act(low, x, AF.Copy, -256.0))
-    for k in "ez":
-        for h in range(NH):
-            ts(R(k + "o", 128 * h, 128 * h + 128), R(k + "i", 128 * h, 128 * h + 128), col(7), A.add)
-        ts(R(k + "s", 0, 256), R(k + "o", 0, 256), col(8), A.add)
+    if LATE:
+        low = R("m256", 0, 512)
+        either(lambda: fill(low, -256.0), lambda: iota(low, [[0, 512]], -256, 0))
+        for j in range(8):
+            f = lambda g, T, j=j: g.sync.dma_start(T["ct"][:, 8192 + 512 * j:8704 + 512 * j], T["m256"][:, 0:512])
+            op("Y", DMA, [f], [low], [("dma_lcm", j, j + 1, 1), ("turnY", 0, 1, 1)])
+        op("X", 2500.0, [], [("dma_lcm", 0, 8, 1)], [R("ct", 8192, 12288)], sem="lcm", inc=128)
+        f = lambda g, T: g.dma_start(T["ct"][:, 8192:12288], T["cont"][:, 0:4096], accum_op=A.add, max_dma_last_dim=4096)
+        op("D", 2500.0, [f], [R("ct", 8192, 12288)], [("dma_lca", 0, 1, 1)])
+        op("X", 5000.0, [], [("dma_lca", 0, 1, 1)], [R("ct", 8192, 12288)], sem="lca", inc=16)
+    for h in range(NH):
+        c = lambda n: R(n, 128 * h, 128 * h + 128)
+        if LATE:
+            either(lambda: cp(c("eo"), c("ei")), lambda: act(c("eo"), c("ei"), AF.Copy))
+        else:
+            ts(c("eo"), c("ei"), col(7), A.add)
+        either(lambda: cp(c("zo"), c("zi")), lambda: act(c("zo"), c("zi"), AF.Copy))
+    ts(R("es", 0, 256), R("eo", 0, 256), -2048.0 if LATE else col(8), A.add)
+    ts(R("zs", 0, 256), R("zo", 0, 256), -2048.0, A.add)
     constants()
     for t in range(1, RO + 1):
         for h in range(NH):
             half_round(t, h, hop)
     o = 256 * RO
-    ts(R("yz", 0, 256), R("zo", o, o + 256), col(7), A.subtract)
+    part("end", RO + 1, 0)
+    either(lambda: ts(R("yz", 0, 256), R("zo", o, o + 256), col(7), A.subtract),
+           lambda: act(R("yz", 0, 256), R("zo", o, o + 256), AF.Identity, col(10)))
     for src, dst, parts in (("yz", "ysub", 1), ("ef", "yenz", NH)):
         w = 256 // parts
         for h in range(parts):
-            op("Y", DMA, [lambda g, T, src=src, dst=dst, c=w * h, w=w: g.sync.dma_start(T[dst][:, c:c + w], T[src][:, c:c + w])],
+            e = "Z" if parts > 1 and h == 0 else "Y"
+            op(e, DMA, [lambda g, T, src=src, dst=dst, c=w * h, w=w, e=e:
+                        (g.sync if e == "Y" else g.scalar).dma_start(T[dst][:, c:c + w], T[src][:, c:c + w])],
                [R(src, w * h, w * h + w)], [], sem="out", inc=16)
 
 
@@ -534,14 +730,12 @@ def analyse():
     hist = {}
     for i, x in enumerate(OPS):
         deps = {}
-        acc = [(r[:4], False) for r in x["r"]] + [(w[:4], True) for w in x["w"]]
-        for (buf, lo, hi, stp), wr in acc:
+        acc = [(r[0], cover(r), False) for r in x["r"]] + [(w[0], cover(w), True) for w in x["w"]]
+        for buf, bits, wr in acc:
             psum = buf in SCRATCH and SCRATCH[buf][0] == "psum"
-            for (l2, h2, s2, w2, j) in hist.get(buf, []):
-                over = lo < h2 and l2 < hi
+            for (other, w2, j) in hist.get(buf, []):
+                over = bits & other != 0
                 y = OPS[j]
-                if over and stp == s2 and stp > 1 and (lo - l2) % stp != 0:
-                    over = False
                 if psum and (y["e"] != x["e"] or x["e"] == "VS"):
                     deps[j] = True
                 elif psum and x["e"] == "P":
@@ -551,14 +745,14 @@ def analyse():
                 elif over and (wr or w2):
                     deps[j] = deps.get(j, False) or y["e"] != x["e"] or x["e"] != "P"
         x["deps"] = deps
-        for (buf, lo, hi, stp), wr in acc:
+        for buf, bits, wr in acc:
             lst = hist.setdefault(buf, [])
-            if wr and stp == 1 and len(x["w"][0]) == 4 and buf[:2] != "ps":
-                lst[:] = [e for e in lst if not (lo <= e[0] and e[1] <= hi) or e[4] == i]
-            lst.append((lo, hi, stp, wr, i))
+            if wr and len(x["w"][0]) == 4 and buf[:2] != "ps":
+                lst[:] = [e for e in lst if e[0] & ~bits or e[2] == i]
+            lst.append((bits, wr, i))
 
 
-QN = {"G": "g", "R": "g", "Z": "S"}
+QN = {"G": "g", "R": "g", "D": "g", "Z": "S"}
 
 
 def schedule(lead=LEAD, tries=TRIES, seed=1, moves=MOVES):
@@ -634,7 +828,7 @@ def schedule(lead=LEAD, tries=TRIES, seed=1, moves=MOVES):
         return best
 
     def other(far, jump, pace, more):
-        return [{e: d * far if e == "X" and d == NET else d * jump * pace if y["r"][:1] == [R("ct", 0, 8192)] else
+        return [{e: d * far if e == "X" and d == NET else d * jump * pace if y.get("g") else
                  (d + more * (e == "S")) * pace if e in "VSP" or y["e"] != "R" and e == "g" else d for e, d in c.items()} for y, c in zip(OPS, can)]
 
     sets = [(other(far, jump, pace, more), lag / LAG, pace) for far, jump, pace, lag, more in OTHER]
@@ -856,6 +1050,223 @@ def schedule(lead=LEAD, tries=TRIES, seed=1, moves=MOVES):
     return sorted(range(n), key=lambda i: (best[1][i], i)), best[0], names
 
 
+def refine(order, names, seed=1, laps=None, drift=False):
+    n = len(OPS)
+    code = {"V": 0, "S": 1, "P": 2, "G": 3, "R": 3, "D": 3, "Y": 4, "Z": 1, "X": 5}
+    pred, succ, above = [], [[] for _ in range(n)], []
+    for x in OPS:
+        p, seen, every = [], 0, 0
+        for j in sorted(x["deps"], reverse=True):
+            if not seen >> j & 1:
+                p.append((j, x["deps"][j]))
+                seen |= above[j] if x["deps"][j] else 0
+            every |= above[j] | 1 << j
+        pred.append(p)
+        above.append(every)
+    for i, p in enumerate(pred):
+        for j, w in p:
+            succ[j].append((i, w))
+    can = [sorted(x["alt"]) if "alt" in x else [x["e"]] for x in OPS]
+
+    def lasts(x, e, sc, gc, pc, fv, fs, net, first):
+        d = x["alt"][e][0] if "alt" in x else x["d"]
+        if x.get("g"):
+            return (d - 60) / (GC * SC) * gc * sc + 30 + (fv if e == "V" else fv + 15)
+        if e == "V":
+            return (d - FV) / SC * sc + fv
+        if e == "S":
+            return (d - FS) / SC * sc + fs
+        if e == "P":
+            return d / PC * pc
+        if e == "G":
+            return d / SC * sc * 1.1
+        return net if d == NET else ISSUE + first if d == ISSUE + FIRST else d
+
+    sets = [([{e: lasts(x, e, sc, gc, pc, fv, fs, net, first) for e in c} for x, c in zip(OPS, can)],
+             [[(j, lag * w) for j, w in p] for p in pred], [[(j, lag * w) for j, w in p] for p in succ], pace)
+            for sc, gc, pc, fv, fs, lag, net, first, pace in SETS]
+    x = [seed]
+
+    def draw():
+        x[0] = (x[0] * 1103515245 + 12345) % 2147483648
+        return x[0] / 2147483648
+
+    on = list(names)
+    q = [code[e] for e in on]
+
+    def reach(part, links, c):
+        end, free = {}, [0.0] * 6
+        for i in part:
+            e = q[i]
+            t = free[e]
+            for j, w in links[i]:
+                if end[j] + w > t:
+                    t = end[j] + w
+            end[i] = t = t + c[i][on[i]]
+            if e < 5:
+                free[e] = t
+        return end, free
+
+    def total(order):
+        r = [max(reach(order, pr, c)[0].values()) / p for (c, pr, _, _), p in zip(sets, PACE)]
+        w = [math.exp((y - max(r)) / EVEN) + 0.2 for y in r]
+        pool[:] = [y[:3] + (p * sum(w) / len(w) / v,) for y, p, v in zip(sets, PACE, w)]
+        return (sum(r) / len(r) + sum(sorted(r)[-4:]) / 4) / 2
+
+    if not PACE:
+        PACE.extend(max(reach(order, pr, c)[0].values()) / 85000.0 for c, pr, _, _ in sets)
+    pool = [y[:3] + (p,) for y, p in zip(sets, PACE)]
+
+    def anneal(a, z, heat, steps):
+        win = order[a:z]
+        m = len(win)
+        inside = {i: k for k, i in enumerate(win)}
+        away = [i for i in win if on[i] == "X"]
+        for k, i in enumerate(away):
+            q[i] = 5 + k
+        before = {i: {j for j, _ in pred[i] if j in inside} for i in win}
+        after = {i: {j for j, _ in succ[i] if j in inside} for i in win}
+        edges = []
+        for c, pr, su, pace in sets[12:]:
+            end, free = reach(order[:a], pr, c)
+            rest, late = reach(order[:z - 1:-1] if z < n else [], su, c)
+            tail = lambda i: max([rest[j] + w for j, w in su[i] if j in rest], default=0.0)
+            past = max([end[i] + tail(i) for i in order[max(0, a - 120):a]], default=0.0)
+            near = {i: (inside[i], max([end[j] + w for j, w in pr[i] if j in end], default=0.0), tail(i),
+                        [(inside[j], w) for j, w in pr[i] if j in inside], c[i]) for i in win}
+            edges.append((near, 1.0 / pace, late, [0.0] * m, [(free[:5] + [0.0] * len(away), past)] * (m // 8 + 2)))
+        undo = []
+
+        def length(lo, most_of):
+            lo -= lo % 8
+            tot = []
+            parts = [win[p:p + 8] for p in range(lo, m, 8)]
+            del undo[:]
+            for near, k, late, end, marks in edges:
+                free, most = marks[lo // 8]
+                free = list(free)
+                undo.append((end, end[:], marks, marks[:]))
+                p = lo // 8
+                for part in parts:
+                    marks[p] = (free[:], most)
+                    p += 1
+                    for i in part:
+                        e = q[i]
+                        y, t, rest, ins, c = near[i]
+                        if free[e] > t:
+                            t = free[e]
+                        for j, w in ins:
+                            if end[j] + w > t:
+                                t = end[j] + w
+                        end[y] = free[e] = t = t + c[on[i]]
+                        if t + rest > most:
+                            most = t + rest
+                a, b, d = free[0] + late[0], free[1] + late[1], free[2] + late[2]
+                tot.append((max(most, a, b, d, free[3] + late[3], free[4] + late[4]) + SOFT * (a + b + d)) * k)
+                if most_of and tot[0] > most_of:
+                    return None
+            return tot
+
+        each = length(0, 0)
+        now = least = sum(each)
+        kept = (list(win), [on[i] for i in win])
+        for _ in range(steps):
+            p = int(draw() * m)
+            v = win[p]
+            was = on[v]
+            if was == "X" or was == "P" and draw() < 0.4:
+                continue
+            if len(can[v]) > 1 and draw() < 0.3:
+                es = [e for e in can[v] if e != was]
+                on[v] = es[int(draw() * len(es))]
+                q[v] = code[on[v]]
+            e, j, skip = q[v], p, 1 + int(12 * draw() ** 4) - (on[v] != was)
+            if draw() < 0.5:
+                no = before[v]
+                while skip and j and win[j - 1] not in no:
+                    j -= 1
+                    skip -= q[win[j]] == e
+            else:
+                no = after[v]
+                while skip and j < m - 1 and win[j + 1] not in no:
+                    j += 1
+                    skip -= q[win[j]] == e
+            if skip and on[v] == was or j == p and on[v] == was:
+                on[v], q[v] = was, code[was]
+                continue
+            win.insert(j, win.pop(p))
+            lo = min(p, j)
+            room = -heat * math.log(draw() + 1e-9)
+            new = length(lo, each[0] + room + SPARE)
+            if new is not None and sum(new) <= now + room:
+                each, now = new, sum(new)
+                if now < least:
+                    least, kept = now, (list(win), [on[i] for i in win])
+            else:
+                win.insert(p, win.pop(j))
+                on[v], q[v] = was, code[was]
+                for end, old, marks, were in undo:
+                    end[:], marks[:] = old, were
+        if drift:
+            kept = (win, [on[i] for i in win])
+        order[a:z] = kept[0]
+        for i, e in zip(*kept):
+            on[i], q[i] = e, code[e]
+
+    twin = {}
+    for i, y in enumerate(OPS):
+        twin[y["tag"]] = i
+
+    def lay(src, dst):
+        end, _ = reach(order, sets[0][1], sets[0][0])
+        at = lambda t: end[twin[(t, 0, "b", 0)]]
+        pri = [end[i] - sets[0][0][i][on[i]] for i in range(n)]
+        new, to = list(pri), list(on)
+        for i, y in enumerate(OPS):
+            t = y["tag"]
+            j = twin.get((src,) + t[1:]) if t[0] == dst else None
+            if j is not None and can[i] == can[j]:
+                new[i], to[i] = pri[j] + at(dst) - at(src), on[j]
+            elif t[0] > dst:
+                new[i] += at(src + 1) - at(src) - at(dst + 1) + at(dst) if max(src, dst) < RO else 0.0
+        for i in range(n):
+            for j, _ in pred[i]:
+                if new[j] >= new[i]:
+                    new[i] = new[j] + 1e-3
+        return sorted(range(n), key=lambda i: new[i]), to
+
+    def span(t):
+        at = [k for k, i in enumerate(order) if OPS[i]["tag"][0] == t]
+        return at[0], at[-1]
+
+    def sweep(lo, hi, count, hot):
+        for s in range(count):
+            a = lo - WIDE + int(draw() * (hi - lo + WIDE))
+            a, z = max(a, 0), min(a + WIDE + int(4 * WIDE * draw() ** 2), n)
+            if z - a >= 10:
+                anneal(a, z, hot * (1 - s / count) ** 2 + 2.0, STEPS)
+
+    log = []
+    for count, hot, tries in (laps or LAPS):
+        sweep(0, n, count, hot)
+        log.append(total(order))
+        for _ in range(tries):
+            src, dst = 1 + int(draw() * RO), 1 + int(draw() * RO)
+            if src == dst:
+                continue
+            old = (list(order), list(on), total(order))
+            order[:], on[:] = lay(src, dst)
+            q[:] = [code[e] for e in on]
+            sweep(*span(dst), MEND, hot / 2)
+            if total(order) > old[2]:
+                order[:], on[:] = old[:2]
+                q[:] = [code[e] for e in on]
+            log.append((src, dst, total(order)))
+    log = [round(max(reach(order, pr, c)[0].values())) for c, pr, _, pace in sets]
+    log.append(round(sum(y["d"] for y, e in zip(OPS, on) if y.get("g") and e == "V") / 570.0))
+    return order, total(order), on, log
+
+
 PLAN = []
 
 
@@ -863,7 +1274,10 @@ def plan():
     if not PLAN:
         build()
         analyse()
-        PLAN.extend(schedule())
+        some = [schedule(lead=lead, moves=0) for lead in LEADS]
+        for count, hot, keep, drift in LAPS:
+            some = sorted((refine(x[0], x[2], laps=[(count, hot, 0)], drift=drift) for x in some), key=lambda x: x[1])[:keep]
+        PLAN.extend(some[0])
     return PLAN[0]
 
 
@@ -874,7 +1288,7 @@ def rank_program(g, core, T, topo):
     if T.rank_of(core) is None:
         return
     order = plan()
-    queue = {"P": g.tensor, "V": g.vector, "S": g.scalar, "G": g, "R": g, "Y": g.sync, "Z": g.scalar}
+    queue = {"P": g.tensor, "V": g.vector, "S": g.scalar, "G": g, "R": g, "D": g, "Y": g.sync, "Z": g.scalar}
     cnt, done, know, clock, sent = {}, {}, {}, {}, 0
     for i in order:
         x = OPS[i]

import math
import numpy as np
from concourse.bass import DstId, RemoteDMATransfer
from concourse.mybir import AluOpType as A, ActivationFunctionType as AF

RO, LH = 4, 128
NH = 2
FV = 20.0
FS = 50.0
SC = 0.92
PC = 0.46
GC = 1.7
OTHER = [(1.2, 0.7, 1.1, 130.0, 0.0), (1.0, 1.15, 1.1, 150.0, 15.0)]
ISSUE, NET = 600.0, 1600.0
DMA = 300.0
FIRST = 4000.0
LAG = 150.0
LEAD = 3000.0
TRIES = 60
MOVES = 2200
HEAT = 250.0
WIDE = 40
STEPS = 400
SOFT = 0.1
SETS = [(1.15, 2.0, 0.62, 26.0, 65.0, 160.0, 1600.0, 5000.0, 1.32), (0.9, 1.6, 0.48, 20.0, 50.0, 130.0, 1500.0, 3000.0, 0.96), (1.04, 1.15, 0.56, 24.0, 58.0, 135.0, 1900.0, 3000.0, 1.03)]
PACE = [_x / 85.0 for _x in (81.5, 85.7, 86.2, 86.1, 93.4, 92.3, 96.2, 98.2, 102.3, 100.0, 105.0, 113.1)]
EVEN = 1500.0
RANGES = [(0.83, 1.245, 1), (1.04, 2.08, 5), (0.48, 0.54, 7), (12.0, 28.0, 7), (35.0, 60.0, 11), (140.0, 210.0, 7), (1300.0, 2100.0, 11), (2500.0, 5500.0, 5)]
if RANGES:
    SETS = []
    for _k in range(12):
        _v = [lo + (hi - lo) * ((_k * s + 3 * j) % 12 + 0.5) / 12 for j, (lo, hi, s) in enumerate(RANGES)]
        _v[2] *= _v[0]
        SETS.append(tuple(_v) + ((_v[0] * (37.0 + 17.0 * _v[1]) + 0.09 * _v[5] + 0.2 * _v[3] + 0.08 * _v[4] + 0.002 * _v[6]) / 80.0,))
TRAIN = [(1.15, 1.95, 0.58, 24.0, 60.0, 165.0, 1500.0, 4500.0, 1.32), (0.86, 1.56, 0.44, 18.0, 48.0, 155.0, 1300.0, 3500.0, 0.95), (1.02, 1.25, 0.52, 20.0, 54.0, 155.0, 1600.0, 3500.0, 1.05)]
SETS += TRAIN
LEADS = [2100, 2300, 2400, 2500, 2600, 2700, 2900, 3100]
LAPS = [(100, 400.0, 2, False), (300, 400.0, 1, False), (6000, 85.0, 1, True)]
DRIFT = 0.0
MEND = 40
SPARE = 150.0
VCUT = ["EEEE"] * 8
YCUT = ["4444"] * 2 + ["6222211"] * 6
CUT = 1024
PARTS = [0, 2048, 3584, 4096]
RUNS = False
COPY = False
LV = 4
RW = 4
EARLY = [0, 0, 1, 1, 1, 1]
ABS = [0] * 8
RAMPS = ["SSSSSSSS"] * 8
SPLIT = 2
FARB = ["psb0", "psb1"]
MERGE = 1
SIG = False
LATE = False
OWNX = True
ONSC = [{}, {}]
SCRATCH, SEMAPHORES = {}, []


def _sb(name, cols, dtype="bfloat16"):
    SCRATCH[name] = ("sbuf", [128] + (cols if isinstance(cols, list) else [cols]), dtype)


F32, BF, I32, U16, F16 = "float32", "bfloat16", "int32", "uint16", "float16"
_sb("ct", 12288)
_sb("ei", 256, I32); _sb("zi", 256, I32)
_sb("eo", 1024, U16); _sb("es", 1024, F16); _sb("zo", 1280, U16); _sb("zs", 1024, F16)
_sb("po", 768, U16)
_sb("pz", 256, F32); _sb("ef", 256, F32); _sb("yz", 256, F32)
IDENT = {"nI": -1.0, "p4096": 4096.0, "m4096": -4096.0, "pX": 131072.0, "mX": -131072.0, "pL": 12288.0,
         "pB": 2.0 ** 23, "mB": -2.0 ** 23}
for _t in range(1, RO + 1):
    IDENT["wt%d" % _t] = 77.0 * _t
CB = {}
for _n, _w in [("I", 128)] + [(_x, 128) for _x in IDENT] + [(_x, 128) for _x in (
        "ones", "zero", "c16", "c256", "cD", "neg", "pos", "keep", "U0", "GG", "tri", "odd", "Sh0", "Sh1", "Sh2", "Sh3", "t2",
        "t3", "gam", "Sp")] + [("lev", 512), ("NB", 256), ("b24", 16), ("b24s", 16), ("b32", 16), ("bm16", 16), ("b16", 16)]:
    CB[_n] = (sum(w for _, w in CB.values()), _w)
_sb("cb", sum(w for _, w in CB.values()))
_sb("cf", 512, F32); _sb("ch", 1024, F16)
_sb("c511", 128, F16); _sb("m256", 1024)
_sb("b8", 16, F32); _sb("w16", 48, F32)
_sb("col", 16, F32)
for _n, _w, _d in (("pi", 4, I32), ("u64", 64, F32), ("o64", 64, F32), ("n64", 64, I32), ("w64", 64, F32), ("x64", 64, F32), ("a64", 64, F32),
                   ("hl", 128, F16)):
    _sb("k_" + _n, _w, _d)
for _h in range(NH):
    _y = [128 // LV, 16 * (LV + 1)] if RUNS else 2048
    for _n, _w, _d in (("V", 2080, BF), ("Ya", _y, F16), ("Yb", _y, F16), ("cmp", 2064, BF), ("c15", 128, BF), ("mx", _y, F16), ("PK", 1024, F32),
                       ("Vr", [128 // LV, RW * (LV + 1)], F16),
                       ("km", 720, F32), ("P", 128, F16), ("d", 688, BF), ("L", 128, BF), ("r", 128, BF), ("Xr", 128, BF), ("X", 128, BF),
                       ("Mx", 128, BF), ("Mn", 128, BF), ("LT", 128, BF), ("r16", 128, BF), ("r2", 64, BF), ("Bs", 64, F32),
                       ("v", 128, I32), ("w", 128, I32), ("S2", 128, F32), ("pr", 128, I32), ("F", 128, I32), ("v0", 128, I32), ("v1", 128, I32),
                       ("val", 128, F16), ("del", 144, BF), ("rb", 640, BF), ("tk", 512, F16),
                       ("h", 128, BF), ("H", 128, F32), ("PP", 256, F32), ("fm", 128, F16)):
        _sb("%s%d" % (_n, _h), _w, _d)
    for _n in "abcd":
        SCRATCH["ps%s%d" % (_n, _h)] = ("psum", [128, 64, 8] if _n == "b" else [128, 512], F32)
LOADS = ["ld0", "ld2", "lcf", "lch", "lcc", "lcm", "lca"] + ["lc%d" % _j for _j in range(len(PARTS) - 1)]
SEMAPHORES += ["qP", "qV", "qS", "qG", "snt", "out"] + LOADS
for _t in range(1, RO + 1):
    for _h in range(NH):
        SEMAPHORES += ["%s%d%d" % (_k, _t, _h) for _k in "ey"]


def R(buf, c0, c1, step=1):
    return (buf, c0, c1, step)


def R3(buf, j0, j1, step=1, a0=0, a1=None):
    return (buf, "3", (a0, SCRATCH[buf][1][1] if a1 is None else a1, -1 if step == -1 else 1), (j0, j1, step))


def cut(a, z, s):
    return slice(a, z, s) if s > 0 else slice(z - 1, a - 1 if a else None, -1)


def cover(r):
    if r[1] == "3":
        w = SCRATCH[r[0]][1][2]
        one = sum(1 << j for j in range(r[3][0], r[3][1], max(1, abs(r[3][2]))))
        return sum(one << w * a for a in range(r[2][0], r[2][1]))
    return (1 << r[2]) - (1 << r[1]) if abs(r[3]) == 1 else sum(1 << j for j in range(r[1], r[2], r[3]))


def cb(n, lo=0, hi=None):
    c, w = CB[n]
    return R("cb", c + lo, c + (w if hi is None else hi))


def table(j, x):
    return [(R("ch", 2 * j + c, 1024, 8), x) for c in (0, 1)]


def ap(T, r):
    if r[1] == "3":
        return T[r[0]][:, cut(*r[2]), cut(*r[3]) if r[3][2] else r[3][0]]
    if r[0] in SCRATCH and len(SCRATCH[r[0]][1]) == 3:
        w = SCRATCH[r[0]][1][2]
        a, z, j = r[1] // w, (r[2] + w - 1) // w, r[1] % w
        return T[r[0]][:, a:z, j::r[3]] if r[3] < w else T[r[0]][:, a:z, j]
    if len(r) > 4:
        return T[r[0]][r[4]:r[5], r[1]:r[2]:r[3]]
    if r[3] == -1:
        return T[r[0]][:, r[2] - 1:r[1] - 1:-1] if r[1] else T[r[0]][:, r[2] - 1::-1]
    return T[r[0]][:, r[1]:r[2]:r[3]] if r[3] != 1 else T[r[0]][:, r[1]:r[2]]


def ncol(r):
    if r[1] == "3":
        return ncol((0,) + r[2]) * ncol((0,) + r[3])
    s = max(1, abs(r[3]))
    return (r[2] - r[1] + s - 1) // s


def dts(r):
    return SCRATCH[r[0]][2]


def isp(r):
    return SCRATCH[r[0]][0] == "psum"


OPS, MARK, PART = [], [], [0, 0, "", 0]


def op(eng, dur, fns, reads, writes, sem=None, inc=1):
    OPS.append({"e": eng, "d": dur, "f": fns, "r": reads, "w": writes, "sem": sem, "inc": inc, "tag": tuple(PART)})
    PART[3] += 1
    return len(OPS) - 1


def part(name, t=None, h=None):
    PART[:] = [PART[0] if t is None else t, PART[1] if h is None else h, name, 0]


def either(*ways):
    for f in ways:
        f()
    ys = [OPS.pop() for _ in ways][::-1]
    PART[3] -= len(ways)
    op("VS", ys[0]["d"], ys[0]["f"], [r for y in ys for r in y["r"]], ys[0]["w"])
    OPS[-1]["alt"] = {y["e"]: (y["d"], y["f"]) for y in ys}
    OPS[-1]["g"] = ys[0].get("g")


def two(rs):
    return all(dts(r) in (BF, F16, U16) and not isp(r) for r in rs)


def cyc(n, x):
    return max(64, n * x) * SC + FV


def ts(out, a, s1, op0, s2=None, op1=None):
    cols = [s for s in (s1, s2) if isinstance(s, tuple)]

    def f(g, T):
        x = ap(T, s1) if isinstance(s1, tuple) else s1
        y = ap(T, s2) if isinstance(s2, tuple) else s2
        if op1 is None:
            return g.vector.tensor_scalar(ap(T, out), ap(T, a), x, None, op0)
        return g.vector.tensor_scalar(ap(T, out), ap(T, a), x, y, op0, op1)
    return op("V", cyc(ncol(out), 0.5 if two([out, a]) else 1), [f], [a] + cols, [out])


def tt(out, a, b, o):
    return op("V", cyc(ncol(out), 1 if isp(a) or isp(b) else 2), [lambda g, T: g.vector.tensor_tensor(ap(T, out), ap(T, a), ap(T, b), o)], [a, b], [out])


def cp(out, a):
    return op("V", cyc(ncol(out), 0.5 if two([out, a]) else 1), [lambda g, T: g.vector.tensor_copy(ap(T, out), ap(T, a))], [a], [out])


def fill(out, c):
    return op("V", cyc(ncol(out), 0.5), [lambda g, T: g.vector.memset(ap(T, out), c)], [], [out])


def scan(out, d0, d1, o0, o1, first=0.0):
    return op("V", cyc(ncol(out), 0.5 if two([out, d0, d1]) else 1),
              [lambda g, T: g.vector.tensor_tensor_scan(ap(T, out), ap(T, d0), ap(T, d1), first, o0, o1)], [d0, d1], [out])


def less(out, a, b):
    return scan(out, a, b, A.max, A.subtract)


def act(out, a, func, bias=None, scale=None):
    def f(g, T):
        kw = {}
        if bias is not None:
            kw["bias"] = ap(T, bias) if isinstance(bias, tuple) else bias
        if scale is not None:
            kw["scale"] = ap(T, scale) if isinstance(scale, tuple) else scale
        return g.scalar.activation(ap(T, out), ap(T, a), func, **kw)
    return op("S", max(64, ncol(out)) * SC + FS, [f], [a] + [s for s in (bias, scale) if isinstance(s, tuple)], [out])


def times(out, a, c):
    either(lambda: ts(out, a, c, A.mult), lambda: act(out, a, AF.Copy, scale=c))


def gather(eng, out, offs, width, more=0.0):
    if eng == "E":
        return either(lambda: gather("V", out, offs, width, more), lambda: gather("S", out, offs, width, more))
    n = ncol(out)
    win = lambda T: ap(T, width).indirect(ap(T, offs))
    if eng == "S":
        f = lambda g, T: g.scalar.activation(ap(T, out), win(T), AF.Copy, bias=more)
    elif more:
        f = lambda g, T: g.vector.tensor_scalar(ap(T, out), win(T), more, None, A.add)
    else:
        f = lambda g, T: g.vector.tensor_copy(ap(T, out), win(T))
    i = op(eng, n * GC * SC + 60, [f], [width, offs], [out])
    OPS[i]["g"] = True
    return i


def mm(lst):
    fns, rd, wr, d = [], [], [], 0.0
    for out, l, r, st, sp in lst:
        fns.append(lambda g, T, out=out, l=l, r=r, st=st, sp=sp: g.tensor.matmul(ap(T, out), ap(T, l), ap(T, r), st, sp))
        rd += [l, r]; wr.append(out)
        d += max(min(64, ncol(l)), ncol(r)) * PC * (4 if dts(l) == F32 else 1)
    return op("P", d, fns, rd, wr)


def group(out, terms):
    return [(out, l, r, i == 0, i == len(terms) - 1) for i, (l, r) in enumerate(terms)]


def apart(out, terms):
    for x in group(out, terms):
        mm([x])


def iota(out, pattern, base, cm):
    kw = {} if dts(out) == I32 else {"allow_small_or_imprecise_dtypes": True}
    return op("G", 130 + 2 * ncol(out) * SC, [lambda g, T: g.iota(ap(T, out), pattern, base, cm, **kw)], [], [out])


def select(out, a, pattern, base, cm, cmp, other):
    return op("G", 170 + 2 * ncol(out) * SC, [lambda g, T: g.affine_select(ap(T, out), ap(T, a), pattern, cmp, other, base, cm)], [a], [out])


ALPHA, BETA = 70.0 / 256, 48.0 / 256
BASE = 8192.0 + 65536
M1, M16 = 1.5 * 2 ** 23, 1.5 * 2 ** 27
MID = 192 * 256 + 128.0


def col(j):
    return R("col", j, j + 1)


def columns():
    K = lambda n, lo=0, hi=64: R("k_" + n, lo, hi)
    iota(K("pi", 0, 3), [[0, 3]], 0, 1)
    for j, c in enumerate((15, 1, 2)):
        ts(K("pi", j, j + 1), K("pi", j, j + 1), c, A.bitwise_and)
    cp(R("col", 0, 2), K("pi", 0, 2))
    ts(col(7), K("pi", 2, 3), 2048.0, A.mult)
    act(col(8), col(7), AF.Copy, -2048.0, -1.0)
    act(col(9), col(7), AF.Copy, M1, -1.0)
    act(col(10), col(7), AF.Copy, scale=-1.0)


def constants():
    K = lambda n, lo=0, hi=64: R("k_" + n, lo, hi)
    diag, row, blk, flat = [[-1, 128]], [[0, 8], [1, 16]], [[-16, 8], [0, 16]], [[1, 128]]
    whole = lambda out, c: either(lambda: fill(out, float(c)), lambda: iota(out, [[0, ncol(out)]], c, 0))
    fill(cb("zero"), 0.0); fill(cb("ones"), 1.0); whole(cb("c16"), 16); fill(cb("c256"), 1.0 / 256)
    for h in range(NH):
        whole(R("del%d" % h, 0, 16), 0)
        whole(R("V%d" % h, 14, 16), 0)
        whole(R("V%d" % h, 2064, 2066), 0)
        fill(R("km%d" % h, 11, 720, 16), M16)
        fill(R("km%d" % h, 27, 720, 80), -M16)
        whole(R("km%d" % h, 43, 720, 80), 0)
        for n in ("Ya", "Yb") * RUNS:
            whole(R3("%s%d" % (n, h), LV, 16 * (LV + 1), LV + 1), 0)
    if RUNS:
        n = 128 // LV * (1 if COPY else RW)
        iota(cb("lev", 0, n * (LV + 1)), [[0, n], [-2, LV + 1]], 2 * LV, 0)
        fill(R("cb", CB["lev"][0] + LV, CB["lev"][0] + n * (LV + 1), LV + 1), 16.0)
    select(cb("I"), cb("zero"), diag, 0, 1, A.not_equal, 1.0)
    for n, c in IDENT.items():
        either(lambda: ts(cb(n), cb("I"), c, A.mult), lambda: act(cb(n), cb("I"), AF.Copy, scale=c),
               lambda: select(cb(n), cb("zero"), diag, 0, 1, A.not_equal, c))
    b8, t8 = R("b8", 0, 8), R("b8", 8, 16)
    select(t8, cb("ones", 0, 8), [[-16, 8]], 0, 1, A.is_ge, 0.0)
    select(b8, t8, [[16, 8]], 15, -1, A.is_ge, 0.0)
    for j, c in enumerate((2.0, ALPHA)):
        times(cb("b24", 8 * j, 8 * j + 8), b8, c)
    times(cb("b24s"), cb("b24"), 1.0 / 256)
    iota(cb("t3"), [[0, 64], [192, 2]], -96, 0)
    fill(cb("t3") + (64, 128), 0.0)
    fill(cb("t3", 3)[:3] + (4, 64, 96), 2.0)
    select(cb("t3") + (0, 64), cb("t3") + (0, 64), row, -15, 0, A.not_equal, -64.0)
    fill(cb("t3", 15)[:3] + (16, 64, 96), 0.0)
    for j, c in enumerate((2.0, ALPHA)):
        times(cb("NB", 128 * j, 128 * j + 128), cb("t3"), c / 2)
    fill(cb("NB", 128, 256) + (96, 128), 127.0 / 32)
    for n, c in (("b32", 32.0), ("bm16", -16.0), ("b16", 16.0))[:2 + (any(ABS) and not SPLIT)]:
        times(cb(n, 0, 8), b8, c)
    iota(cb("cD"), [[0, 8], [2, 16]], -15, 0)
    if SIG:
        act(cb("keep"), cb("cD"), AF.Sigmoid, 128.0 * 14, 128.0)
        OPS[-1]["d"] += 1300.0
    else:
        either(lambda: ts(cb("keep"), cb("cD"), -14.0, A.is_ge), lambda: select(cb("keep"), cb("ones"), row, 0, 0, A.not_equal, 0.0))
    for out, c, a in ((cb("neg"), 1024.0, -1024.0), (cb("pos"), -1048576.0, 1048576.0), (R("c511", 0, 128), 1000.0, 511.0)):
        either(lambda: ts(out, cb("keep"), c, A.mult, a, A.add), lambda: act(out, cb("keep"), AF.Copy, a, c))
    ri = col(0)
    act(col(2), col(1), AF.Copy, 1.0, -1.0)
    act(col(4), col(1), AF.Copy, -768.0 * 65536, 766.0 * 65536)
    act(col(5), ri, AF.Copy, 16.0, -1.0)
    act(col(6), col(1), AF.Copy, scale=BETA / 8192)
    for c in (0, 1):
        times(R("w16", 8 * c, 8 * c + 8), b8, col(2 - c))
    times(R("w16", 16, 48, 2), R("w16", 0, 16), -1.0)
    times(R("w16", 17, 48, 2), R("w16", 0, 16), 1.0)
    times(cb("U0", 0, 64), cb("ones", 0, 64), col(4))
    whole(cb("U0", 64, 128), 0)
    act(col(3), ri, AF.Copy, scale=512.0)
    select(cb("Sp"), cb("p4096"), diag, -1, 1, A.not_equal, -4096.0)
    select(cb("Sp"), cb("Sp"), row, -15, 0, A.not_equal, 0.0)
    for s in range(4):
        select(cb("Sh%d" % s), cb("nI"), diag, -2 ** s, 1, A.not_equal, 1.0)
        select(cb("Sh%d" % s, 120, 128), cb("Sh%d" % s, 120, 128), [[-1, 8]], 8 - 2 ** s, 1, A.not_equal, 1.0)
    whole(cb("t2"), -8192)
    select(cb("t2"), cb("t2"), blk, 0, 1, A.is_ge, 0.0)
    select(cb("GG"), cb("t2"), [[16, 8], [0, 16]], 15, -1, A.is_ge, 0.0)
    select(cb("tri"), cb("GG"), flat, 0, -1, A.is_ge, 0.0)
    times(cb("odd"), cb("GG"), col(6))
    off, n, W, X2, AC = K("o64"), K("n64"), K("w64"), K("x64"), K("a64")
    iota(K("u64"), [[1, 16], [0, 4]], 0, 0)
    iota(K("o64"), [[0, 16], [2, 4]], 14, 0)
    ts(K("u64"), K("u64"), ri, A.mult)
    tt(n, K("u64"), K("o64"), A.add)
    ts(n, n, 15, A.bitwise_and)
    act(off, n, AF.Abs, -8.0)
    act(W, off, AF.Copy, -4.0)
    act(X2, W, AF.Square)
    w4 = np.arange(1.0, 5.0)
    cc = [float(c) for c in np.linalg.solve(np.stack([w4 ** (2 * k + 1) for k in range(4)], 1), np.sin(w4 * math.pi / 8))]
    ts(AC, X2, cc[3], A.mult, cc[2], A.add)
    for k in (1, 0):
        tt(AC, AC, X2, A.mult)
        act(AC, AC, AF.Copy, cc[k])
    tt(AC, AC, W, A.mult)
    hi, lo = R("k_hl", 0, 128, 2), R("k_hl", 1, 128, 2)
    cp(hi, AC)
    tt(lo, AC, hi, A.subtract)
    for dst, src, w in (("ch", "k_hl", 128), ("cf", "k_a64", 64)):
        fill(R(dst, 0, 8 * w), 0.0)
        for q in range(8):
            f = lambda g, T, dst=dst, src=src, w=w, q=q: g.sync.dma_start(T[dst][16 * q:16 * q + 16, w * q:w * q + w], T[src][16 * q:16 * q + 16, 0:w])
            op("Y", 2 * DMA, [f], [R(src, 0, w), R(dst, w * q, w * q + w)], [("dma_l" + dst, q, q + 1, 1)])
        op("X", 3000.0, [], [("dma_l" + dst, 0, 8, 1)], [R(dst, 0, 8 * w)], sem="l" + dst, inc=128)


def half_round(t, h, hop):
    MARK.append((len(OPS), 2 * t + h))
    ONS = ONSC[t == RO]
    b = lambda n, lo=0, hi=128: R("%s%d" % (n, h), lo, hi)
    pa, pb, pc, pd = ["ps%s%d" % (x, h) for x in "abcd"]
    q = lambda p, j, k=1: R(p, 128 * j, 128 * (j + k))
    o = 256 * (t - 1) + 128 * h
    eo, es, zo, zs = R("eo", o, o + 128), R("es", o, o + 128), R("zo", o, o + 128), R("zs", o, o + 128)
    rev = lambda r: r[:3] + (-1,)

    def who(n, v, s):
        e = ONS.get(n, "E")
        if e == "E":
            either(v, s)
        else:
            (v if e == "V" else s)()

    rnd = lambda n, out, x, c: who(n, lambda: ts(out, x, c, A.add), lambda: act(out, x, AF.Identity, c))
    step = lambda n, out, x, c, k=256.0: who(n, lambda: ts(out, x, c, A.is_ge), lambda: act(out, x, AF.Sigmoid, -c * k, k))
    V, Y = "V%d" % h, "Y%s%d" % ("ab"[t % 2], h)
    LI = 128 // LV

    def substrates(t, bank):
        o = 256 * (t - 1) + 128 * h
        cuts, buf = YCUT[2 * t + h - 2], "Y%s%d" % ("ab"[t % 2], h)
        w = 128 // len(cuts)
        if RUNS:
            for c in range(LV):
                for j in range(0, LI, w):
                    gather(cuts[(LI * c + j) // w], R3(buf, c, 16 * (LV + 1), LV + 1, j, j + w),
                           R("zo", o + LI * c + j, o + LI * c + j + w), 4096, 256.0 * (LV - 1 - c))
        else:
            a = 0
            for c in cuts:
                w = 8 * int(c)
                gather("E", R(buf, 16 * a, 16 * (a + w)), R("zo", o + a, o + a + w), R("ct", 4096, 8192) if t == 1 else R("ct", 0, 8192), -256.0)
                a += w

    part("a", t, h)
    hop(t, h, "z")
    if t == 1:
        substrates(t, pd)
    else:
        rnd("es", es, eo, col(8))
        if h == 0:
            rnd("zs", R("zs", o, o + 256), R("zo", o, o + 256), -2048.0 if t == 2 and LATE else col(8))
    part("b")
    cuts = VCUT[2 * t + h - 2]
    for c, eng in enumerate(cuts):
        w = 128 // len(cuts)
        gather(eng, R(V, 16 + 16 * w * c, 16 + 16 * w * (c + 1)), R("eo", o + w * c, o + w * (c + 1)),
               R("ct", 4096, 8192 if t == 1 and LATE else 12288))
    part("b1")
    if t == 1 and LATE:
        for a in (16, 1040):
            for j in (2, 3):
                x = R(V, a + j, a + 1024, 4)
                either(lambda: ts(x, x, -256.0, A.add), lambda: act(x, x, AF.Copy, -256.0))
    part("b15")
    early = False
    v0, v15 = R(V, 16, 2064, 16), R(V, 31, 2064, 16)
    scan(b("cmp", 15, 15 + CUT), R(V, 14, 14 + CUT), R(V, 16, 16 + CUT), A.subtract, A.subtract, MID)
    scan(rev(b("cmp", 16 + CUT, 2064)), rev(R(V, 16 + CUT, 2064)), rev(R(V, 18 + CUT, 2066)), A.subtract, A.subtract, MID)
    last = q(pa, 2) if SPLIT else q(pb, 3)
    mm(group(last, [(cb("I"), v15), (cb("nI"), v0)]))
    over = 128.5 + 255.5 / 1024
    who("c15", lambda: ts(b("c15"), last, 1.0 / 1024, A.mult, over, A.add), lambda: act(b("c15"), last, AF.Copy, over, 1.0 / 1024))
    mx = "mx%d" % h
    mm([(q(pd, 1), cb("c256"), cb("cD"), True, False), (q(pd, 1), cb("ones"), cb("pX"), False, False)])
    if RUNS:
        run, wide = LV + 1, RW * (LV + 1)
        line = lambda buf, p, k: R3(buf, run * p, run * p + k)
        many = 1 if COPY else RW
        vr = R(pc, 0, LI * run * many)
        mm([(vr, cb("ones"), cb("lev", 0, LI * run * many), True, False)])
        for c in range(LV):
            mm([(R(pc, run * j + c, LI * run * many, run * many), cb("I"), R(V, 31 + 16 * LI * c, 31 + 16 * LI * (c + 1), 16), False,
                 c == LV - 1 and j == many - 1) for j in range(many)])
        first = line("Vr%d" % h, 0, run * many)
        who("Vr", lambda: cp(first, vr), lambda: act(first, vr, AF.Copy))
        for j in range(many, RW):
            cp(line("Vr%d" % h, j, run), first)
        sums = lambda buf, p, w, end: [(R(pd, 128 + p, 256, 16) + (LI * c, LI * c + LI), R3(buf, run * p + c, run * p + c + 1, 0),
                                        cb(w, 0, 8), False, end and c == LV - 1) for c in range(LV)]
        for p in range(0, 16, 2):
            mm(sums(Y, p, "bm16", False) + sums(Y, p + 1, "bm16", False))
        for k in range(0, 16, RW):
            scan(line(mx, k, wide), line(Y, k, wide), line("Vr%d" % h, 0, wide), A.min, A.max, 4096.0)
            mm([x for p in range(k, k + RW) for x in sums(mx, p, "b32", p == 15)])
    elif SPLIT:
        n, w, far = 16 // RW, 128 // SPLIT, ABS[2 * t + h - 2]
        near = 128 - w * far
        for k in range(0, 16, 4):
            mm([(R(pd, 128 + p, 256, 16) + (0, near) * far, R(Y, p, 16 * near, 16), cb("bm16", 0, 8), False, False) for p in range(k, k + 4)])
        for s in range(SPLIT):
            part("b2%d" % s)
            bank, last15 = (pc, pb)[s % 2], R(V, 31 + 16 * w * s, 31 + 16 * w * (s + 1), 16)
            if s < SPLIT - far:
                mm([(R(bank, j, w * RW, RW), cb("I"), last15, True, True) for j in range(RW)])
            for c in range(n):
                x, y = 128 * RW * c + w * RW * s, R(Y, c + 16 * w * s, 16 * w * (s + 1), n)
                if s < SPLIT - far:
                    tt(R(mx, x, x + w * RW), y, R(bank, 0, w * RW), A.max)
                else:
                    bank = (pb, FARB[h])[c % 2]
                    mm([(R(bank, 0, w * RW), cb("I"), y, True, False)])
                    mm([(R(bank, j, w * RW, RW), cb("nI"), last15, False, j == RW - 1) for j in range(RW)])
                    act(R(mx, x, x + w * RW), R(bank, 0, w * RW), AF.Abs, scale=0.5)
                if s == SPLIT - 1:
                    mm([(R(pd, 128 + c + n * j, 256, 16), R(mx, 128 * RW * c + j, 128 * RW * (c + 1), RW), cb("b32", 0, 8), False,
                         c == n - 1 and j == RW - 1) for j in range(RW)])
    else:
        n, far = 16 // RW, ABS[2 * t + h - 2]
        rows = [p for p in range(16) if p % n >= far]
        for k in range(0, len(rows), 4):
            mm([(R(pd, 128 + p, 256, 16), R(Y, p, 2048, 16), cb("bm16", 0, 8), False, False) for p in rows[k:k + 4]])
        mm([(R(pc, j, 128 * RW, RW), cb("I"), v15, True, True) for j in range(RW)])
        part("b2")
        for c in range(far):
            x, bank = R(mx, 128 * RW * c, 128 * RW * (c + 1)), R((pb, pa)[c % 2], 0, 128 * RW)
            mm([(R(pd, 128 + c + n * j, 256, 16), v15, cb("b16", 0, 8), False, False) for j in range(RW)])
            mm([(bank, cb("I"), R(Y, c, 2048, n), True, False)])
            mm([(R(bank[0], j, 128 * RW, RW), cb("nI"), v15, False, j == RW - 1) for j in range(RW)])
            act(x, bank, AF.Abs)
            mm([(R(pd, 128 + c + n * j, 256, 16), R(mx, x[1] + j, x[2], RW), cb("b16", 0, 8), False, False) for j in range(RW)])
        for c in range(far, n):
            part("b3%d" % c)
            x = R(mx, 128 * RW * c, 128 * RW * (c + 1))
            tt(x, R(Y, c, 2048, n), R(pc, 0, 128 * RW), A.max)
            mm([(R(pd, 128 + c + n * j, 256, 16), R(mx, x[1] + j, x[2], RW), cb("b32", 0, 8), False, c == n - 1 and j == RW - 1) for j in range(RW)])
        part("b4")
    km = "km%d" % h
    scan(R(km, 0, 640, 5), cb("pos"), q(pd, 1), A.add, A.min)
    part("c")
    if t < RO and not early:
        substrates(t + 1, pd)
    part("d")
    mm([(q(pa, 0, 2), cb("ones"), cb("NB"), True, False)])
    part("e")
    if t > 1:
        mm([(q(pa, 1), b("h"), cb("odd"), False, False)])
    part("f")
    mm([(R(pa, 15, 256, 16), b("c15"), cb("b24"), False, False)])
    for k in range(0, 15, 5):
        mm([(R(pa, j, 256, 16), R("cmp%d" % h, 16 + j, 2064, 16), cb("b24s"), False, j == 14) for j in range(k, k + 5)])
    scan(b("P"), R("c511", 0, 128), q(pa, 0), A.min, A.add, 1000.0)
    ts(b("L"), q(pa, 1), 128.0, A.max, 130.0, A.min)
    who("r", lambda: cp(b("r"), b("P")), lambda: act(b("r"), b("P"), AF.Copy))
    if OWNX:
        scan(b("Xr"), b("r"), b("P"), A.add, A.subtract)
    d = R("d%d" % h, 48, 688, 5)
    less(d, b("P"), b("r"))
    scan(R("d%d" % h, 0, 640, 16), R(km, 75, 715, 16), R(km, 27, 667, 16), A.max, A.subtract)
    scan(b("X"), cb("keep"), d, A.mult, A.subtract)
    walk = rev(b("Xr" if OWNX else "X"))
    scan(rev(b("Mx")), cb("neg"), walk, A.add, A.max)
    scan(rev(b("Mn")), cb("pos"), walk, A.add, A.min)
    apart(q(pb, 0), [(b("Mx"), cb("I")), (b("Mn"), cb("nI"))])
    who("LT", lambda: ts(b("LT"), q(pb, 0), 512.0, A.mult, col(3), A.add), lambda: act(b("LT"), q(pb, 0), AF.Identity, col(3), 512.0))
    ts(b("r16"), b("X"), M16, A.add, M16, A.subtract)
    even = R("X%d" % h, 0, 128, 2)
    rnd("r2", b("r2", 0, 64), even, 385.0)
    key, wt = q(pc, 2), cb("wt%d" % t)
    ramps = RAMPS[2 * t + h - 2]
    keys = {e: k for e, k in zip(sorted(set(ramps)), (key, q(pd, 2)))}
    for k in keys.values():
        part("k" + k[0])
        terms = group(k, [(b("L"), cb("pL")), (b("L"), wt), (cb("I"), es), (b("X"), cb("pX")), (cb("Sp"), b("LT")), (b("r16"), cb("mX"))])
        for lo, hi in ((0, 2), (2, 3), (3, 4), (4, 5), (5, 6)):
            mm(terms[lo:hi])
    part("g")
    more = 129 * (12288 + 77 * t) - 2048
    mm(group(q(pa, 2), table(0, es)))
    who("H", lambda: ts(b("H"), q(pa, 2), 0.125, A.mult), lambda: act(b("H"), q(pa, 2), AF.Copy, scale=0.125))
    mm(group(q(pa, 0), [(zs, cb("I")), (cb("ones"), cb("c16"))]))
    UA = R(pb, 256, 320)
    mm([(q(pb, 2), cb("ones"), cb("U0"), True, False), (UA, cb("mB"), even, False, False), (UA, cb("pB"), b("r2", 0, 64), False, False)])
    for p in range(8):
        lo, pk = 131072 * (2 * p - 7.5) - BASE + more, b("PK", 128 * p, 128 * p + 128)
        if ramps[p] == "S":
            act(pk, keys["S"], AF.Relu, -lo)
        else:
            ts(pk, keys["V"], -lo, A.add, 0.0, A.max)
        if p:
            mm([(R3(pb, p - 1, p + 1, 1, 32, 48), pk, R("w16", 16, 48), False, p == 7)])
        else:
            mm([(R(pb, 256 + p, 384, 8), pk, R("w16", 0, 16), False, p == 7)])
    who("Bs", lambda: cp(b("Bs", 0, 64), R(pb, 320, 384)), lambda: act(b("Bs", 0, 64), R(pb, 320, 384), AF.Copy))
    tt(R("v%d" % h, 0, 128, 2), b("Bs", 0, 64), UA, A.max)
    tt(R("v%d" % h, 1, 128, 2), b("Bs", 0, 64), UA, A.min)
    ts(b("w"), b("v"), 65535, A.bitwise_and)
    who("S2", lambda: ts(b("S2"), b("w"), -(20480.0 + 77 * t), A.add, 0.0, A.max), lambda: act(b("S2"), b("w"), AF.Relu, -(20480.0 + 77 * t)))
    gone = b("del", 16, 144)
    if SIG:
        step("del", gone, b("w"), 32767.5)
    else:
        ts(gone, b("w"), 32767.5, A.is_ge)
    tt(b("pr"), b("S2"), q(pa, 0), A.mult)
    ts(b("F"), b("pr"), 5, A.arith_shift_right, 4095, A.bitwise_and)
    tt(q(pa, 1), b("w"), q(pa, 0), A.max)
    tt(b("v0"), b("F"), q(pa, 1), A.add)
    ts(b("v1"), b("v0"), 65536 + 32768 + 4095, A.bitwise_and)
    ts(b("val"), b("v1"), -2048.0, A.add, 2048.0, A.min)
    rb = lambda s: b("rb", 128 * s, 128 * s + 128)
    scan(rb(0), b("del", 15, 143), cb("keep"), A.add, A.mult)
    scan(rev(rb(4)), cb("keep"), rev(gone), A.mult, A.add)
    under = (0.0, 384.0, 768.0, 1536.0, 0.0)
    for s in (1, 2, 3):
        rnd("rb", rb(s), rb(0), under[s] - (2 ** s - 1) / 2)
    mm(group(q(pd, 0), [(rb(0), cb("I")), (rb(4), cb("I"))]))
    ts(b("h"), q(pd, 0), col(5), A.is_equal)
    for j in (0, 1):
        mm(group(q(pd, 1 + j), table(1 + 2 * j, b("h"))))
    for j in (0, 1):
        tt(b("PP", 128 * j, 128 * j + 128), b("H"), q(pd, 1 + j), A.mult)
    apart(q(pd, 3), [(cb("tri"), b("h"))] + [(R("cf", 2 * j, 512, 4), b("PP", 128 * j, 128 * j + 128)) for j in (0, 1)])
    ts(b("fm"), q(pd, 3), 8192.0, A.add, 2048.0, A.min)
    tk = lambda s: b("tk", 128 * s, 128 * s + 128)
    for s, bank in enumerate((pc, pb, pa, pc, pb)):
        K = q(bank, 0)
        bit = [(rb(s), cb("m4096"))] + ([(rb(s + 1), cb("p4096"))] if s < 3 else []) if s < 4 else [(cb("I"), b("fm"))]
        moved = [(cb("Sh%d" % j), tk(j)) for j in range(s)]
        terms = bit + [(b("val"), cb("I"))] + moved if s < 4 else [(b("val"), cb("I"))] + moved[:3] + bit + moved[3:]
        apart(K, terms)
        if s < 4:
            ts(tk(s), K, 4096.0 * (2 ** s + under[s] - under[s + 1]), A.add, 2048.0, A.min)
    out = R("po", o, o + 128) if t < RO else R("pz", 128 * h, 128 * h + 128)
    ts(out, K, M1, A.add, col(9) if t < RO else M1, A.subtract)
    hop(t, h, "e")


def build():
    def load(q, sem, dst, src, dur, behind=()):
        f = lambda g, T: (g.sync if q == "Y" else g.scalar).dma_start(ap(T, dst), T[src][:, dst[1] % 4096:(dst[2] - 1) % 4096 + 1])
        op(q, DMA, [f], list(behind), [("dma_" + sem, 0, 1, 1), ("turn" + q, 0, 1, 1)])
        op("X", dur, [], [("dma_" + sem, 0, 1, 1)], [dst], sem=sem, inc=16)

    load("Z", "ld0", R("ei", 0, 256), "enz", 2000)
    parts = list(zip(PARTS, PARTS[1:]))
    for j, (a, z) in enumerate(parts):
        load("YZ"[j % 2], "lc%d" % j, R("ct", 4096 + a, 4096 + z), "cont", 2400 + 1600 * z / 4096 - (DMA + LAG) * ((j + 1) // 2 + 1))
    load("Z", "ld2", R("zi", 0, 256), "subs", 2900)
    load("Y", "lcc", R("ct", 0, 4096), "cont", 5000, [R("ct", 4096, 8192)])

    def send(src, ways):
        def f(g, T, core, topo):
            sent, tr = 0, []
            for j, (ahead, dst, sem) in enumerate(ways):
                to = T.cores[(T.rank_of(core) + ahead) % len(T.cores)]
                rid, pid, _ = topo.addr(to)
                es = topo.engines(core, to)
                es = es[len(es) * j // len(ways):len(es) * (j + 1) // len(ways)]
                m = sum(1 << e for e in es)
                sent += len(es)
                if len(ways) == 1:
                    g.remote_dma(ap(T, dst), ap(T, src), T.sem[sem], T.sem.snt, pid, rid, m)
                else:
                    tr.append(RemoteDMATransfer(dst_ids=[DstId(rid=rid, pnc=pid)], dma_engine_mask=m, remote_sem=T.sem[sem],
                                                src=ap(T, src), dst=ap(T, dst)))
            if tr:
                g.remote_dma_fused(tr, local_sem=T.sem.snt)
            return sent
        sem, first = ways[0][2], [("first", 0, 1, 1)]
        op("R", ISSUE + FIRST * (sem == "y10"), [f], [src] + first * (sem != "y10"), [("net_" + sem, 0, 1, 1)] + first * (sem == "y10"))
        for _, dst, s in ways:
            op("X", NET + 1500.0 * (s[0] == "y"), [], [("net_" + sem, 0, 1, 1)], [dst], sem=s, inc=8 // len(ways))

    def hop(t, h, kind):
        o = 256 * (t - 1) + 128 * h
        n = o + 256
        s = "%s%d%d" % (kind, t, h)
        if kind == "z":
            if t == 1 and (h == 0 or not MERGE):
                w = 256 if MERGE else 128
                send(R("eo", o, o + w), [(1, R("zo", n, n + w), "y%d%d" % (t, h))])
        elif t < RO:
            send(R("po", o, o + 128), [(2, R("eo", n, n + 128), s)])
            if h == 1 or not MERGE:
                a = o - 128 * MERGE
                send(R("po", a, o + 128), [(3, R("zo", a + 512, o + 640), "y%d%d" % (t + 1, h))])
        else:
            send(R("pz", 128 * h, 128 * h + 128), [(2, R("ef", 128 * h, 128 * h + 128), s)])

    columns()
    for a, z in parts * (not LATE):
        low, x = R("ct", 8192 + a, 8192 + z), R("ct", 4096 + a, 4096 + z)
        either(lambda: ts(low, x, -256.0, A.add), lambda: act(low, x, AF.Copy, -256.0))
    if LATE:
        low = R("m256", 0, 512)
        either(lambda: fill(low, -256.0), lambda: iota(low, [[0, 512]], -256, 0))
        for j in range(8):
            f = lambda g, T, j=j: g.sync.dma_start(T["ct"][:, 8192 + 512 * j:8704 + 512 * j], T["m256"][:, 0:512])
            op("Y", DMA, [f], [low], [("dma_lcm", j, j + 1, 1), ("turnY", 0, 1, 1)])
        op("X", 2500.0, [], [("dma_lcm", 0, 8, 1)], [R("ct", 8192, 12288)], sem="lcm", inc=128)
        f = lambda g, T: g.dma_start(T["ct"][:, 8192:12288], T["cont"][:, 0:4096], accum_op=A.add, max_dma_last_dim=4096)
        op("D", 2500.0, [f], [R("ct", 8192, 12288)], [("dma_lca", 0, 1, 1)])
        op("X", 5000.0, [], [("dma_lca", 0, 1, 1)], [R("ct", 8192, 12288)], sem="lca", inc=16)
    for h in range(NH):
        c = lambda n: R(n, 128 * h, 128 * h + 128)
        if LATE:
            either(lambda: cp(c("eo"), c("ei")), lambda: act(c("eo"), c("ei"), AF.Copy))
        else:
            ts(c("eo"), c("ei"), col(7), A.add)
        either(lambda: cp(c("zo"), c("zi")), lambda: act(c("zo"), c("zi"), AF.Copy))
    ts(R("es", 0, 256), R("eo", 0, 256), -2048.0 if LATE else col(8), A.add)
    ts(R("zs", 0, 256), R("zo", 0, 256), -2048.0, A.add)
    constants()
    for t in range(1, RO + 1):
        for h in range(NH):
            half_round(t, h, hop)
    o = 256 * RO
    part("end", RO + 1, 0)
    either(lambda: ts(R("yz", 0, 256), R("zo", o, o + 256), col(7), A.subtract),
           lambda: act(R("yz", 0, 256), R("zo", o, o + 256), AF.Identity, col(10)))
    for src, dst, parts in (("yz", "ysub", 1), ("ef", "yenz", NH)):
        w = 256 // parts
        for h in range(parts):
            e = "Z" if parts > 1 and h == 0 else "Y"
            op(e, DMA, [lambda g, T, src=src, dst=dst, c=w * h, w=w, e=e:
                        (g.sync if e == "Y" else g.scalar).dma_start(T[dst][:, c:c + w], T[src][:, c:c + w])],
               [R(src, w * h, w * h + w)], [], sem="out", inc=16)


def analyse():
    hist = {}
    for i, x in enumerate(OPS):
        deps = {}
        acc = [(r[0], cover(r), False) for r in x["r"]] + [(w[0], cover(w), True) for w in x["w"]]
        for buf, bits, wr in acc:
            psum = buf in SCRATCH and SCRATCH[buf][0] == "psum"
            for (other, w2, j) in hist.get(buf, []):
                over = bits & other != 0
                y = OPS[j]
                if psum and (y["e"] != x["e"] or x["e"] == "VS"):
                    deps[j] = True
                elif psum and x["e"] == "P":
                    deps[j] = deps.get(j, False)
                elif over and w2 and not wr:
                    deps[j] = True
                elif over and (wr or w2):
                    deps[j] = deps.get(j, False) or y["e"] != x["e"] or x["e"] != "P"
        x["deps"] = deps
        for buf, bits, wr in acc:
            lst = hist.setdefault(buf, [])
            if wr and len(x["w"][0]) == 4 and buf[:2] != "ps":
                lst[:] = [e for e in lst if e[0] & ~bits or e[2] == i]
            lst.append((bits, wr, i))


QN = {"G": "g", "R": "g", "D": "g", "Z": "S"}


def schedule(lead=LEAD, tries=TRIES, seed=1, moves=MOVES):
    n = len(OPS)
    pred, succ, half, tail, above = [], [[] for _ in range(n)], [0] * n, [0.0] * n, []
    for x in OPS:
        p, seen, every = [], 0, 0
        for j in sorted(x["deps"], reverse=True):
            if not seen >> j & 1:
                p.append((j, LAG if x["deps"][j] else 0.0))
                seen |= above[j] if x["deps"][j] else 0
            every |= above[j] | 1 << j
        pred.append(p)
        above.append(every)
    for i, p in enumerate(pred):
        for j, w in p:
            succ[j].append((i, w))
    for (a, k), (z, _) in zip(MARK, MARK[1:] + [(n, 0)]):
        half[a:z] = [k % 2] * (z - a)
    can = [{QN.get(e, e): d for e, (d, _) in x["alt"].items()} if "alt" in x else {QN.get(x["e"], x["e"]): x["d"]} for x in OPS]
    for i in range(n - 1, -1, -1):
        tail[i] = min(can[i].values()) + max([tail[s] + w for s, w in succ[i]], default=0.0)
    x = [seed]

    def draw():
        x[0] = (x[0] * 1103515245 + 12345) % 2 ** 31
        return x[0] / 2 ** 31

    def place(pri, forward, on, bias=0.0):
        up, down = (pred, succ) if forward else (succ, pred)
        pri = list(pri)
        for i in (range(n) if forward else range(n - 1, -1, -1)):
            for j, _ in up[i]:
                if pri[j] >= pri[i]:
                    pri[i] = pri[j] + 1e-3
        t0, st, busy, got = [0.0] * n, [0.0] * n, {e: ([], []) for e in "VSPgY"}, [""] * n
        for i in sorted(range(n), key=lambda i: pri[i]):
            best = None
            for e in (on[i] if on and on[i] else can[i]):
                d, t, j = can[i][e], t0[i], 0
                if e != "X":
                    a, z = busy[e]
                    j = len(z)
                    while j and z[j - 1] > t:
                        j -= 1
                    while j < len(a) and a[j] < t + d:
                        t = max(t, z[j])
                        j += 1
                c = t + d + (bias if e == "V" else 0.0)
                if best is None or c < best[0]:
                    best = (c, e, t, d, j)
            _, e, t, d, j = best
            if e != "X":
                busy[e][0].insert(j, t)
                busy[e][1].insert(j, t + d)
            st[i], got[i] = t, e
            t += d
            for s, w in down[i]:
                if t + w > t0[s]:
                    t0[s] = t + w
        return st, got

    def passes(pri, k, on, bias):
        best = None
        for j in range(k):
            st, got = place(pri, True, on, bias)
            end = [st[i] + can[i][got[i]] for i in range(n)]
            if best is None or max(end) < best[0]:
                best = (max(end), st, got)
            if j < k - 1:
                back, _ = place([-e for e in end], False, got)
                pri = [-(back[i] + can[i][got[i]]) for i in range(n)]
        return best

    def other(far, jump, pace, more):
        return [{e: d * far if e == "X" and d == NET else d * jump * pace if y.get("g") else
                 (d + more * (e == "S")) * pace if e in "VSP" or y["e"] != "R" and e == "g" else d for e, d in c.items()} for y, c in zip(OPS, can)]

    sets = [(other(far, jump, pace, more), lag / LAG, pace) for far, jump, pace, lag, more in OTHER]

    def rate(new):
        tot, st, on = new
        order = sorted(range(n), key=lambda i: (st[i], i))
        for c, k, pace in sets:
            end, free = [0.0] * n, dict.fromkeys("VSPgYX", 0.0)
            for i in order:
                e = on[i]
                t = free[e]
                for j, w in pred[i]:
                    if end[j] + k * w > t:
                        t = end[j] + k * w
                end[i] = t + c[i][e]
                if e != "X":
                    free[e] = end[i]
            tot += max(end) / pace
        return tot / (1 + len(sets)), st, on

    best = min((rate(passes([lead * half[i] - tail[i] for i in range(n)], 8, None, bias)) for bias in (0.0, 150.0, 400.0)), key=lambda y: y[0])
    for _ in range(tries):
        lo = draw() * (best[0] + 10000) - 10000
        hi, size = lo + 3000 + 27000 * draw(), 3000 * draw() ** 2
        on = ["" if lo < s < hi and draw() < 0.5 else e for s, e in zip(best[1], best[2])]
        new = rate(passes([s + size * (draw() - 0.5) if lo < s < hi else s for s in best[1]], 2, on, 600 * draw() - 100))
        if new[0] <= best[0]:
            best = new

    sets.insert(0, (can, 1.0, 1.0))
    on = list(best[2])
    order = sorted(range(n), key=lambda i: (best[1][i], i))
    idle = dict.fromkeys("VSPgYX", 0.0)

    def reach(part, links, c, k):
        end, free = {}, dict(idle)
        for i in part:
            e = on[i]
            t = free[e]
            for j, w in links[i]:
                if end[j] + k * w > t:
                    t = end[j] + k * w
            end[i] = t + c[i][e]
            if e != "X":
                free[e] = end[i]
        return end, free

    for sweep in range(moves):
        heat = HEAT * (1 - sweep / moves) ** 2 + 2.0
        a = int(draw() * (n + WIDE)) - WIDE
        a, z = max(a, 0), min(a + WIDE + int(4 * WIDE * draw() ** 2), n)
        win = order[a:z]
        if len(win) < 10:
            continue
        inside = set(win)
        inn = {i: [(j, w) for j, w in pred[i] if j in inside] for i in win}
        before = {i: [j for j, _ in inn[i]] for i in win}
        after = {i: [j for j, _ in succ[i] if j in inside] for i in win}
        edges = []
        for c, k, pace in sets:
            end, free = reach(order[:a], pred, c, k)
            rest, late = reach(order[:z - 1:-1] if z < n else [], succ, c, k)
            tail = lambda i: max([rest[j] + k * w for j, w in succ[i] if j in rest], default=0.0)
            past = max([end[i] + tail(i) for i in order[max(0, a - 3 * WIDE):a]], default=0.0)
            edges.append((c, pace, free, late, past, {i: (max([end[j] + k * w for j, w in pred[i] if j in end], default=0.0), tail(i),
                                                          [(j, k * w) for j, w in inn[i]]) for i in win}))

        def length():
            tot = 0.0
            for c, pace, free, late, most, near in edges:
                free, end = dict(free), {}
                for i in win:
                    e = on[i]
                    t, rest, ins = near[i]
                    if free[e] > t:
                        t = free[e]
                    for j, w in ins:
                        if end[j] + w > t:
                            t = end[j] + w
                    end[i] = t = t + c[i][e]
                    if e != "X":
                        free[e] = t
                    if t + rest > most:
                        most = t + rest
                ends = [free[e] + late[e] for e in "VSPgY"]
                tot += (max(most, max(ends)) + SOFT * (ends[0] + ends[1] + ends[2])) / pace
            return tot

        now = length()
        least, kept, m = now, (list(win), [on[i] for i in win]), len(win)
        for _ in range(STEPS):
            p = int(draw() * m)
            v = win[p]
            was = on[v]
            if was == "X":
                continue
            if len(can[v]) > 1 and draw() < 0.3:
                es = [e for e in can[v] if e != was]
                on[v] = es[int(draw() * len(es))]
            e, j, skip = on[v], p, 1 + int(12 * draw() ** 4) - (on[v] != was)
            if draw() < 0.5:
                while skip and j and win[j - 1] not in before[v]:
                    j -= 1
                    skip -= on[win[j]] == e
            else:
                while skip and j < m - 1 and win[j + 1] not in after[v]:
                    j += 1
                    skip -= on[win[j]] == e
            if j == p and e == was:
                continue
            win.insert(j, win.pop(p))
            new = length()
            if new <= now or draw() < math.exp((now - new) / heat):
                now = new
                if now < least:
                    least, kept = now, (list(win), [on[i] for i in win])
            else:
                win.insert(p, win.pop(j))
                on[v] = was
        order[a:z] = kept[0]
        for i, e in zip(*kept):
            on[i] = e
    tot = sum(max(reach(order, pred, c, k)[0].values()) / pace for c, k, pace in sets) / len(sets)
    return order, tot, [e.upper() if "alt" in y else y["e"] for e, y in zip(on, OPS)]
    d = [can[i][on[i]] for i in range(n)]
    line = {e: [] for e in "VSPgYX"}
    for i in sorted(range(n), key=lambda i: (best[1][i], i)):
        line[on[i]].append(i)
    line["X"] = []
    waits = [len(p) for p in pred]

    def lengths():
        nxt, left, r, t = [-1] * n, list(waits), [0.0] * n, [0.0] * n
        for q in line.values():
            for u, v in zip(q, q[1:]):
                nxt[u] = v
                left[v] += 1
        top = [i for i in range(n) if not left[i]]
        for i in top:
            e = r[i] + d[i]
            for s, w in succ[i]:
                if e + w > r[s]:
                    r[s] = e + w
                left[s] -= 1
                if not left[s]:
                    top.append(s)
            s = nxt[i]
            if s >= 0:
                if e > r[s]:
                    r[s] = e
                left[s] -= 1
                if not left[s]:
                    top.append(s)
        if len(top) < n:
            return None
        for i in reversed(top):
            m = t[nxt[i]] if nxt[i] >= 0 else 0.0
            for s, w in succ[i]:
                if t[s] + w > m:
                    m = t[s] + w
            t[i] = m + d[i]
        return r, t, max(t)

    r, t, now = lengths()
    least, banned = now, {}
    for step in range(moves):
        offers = []
        at = {v: j for q in line.values() for j, v in enumerate(q)}
        for v in range(n):
            if r[v] + t[v] < now - 0.01 or on[v] == "X" or banned.get(v, -1) > step or draw() < 0.5:
                continue
            head = max([r[j] + d[j] + w for j, w in pred[v]], default=0.0)
            rest = max([t[s] + w for s, w in succ[v]], default=0.0)
            for e, dv in can[v].items():
                q = line[e]
                own = at[v] if e == on[v] else -1
                lo, hi = 0, len(q)
                while lo < hi:
                    mid = (lo + hi) // 2
                    if r[q[mid]] + d[q[mid]] > head:
                        hi = mid
                    else:
                        lo = mid + 1
                j = lo
                while j <= len(q):
                    u = j - 1 if j - 1 != own else j - 2
                    w = j if j != own else j + 1
                    if j != own and j != own + 1 or own < 0:
                        a = max(head, r[q[u]] + d[q[u]] - (d[v] if own >= 0 and u > own else 0.0)) if u >= 0 else head
                        z = max(rest, t[q[w]] - (d[v] if own >= 0 and w < own else 0.0)) if w < len(q) else rest
                        offers.append((a + dv + z + (dv - d[v]) * 0.3 + 40 * draw(), v, e, j))
                    if j == len(q) or t[q[j]] <= rest and j != own or above[q[j]] >> v & 1:
                        break
                    j += 1
        if not offers:
            banned.clear()
            continue
        offers.sort()
        for _, v, e, j in offers[:6]:
            was, old = on[v], at[v]
            line[was].pop(old)
            line[e].insert(j - (e == was and j > old), v)
            on[v], d[v] = e, can[v][e]
            new = lengths()
            if new:
                r, t, now = new
                banned[v] = step + 4 + int(14 * draw())
                break
            line[e].remove(v)
            line[was].insert(old, v)
            on[v], d[v] = was, can[v][was]
        if now < least + NEAR:
            least = min(least, now)
            new = rate((now, r, on))
            if new[0] < best[0]:
                best = (new[0], r, list(on))
    names = [e.upper() if "alt" in y else y["e"] for e, y in zip(best[2], OPS)]
    return sorted(range(n), key=lambda i: (best[1][i], i)), best[0], names


def refine(order, names, seed=1, laps=None, drift=False):
    n = len(OPS)
    code = {"V": 0, "S": 1, "P": 2, "G": 3, "R": 3, "D": 3, "Y": 4, "Z": 1, "X": 5}
    pred, succ, above = [], [[] for _ in range(n)], []
    for x in OPS:
        p, seen, every = [], 0, 0
        for j in sorted(x["deps"], reverse=True):
            if not seen >> j & 1:
                p.append((j, x["deps"][j]))
                seen |= above[j] if x["deps"][j] else 0
            every |= above[j] | 1 << j
        pred.append(p)
        above.append(every)
    for i, p in enumerate(pred):
        for j, w in p:
            succ[j].append((i, w))
    can = [sorted(x["alt"]) if "alt" in x else [x["e"]] for x in OPS]

    def lasts(x, e, sc, gc, pc, fv, fs, net, first):
        d = x["alt"][e][0] if "alt" in x else x["d"]
        if x.get("g"):
            return (d - 60) / (GC * SC) * gc * sc + 30 + (fv if e == "V" else fv + 15)
        if e == "V":
            return (d - FV) / SC * sc + fv
        if e == "S":
            return (d - FS) / SC * sc + fs
        if e == "P":
            return d / PC * pc
        if e == "G":
            return d / SC * sc * 1.1
        return net if d == NET else ISSUE + first if d == ISSUE + FIRST else d

    sets = [([{e: lasts(x, e, sc, gc, pc, fv, fs, net, first) for e in c} for x, c in zip(OPS, can)],
             [[(j, lag * w) for j, w in p] for p in pred], [[(j, lag * w) for j, w in p] for p in succ], pace)
            for sc, gc, pc, fv, fs, lag, net, first, pace in SETS]
    x = [seed]

    def draw():
        x[0] = (x[0] * 1103515245 + 12345) % 2147483648
        return x[0] / 2147483648

    on = list(names)
    q = [code[e] for e in on]

    def reach(part, links, c):
        end, free = {}, [0.0] * 6
        for i in part:
            e = q[i]
            t = free[e]
            for j, w in links[i]:
                if end[j] + w > t:
                    t = end[j] + w
            end[i] = t = t + c[i][on[i]]
            if e < 5:
                free[e] = t
        return end, free

    def total(order):
        r = [max(reach(order, pr, c)[0].values()) / p for (c, pr, _, _), p in zip(sets, PACE)]
        w = [math.exp((y - max(r)) / EVEN) + 0.2 for y in r]
        pool[:] = [y[:3] + (p * sum(w) / len(w) / v,) for y, p, v in zip(sets, PACE, w)]
        return (sum(r) / len(r) + sum(sorted(r)[-4:]) / 4) / 2

    if not PACE:
        PACE.extend(max(reach(order, pr, c)[0].values()) / 85000.0 for c, pr, _, _ in sets)
    pool = [y[:3] + (p,) for y, p in zip(sets, PACE)]

    def anneal(a, z, heat, steps):
        win = order[a:z]
        m = len(win)
        inside = {i: k for k, i in enumerate(win)}
        away = [i for i in win if on[i] == "X"]
        for k, i in enumerate(away):
            q[i] = 5 + k
        before = {i: {j for j, _ in pred[i] if j in inside} for i in win}
        after = {i: {j for j, _ in succ[i] if j in inside} for i in win}
        edges = []
        for c, pr, su, pace in sets[12:]:
            end, free = reach(order[:a], pr, c)
            rest, late = reach(order[:z - 1:-1] if z < n else [], su, c)
            tail = lambda i: max([rest[j] + w for j, w in su[i] if j in rest], default=0.0)
            past = max([end[i] + tail(i) for i in order[max(0, a - 120):a]], default=0.0)
            near = {i: (inside[i], max([end[j] + w for j, w in pr[i] if j in end], default=0.0), tail(i),
                        [(inside[j], w) for j, w in pr[i] if j in inside], c[i]) for i in win}
            edges.append((near, 1.0 / pace, late, [0.0] * m, [(free[:5] + [0.0] * len(away), past)] * (m // 8 + 2)))
        undo = []

        def length(lo, most_of):
            lo -= lo % 8
            tot = []
            parts = [win[p:p + 8] for p in range(lo, m, 8)]
            del undo[:]
            for near, k, late, end, marks in edges:
                free, most = marks[lo // 8]
                free = list(free)
                undo.append((end, end[:], marks, marks[:]))
                p = lo // 8
                for part in parts:
                    marks[p] = (free[:], most)
                    p += 1
                    for i in part:
                        e = q[i]
                        y, t, rest, ins, c = near[i]
                        if free[e] > t:
                            t = free[e]
                        for j, w in ins:
                            if end[j] + w > t:
                                t = end[j] + w
                        end[y] = free[e] = t = t + c[on[i]]
                        if t + rest > most:
                            most = t + rest
                a, b, d = free[0] + late[0], free[1] + late[1], free[2] + late[2]
                tot.append((max(most, a, b, d, free[3] + late[3], free[4] + late[4]) + SOFT * (a + b + d)) * k)
                if most_of and tot[0] > most_of:
                    return None
            return tot

        each = length(0, 0)
        now = least = sum(each)
        kept = (list(win), [on[i] for i in win])
        for _ in range(steps):
            p = int(draw() * m)
            v = win[p]
            was = on[v]
            if was == "X" or was == "P" and draw() < 0.4:
                continue
            if len(can[v]) > 1 and draw() < 0.3:
                es = [e for e in can[v] if e != was]
                on[v] = es[int(draw() * len(es))]
                q[v] = code[on[v]]
            e, j, skip = q[v], p, 1 + int(12 * draw() ** 4) - (on[v] != was)
            if draw() < 0.5:
                no = before[v]
                while skip and j and win[j - 1] not in no:
                    j -= 1
                    skip -= q[win[j]] == e
            else:
                no = after[v]
                while skip and j < m - 1 and win[j + 1] not in no:
                    j += 1
                    skip -= q[win[j]] == e
            if skip and on[v] == was or j == p and on[v] == was:
                on[v], q[v] = was, code[was]
                continue
            win.insert(j, win.pop(p))
            lo = min(p, j)
            room = -heat * math.log(draw() + 1e-9)
            new = length(lo, each[0] + room + SPARE)
            if new is not None and sum(new) <= now + room:
                each, now = new, sum(new)
                if now < least:
                    least, kept = now, (list(win), [on[i] for i in win])
            else:
                win.insert(p, win.pop(j))
                on[v], q[v] = was, code[was]
                for end, old, marks, were in undo:
                    end[:], marks[:] = old, were
        if drift:
            kept = (win, [on[i] for i in win])
        order[a:z] = kept[0]
        for i, e in zip(*kept):
            on[i], q[i] = e, code[e]

    twin = {}
    for i, y in enumerate(OPS):
        twin[y["tag"]] = i

    def lay(src, dst):
        end, _ = reach(order, sets[0][1], sets[0][0])
        at = lambda t: end[twin[(t, 0, "b", 0)]]
        pri = [end[i] - sets[0][0][i][on[i]] for i in range(n)]
        new, to = list(pri), list(on)
        for i, y in enumerate(OPS):
            t = y["tag"]
            j = twin.get((src,) + t[1:]) if t[0] == dst else None
            if j is not None and can[i] == can[j]:
                new[i], to[i] = pri[j] + at(dst) - at(src), on[j]
            elif t[0] > dst:
                new[i] += at(src + 1) - at(src) - at(dst + 1) + at(dst) if max(src, dst) < RO else 0.0
        for i in range(n):
            for j, _ in pred[i]:
                if new[j] >= new[i]:
                    new[i] = new[j] + 1e-3
        return sorted(range(n), key=lambda i: new[i]), to

    def span(t):
        at = [k for k, i in enumerate(order) if OPS[i]["tag"][0] == t]
        return at[0], at[-1]

    def sweep(lo, hi, count, hot):
        for s in range(count):
            a = lo - WIDE + int(draw() * (hi - lo + WIDE))
            a, z = max(a, 0), min(a + WIDE + int(4 * WIDE * draw() ** 2), n)
            if z - a >= 10:
                anneal(a, z, hot * (1 - s / count) ** 2 + 2.0, STEPS)

    log = []
    for count, hot, tries in (laps or LAPS):
        sweep(0, n, count, hot)
        log.append(total(order))
        for _ in range(tries):
            src, dst = 1 + int(draw() * RO), 1 + int(draw() * RO)
            if src == dst:
                continue
            old = (list(order), list(on), total(order))
            order[:], on[:] = lay(src, dst)
            q[:] = [code[e] for e in on]
            sweep(*span(dst), MEND, hot / 2)
            if total(order) > old[2]:
                order[:], on[:] = old[:2]
                q[:] = [code[e] for e in on]
            log.append((src, dst, total(order)))
    log = [round(max(reach(order, pr, c)[0].values())) for c, pr, _, pace in sets]
    log.append(round(sum(y["d"] for y, e in zip(OPS, on) if y.get("g") and e == "V") / 570.0))
    return order, total(order), on, log


PLAN = []


def plan():
    if not PLAN:
        build()
        analyse()
        some = [schedule(lead=lead, moves=0) for lead in LEADS]
        for count, hot, keep, drift in LAPS:
            some = sorted((refine(x[0], x[2], laps=[(count, hot, 0)], drift=drift) for x in some), key=lambda x: x[1])[:keep]
        PLAN.extend(some[0])
    return PLAN[0]


QS = {"P": "qP", "V": "qV", "S": "qS", "G": "qG"}


def rank_program(g, core, T, topo):
    if T.rank_of(core) is None:
        return
    order = plan()
    queue = {"P": g.tensor, "V": g.vector, "S": g.scalar, "G": g, "R": g, "D": g, "Y": g.sync, "Z": g.scalar}
    cnt, done, know, clock, sent = {}, {}, {}, {}, 0
    for i in order:
        x = OPS[i]
        e = PLAN[2][i]
        if e == "X":
            done[i] = (x["sem"], x["inc"])
            clock[i] = {}
            continue
        kn = know.setdefault(QN.get(e, e), {})
        need = {}
        for j, w in x["deps"].items():
            if w and done.get(j) is not None:
                s, v = done[j]
                if need.get(s, (0, 0))[0] < v:
                    need[s] = (v, j)
        for s, (v, j) in sorted(need.items(), key=lambda z: -z[1][1]):
            if kn.get(s, 0) >= v:
                continue
            queue[e].wait_ge(T.sem[s], v)
            for s2, v2 in clock[j].items():
                kn[s2] = max(kn.get(s2, 0), v2)
            kn[s] = max(kn.get(s, 0), v)
        clock[i] = dict(kn)
        if e in QS:
            s = QS[e]
            for f in x["alt"][e][1] if "alt" in x else x["f"]:
                f(g, T).then_inc(T.sem[s], 1)
                cnt[s] = cnt.get(s, 0) + 1
            done[i] = (s, cnt[s])
        elif e == "R":
            for f in x["f"]:
                sent += f(g, T, core, topo)
            done[i] = None
        else:
            sem = x["sem"]
            if sem is None:
                sem = OPS[i]["w"][0][0][4:]
            for f in x["f"]:
                f(g, T).then_inc(T.sem[sem], 16)
                cnt[sem] = cnt.get(sem, 0) + 16
            done[i] = None
    for s in list(QS.values()) + ["out"] + LOADS:
        if cnt.get(s, 0):
            g.sync.wait_ge(T.sem[s], cnt[s])
    g.wait_ge(T.sem.snt, sent)
